import numpy as np, ml_dtypes
CORES = [113,118,241,246]
N = 4
BF = ml_dtypes.bfloat16
def gentries(a):
    return np.ascontiguousarray(a.reshape(8, 16, -1).transpose(0, 2, 1)).reshape(8, -1)
def gtable(e):
    e = np.asarray(e); return np.ascontiguousarray(e.reshape(8, -1, 16).transpose(0, 2, 1)).reshape(128, -1).astype(np.int32)
E, T, C, RO = 2048, 256, 4, 3
A = N * T
VM = 0.125
def floats(rng, far):
    def size(n):
        if far: return np.exp2(-rng.integers(0, 3, (N, 8, 1, n))).astype(np.float32)
        return 0.75 + 0.25 * rng.random((N, 8, 1, n), dtype=np.float32)
    x = 0.25 + 0.75 * rng.random((N, 8, 16, T), dtype=np.float32)
    if far: x = x * size(T)
    u = 0.1875 * (0.5 + 0.5 * rng.random((N, 8, 16, E), dtype=np.float32)) * size(E)
    v = VM * (0.5 + 0.5 * rng.random((N, 8, 16, E), dtype=np.float32)) * size(E)
    w = np.exp(1.5 * rng.standard_normal((N, 128, 128))); w = w * np.reciprocal(np.add.reduce(w, axis=1, keepdims=True))
    one = np.arange(128)[None, :, None] == np.argsort(rng.random((N, 128)), axis=1)[:, None, :]
    share = 0.5 + 0.45 * rng.random((N, 1, 128))
    return x, u, v, (1.3 + 0.08 * rng.random((N, 1, 128))) * (share * one + (1.0 - share) * w)
def lone(rng, fl, b):
    x, u, v, m = fl; a = int(rng.integers(0, N)); c = (a + 1) % N
    u[:, b] = 0.1875 * (0.9375 + 0.0625 * rng.random((N, 16, E)))
    v[:, b] = VM * (0.875 + 0.125 * rng.random((N, 16, E)))
    level = np.where(np.argsort(rng.random(T)) < 3 * T // 8, 0.18 + 0.07 * rng.random(T), 0.0625 + 0.0125 * rng.random(T))
    x[a, b] = np.maximum(level[None, :] * (0.9375 + 0.125 * rng.random((16, T))), 0.0625)
    i = 16 * b + np.arange(16); m[a] = 0.0625 * m[a]; m[a][:, i] = 0.0
    m[a][np.ix_(i, i)] = 1.38 * (0.9 * np.eye(16) + 0.1 * 0.0625)
    p = np.argsort(rng.random(128))[:16]; w = 0.5 + 0.5 * rng.random((128, 16))
    m[c][:, p] = 1.38 * w * np.reciprocal(np.add.reduce(w, axis=0, keepdims=True))
    return x, u, v, m
def small(rng):
    q = rng.integers(-4, 5, (N, 8, 16, T), dtype=np.int32); q[:, :, 15] = rng.integers(-8, 33, (N, 8, T))
    k = rng.integers(-4, 5, (N, 8, 16, E), dtype=np.int32); k[:, :, 15] = rng.integers(-2, 3, (N, 8, E))
    return q, k, rng.integers(0, E, (N, 8, C, A), dtype=np.int32)
def pack(fl, q, k, n):
    x, u, v, m = fl
    return {"x0": x.reshape(N, 128, T).astype(BF), "rq": q.reshape(N, 128, T).astype(np.float32).astype(BF), "ke": k.reshape(N, 128, E).astype(np.float32).astype(BF),
            "ue": u.reshape(N, 128, E).astype(BF), "ve": v.reshape(N, 128, E).astype(BF), "nm": np.stack([gtable(a.reshape(8, -1)) for a in n]), "mm": m.astype(np.float32).astype(BF)}
def route(q, k, n):
    k = k.astype(np.int32); n = n.astype(np.int32)
    qa = np.ascontiguousarray(q.astype(np.int32).transpose(1, 2, 0, 3)).reshape(8, 16, A)
    h = np.zeros((8, A), np.int32); wins = []; names = []
    for l in range(RO):
        nn = (n + h[None, :, None, :]) & (E - 1); w = np.zeros((N, 8, A), np.int32)
        for s in range(N):
            c = np.take_along_axis(k[s], nn[s].reshape(8, 1, C * A), 2).reshape(8, 16, C, A)
            score = np.add.reduce(c * qa[:, :, None, :], axis=1)
            best = np.argmax(score, axis=1)
            w[s] = np.take_along_axis(nn[s], best[:, None, :], 1)[:, 0]
            count = np.bincount((w[s] + E * np.arange(8)[:, None]).reshape(-1), minlength=8 * E).reshape(8, E)
            k[s, :, 15] += np.sign(1 - count).astype(np.int32)
        h = np.roll(np.add.reduce(w, axis=0) & (E - 1), 1, axis=0).astype(np.int32)
        wins.append(w); names.append(nn)
    return wins, names, k[:, :, 15]
def setup_inputs(rng):
    return pack(floats(rng, False), *small(rng))
def setup_inputs_spread(rng):
    q = np.rint(np.exp2(5 * rng.random((N, 8, 1, T))) * (2 * rng.random((N, 8, 16, T)) - 1)).astype(np.int32)
    q[:, :, 15] = np.rint(np.exp2(5 * rng.random((N, 8, T))))
    k = np.rint(np.exp2(5 * rng.random((N, 8, 1, E))) * (2 * rng.random((N, 8, 16, E)) - 1)).astype(np.int32)
    k[:, :, 15] = np.where(rng.random((N, 8, E)) < 0.5, rng.integers(-2, 3, (N, 8, E)), rng.integers(-32, 33, (N, 8, E)))
    n = np.minimum((E * rng.random((N, 8, C, A)) ** 3).astype(np.int32), E - 1)
    return pack(floats(rng, True), q, k, n)
def setup_inputs_ends(rng):
    q = (64 * rng.integers(0, 2, (N, 8, 16, T)) - 32).astype(np.int32); a = rng.random((N, 8, 1, T))
    q = np.where(a < 0.35, 32, np.where(a < 0.5, -32, q)); q[..., T - 1] = 32; q[..., 0] = -32
    k = (64 * rng.integers(0, 2, (N, 8, 16, E)) - 32).astype(np.int32); a = rng.random((N, 8, 1, E))
    k = np.where(a < 0.3, 32, np.where(a < 0.4, -32, k))
    kind = rng.integers(0, 3, (N, 8)); kind[N - 1, 7] = 0; kind[0, 0] = 1; kind[0, 1] = 2
    k[..., E - 1] = np.where((kind < 2)[:, :, None], 32, k[..., E - 1]); k[..., 0] = np.where((kind == 0)[:, :, None], 32, np.where((kind == 1)[:, :, None], -32, k[..., 0]))
    n = (E - 1) * rng.integers(0, 2, (N, 8, C, A))
    n[:, 8 - RO:7, :, A - 1] = E - 1; n[:, 7, :, A - 1] = (E - 1) * (np.arange(C) % 2)
    wins, names, b = route(q, k, n)
    for s in range(N):
        for g in range(8):
            used = np.zeros(E, bool); last = np.zeros(E, bool)
            for l in range(RO - 1): used[names[l][s, g].reshape(-1)] = True
            last[names[RO - 1][s, g].reshape(-1)] = True
            e = np.nonzero(last & ~used)[0]
            k[s, g][:, e] = np.where(rng.random(e.size) < 0.7, 32, -32)
            if g == 7:
                e = names[RO - 1][s, g, :, A - 1]; k[s, g][:, e[~used[e]]] = 32
    return pack(floats(rng, False), q, k, n)
def setup_inputs_crowd(rng):
    q, k, n = small(rng); q[:, :6, 15] = rng.integers(1, 33, (N, 6, T)); k[:, :6, :15] = rng.integers(-4, 5, (N, 6, 15, 1))
    o = rng.permutation(A); n[:, :2] = rng.integers(0, E, (N, 2, C, 1))
    for s in range(N):
        for g in range(2, 8):
            p = rng.permutation(E); v = n[s, g]
            if g < 4:
                v[:] = p[:C, None]; v[:, o[0]] = p[C:2 * C]
            elif g < 6:
                v[:, o[:256]] = p[:C, None]; v[:, o[256:511]] = p[C:2 * C, None]; v[:, o[511:]] = p[rng.integers(2 * C, E, (C, A - 511))]
            else:
                v[:] = p[rng.integers(0, 4, (C, A))]
    return pack(floats(rng, False), q, k, n)
def setup_inputs_calm(rng):
    q, k, n = small(rng); q[:, :, 0] = rng.integers(8, 17, (N, 8, T))
    a = rng.integers(1, 33, (N, 8, T)); q[:, :, 15] = np.where(rng.random((N, 8, T)) < 0.125, -a, a)
    tp = np.argsort(rng.random((8, A)), axis=1)[:, :16]
    for g in range(8): q[tp[g] // T, g, :, tp[g] % T] = np.array([1, 1] + [32] * 13 + [1])
    for s in range(0, N, 2):
        for g in range(8):
            size = np.argsort(rng.random((A // 4, 4)), axis=1).reshape(-1) + 1
            fam = np.repeat(np.arange(size.size), size)[:A]; F = int(fam[-1]) + 1
            p = rng.permutation(E); ex = p[:F * C].reshape(F, C); pair = p[E - 16:].reshape(2, 8)
            n[s, g] = ex[fam[rng.permutation(A)]].T
            k[s, g][:, ex] = rng.integers(-4, 5, (16, F, 1))
            k[s, g, 15][ex] = np.clip(rng.choice(np.array([0, 0, 0, -32, 32]), (F, 1)) + rng.integers(-2, 3, (F, C)), -32, 32)
            lead = rng.random(F) < 0.25; d = rng.integers(0, C, F)
            k[s, g, 0][ex[lead]] = np.where(np.arange(C)[None, :] == d[lead][:, None], 32, -32)
            k[s, g][:, pair[0]] = np.array([32, 31] + [32] * 13 + [-32])[:, None]
            k[s, g][:, pair[1]] = np.array([1 - RO, 1 - RO] + [32] * 13 + [32])[:, None]
            n[s, g][:, tp[g]] = np.where(np.arange(C)[:, None] % 2 == 0, np.repeat(pair[0], 2)[None, :], np.repeat(pair[1], 2)[None, :])
        k[s + 1] = k[s][:, :, (-np.arange(E)) % E]; n[s + 1] = (-n[s]) % E
    return pack(floats(rng, False), q, k, n)
def setup_inputs_corners(rng):
    q, k, n = small(rng)
    q[:, 0] *= (rng.random((N, 1, T)) < 0.5)
    n[:, 1] = n[:, 1, :1]; n[:, 2, C // 2:] = n[:, 2, :C // 2].copy()
    n[:, 3] = rng.choice(np.array([0, 1, E // 2, E - 1]), (N, C, A))
    k[:, 4, :15] = 0; q[:, 4, 15] = rng.choice(np.array([0, 1, -1, 32, -32]), (N, T))
    k[:, 5, :15] = k[:, 5, :15, :1].copy(); q[:, 5, 15] *= (rng.random((N, T)) < 0.75)
    q[:, 6] = rng.integers(-32, 33, (N, 16, T)); k[:, 6] = rng.integers(-32, 33, (N, 16, E))
    k[:, 7] = k[:, 7][:, :, np.arange(E) // 2 * 2]
    k[:, :, 15, 0] = 32; k[:, :, 15, E - 1] = -32
    return pack(lone(rng, floats(rng, False), 6), q, k, n)
def check_ranges(d):
    bad = []
    for a, lo, hi in (("rq", -32, 32), ("ke", -32, 32), ("nm", 0, E - 1)):
        v = np.asarray(d[a]).astype(np.float64)
        if not bool(np.all((v >= lo) & (v <= hi))): bad.append("range of " + a)
        elif not bool(np.all(np.floor(v) == v)): bad.append("whole numbers of " + a)
    for a, lo, hi in (("x0", 0.0625, 1.0), ("ue", 0.0234375, 0.1875), ("ve", 0.125 * VM, VM), ("mm", 0.0, 1.4)):
        v = np.asarray(d[a]).astype(np.float64)
        if not bool(np.all((v >= lo) & (v <= hi))): bad.append("range of " + a)
    if not bool(np.all(np.add.reduce(np.asarray(d["mm"]).astype(np.float64), axis=1) <= 1.4)): bad.append("column sums of mm")
    return bad
def reference(x0, rq, ke, ue, ve, nm, mm):
    q = rq.astype(np.float32).astype(np.int32).reshape(N, 8, 16, T); k = ke.astype(np.float32).astype(np.int32).reshape(N, 8, 16, E)
    n = np.stack([gentries(a) for a in nm]).reshape(N, 8, C, A)
    wins, names, b = route(q, k, n)
    x = np.ascontiguousarray(x0.astype(np.float64).reshape(N, 8, 16, T).transpose(1, 2, 0, 3)).reshape(8, 16, A)
    u = ue.astype(np.float64).reshape(N, 8, 16, E); v = ve.astype(np.float64).reshape(N, 8, 16, E); m = mm.astype(np.float64)
    for l in range(RO):
        y = np.zeros((8, 16, A))
        for s in range(N):
            w = wins[l][s][:, None, :]
            d = np.add.reduce(np.take_along_axis(u[s], w, 2) * x, axis=1)
            y = y + (0.5 * d * (1.0 + np.tanh(0.5 * d)))[:, None, :] * np.take_along_axis(v[s], w, 2)
        z = (0.5 * x + 0.25 * y).reshape(128, N, T)
        x = np.stack([np.tanh(m[r].T @ z[:, r]) for r in range(N)], axis=1).reshape(8, 16, A)
    return {"yx": np.ascontiguousarray(x.reshape(128, N, T).transpose(1, 0, 2)).astype(np.float32), "yb": b.astype(np.float32)}

def check_inputs(d):
    bad = list(check_ranges(d))
    if not bad:
        for name, y in reference(**d).items():
            for q in range(N):
                v = np.abs(np.asarray(y[q], np.float64)); s = np.sqrt(np.mean(v * v))
                if v.max() > 7 * s or s < 2.0 ** -5: bad.append('%s of rank %d is uneven or too small' % (name, q))
    return bad

@@ -1,0 +1,473 @@
+from concourse.bass import DstId, RemoteDMATransfer
+from concourse.mybir import AluOpType as Op, ActivationFunctionType as Act, AxisListType
+
+NL = 3
+BF, F32, F16, I32, U16 = "bfloat16", "float32", "float16", "int32", "uint16"
+SCRATCH = {
+    "qall": ("sbuf", [128, 1024], BF), "nmi": ("sbuf", [128, 256], I32), "nmh": ("sbuf", [128, 256], F16),
+    "off": ("sbuf", [128, 256], U16), "kw": ("sbuf", [128, 2048], BF), "uw": ("sbuf", [128, 2048], BF),
+    "vw": ("sbuf", [128, 2048], BF), "xb": ("sbuf", [128, 256], BF), "mb": ("sbuf", [128, 128], BF),
+    "m32": ("sbuf", [128, 128], F32), "xs2": ("sbuf", [128, 256], F32), "xo": ("sbuf", [128, 256], F32),
+    "kw0": ("sbuf", [128, 2048], BF), "bg": ("sbuf", [128, 1024], BF), "z15": ("sbuf", [128, 144], BF),
+    "row15": ("sbuf", [128, 1], F32), "rows": ("sbuf", [128, 1], F32), "q15": ("sbuf", [128, 64], F32), "bq": ("sbuf", [128, 64], F32),
+    "rawk": ("sbuf", [128, 4096], BF),
+    "prod": ("sbuf", [128, 4096], F16),
+    "zb": ("sbuf", [128, 144], BF), "zh": ("sbuf", [128, 144], F16),
+    "wb": ("sbuf", [128, 16, 16], BF), "wh": ("sbuf", [128, 16, 16], F16), "bd": ("sbuf", [128, 128], F32),
+    "cbig": ("sbuf", [128, 256], BF), "cmid": ("sbuf", [128, 64], BF), "hb": ("sbuf", [128, 256], BF),
+    "s0": ("sbuf", [128, 64], F32), "n0": ("sbuf", [128, 64], F32), "n1": ("sbuf", [128, 64], F32),
+    "n2": ("sbuf", [128, 64], F32), "m1": ("sbuf", [128, 64], F32), "m2": ("sbuf", [128, 64], F32),
+    "dn": ("sbuf", [128, 3, 64], F32),
+    "w16": ("sbuf", [128, 7 * 64], F16), "wu": ("sbuf", [128, NL, 64], U16), "wr": ("sbuf", [128, 2, 4, 64], F16),
+    "dv": ("sbuf", [128, 8, 64], BF), "ev": ("sbuf", [128, 8, 4, 8], BF),
+    "oh": ("sbuf", [128, 8, 8, 64], BF), "th": ("sbuf", [128, 8, 33, 8], BF),
+    "bs": ("sbuf", [128, NL, 4, 32], BF), "bhi": ("sbuf", [128, 4, 32], BF), "blo": ("sbuf", [128, NL, 4, 32], BF),
+    "t1": ("sbuf", [128, 4, 32], F32), "bout": ("sbuf", [128, 4, 32], F32),
+    "us": ("sbuf", [128, NL, 1024], BF), "vs": ("sbuf", [128, NL, 1024], BF),
+    "ur": ("sbuf", [128, NL, 1024], BF), "vr": ("sbuf", [128, NL, 1024], BF),
+    "pu": ("sbuf", [128, 1024], F32), "yy": ("sbuf", [128, 1024], F32), "sg": ("sbuf", [128, 1024], F32),
+    "pA": ("psum", [128, 4, 128], F32), "pB": ("psum", [128, 4, 128], F32), "pN": ("psum", [128, 512], F32),
+    "pH": ("psum", [128, 512], F32), "pX": ("psum", [128, 512], F32), "pM": ("psum", [128, 512], F32),
+    "pD0": ("psum", [128, 512], F32), "pD1": ("psum", [128, 512], F32),
+}
+SEMAPHORES = (["cv", "cs", "ct", "cg", "sent", "sentq", "lq", "lnm", "lke", "lb", "lx", "lu", "lv", "aqm", "aqr", "oyx", "oyb"]
+              + ["aw%d" % l for l in range(2)] + ["bias%d" % l for l in range(2)]
+              + ["am%d" % l for l in range(NL)] + ["ar%d" % l for l in range(NL)])
+FORM = ["silu", "tanh", "tanh"]
+ROUND32 = 1.5 * 2.0 ** 28
+ROUND2048 = 1.5 * 2.0 ** 18
+
+ORDER = """gather,3,o raw,s,0,m gather,1,o raw,s,1,r hold,1,r gather,0,o raw,s,1,m hold,0,m hold,1,m raw,s,2,m raw,s,0,r gather,2,o times_q,1,m hold,2,m hold,0,r raw,s,3,m hold,3,m times_q,0,m fixed_keys times_q,2,m score,1,l score,2,l times_q,3,m times_q,0,r bias_ends,0 score,0,l score,0,r query_list times_q,1,r score,1,r gather,2,r score,2,r first gather,3,r score,3,l score,3,r select,0,a turn,0 query_keep name_sum,0,H offsets,0,a pick,s,u,0,r send_w,0 digits onehot,0,0,8 pick,s,v,0,r steps,0 name_sum,0,N pick,v,v,0,m pick,v,u,0,m onehot,1,0,8 counts,0 bias,0,0 name_rest,0,H steps,1 name_floor pick,v,v,0,o pick,v,u,0,o name_rest,0,N send_far,0 start_m send_near,0 start_x counts,1 bias,0,1 bias_ends,1 name_mod name_off name_first gather,0,a,T bias_pick score,0,a mul_u,0,l dsum,l act,0,l bias_list gather,2,a gather,1,a score,1,a score,2,a gather,3,a bias_add score,3,a select,1,a offsets,1,a mix_x turn,1 digits name_sum,1,N mul_u,0,r name_sum,1,H steps,0 onehot,0,0,8 steps,1 dsum,r counts,0 onehot,1,0,8 send_w,1 counts,1 pick,s,v,1,r bias,1,0 pick,v,u,1,r send_far,1 act,0,r name_rest,1,H name_rest,1,N bias,1,1 mul_v,0,l name_floor pick,s,u,1,o name_mod mul_v,0,r name_off pick,s,u,1,m bias_ends,2 gather,0,a,T mix,l,F mix,r,T pick,s,v,1,m send_near,1 gather,1,r score,0,a gather,2,r score,1,r name_first bias_pick bias_list new_x,0 score,2,r gather,3,r score,3,r bias_add select,2,r offsets,2,r gather,1,l mix_x mul_u,1,l pick,s,u,2,r pick,s,v,2,r score,1,l pick,s,v,1,o dsum,l gather,2,l score,2,l act,1,l gather,3,l score,3,l mul_u,1,r dsum,r select,2,l act,1,r mul_v,1,l turn,2 offsets,2,l pick,s,v,2,m pick,s,u,2,o mul_v,1,r pick,s,v,2,o mix,l,F mix,r,T pick,v,u,2,m digits onehot,0,0,4 new_x,1 mix_x send_far,2 mul_u,2,r steps,0 onehot,1,4,8 mul_u,2,o onehot,1,0,4 onehot,0,4,8 send_near,2 dsum,r mul_u,2,m act,2,r mul_v,2,r dsum,o counts,0 act,2,o steps,1 dsum,m mul_v,2,o mix,r,F bias,2,0 counts,1 act,2,m mul_v,2,m mix,o,F mix,m,T bias,2,1 new_x,2"""
+STEPS = [tuple(int(x) if x.isdigit() else (x == "T") if x in ("T", "F") else x for x in w.split(",")) for w in ORDER.split()]
+
+
+def rank_program(g, core, T, topo):
+    rank = T.rank_of(core)
+    if rank is None:
+        return
+    N = len(T.cores)
+    near = topo.cores_of(core)
+    mate = [r for r in range(N) if r != rank and T.cores[r] in near][0]
+    rem = [r for r in range(N) if T.cores[r] not in near]
+    loc0, rem0 = min(rank, mate), min(rem)
+    assert abs(rank - mate) == 1 and rem == [rem0, rem0 + 1]
+    e_off = topo.engines(core, T.cores[rem0])
+    e_on = [e for e in topo.engines(core, T.cores[mate]) if e not in e_off]
+
+    def mask(es):
+        return sum(1 << e for e in es)
+
+    def part(es, i, n):
+        k = len(es) // n
+        return mask(es[i * k:(i + 1) * k])
+
+    Q = {"v": g.vector, "s": g.scalar, "t": g.tensor, "g": g, "y": g.sync}
+    CS = {"v": "cv", "s": "cs", "t": "ct", "g": "cg"}
+    known = {q: {} for q in Q}
+    count = {}
+    lastw, readers, bank = {}, {}, {}
+
+    def wait(q, ev):
+        sem, n, snap, _src = ev
+        if known[q].get(sem, 0) >= n:
+            return
+        Q[q].wait_ge(T.sem[sem], n)
+        known[q][sem] = n
+        for k, m in snap.items():
+            if known[q].get(k, 0) < m:
+                known[q][k] = m
+
+    def order(q, src, reads, writes, banks):
+        need = []
+        for r in reads:
+            need.append(lastw[r])
+        for r in writes:
+            if r in lastw and lastw[r][3] != src:
+                need.append(lastw[r])
+            need += [ev for ev in readers.get(r, []) if ev[3] != src]
+        for b in banks:
+            need += [ev for o, ev in bank.get(b, {}).items() if o != q]
+        need.sort(key=lambda ev: -ev[1])
+        for ev in need:
+            wait(q, ev)
+
+    def note(ev, q, reads, writes, banks):
+        for r in reads:
+            readers.setdefault(r, []).append(ev)
+        for r in writes:
+            lastw[r] = ev
+            readers[r] = []
+        for b in banks:
+            bank.setdefault(b, {})[q] = ev
+
+    def op(q, fns, reads, writes, banks=()):
+        order(q, q, reads, writes, banks)
+        if not isinstance(fns, list):
+            fns = [fns]
+        for f in fns[:-1]:
+            f()
+        sem = CS[q]
+        fns[-1]().then_inc(T.sem[sem], 1)
+        count[sem] = count.get(sem, 0) + 1
+        note((sem, count[sem], dict(known[q]), q), q, reads, writes, banks)
+
+    def dma(q, sem, out, in_, reads, writes):
+        order(q, sem, reads, writes, ())
+        Q[q].dma_start(out, in_).then_inc(T.sem[sem], 16)
+        count[sem] = count.get(sem, 0) + 16
+        note((sem, count[sem], dict(known[q]), sem), q, reads, writes, ())
+
+    def send(items, reads, local="sent"):
+        order("g", "sent", reads, (), ())
+        tr = []
+        for r, m, sem, src, dst in items:
+            rid, pid = topo.addr(T.cores[r], core)
+            tr.append(RemoteDMATransfer(dst_ids=[DstId(rid=rid, pnc=pid)], dma_engine_mask=m, remote_sem=T.sem[sem], src=src, dst=dst))
+            count[local] = count.get(local, 0) + bin(m).count("1")
+        g.remote_dma_fused(tr, local_sem=T.sem[local])
+
+    def lands(sem, n, writes):
+        count[sem] = n
+        note((sem, n, {}, sem), None, (), writes, ())
+
+    V, S, PE = g.vector, g.scalar, g.tensor
+    ident, identh, shifth = T.wb[:, 0:8, :], T.wh[:, 0:8, :], T.wh[:, 7:15, :]
+
+    dma("y", "lq", T.qall[:, rank * 256:(rank + 1) * 256], T.rq[:], (), ["q%d" % rank])
+    dma("y", "lnm", T.nmi[:], T.nm[:], (), ["nmi"])
+    dma("y", "lke", T.kw[:], T.ke[:], (), ["kw"])
+    op("v", lambda: V.memset(T.wb[:], 1.0), (), ["wb"])
+    op("v", lambda: V.memset(T.zb[:], 0.0), (), ["zb"])
+    op("v", lambda: V.memset(T.bd[:], 1.0), (), ["bd"])
+    op("v", lambda: V.memset(T.zb[:, 15::16], 1.0), ["zb"], ["zb"])
+    op("g", lambda: g.affine_select(T.wb[:], T.wb[:], [[0, 2], [-1, 128]], Op.is_equal, 0.0, 0, 1), ["wb"], ["wb"])
+    op("g", lambda: g.affine_select(T.zb[:, 15::16], T.zb[:, 15::16], [[-16, 9]], Op.is_ge, 0.0, 0, 1), ["zb"], ["zb"])
+    op("g", lambda: g.affine_select(T.zb[:, 15::16], T.zb[:, 15::16], [[16, 9]], Op.is_ge, 0.0, 15, -1), ["zb"], ["zb"])
+    mine = T.qall[:, rank * 256:(rank + 1) * 256]
+    send([(rem[0], part(e_off, 0, 2), "aqr", mine, mine), (rem[1], part(e_off, 1, 2), "aqr", mine, mine),
+          (mate, mask(e_on), "aqm", mine, mine)], ["q%d" % rank], "sentq")
+    lands("aqm", len(e_on), ["q%d" % mate])
+    lands("aqr", len(e_off), ["q%d" % r for r in rem])
+    op("g", lambda: g.affine_select(T.bd[:], T.bd[:], [[-16, 8], [0, 16]], Op.is_ge, 0.0, 0, 1), ["bd"], ["bd"])
+    op("g", lambda: g.affine_select(T.bd[:], T.bd[:], [[16, 8], [0, 16]], Op.is_ge, 0.0, 15, -1), ["bd"], ["bd"])
+    op("v", lambda: V.memset(T.w16[:], 0.0), (), ["wz"])
+    op("v", lambda: V.memset(T.cbig[:], ROUND2048), (), ["cbig"])
+    op("v", lambda: V.memset(T.cmid[:], -15.5), (), ["cmid"])
+    op("v", lambda: V.memset(T.th[:, :, 32, :], -1.0), (), ["th32"])
+    op("v", lambda: V.tensor_copy(T.wh[:], T.wb[:]), ["wb"], ["wh"])
+    op("v", lambda: V.tensor_copy(T.zh[:], T.zb[:]), ["zb"], ["zh"])
+    op("v", lambda: V.tensor_copy(T.off[:], T.nmi[:]), ["nmi"], ["off"])
+    op("v", lambda: V.tensor_copy(T.nmh[:], T.nmi[:]), ["nmi"], ["nmh"])
+    op("v", lambda: V.tensor_reduce(T.row15[:], T.wb[:, 0:8, 15], AxisListType.X, Op.add), ["wb"], ["row15"])
+    op("v", lambda: V.tensor_scalar(T.rows[:], T.row15[:], -1.0, 1.0, Op.mult, Op.add), ["row15"], ["rows"])
+    op("v", lambda: V.tensor_scalar(T.z15[:], T.zb[:], T.row15[:], None, Op.mult), ["zb", "row15"], ["z15"])
+    wait("y", ("sentq", count["sentq"], {}, None))
+    for p in range(4):
+        dma("y", "lb", T.bs[:, 0, p, :], T.ke[32 * p + 15:32 * p + 32:16, :], (), ["b0"])
+    dma("y", "lu", T.uw[:], T.ue[:], (), ["uw"])
+    dma("y", "lv", T.vw[:], T.ve[:], (), ["vw"])
+    dma("y", "lx", T.xb[:], T.x0[:], (), ["xb", "mb"])
+    dma("y", "lx", T.mb[:], T.mm[:], (), ["xb", "mb"])
+    op("t", lambda: PE.matmul(T.pN[:, 0:256], identh, T.nmh[:], True, True), ["wh", "nmh"], ["N"], ["N"])
+    op("s", lambda: S.activation(T.n0[:], T.pN[:, 0:64], Act.Copy), ["N"], ["n0"], ["N"])
+
+    def span(h):
+        return {"a": (0, 4), "l": (loc0, 2), "r": (rem0, 2), "o": (rank, 1), "m": (mate, 1)}[h]
+
+    def rs(name, r0, n):
+        return ["%s%d" % (name, r) for r in range(r0, r0 + n)]
+
+    def tok(r0, n=1):
+        return slice(256 * r0, 256 * (r0 + n))
+
+    def tags(name, h):
+        return rs(name + "_", *span(h))
+
+    def gather(c, h, fixed=False):
+        r0, n = span(h)
+        a, k = c * 1024 + r0 * 256, c * 64 + r0 * 16
+        win = T.kw0 if fixed else T.kw
+        op("v", lambda: V.tensor_tensor(T.prod[:, a:a + 256 * n], win[:].indirect(T.off[:, k:k + 16 * n]), T.qall[:, tok(r0, n)], Op.mult),
+           ["kw0" if fixed else "kw", "off"] + rs("q", r0, n), tags("prod%d" % c, h))
+
+    def held(c, h):
+        if h == "m":
+            b, j = ("pX", "pM")[c // 2], c % 2
+            return b, T[b][:, tok(j)]
+        b = ("pD0", "pD1", "pX", "pM")[c]
+        return b, T[b][:]
+
+    def owners(b):
+        return {"pX": ["X"], "pM": ["M"], "pD0": rs("D", loc0, 2), "pD1": rs("D", rem0, 2)}[b]
+
+    def raw(q, c, h):
+        r0, n = span(h)
+        a, k = c * 1024 + r0 * 256, c * 64 + r0 * 16
+        out, src = T.rawk[:, a:a + 256 * n], T.kw[:].indirect(T.off[:, k:k + 16 * n])
+        op(q, (lambda: V.tensor_copy(out, src)) if q == "v" else (lambda: S.activation(out, src, Act.Copy)), ["kw", "off"], tags("raw%d" % c, h))
+
+    def hold(c, h):
+        r0, n = span(h)
+        a = c * 1024 + r0 * 256
+        b, place = held(c, h)
+        op("t", lambda: PE.matmul(place, ident, T.rawk[:, a:a + 256 * n], True, True), ["wb"] + tags("raw%d" % c, h), owners(b), [b])
+
+    def times_q(c, h):
+        r0, n = span(h)
+        a = c * 1024 + r0 * 256
+        b, place = held(c, h)
+        op("v", lambda: V.tensor_tensor(T.prod[:, a:a + 256 * n], place, T.qall[:, tok(r0, n)], Op.mult),
+           owners(b) + rs("q", r0, n), tags("prod%d" % c, h), [b])
+
+    def to_list(out, z, src, a, n):
+        return [lambda i=i: PE.matmul(out, z[:, 15 - i:143 - i], src[:, a + i:a + n:16], i == 0, i == 15) for i in range(16)]
+
+    def score(c, h):
+        r0, n = span(h)
+        cols = slice(r0 * 16, (r0 + n) * 16)
+        b, out = [("H", T.pH[:, cols]), ("pA", T.pA[:, 0, cols]), ("pA", T.pA[:, 1, cols]), ("pB", T.pB[:, 1, cols])][c]
+        op("t", to_list(out, T.zh, T.prod, c * 1024 + r0 * 256, 256 * n), ["zh"] + tags("prod%d" % c, h), tags("S%d" % c, h), [b])
+
+    def first():
+        op("s", lambda: S.activation(T.s0[:], T.pH[:, 0:64], Act.Copy), tags("S0", "a"), ["s0"], ["H"])
+
+    def bias_pick():
+        op("s", lambda: S.activation(T.bg[:], T.kw[:].indirect(T.off[:, 0:64]), Act.Copy), ["kw", "off"], ["bg"])
+
+    def bias_list():
+        op("t", to_list(T.pH[:, 64:128], T.z15, T.bg, 0, 1024), ["z15", "bg"], ["Bc"], ["H"])
+
+    def bias_add():
+        op("v", lambda: V.tensor_tensor(T.bq[:], T.pH[:, 64:128], T.q15[:], Op.mult), ["Bc", "q15"], ["bq"], ["H"])
+        op("v", lambda: V.tensor_tensor(T.s0[:], T.pH[:, 0:64], T.bq[:], Op.add), tags("S0", "a") + ["bq"], ["s0"], ["H"])
+
+    def select(l, h):
+        r0, n = span(h)
+        a, b = r0 * 16, (r0 + n) * 16
+        A, B = T.pA, T.pB
+
+        def tt(out, x, y, o, reads, writes, banks):
+            op("v", lambda: V.tensor_tensor(out, x, y, o), reads, writes, banks)
+
+        def nm(c):
+            return T.pN[:, c * 64 + a:c * 64 + b]
+        tt(T.dn[:, 0, a:b], nm(1), T.n0[:, a:b], Op.subtract, ["N", "n0"], ["dn1"], ["N"])
+        tt(A[:, 2, a:b], A[:, 0, a:b], T.s0[:, a:b], Op.is_gt, tags("S1", h) + ["s0"], ["g1"], ["pA"])
+        tt(T.m1[:, a:b], A[:, 0, a:b], T.s0[:, a:b], Op.max, tags("S1", h) + ["s0"], ["m1"], ["pA"])
+        tt(A[:, 3, a:b], A[:, 2, a:b], T.dn[:, 0, a:b], Op.mult, ["g1", "dn1"], ["t1"], ["pA"])
+        tt(A[:, 2, 64 + a:64 + b], A[:, 1, a:b], T.m1[:, a:b], Op.is_gt, tags("S2", h) + ["m1"], ["g2"], ["pA"])
+        tt(T.n1[:, a:b], A[:, 3, a:b], T.n0[:, a:b], Op.add, ["t1", "n0"], ["n1"], ["pA"])
+        tt(T.m2[:, a:b], A[:, 1, a:b], T.m1[:, a:b], Op.max, tags("S2", h) + ["m1"], ["m2"], ["pA"])
+        tt(T.dn[:, 1, a:b], nm(2), T.n1[:, a:b], Op.subtract, ["N", "n1"], ["dn2"], ["N"])
+        tt(A[:, 3, 64 + a:64 + b], A[:, 2, 64 + a:64 + b], T.dn[:, 1, a:b], Op.mult, ["g2", "dn2"], ["t2"], ["pA"])
+        tt(T.n2[:, a:b], A[:, 3, 64 + a:64 + b], T.n1[:, a:b], Op.add, ["t2", "n1"], ["n2"], ["pA"])
+        tt(T.dn[:, 2, a:b], nm(3), T.n2[:, a:b], Op.subtract, ["N", "n2"], ["dn3"], ["N"])
+        tt(B[:, 2, a:b], B[:, 1, a:b], T.m2[:, a:b], Op.is_gt, tags("S3", h) + ["m2"], ["g3"], ["pB"])
+        tt(B[:, 3, a:b], B[:, 2, a:b], T.dn[:, 2, a:b], Op.mult, ["g3", "dn3"], ["t3"], ["pB"])
+        w0 = (2 * l + 1) * 64
+        tt(T.w16[:, w0 + a:w0 + b], B[:, 3, a:b], T.n2[:, a:b], Op.add, ["t3", "n2", "wz"], tags("w%d" % l, h), ["pB"])
+
+    def offsets(l, h):
+        r0, n = span(h)
+        a, b = r0 * 16, (r0 + n) * 16
+        w0 = (2 * l + 1) * 64
+        op("v", lambda: V.tensor_copy(T.wu[:, l, a:b], T.w16[:, w0 + a:w0 + b]), tags("w%d" % l, h), tags("wu%d" % l, h))
+
+    def send_w(l):
+        w0 = (2 * l + 1) * 64
+        src, dst, sem = T.w16[:, w0:w0 + 64], T.wr[:, l, rank, :], "aw%d" % l
+        send([(rem[0], part(e_off, 0, 2), sem, src, dst), (rem[1], part(e_off, 1, 2), sem, src, dst),
+              (mate, mask(e_on), sem, src, dst)], tags("w%d" % l, "a"))
+        lands(sem, len(e_off) + len(e_on), ["wr%d" % l])
+
+    def name_sum(l, bankname, out):
+        w0 = (2 * l + 1) * 64
+        fns = [lambda: PE.matmul(out[:, 0:256], identh, T.nmh[:], True, False)]
+        if bankname == "N":
+            fns.append(lambda: PE.matmul(out[:, 0:256], ident, T.cbig[:], False, False))
+        fns += [lambda c=c: PE.matmul(out[:, c * 64:c * 64 + 64], shifth, T.w16[:, w0:w0 + 64], False, False) for c in range(4)]
+        op("t", fns, ["wh", "wb", "nmh", "cbig"] + tags("w%d" % l, "a"), [bankname], [bankname])
+
+    def name_rest(l, bankname, out):
+        others = [r for r in range(N) if r != rank]
+        pairs = [(r, c) for r in others for c in range(4)]
+        op("t", [lambda r=r, c=c: PE.matmul(out[:, c * 64:c * 64 + 64], shifth, T.wr[:, l, r, :], False,
+                                             bankname == "H" and (r, c) == pairs[-1]) for r, c in pairs],
+           ["wh", "wr%d" % l], [bankname], [bankname])
+
+    def name_floor():
+        op("s", lambda: S.activation(T.hb[:], T.pH[:, 0:256], Act.Identity, bias=-(ROUND2048 - 1023.5), scale=-1.0), ["H"], ["hb"], ["H"])
+
+    def name_mod():
+        op("t", lambda: PE.matmul(T.pN[:, 0:256], ident, T.hb[:], False, True), ["wb", "hb"], ["N"], ["N"])
+
+    def name_off():
+        op("v", lambda: V.tensor_copy(T.off[:], T.pN[:, 0:256]), ["N"], ["off"], ["N"])
+
+    def name_first():
+        op("s", lambda: S.activation(T.n0[:], T.pN[:, 0:64], Act.Copy), ["N"], ["n0"], ["N"])
+
+    WT = T.pB[:, 0, 64:128]
+
+    def turn(l):
+        w0 = (2 * l + 1) * 64
+        op("t", [lambda: PE.matmul(WT, ident, T.cmid[:], True, False),
+                 lambda: PE.matmul(WT, T.w16[:, w0:w0 + 128], T.wh[:, 0:8, 0:8], False, False),
+                 lambda: PE.matmul(WT, T.w16[:, w0 - 64:w0 + 64], T.wh[:, 0:8, 8:16], False, True)],
+           ["wb", "wh", "cmid", "wz"] + tags("w%d" % l, "a"), ["WT"], ["pB"])
+
+    def digits():
+        op("v", lambda: V.tensor_scalar(T.dv[:, :, 0:8], WT, ROUND32, -ROUND32, Op.add, Op.add), ["WT"], ["d0"], ["pB"])
+        op("v", lambda: V.tensor_tensor(T.ev[:, :, 0, :], WT, T.dv[:, :, 0:8], Op.subtract), ["WT", "d0"], ["e0"], ["pB"])
+        op("v", lambda: V.tensor_scalar(T.dv[:, :, 8:16], T.dv[:, :, 0:8], -32.0, None, Op.add), ["d0"], ["d1"])
+        op("s", lambda: S.activation(T.ev[:, :, 1, :], T.ev[:, :, 0, :], Act.Identity, bias=-8.0), ["e0"], ["e1"])
+        op("v", lambda: V.tensor_scalar(T.dv[:, :, 16:32], T.dv[:, :, 0:16], -64.0, None, Op.add), ["d0", "d1"], ["d2"])
+        op("s", lambda: S.activation(T.ev[:, :, 2:4, :], T.ev[:, :, 0:2, :], Act.Identity, bias=-16.0), ["e0", "e1"], ["e2"])
+        op("v", lambda: V.tensor_scalar(T.dv[:, :, 32:64], T.dv[:, :, 0:32], -128.0, None, Op.add), ["d0", "d1", "d2"], ["d3"])
+
+    def onehot(k, us=range(8)):
+        op("v", [lambda u=u: V.tensor_scalar(T.oh[:, 4 * k:4 * k + 4, u, :], T.dv[:, 4 * k:4 * k + 4, :], 256.0 * u, 0.5, Op.is_equal, Op.mult)
+                 for u in us], ["d0", "d1", "d2", "d3"], ["oh%d%d" % (k, u) for u in us])
+
+    def steps(k):
+        op("s", [lambda u=u: S.activation(T.th[:, 4 * k:4 * k + 4, u:32:8, :], T.ev[:, 4 * k:4 * k + 4, :, :], Act.Sign, bias=16.0 - u)
+                 for u in range(8)], ["e0", "e1", "e2"], ["th%d" % k])
+
+    def counts(k):
+        b = "pA" if k == 0 else "pB"
+        op("t", [lambda pp=pp, i=i: PE.matmul(T[b][:, pp, 0:66], T.oh[:, 4 * k + 2 * pp:4 * k + 2 * pp + 2, :, i::8],
+                                               T.th[:, 4 * k + 2 * pp:4 * k + 2 * pp + 2, :, i], i == 0, i == 7)
+                 for pp in range(2) for i in range(8)],
+           ["th32", "th%d" % k] + ["oh%d%d" % (k, u) for u in range(8)], ["C%d" % k], [b])
+
+    def bias_ends(l):
+        last = l == NL - 1
+        if last:
+            op("s", lambda: S.activation(T.bhi[:], T.bs[:, l], Act.Identity, bias=float(NL)), ["b%d" % l], ["bhi"])
+        op("s", lambda: S.activation(T.blo[:, l], T.bs[:, l], Act.Identity, bias=float(NL - 2) if last else -2.0), ["b%d" % l], ["blo%d" % l])
+
+    def bias(l, k):
+        b = "pA" if k == 0 else "pB"
+        C, last, pp = T[b], l == NL - 1, slice(2 * k, 2 * k + 2)
+        for par in range(2):
+            rows = slice(64 * par, 64 * par + 64)
+            old = T.bhi[rows, pp, :] if last else T.bs[rows, l, pp, :]
+            op("v", lambda: V.tensor_tensor(T.t1[rows, pp, :], old, C[rows, 0:2, 33 * par:33 * par + 32], Op.subtract),
+               ["C%d" % k, "bhi" if last else "b%d" % l], ["u%d%d" % (k, par)], [b])
+        for par in range(2):
+            rows = slice(64 * par, 64 * par + 64)
+            op("v", lambda: V.tensor_tensor(C[rows, 2:4, 0:32], C[rows, 0:2, 33 * par + 1:33 * par + 33], T.t1[rows, pp, :], Op.add),
+               ["C%d" % k, "u%d%d" % (k, par)], ["v%d%d" % (k, par)], [b])
+        new = T.bout[:, pp, :] if last else T.bs[:, l + 1, pp, :]
+        op("v", lambda: V.tensor_tensor(new, C[:, 2:4, 0:32], T.blo[:, l, pp, :], Op.max),
+           ["v%d0" % k, "v%d1" % k, "blo%d" % l], ["nb%d%d" % (l, k)] + (["b%d" % (l + 1)] if k == 1 else []), [b])
+        for p in range(2 * k, 2 * k + 2):
+            if last:
+                dma("y", "oyb", T.yb[2 * p:2 * p + 2, :], T.bout[:, p, :], ["nb%d%d" % (l, k)], ["yb"])
+            else:
+                dma("y", "bias%d" % l, T.kw[32 * p + 15:32 * p + 32:16, :], T.bs[:, l + 1, p, :], ["nb%d%d" % (l, k)], ["kw"])
+
+    def pick(q, kind, l, r0, n):
+        win, to = (T.uw, T.ur if r0 == rank else T.us) if kind == "u" else (T.vw, T.vr if r0 == rank else T.vs)
+        src = win[:].indirect(T.wu[:, l, 16 * r0:16 * (r0 + n)])
+        out = to[:, l, tok(r0, n)]
+        name = ("%sr%d%d" if r0 == rank else "%ss%d%d") % (kind, l, r0)
+        op(q, (lambda: V.tensor_copy(out, src)) if q == "v" else (lambda: S.activation(out, src, Act.Copy)),
+           [kind + "w"] + rs("wu%d_" % l, r0, n), [name])
+
+    def send_far(l):
+        sem = "ar%d" % l
+        send([(rem[0], part(e_off, 0, 4), sem, T.us[:, l, tok(rem[0])], T.ur[:, l, tok(rank)]),
+              (rem[1], part(e_off, 1, 4), sem, T.us[:, l, tok(rem[1])], T.ur[:, l, tok(rank)]),
+              (rem[0], part(e_off, 2, 4), sem, T.vs[:, l, tok(rem[0])], T.vr[:, l, tok(rank)]),
+              (rem[1], part(e_off, 3, 4), sem, T.vs[:, l, tok(rem[1])], T.vr[:, l, tok(rank)])],
+             ["us%d%d" % (l, rem0), "vs%d%d" % (l, rem0)])
+        lands(sem, len(e_off), ["%sr%d%d" % (k, l, r) for k in "uv" for r in rem])
+
+    def send_near(l):
+        sem = "am%d" % l
+        send([(mate, part(e_on, 0, 2), sem, T.us[:, l, tok(mate)], T.ur[:, l, tok(rank)]),
+              (mate, part(e_on, 1, 2), sem, T.vs[:, l, tok(mate)], T.vr[:, l, tok(rank)])],
+             ["us%d%d" % (l, mate), "vs%d%d" % (l, mate)])
+        lands(sem, len(e_on), ["ur%d%d" % (l, mate), "vr%d%d" % (l, mate)])
+
+    def dplace(r0, n):
+        b = "pD1" if r0 in rem else "pD0"
+        j = r0 - (rem0 if r0 in rem else loc0)
+        return b, T[b][:, tok(j, n)]
+
+    def mul_u(l, r0, n):
+        for r in range(r0, r0 + n):
+            op("v", lambda: V.tensor_tensor(T.pu[:, tok(r)], T.pX[:, 0:256], T.ur[:, l, tok(r)], Op.mult),
+               ["X", "ur%d%d" % (l, r)], ["pu%d" % r], ["pX"])
+
+    def dsum(r0, n):
+        b, D = dplace(r0, n)
+        op("t", lambda: PE.matmul(D, T.bd[:], T.pu[:, tok(r0, n)], True, True), ["bd"] + rs("pu", r0, n), rs("D", r0, n), [b])
+
+    def act(l, r0, n):
+        b, D = dplace(r0, n)
+        sg = T.sg[:, tok(r0, n)]
+        if FORM[l] == "silu":
+            op("s", lambda: S.activation(D, D, Act.Silu), rs("D", r0, n), rs("D", r0, n), [b])
+        else:
+            op("s", lambda: S.activation(sg, D, Act.Tanh, scale=0.5), rs("D", r0, n), rs("sg", r0, n), [b])
+            op("s", lambda: S.activation(sg, sg, Act.Identity, bias=0.5, scale=0.5), rs("sg", r0, n), rs("sg", r0, n))
+
+    def mul_v(l, r0, n):
+        b, D = dplace(r0, n)
+        if FORM[l] != "silu":
+            op("v", lambda: V.tensor_tensor(D, D, T.sg[:, tok(r0, n)], Op.mult), rs("D", r0, n) + rs("sg", r0, n), rs("D", r0, n), [b])
+        op("v", lambda: V.tensor_tensor(T.yy[:, tok(r0, n)], D, T.vr[:, l, tok(r0, n)], Op.mult),
+           rs("D", r0, n) + rs("vr%d" % l, r0, n), rs("y", r0, n), [b])
+
+    def mix_x():
+        op("t", lambda: PE.matmul(T.pM[:, 0:256], T.m32[:], T.xs2[:], True, False), ["m32", "xs2"], ["M"], ["pM"])
+
+    def mix(r0, n, end):
+        op("t", [lambda r=r: PE.matmul(T.pM[:, 0:256], T.m32[:], T.yy[:, tok(r)], False, end and r == r0 + n - 1)
+                 for r in range(r0, r0 + n)], ["m32"] + rs("y", r0, n), ["M"], ["pM"])
+
+    def new_x(l):
+        if l == NL - 1:
+            op("s", lambda: S.activation(T.xo[:], T.pM[:, 0:256], Act.Tanh, scale=0.25), ["M"], ["xo"], ["pM"])
+            dma("s", "oyx", T.yx[:], T.xo[:], ["xo"], ["yx"])
+        else:
+            op("s", lambda: S.activation(T.pX[:, 0:256], T.pM[:, 0:256], Act.Tanh, scale=0.25), ["M"], ["X"], ["pM", "pX"])
+            op("s", lambda: S.activation(T.xs2[:], T.pX[:, 0:256], Act.Identity, scale=2.0), ["X"], ["xs2"], ["pX"])
+
+    def fixed_keys():
+        op("s", lambda: S.activation(T.kw0[:], T.kw[:], Act.Identity, scale=T.rows[:]), ["kw", "rows"], ["kw0"])
+
+    def query_list():
+        op("t", to_list(T.pH[:, 128:192], T.z15, T.qall, 0, 1024), ["z15"] + rs("q", 0, 4), ["qc"], ["H"])
+
+    def query_keep():
+        op("s", lambda: S.activation(T.q15[:], T.pH[:, 128:192], Act.Copy), ["qc"], ["q15"], ["H"])
+
+    def start_m():
+        op("s", lambda: S.activation(T.m32[:], T.mb[:], Act.Copy), ["mb"], ["m32"])
+
+    def start_x():
+        op("s", lambda: S.activation(T.pX[:, 0:256], T.xb[:], Act.Copy), ["xb"], ["X"], ["pX"])
+        op("s", lambda: S.activation(T.xs2[:], T.xb[:], Act.Identity, scale=2.0), ["xb"], ["xs2"])
+
+    nb = {"H": T.pH, "N": T.pN}
+    do = {"raw": raw, "hold": hold, "times_q": times_q, "gather": gather, "score": score, "first": first,
+          "bias_pick": bias_pick, "bias_list": bias_list, "bias_add": bias_add,
+          "select": select, "offsets": offsets, "send_w": send_w, "name_floor": name_floor, "name_mod": name_mod,
+          "name_sum": lambda l, b: name_sum(l, b, nb[b]), "name_rest": lambda l, b: name_rest(l, b, nb[b]),
+          "name_off": name_off, "name_first": name_first, "turn": turn, "digits": digits, "steps": steps, "counts": counts,
+          "onehot": lambda k, a, b: onehot(k, range(a, b)), "bias_ends": bias_ends, "bias": bias,
+          "pick": lambda q, kind, l, h: pick(q, kind, l, *span(h)), "send_far": send_far, "send_near": send_near,
+          "mul_u": lambda l, h: mul_u(l, *span(h)), "dsum": lambda h: dsum(*span(h)), "act": lambda l, h: act(l, *span(h)),
+          "mul_v": lambda l, h: mul_v(l, *span(h)), "mix_x": mix_x, "mix": lambda h, end: mix(*span(h), end), "new_x": new_x,
+          "fixed_keys": fixed_keys, "query_list": query_list, "query_keep": query_keep, "start_m": start_m, "start_x": start_x}
+    for step in STEPS:
+        do[step[0]](*step[1:])
+
+    for sem in count:
+        if sem not in ("oyx", "oyb"):
+            wait("g", (sem, count[sem], {}, None))
+    wait("g", ("oyx", count["oyx"], {}, None))
+    wait("g", ("oyb", count["oyb"], {}, None))

@@ -1,44 +1,53 @@
+import math
 from concourse.bass import DstId, RemoteDMATransfer
-from concourse.mybir import AluOpType as Op, ActivationFunctionType as Act, AxisListType
+from concourse.mybir import AluOpType as Op, ActivationFunctionType as Act
 
 NL = 3
 BF, F32, F16, I32, U16 = "bfloat16", "float32", "float16", "int32", "uint16"
 SCRATCH = {
-    "qall": ("sbuf", [128, 1024], BF), "nmi": ("sbuf", [128, 256], I32), "nmh": ("sbuf", [128, 256], F16),
+    "qall": ("sbuf", [128, 1024], BF), "nmi": ("sbuf", [128, 4, 64], I32), "nmh": ("sbuf", [128, 256], F16),
     "off": ("sbuf", [128, 256], U16), "kw": ("sbuf", [128, 2048], BF), "uw": ("sbuf", [128, 2048], BF),
     "vw": ("sbuf", [128, 2048], BF), "xb": ("sbuf", [128, 256], BF), "mb": ("sbuf", [128, 128], BF),
-    "m32": ("sbuf", [128, 128], F32), "xs2": ("sbuf", [128, 256], F32), "xo": ("sbuf", [128, 256], F32),
-    "kw0": ("sbuf", [128, 2048], BF), "bg": ("sbuf", [128, 1024], BF), "z15": ("sbuf", [128, 144], BF),
-    "row15": ("sbuf", [128, 1], F32), "rows": ("sbuf", [128, 1], F32), "q15": ("sbuf", [128, 64], F32), "bq": ("sbuf", [128, 64], F32),
-    "rawk": ("sbuf", [128, 4096], BF),
-    "prod": ("sbuf", [128, 4096], F16),
+    "m32": ("sbuf", [128, 128], F32), "xs2": ("sbuf", [128, 256], F32), "xo": ("sbuf", [128, 256], F32), "sx": ("sbuf", [128, 256], F32),
+    "rawk": ("sbuf", [128, 4, 1024], BF), "prod": ("sbuf", [128, 4, 1024], F16),
     "zb": ("sbuf", [128, 144], BF), "zh": ("sbuf", [128, 144], F16),
-    "wb": ("sbuf", [128, 16, 16], BF), "wh": ("sbuf", [128, 16, 16], F16), "bd": ("sbuf", [128, 128], F32),
-    "cbig": ("sbuf", [128, 256], BF), "cmid": ("sbuf", [128, 64], BF), "hb": ("sbuf", [128, 256], BF),
-    "s0": ("sbuf", [128, 64], F32), "n0": ("sbuf", [128, 64], F32), "n1": ("sbuf", [128, 64], F32),
-    "n2": ("sbuf", [128, 64], F32), "m1": ("sbuf", [128, 64], F32), "m2": ("sbuf", [128, 64], F32),
-    "dn": ("sbuf", [128, 3, 64], F32),
-    "w16": ("sbuf", [128, 7 * 64], F16), "wu": ("sbuf", [128, NL, 64], U16), "wr": ("sbuf", [128, 2, 4, 64], F16),
-    "dv": ("sbuf", [128, 8, 64], BF), "ev": ("sbuf", [128, 8, 4, 8], BF),
-    "oh": ("sbuf", [128, 8, 8, 64], BF), "th": ("sbuf", [128, 8, 33, 8], BF),
-    "bs": ("sbuf", [128, NL, 4, 32], BF), "bhi": ("sbuf", [128, 4, 32], BF), "blo": ("sbuf", [128, NL, 4, 32], BF),
-    "t1": ("sbuf", [128, 4, 32], F32), "bout": ("sbuf", [128, 4, 32], F32),
-    "us": ("sbuf", [128, NL, 1024], BF), "vs": ("sbuf", [128, NL, 1024], BF),
-    "ur": ("sbuf", [128, NL, 1024], BF), "vr": ("sbuf", [128, NL, 1024], BF),
+    "wb": ("sbuf", [128, 16, 16], BF), "wh": ("sbuf", [128, 16, 16], F16), "neg": ("sbuf", [128, 8, 16], BF),
+    "bd": ("sbuf", [128, 128], F32), "bdb": ("sbuf", [128, 128], BF),
+    "sel": ("sbuf", [128, 8, 4, 16], F16), "c1": ("sbuf", [128, 128], BF), "c2": ("sbuf", [128, 128], BF),
+    "c3": ("sbuf", [128, 128], BF), "zero": ("sbuf", [128, 66], BF), "cbig": ("sbuf", [128, 256], BF), "hb": ("sbuf", [128, 256], BF),
+    "sl": ("sbuf", [128, 2, 64], F32), "nl": ("sbuf", [128, 2, 64], F32), "dn": ("sbuf", [128, 2, 64], F32),
+    "mx": ("sbuf", [128, 2, 64], F32), "nx": ("sbuf", [128, 2, 64], F32), "px": ("sbuf", [128, 2, 64], F32),
+    "w16": ("sbuf", [128, NL, 64], F16), "wu": ("sbuf", [128, NL, 64], U16), "wr": ("sbuf", [128, 2, 4, 64], F16),
+    "dv": ("sbuf", [128, 2, 8, 16], BF), "oh": ("sbuf", [128, 16, 8, 16], BF), "th": ("sbuf", [128, 16, 32, 4], BF),
+    "bs": ("sbuf", [128, NL + 1, 2, 72], BF), "blo": ("sbuf", [128, NL, 2, 64], BF), "bout": ("sbuf", [128, 2, 64], F32),
+    "i2": ("sbuf", [128, 2, 33], F32), "im": ("sbuf", [128, 2, 33], F32), "ee": ("sbuf", [128, 2, 33], F32),
+    "uvs": ("sbuf", [128, NL * 4, 2, 256], BF), "uvr": ("sbuf", [128, NL * 4, 2, 256], BF),
     "pu": ("sbuf", [128, 1024], F32), "yy": ("sbuf", [128, 1024], F32), "sg": ("sbuf", [128, 1024], F32),
-    "pA": ("psum", [128, 4, 128], F32), "pB": ("psum", [128, 4, 128], F32), "pN": ("psum", [128, 512], F32),
-    "pH": ("psum", [128, 512], F32), "pX": ("psum", [128, 512], F32), "pM": ("psum", [128, 512], F32),
-    "pD0": ("psum", [128, 512], F32), "pD1": ("psum", [128, 512], F32),
+    "pA": ("psum", [128, 8, 64], F32), "pB": ("psum", [128, 8, 64], F32), "pW": ("psum", [128, 8, 64], F32),
+    "pF": ("psum", [128, 8, 64], F32), "pX": ("psum", [128, 8, 64], F32), "pM": ("psum", [128, 8, 64], F32),
+    "pD0": ("psum", [128, 8, 64], F32), "pD1": ("psum", [128, 8, 64], F32),
 }
-SEMAPHORES = (["cv", "cs", "ct", "cg", "sent", "sentq", "lq", "lnm", "lke", "lb", "lx", "lu", "lv", "aqm", "aqr", "oyx", "oyb"]
+SEMAPHORES = (["cv", "cs", "ct", "cg", "sent", "lq", "lnm", "lke", "lb", "lx", "lm", "lu", "lv", "aqm", "aqr", "oyx", "oyb"]
               + ["aw%d" % l for l in range(2)] + ["bias%d" % l for l in range(2)]
-              + ["am%d" % l for l in range(NL)] + ["ar%d" % l for l in range(NL)])
-FORM = ["silu", "tanh", "tanh"]
-ROUND32 = 1.5 * 2.0 ** 28
+              + ["a%d%s%s" % (l, k, h) for l in range(NL) for k in ("u", "v", "uv") for h in ("m", "ra", "rb")])
+ROUND64 = 1.5 * 2.0 ** 13
 ROUND2048 = 1.5 * 2.0 ** 18
+ROUND1 = 1.5 * 2.0 ** 23
+ROUND4096 = 1.5 * 2.0 ** 35
+EDGE = math.log(4095.0)
 
-ORDER = """gather,3,o raw,s,0,m gather,1,o raw,s,1,r hold,1,r gather,0,o raw,s,1,m hold,0,m hold,1,m raw,s,2,m raw,s,0,r gather,2,o times_q,1,m hold,2,m hold,0,r raw,s,3,m hold,3,m times_q,0,m fixed_keys times_q,2,m score,1,l score,2,l times_q,3,m times_q,0,r bias_ends,0 score,0,l score,0,r query_list times_q,1,r score,1,r gather,2,r score,2,r first gather,3,r score,3,l score,3,r select,0,a turn,0 query_keep name_sum,0,H offsets,0,a pick,s,u,0,r send_w,0 digits onehot,0,0,8 pick,s,v,0,r steps,0 name_sum,0,N pick,v,v,0,m pick,v,u,0,m onehot,1,0,8 counts,0 bias,0,0 name_rest,0,H steps,1 name_floor pick,v,v,0,o pick,v,u,0,o name_rest,0,N send_far,0 start_m send_near,0 start_x counts,1 bias,0,1 bias_ends,1 name_mod name_off name_first gather,0,a,T bias_pick score,0,a mul_u,0,l dsum,l act,0,l bias_list gather,2,a gather,1,a score,1,a score,2,a gather,3,a bias_add score,3,a select,1,a offsets,1,a mix_x turn,1 digits name_sum,1,N mul_u,0,r name_sum,1,H steps,0 onehot,0,0,8 steps,1 dsum,r counts,0 onehot,1,0,8 send_w,1 counts,1 pick,s,v,1,r bias,1,0 pick,v,u,1,r send_far,1 act,0,r name_rest,1,H name_rest,1,N bias,1,1 mul_v,0,l name_floor pick,s,u,1,o name_mod mul_v,0,r name_off pick,s,u,1,m bias_ends,2 gather,0,a,T mix,l,F mix,r,T pick,s,v,1,m send_near,1 gather,1,r score,0,a gather,2,r score,1,r name_first bias_pick bias_list new_x,0 score,2,r gather,3,r score,3,r bias_add select,2,r offsets,2,r gather,1,l mix_x mul_u,1,l pick,s,u,2,r pick,s,v,2,r score,1,l pick,s,v,1,o dsum,l gather,2,l score,2,l act,1,l gather,3,l score,3,l mul_u,1,r dsum,r select,2,l act,1,r mul_v,1,l turn,2 offsets,2,l pick,s,v,2,m pick,s,u,2,o mul_v,1,r pick,s,v,2,o mix,l,F mix,r,T pick,v,u,2,m digits onehot,0,0,4 new_x,1 mix_x send_far,2 mul_u,2,r steps,0 onehot,1,4,8 mul_u,2,o onehot,1,0,4 onehot,0,4,8 send_near,2 dsum,r mul_u,2,m act,2,r mul_v,2,r dsum,o counts,0 act,2,o steps,1 dsum,m mul_v,2,o mix,r,F bias,2,0 counts,1 act,2,m mul_v,2,m mix,o,F mix,m,T bias,2,1 new_x,2"""
-STEPS = [tuple(int(x) if x.isdigit() else (x == "T") if x in ("T", "F") else x for x in w.split(",")) for w in ORDER.split()]
+PLAN = [
+    "judge,l,pA count,0,l,pA judge,r,pB tell count,1,r,pB biases names send,u,ra+rb,vv send,uv,m,vv send,v,ra+rb,ss send,uv,o,ss",
+    "judge,r,pA send,u,ra+rb,SS count,0,r,pA judge,l,pB tell count,1,l,pB biases names send,v,ra+rb,ss send,uv,m,ss send,uv,o,ss",
+    "judge,r,pA send,u,ra+rb,vS send,v,ra+rb,SS count,0,r,pA judge,l,pB send,uv,m,vs send,uv,o,vs count,1,l,pB biases",
+]
+PLAN = [[tuple(int(x) if x.isdigit() else x for x in step.split(",")) for step in layer.split()] for layer in PLAN]
+HELD = {0: "pW", 2: "pF"}
+DUE = (20, 10)
+CYCLE = {"v": 0.9e-3, "s": 0.9e-3, "t": 0.45e-3, "g": 1.8e-3}
+CALL = {"v": 0.03, "s": 0.065, "t": 0.0, "g": 0.17}
+GATHER, HOP, LOCAL, ISSUE = 1.4, 0.13, 2.1, 0.6
+FLIGHT, FIRST, PORT, WAKE = 1.5, 3.6, 1.1, 0.8
 
 
 def rank_program(g, core, T, topo):
@@ -54,18 +63,352 @@ def rank_program(g, core, T, topo):
     e_off = topo.engines(core, T.cores[rem0])
     e_on = [e for e in topo.engines(core, T.cores[mate]) if e not in e_off]
 
-    def mask(es):
-        return sum(1 << e for e in es)
-
     def part(es, i, n):
         k = len(es) // n
-        return mask(es[i * k:(i + 1) * k])
+        return sum(1 << e for e in es[i * k:(i + 1) * k])
 
+    calls = []
+
+    def op(q, fns, cycles, reads, writes, banks=(), line=None):
+        fns = fns if isinstance(fns, list) else [fns]
+        busy = len(fns) * (CALL[q] + max(cycles, 32 if q == "t" else 64) * CYCLE[q])
+        calls.append(dict(kind="op", q=q, fns=fns, reads=reads, writes=writes, banks=banks, busy=busy, late=HOP, line=line))
+
+    def dma(q, sem, pairs, reads, writes, late=LOCAL, line=None):
+        calls.append(dict(kind="dma", q=q, sem=sem, pairs=pairs, reads=reads, writes=writes, banks=(), busy=0.05 * len(pairs), late=late, line=line))
+
+    def send(items, reads, lands, flight=FLIGHT):
+        calls.append(dict(kind="send", q="g", items=items, local="sent", reads=reads, writes=[], banks=(), busy=ISSUE, late=0.0, line="sends"))
+        me = len(calls) - 1
+        for sem, writes, pieces in lands:
+            n = sum(bin(m).count("1") for _r, m, s, _a, _b in items if s == sem)
+            calls.append(dict(kind="land", q="port" if pieces else None, sem=sem, n=n, reads=[], writes=writes, banks=(),
+                              busy=max(pieces, 1.1) * PORT, late=WAKE if pieces else 0.3, flight=flight, after=me, line="port" if pieces else None))
+
+    V, S, PE = g.vector, g.scalar, g.tensor
+    ident, identh, shifth = T.wb[:, 0:8, :], T.wh[:, 0:8, :], T.wh[:, 7:15, :]
+
+    def bias_rows(t, half):
+        return t[64 * half + 15:64 * half + 64:16, :]
+
+    def span(h):
+        return {"a": (0, 4), "l": (loc0, 2), "r": (rem0, 2), "o": (rank, 1), "m": (mate, 1),
+                "ra": (rem0 + rank - loc0, 1), "rb": (rem0 + mate - loc0, 1)}[h]
+
+    def rs(name, r0, n):
+        return ["%s%d" % (name, r) for r in range(r0, r0 + n)]
+
+    def tok(r0, n=1):
+        return slice(256 * r0, 256 * (r0 + n))
+
+    def col(h):
+        r0, n = span(h)
+        return slice(16 * r0, 16 * (r0 + n))
+
+    def tags(name, h):
+        return rs(name + "_", *span(h))
+
+    mine = T.qall[:, tok(rank)]
+    dma("y", "lq", [(mine, T.rq[:])], [], ["q%d" % rank], 2.0, "load")
+    dma("y", "lnm", [(T.nmi[:], T.nm[:])], [], ["nmi"], 2.6, "load")
+    dma("y", "lke", [(T.kw[:], T.ke[:])], [], ["kw"], 4.3, "load")
+    dma("y", "lb", [(T.bs[:, 0, half, 8:72], bias_rows(T.ke, half)) for half in range(2)], [], ["b0"], 5.0, "load")
+    op("v", lambda: V.memset(T.wb[:], 1.0), 128, [], ["wb"])
+    op("v", lambda: V.memset(T.zb[:], 0.0), 72, [], ["zb"])
+    op("v", lambda: V.memset(T.bdb[:], 1.0), 64, [], ["bdb"])
+    op("v", lambda: V.memset(T.zb[:, 15::16], 1.0), 9, ["zb"], ["zb"])
+    op("v", lambda: V.memset(T.bs[:, :, :, 0:8], 0.0), 32, [], ["pad"])
+    op("v", lambda: V.memset(T.cbig[:], ROUND2048), 128, [], ["cbig"])
+    op("v", lambda: V.memset(T.c3[:], -31.5), 64, [], ["c3"])
+    op("v", lambda: V.memset(T.zero[:], 0.0), 64, [], ["zero"])
+    op("g", lambda: g.affine_select(T.wb[:], T.wb[:], [[0, 2], [-1, 128]], Op.is_equal, 0.0, 0, 1), 256, ["wb"], ["wb"])
+    op("g", lambda: g.affine_select(T.zb[:, 15::16], T.zb[:, 15::16], [[-16, 9]], Op.is_ge, 0.0, 0, 1), 9, ["zb"], ["zb"])
+    op("g", lambda: g.affine_select(T.zb[:, 15::16], T.zb[:, 15::16], [[16, 9]], Op.is_ge, 0.0, 15, -1), 9, ["zb"], ["zb"])
+    send([(rem[0], part(e_off, 0, 2), "aqr", mine, mine), (rem[1], part(e_off, 1, 2), "aqr", mine, mine), (mate, part(e_on, 0, 1), "aqm", mine, mine)],
+         ["q%d" % rank], [("aqm", ["q%d" % mate], 0), ("aqr", rs("q", rem0, 2) + ["qgone"], 2)], FLIGHT + FIRST)
+    op("g", lambda: g.iota(T.c1[:], [[0, 8], [-64, 4], [0, 4]], int(ROUND64), 0, allow_small_or_imprecise_dtypes=True), 128, [], ["c1"])
+    op("g", lambda: g.iota(T.c2[:], [[0, 8], [-16, 4], [0, 4]], 0, 0, allow_small_or_imprecise_dtypes=True), 128, [], ["c2"])
+    op("g", lambda: g.affine_select(T.bdb[:], T.bdb[:], [[-16, 8], [0, 16]], Op.is_ge, 0.0, 0, 1), 128, ["bdb"], ["bdb"])
+    op("g", lambda: g.affine_select(T.bdb[:], T.bdb[:], [[16, 8], [0, 16]], Op.is_ge, 0.0, 15, -1), 128, ["bdb"], ["bdb"])
+    op("v", lambda: V.tensor_copy(T.wh[:], T.wb[:]), 128, ["wb"], ["wh"])
+    op("v", lambda: V.tensor_copy(T.zh[:], T.zb[:]), 72, ["zb"], ["zh"])
+    op("v", lambda: V.tensor_scalar(T.neg[:], ident, -1.0, None, Op.mult), 64, ["wb"], ["neg"])
+    op("v", [lambda k=k: V.tensor_copy(T.sel[:, :, k, :], ident) for k in range(4)], 64, ["wb"], ["sel"])
+    op("v", lambda: V.tensor_copy(T.off[:], T.nmi[:]), 256, ["nmi"], ["off"])
+    op("v", lambda: V.tensor_copy(T.nmh[:], T.nmi[:]), 256, ["nmi"], ["nmh"])
+    op("v", lambda: V.tensor_copy(T.nl[:], T.nmi[:, 0::2, :]), 128, ["nmi"], ["nl"])
+    op("v", lambda: V.tensor_tensor(T.dn[:], T.nmi[:, 1::2, :], T.nmi[:, 0::2, :], Op.subtract), 256, ["nmi"], ["dn"])
+    dma("y", "lu", [(T.uw[:], T.ue[:])], ["qgone"], ["uw"], 4.0, "load")
+    dma("y", "lv", [(T.vw[:], T.ve[:])], ["qgone"], ["vw"], 6.0, "load")
+    dma("y", "lx", [(T.xb[:], T.x0[:])], ["qgone"], ["xb"], 6.5, "load")
+    dma("y", "lm", [(T.mb[:], T.mm[:])], ["qgone"], ["mb"], 6.5, "load")
+
+    def names_of(c, h):
+        r0, n = span(h)
+        return T.off[:, c * 64 + r0 * 16:c * 64 + (r0 + n) * 16]
+
+    def gather(c, h):
+        r0, n = span(h)
+        op("v", lambda: V.tensor_tensor(T.prod[:, c, tok(r0, n)], T.kw[:].indirect(names_of(c, h)), T.qall[:, tok(r0, n)], Op.mult),
+           256 * n * GATHER, ["kw", "off"] + rs("q", r0, n), tags("prod%d" % c, h), line="keys")
+
+    def owners(b):
+        return {"pX": ["X"], "pM": rs("M", 0, 5), "pD0": rs("D", loc0, 2), "pD1": rs("D", rem0, 2), "pW": ["accpW", "L0", "L1"],
+                "pF": ["F", "Fs", "Ft", "Fu", "Fa"]}[b]
+
+    def hold(q, c, h, b, j):
+        r0, n = span(h)
+        out, src = T.rawk[:, c, tok(r0, n)], T.kw[:].indirect(names_of(c, h))
+        op(q, (lambda: V.tensor_copy(out, src)) if q == "v" else (lambda: S.activation(out, src, Act.Copy)), 256 * n * GATHER,
+           ["kw", "off"], tags("raw%d" % c, h), line="keys" if q == "v" else "steps")
+        op("t", lambda: PE.matmul(T[b][:, 4 * j:4 * (j + n), :], ident, out, True, True), 256 * n, ["wb"] + tags("raw%d" % c, h),
+           tags("held%d" % c, h) + (owners(b) if j == 0 else []), [b])
+
+    def times(c, h, b, j):
+        r0, n = span(h)
+        op("v", lambda: V.tensor_tensor(T.prod[:, c, tok(r0, n)], T[b][:, 4 * j:4 * (j + n), :], T.qall[:, tok(r0, n)], Op.mult), 256 * n,
+           tags("held%d" % c, h) + owners(b) + rs("q", r0, n), tags("prod%d" % c, h), [b], "keys")
+
+    def score(j, h, b):
+        r0, n = span(h)
+        op("t", [lambda i=i: PE.matmul(T[b][:, j, 0:32 * n], T.zh[:, 15 - i:143 - i], T.prod[:, j::2, 256 * r0 + i:256 * (r0 + n):16], i == 0, i == 15)
+                 for i in range(16)], 64, ["zh"] + tags("prod%d" % j, h) + tags("prod%d" % (j + 2), h), ["S%d%s" % (j, b), "acc" + b] + (["h" + b] if j == 0 else []), [b])
+
+    def winners(l, h, b):
+        cs, P = col(h), T[b]
+        w = 16 * span(h)[1]
+        score(0, h, b)
+        op("s", lambda: S.activation(T.sl[:, :, cs], P[:, 0, 0:2 * w], Act.Copy), 2 * w, ["S0" + b], ["sl" + b], [b])
+        score(1, h, b)
+        right, g1, t1 = P[:, 1, 0:2 * w], P[:, 2, 0:2 * w], P[:, 3, 0:2 * w]
+        for out, x, y, o, reads, writes, banks in [
+                (g1, right, T.sl[:, :, cs], Op.is_gt, ["S1" + b, "sl" + b], ["g" + b], [b]),
+                (T.mx[:, :, cs], right, T.sl[:, :, cs], Op.max, ["S1" + b, "sl" + b], ["mx" + b], [b]),
+                (t1, g1, T.dn[:, :, cs], Op.mult, ["g" + b, "dn"], ["t" + b], [b]),
+                (P[:, 0, 0:w], T.mx[:, 0, cs], T.mx[:, 1, cs], Op.is_ge, ["mx" + b], ["S0" + b], [b]),
+                (P[:, 0, w:2 * w], T.mx[:, 1, cs], T.mx[:, 0, cs], Op.is_gt, ["mx" + b], ["h" + b], [b]),
+                (T.nx[:, :, cs], t1, T.nl[:, :, cs], Op.add, ["t" + b, "nl"], ["nx" + b], [b]),
+                (T.px[:, :, cs], P[:, 0, 0:2 * w], T.nx[:, :, cs], Op.mult, ["S0" + b, "h" + b, "nx" + b], ["px" + b], [b]),
+                (T.w16[:, l, cs], T.px[:, 0, cs], T.px[:, 1, cs], Op.add, ["px" + b], tags("w%d" % l, h), [])]:
+            op("v", lambda out=out, x=x, y=y, o=o: V.tensor_tensor(out, x, y, o), 64, reads, writes, banks)
+        op("v", lambda: V.tensor_copy(T.wu[:, l, cs], T.w16[:, l, cs]), 64, tags("w%d" % l, h), tags("wu%d" % l, h))
+
+    def tell(l):
+        src, dst, sem = T.w16[:, l, :], T.wr[:, l, rank, :], "aw%d" % l
+        send([(rem[0], part(e_off, 0, 2), sem, src, dst), (rem[1], part(e_off, 1, 2), sem, src, dst), (mate, part(e_on, 0, 1), sem, src, dst)],
+             tags("w%d" % l, "a"), [(sem, ["wr%d" % l], 0.5)])
+
+    def names(l):
+        NP = T.pA[:, 4:8, :]
+        pairs = [(r, c) for r in range(N) if r != rank for c in range(4)]
+        for b, tag in (("pB", "H"), ("pA", "N")):
+            op("t", [lambda b=b: PE.matmul(T[b][:, 4:8, :], identh, T.nmh[:], True, False)]
+               + ([lambda: PE.matmul(NP, ident, T.cbig[:], False, False)] if tag == "N" else [])
+               + [lambda b=b, c=c: PE.matmul(T[b][:, 4 + c, :], shifth, T.w16[:, l, :], False, False) for c in range(4)], 128,
+               ["wh", "wb", "nmh", "cbig"] + tags("w%d" % l, "a"), [tag, "W" + b, "acc" + b], [b])
+        for b, tag in (("pB", "H"), ("pA", "N")):
+            op("t", [lambda b=b, r=r, c=c, end=tag == "H" and (r, c) == pairs[-1]: PE.matmul(T[b][:, 4 + c, :], shifth, T.wr[:, l, r, :], False, end)
+                     for r, c in pairs], 64, ["wh", "wr%d" % l], [tag, "acc" + b], [b], "names")
+        op("s", lambda: S.activation(T.hb[:], T.pB[:, 4:8, :], Act.Identity, bias=1023.5 - ROUND2048, scale=-1.0), 256, ["H"], ["hb"], ["pB"])
+        op("t", lambda: PE.matmul(NP, ident, T.hb[:], False, True), 256, ["wb", "hb"], ["N", "accpA"], ["pA"])
+        op("v", lambda: V.tensor_copy(T.off[:], NP), 256, ["N"], ["off"], ["pA"])
+        op("s", lambda: S.activation(T.nl[:], T.pA[:, 4::2, :], Act.Copy), 128, ["N"], ["nl"], ["pA"])
+        op("v", lambda: V.tensor_tensor(T.dn[:], T.pA[:, 5::2, :], T.nl[:], Op.subtract), 128, ["N", "nl"], ["dn"], ["pA"])
+
+    F, FS, FT, FA = T.pF[:, 0:2, 0:33], T.pF[:, 2:4, 0:32], T.pF[:, 4:6, :], T.pF[:, 6:8, 0:32]
+
+    def count_start(l):
+        last = l == NL - 1
+        j = NL if last else l
+        if last:
+            op("s", lambda: S.activation(T.bs[:, NL, :, 8:72], T.bs[:, l, :, 8:72], Act.Identity, bias=float(NL)), 128, ["b%d" % l], ["b%d" % NL])
+        op("s", lambda: S.activation(T.blo[:, l], T.bs[:, l, :, 8:72], Act.Identity, bias=float(NL - 2) if last else -2.0), 128, ["b%d" % l], ["blo%d" % l])
+        op("t", [lambda: PE.matmul(FS, ident, T.bs[:, j, :, 8:72:2], True, False), lambda: PE.matmul(FS, ident, T.bs[:, j, :, 7:71:2], False, True),
+                 lambda: PE.matmul(F, ident, T.bs[:, j, :, 7:72:2], True, False)], 64, ["wb", "pad", "b%d" % j], ["F", "Fs", "Ft"], ["pF"])
+
+    def count(l, k, h, b):
+        def turn(b, cols):
+            return [lambda: PE.matmul(T[b][:, cols, :], ident, T.c1[:], True, False)] + [
+                lambda j=j: PE.matmul(T[b][32 * j:32 * j + 32, cols, :], T.w16[:, l, col(h)], T.sel[:, :, :, 4 * j:4 * j + 4], False, False) for j in range(4)]
+        high, low = T[b][:, 4:6, :], T.pW[:, 2 * k:2 * k + 2, :]
+        op("t", turn(b, slice(4, 6)) + [lambda: PE.matmul(high, ident, T.c3[:], False, True)], 128,
+           ["wb", "c1", "c3", "sel"] + tags("w%d" % l, h), ["W" + b, "acc" + b, {"pA": "N", "pB": "H"}[b]], [b], "turn")
+        op("t", turn("pW", slice(2 * k, 2 * k + 2)) + [lambda: PE.matmul(low, ident, T.c2[:], False, False)], 128,
+           ["wb", "c1", "c2", "sel"] + tags("w%d" % l, h), ["L%d" % k, "accpW"], ["pW"], "turn")
+        op("s", lambda: S.activation(T.dv[:, k], high, Act.Copy), 128, ["W" + b], ["dv%d" % k], [b], "steps")
+        op("t", lambda: PE.matmul(low, T.neg[:], T.dv[:, k], False, True), 128, ["neg", "dv%d" % k], ["L%d" % k, "accpW"], ["pW"])
+        for u in range(8):
+            op("v", lambda u=u: V.tensor_scalar(T.oh[:, 8 * k:8 * k + 8, u, :], T.dv[:, k], ROUND64 + 256.0 * u, 4096.0, Op.is_equal, Op.mult), 64,
+               ["dv%d" % k], ["oh%d%d" % (k, u)], line="hot")
+            op("s", lambda u=u: S.activation(T.th[:, 8 * k:8 * k + 8, u::8, :], low, Act.Sigmoid, bias=-256.0 * u - EDGE, scale=128.0), 128,
+               ["L%d" % k], ["th%d%d" % (k, u)], ["pW"], "steps")
+        op("t", [lambda gr=gr, i=i: PE.matmul(T.pF[32 * (gr % 4):32 * (gr % 4) + 32, gr // 4, 0:32], T.oh[:, 8 * k + gr, :, i::4], T.th[:, 8 * k + gr, :, i],
+                                               False, False) for gr in range(8) for i in range(4)]
+           + ([lambda: PE.matmul(F, ident, T.zero[:], False, True)] if k == 1 else []), 32,
+           ["wb", "zero"] + ["%s%d%d" % (x, k, u) for x in ("oh", "th") for u in range(8)], ["F"], ["pF"])
+
+    def biases(l):
+        last = l == NL - 1
+        new = T.bout[:] if last else T.bs[:, l + 1, :, 8:72]
+        for fn, n, reads, writes in [
+                (lambda: V.tensor_scalar(T.i2[:], F, ROUND4096, -ROUND4096, Op.add, Op.add), 66, ["F"], ["i2"]),
+                (lambda: V.tensor_scalar(T.im[:], F, 2.0 ** -12, ROUND1, Op.mult, Op.add), 66, ["F"], ["im"]),
+                (lambda: V.tensor_tensor(T.ee[:], F, T.i2[:], Op.subtract), 66, ["F", "i2"], ["ee"]),
+                (lambda: V.tensor_tensor(FA, T.im[:, :, 1:33], T.im[:, :, 0:32], Op.subtract), 128, ["im"], ["Fa"]),
+                (lambda: V.tensor_tensor(T.pF[:, 4:6, 0::2], FS, T.ee[:, :, 0:32], Op.subtract), 64, ["Fs", "ee"], ["Ft"]),
+                (lambda: V.tensor_tensor(T.pF[:, 4:6, 1::2], FA, T.ee[:, :, 1:33], Op.add), 64, ["Fa", "ee"], ["Fu"]),
+                (lambda: V.tensor_tensor(new, FT, T.blo[:, l], Op.max), 128, ["Ft", "Fu", "blo%d" % l], ["bout" if last else "b%d" % (l + 1)])]:
+            op("v", fn, n, reads, writes, ["pF"])
+        if last:
+            dma("y", "oyb", [(T.yb[4 * half:4 * half + 4, :], T.bout[:, half, :]) for half in range(2)], ["bout"], ["yb"])
+        else:
+            dma("y", "bias%d" % l, [(bias_rows(T.kw, half), T.bs[:, l + 1, half, 8:72]) for half in range(2)], ["b%d" % (l + 1)], ["kw", "kw%d" % l])
+
+    def pick(l, kind, h, q):
+        r = span(h)[0]
+        src = (T.uw if kind == "u" else T.vw)[:].indirect(T.wu[:, l, col(h)])
+        out = (T.uvr if r == rank else T.uvs)[:, 4 * l + r, "uv".index(kind), :]
+        op(q.lower(), (lambda: V.tensor_copy(out, src)) if q == "v" else (lambda: S.activation(out, src, Act.Copy)),
+           256 * GATHER, [kind + "w", "wu%d_%d" % (l, r)], ["%s%s%d%d" % (kind, "r" if r == rank else "s", l, r)], line="steps" if q == "S" else None)
+
+    def parcel(l, kinds, hs, qs):
+        to = [span(h)[0] for h in hs.split("+")]
+        for (kind, h), q in zip([(kind, h) for kind in kinds for h in hs.split("+")], qs):
+            pick(l, kind, h, q)
+        if to != [rank]:
+            sem, k = "a%d%s%s" % (l, kinds, hs[0:2]), slice("uv".index(kinds[0]), "uv".index(kinds[-1]) + 1)
+            send([(r, part(e_on if r == mate else e_off, i, len(to)), sem, T.uvs[:, 4 * l + r, k], T.uvr[:, 4 * l + rank, k]) for i, r in enumerate(to)],
+                 ["%ss%d%d" % (kind, l, r) for kind in kinds for r in to],
+                 [(sem, ["%sr%d%d" % (kind, l, r) for kind in kinds for r in to], 0 if to == [mate] else len(to) * len(kinds))])
+
+    X, M = T.pX[:, 0:4, :], T.pM[:, 0:4, :]
+    mixed = [0]
+
+    def mix(rhs):
+        mixed[0] += 1
+        return PE.matmul(M, T.m32[:], rhs, mixed[0] % 5 == 1, mixed[0] % 5 == 0)
+
+    def expert(l, h):
+        r = span(h)[0]
+        b, j = ("pD1", r - rem0) if r in rem else ("pD0", r - loc0)
+        D = T[b][:, 4 * j:4 * j + 4, :]
+        op("v", lambda: V.tensor_tensor(T.pu[:, tok(r)], X, T.uvr[:, 4 * l + r, 0, :], Op.mult), 256, ["X", "ur%d%d" % (l, r)], ["pu%d" % r], ["pX"])
+        op("t", lambda: PE.matmul(D, T.bd[:], T.pu[:, tok(r)], True, True), 1024, ["bd", "pu%d" % r], ["D%d" % r], [b])
+        op("s", lambda: S.activation(T.sg[:, tok(r)], D, Act.Sigmoid), 256, ["D%d" % r], ["sg%d" % r], [b])
+        op("v", lambda: V.tensor_tensor(D, D, T.sg[:, tok(r)], Op.mult), 256, ["D%d" % r, "sg%d" % r], ["D%d" % r], [b])
+        op("v", lambda: V.tensor_tensor(T.yy[:, tok(r)], D, T.uvr[:, 4 * l + r, 1, :], Op.mult), 256, ["D%d" % r, "vr%d%d" % (l, r)], ["y%d" % r], [b])
+        op("t", lambda: mix(T.yy[:, tok(r)]), 1024, ["m32", "y%d" % r], ["M%d" % r], ["pM"])
+
+    def tokens(l):
+        op("t", lambda: mix(T.xs2[:]), 1024, ["m32", "xs2"], ["M4"], ["pM"])
+        op("s", lambda: S.activation(T.sx[:], M, Act.Sigmoid, scale=0.5), 256, rs("M", 0, 5), ["sx"], ["pM"])
+        if l == NL - 1:
+            op("s", lambda: S.activation(T.xo[:], T.sx[:], Act.Identity, bias=-1.0, scale=2.0), 256, ["sx"], ["xo"])
+            dma("s", "oyx", [(T.yx[:], T.xo[:])], ["xo"], ["yx"])
+        else:
+            op("s", lambda: S.activation(X, T.sx[:], Act.Identity, bias=-1.0, scale=2.0), 256, ["sx"], ["X"], ["pX"])
+            calls[-1]["due"] = DUE[l]
+            op("s", lambda: S.activation(T.xs2[:], T.sx[:], Act.Identity, bias=-2.0, scale=4.0), 256, ["sx"], ["xs2"])
+
+    for l in range(NL):
+        turns = (0, 2, 1, 3)
+        if l == 0:
+            for c in turns:
+                hold("v", c, "m", ("pW", "pF")[c % 2], c // 2)
+                hold("s", c, "r", ("pD0", "pD1", "pX", "pM")[c], 0)
+            for c in turns:
+                gather(c, "o")
+            for c in turns:
+                times(c, "m", ("pW", "pF")[c % 2], c // 2)
+            for c in turns:
+                times(c, "r", ("pD0", "pD1", "pX", "pM")[c], 0)
+        else:
+            for c in HELD:
+                hold("s", c, "l", HELD[c], 0)
+            for step in PLAN[l]:
+                for c in turns if step[0] == "judge" else ():
+                    if c in HELD and step[1] in "lmo":
+                        times(c, step[1], HELD[c], span(step[1])[0] - loc0)
+                    else:
+                        gather(c, step[1])
+        if l == 0:
+            op("s", lambda: S.activation(T.bd[:], T.bdb[:], Act.Sigmoid, bias=-128.0, scale=256.0), 1500, ["bdb"] + tags("raw3", "r"), ["bd", "wide"])
+            op("s", lambda: S.activation(T.m32[:], T.mb[:], Act.Copy), 128, ["mb"], ["m32"])
+            op("s", lambda: S.activation(X, T.xb[:], Act.Copy), 256, ["xb"], ["X"], ["pX"])
+            op("s", lambda: S.activation(T.xs2[:], T.xb[:], Act.Identity, scale=2.0), 256, ["xb"], ["xs2"])
+        count_start(l)
+        for step in PLAN[l]:
+            {"judge": winners, "count": count, "send": parcel, "tell": tell, "names": names, "biases": biases}[step[0]](l, *step[1:])
+        for h in ("o", "m", "ra", "rb"):
+            expert(l, h)
+        tokens(l)
+
+    issue(g, T, topo, core, calls)
+
+
+def arrange(calls):
+    lastw, readers, before = {}, {}, []
+    for i, c in enumerate(calls):
+        need = {lastw[r] for r in list(c["reads"]) + list(c["writes"]) if r in lastw}
+        for r in c["writes"]:
+            need.update(readers.get(r, []))
+        if "after" in c:
+            need.add(c["after"])
+        before.append(need - {i})
+        for r in c["reads"]:
+            readers.setdefault(r, []).append(i)
+        for r in c["writes"]:
+            lastw[r], readers[r] = i, []
+        if c["kind"] == "send":
+            lastw[c["local"]] = i
+    behind, last = {}, {}
+    for i, c in enumerate(calls):
+        if c.get("line"):
+            if c["line"] in last:
+                behind[i] = last[c["line"]]
+            last[c["line"]] = i
+    n = len(calls)
+    edges = [(j, i, calls[j]["late"] + (calls[i]["flight"] if calls[i].get("after") == j else 0.0)) for i in range(n) for j in before[i]]
+    edges += [(j, i, 0.0) for i, j in behind.items()]
+    busy = [c["busy"] + 1e-4 for c in calls]
+
+    def place(order, back):
+        need = [[] for _ in calls]
+        for j, i, lag in edges:
+            need[j if back else i].append((i if back else j, lag))
+        start, taken = {}, {}
+        for i in order:
+            c = calls[i]
+            t = max([c["late"] if back else 0.0] + [start[j] + busy[j] + lag for j, lag in need[i]])
+            spans = [(a, b) for a, b, _q in taken.get(c["q"], []) if b > t]
+            spans += [(a - HOP, b + HOP) for k in c["banks"] for a, b, q in taken.get(k, []) if q != c["q"] and b + HOP > t]
+            for a, b in sorted(spans):
+                if a >= t + busy[i]:
+                    break
+                t = max(t, b)
+            start[i] = t
+            for k in ([c["q"]] if c["q"] else []) + list(c["banks"]):
+                taken.setdefault(k, []).append((t, t + busy[i], c["q"]))
+        return start
+    way = [max(busy[i] + calls[i]["late"], calls[i].get("due", 0)) for i in range(n)]
+    for j, i, lag in sorted(edges, key=lambda e: -e[1]):
+        way[j] = max(way[j], busy[j] + lag + way[i])
+    start = place(sorted(range(n), key=lambda i: -way[i]), False)
+    for _ in range(ROUNDS):
+        back = place(sorted(range(n), key=lambda i: -start[i] - busy[i]), True)
+        start = place(sorted(range(n), key=lambda i: -back[i] - busy[i]), False)
+        LOG.append(max(start[i] + busy[i] + calls[i]["late"] for i in range(n)))
+    return [calls[i] for i in sorted(range(n), key=lambda i: start[i])]
+
+
+ROUNDS = 1
+LOG = []
+
+
+def issue(g, T, topo, core, calls):
     Q = {"v": g.vector, "s": g.scalar, "t": g.tensor, "g": g, "y": g.sync}
-    CS = {"v": "cv", "s": "cs", "t": "ct", "g": "cg"}
     known = {q: {} for q in Q}
-    count = {}
-    lastw, readers, bank = {}, {}, {}
+    count, lastw, readers, bank = {}, {}, {}, {}
 
     def wait(q, ev):
         sem, n, snap, _src = ev
@@ -77,397 +420,45 @@ def rank_program(g, core, T, topo):
             if known[q].get(k, 0) < m:
                 known[q][k] = m
 
-    def order(q, src, reads, writes, banks):
-        need = []
-        for r in reads:
-            need.append(lastw[r])
-        for r in writes:
-            if r in lastw and lastw[r][3] != src:
-                need.append(lastw[r])
-            need += [ev for ev in readers.get(r, []) if ev[3] != src]
-        for b in banks:
-            need += [ev for o, ev in bank.get(b, {}).items() if o != q]
-        need.sort(key=lambda ev: -ev[1])
-        for ev in need:
-            wait(q, ev)
-
-    def note(ev, q, reads, writes, banks):
+    for c in arrange(calls):
+        q, kind, reads, writes = c["q"], c["kind"], c["reads"], c["writes"]
+        if kind == "land":
+            count[c["sem"]] = c["n"]
+            ev, reads = (c["sem"], c["n"], {}, c["sem"]), []
+        else:
+            src = q if kind == "op" else kind
+            need = [lastw[r] for r in reads if r in lastw]
+            for r in writes:
+                need += [ev for ev in [lastw.get(r)] + readers.get(r, []) if ev and (ev[3], src) != ("t", "t")]
+            for b in c["banks"]:
+                need += [ev for o, ev in bank.get(b, {}).items() if o != q]
+            for ev in sorted(need, key=lambda ev: -ev[1]):
+                wait(q, ev)
+            if kind == "op":
+                sem = "c" + q
+                for f in c["fns"][:-1]:
+                    f()
+                c["fns"][-1]().then_inc(T.sem[sem], 1)
+                count[sem] = count.get(sem, 0) + 1
+            elif kind == "dma":
+                sem = c["sem"]
+                for out, in_ in c["pairs"]:
+                    Q[q].dma_start(out, in_).then_inc(T.sem[sem], 16)
+                count[sem] = 16 * len(c["pairs"])
+            else:
+                sem, tr = c["local"], []
+                for r, m, s, a, b in c["items"]:
+                    rid, pid = topo.addr(T.cores[r], core)
+                    tr.append(RemoteDMATransfer(dst_ids=[DstId(rid=rid, pnc=pid)], dma_engine_mask=m, remote_sem=T.sem[s], src=a, dst=b))
+                    count[sem] = count.get(sem, 0) + bin(m).count("1")
+                g.remote_dma_fused(tr, local_sem=T.sem[sem])
+                reads, writes = [], [sem]
+            ev = (sem, count[sem], dict(known[q]), src)
         for r in reads:
             readers.setdefault(r, []).append(ev)
         for r in writes:
-            lastw[r] = ev
-            readers[r] = []
-        for b in banks:
+            lastw[r], readers[r] = ev, []
+        for b in c["banks"]:
             bank.setdefault(b, {})[q] = ev
-
-    def op(q, fns, reads, writes, banks=()):
-        order(q, q, reads, writes, banks)
-        if not isinstance(fns, list):
-            fns = [fns]
-        for f in fns[:-1]:
-            f()
-        sem = CS[q]
-        fns[-1]().then_inc(T.sem[sem], 1)
-        count[sem] = count.get(sem, 0) + 1
-        note((sem, count[sem], dict(known[q]), q), q, reads, writes, banks)
-
-    def dma(q, sem, out, in_, reads, writes):
-        order(q, sem, reads, writes, ())
-        Q[q].dma_start(out, in_).then_inc(T.sem[sem], 16)
-        count[sem] = count.get(sem, 0) + 16
-        note((sem, count[sem], dict(known[q]), sem), q, reads, writes, ())
-
-    def send(items, reads, local="sent"):
-        order("g", "sent", reads, (), ())
-        tr = []
-        for r, m, sem, src, dst in items:
-            rid, pid = topo.addr(T.cores[r], core)
-            tr.append(RemoteDMATransfer(dst_ids=[DstId(rid=rid, pnc=pid)], dma_engine_mask=m, remote_sem=T.sem[sem], src=src, dst=dst))
-            count[local] = count.get(local, 0) + bin(m).count("1")
-        g.remote_dma_fused(tr, local_sem=T.sem[local])
-
-    def lands(sem, n, writes):
-        count[sem] = n
-        note((sem, n, {}, sem), None, (), writes, ())
-
-    V, S, PE = g.vector, g.scalar, g.tensor
-    ident, identh, shifth = T.wb[:, 0:8, :], T.wh[:, 0:8, :], T.wh[:, 7:15, :]
-
-    dma("y", "lq", T.qall[:, rank * 256:(rank + 1) * 256], T.rq[:], (), ["q%d" % rank])
-    dma("y", "lnm", T.nmi[:], T.nm[:], (), ["nmi"])
-    dma("y", "lke", T.kw[:], T.ke[:], (), ["kw"])
-    op("v", lambda: V.memset(T.wb[:], 1.0), (), ["wb"])
-    op("v", lambda: V.memset(T.zb[:], 0.0), (), ["zb"])
-    op("v", lambda: V.memset(T.bd[:], 1.0), (), ["bd"])
-    op("v", lambda: V.memset(T.zb[:, 15::16], 1.0), ["zb"], ["zb"])
-    op("g", lambda: g.affine_select(T.wb[:], T.wb[:], [[0, 2], [-1, 128]], Op.is_equal, 0.0, 0, 1), ["wb"], ["wb"])
-    op("g", lambda: g.affine_select(T.zb[:, 15::16], T.zb[:, 15::16], [[-16, 9]], Op.is_ge, 0.0, 0, 1), ["zb"], ["zb"])
-    op("g", lambda: g.affine_select(T.zb[:, 15::16], T.zb[:, 15::16], [[16, 9]], Op.is_ge, 0.0, 15, -1), ["zb"], ["zb"])
-    mine = T.qall[:, rank * 256:(rank + 1) * 256]
-    send([(rem[0], part(e_off, 0, 2), "aqr", mine, mine), (rem[1], part(e_off, 1, 2), "aqr", mine, mine),
-          (mate, mask(e_on), "aqm", mine, mine)], ["q%d" % rank], "sentq")
-    lands("aqm", len(e_on), ["q%d" % mate])
-    lands("aqr", len(e_off), ["q%d" % r for r in rem])
-    op("g", lambda: g.affine_select(T.bd[:], T.bd[:], [[-16, 8], [0, 16]], Op.is_ge, 0.0, 0, 1), ["bd"], ["bd"])
-    op("g", lambda: g.affine_select(T.bd[:], T.bd[:], [[16, 8], [0, 16]], Op.is_ge, 0.0, 15, -1), ["bd"], ["bd"])
-    op("v", lambda: V.memset(T.w16[:], 0.0), (), ["wz"])
-    op("v", lambda: V.memset(T.cbig[:], ROUND2048), (), ["cbig"])
-    op("v", lambda: V.memset(T.cmid[:], -15.5), (), ["cmid"])
-    op("v", lambda: V.memset(T.th[:, :, 32, :], -1.0), (), ["th32"])
-    op("v", lambda: V.tensor_copy(T.wh[:], T.wb[:]), ["wb"], ["wh"])
-    op("v", lambda: V.tensor_copy(T.zh[:], T.zb[:]), ["zb"], ["zh"])
-    op("v", lambda: V.tensor_copy(T.off[:], T.nmi[:]), ["nmi"], ["off"])
-    op("v", lambda: V.tensor_copy(T.nmh[:], T.nmi[:]), ["nmi"], ["nmh"])
-    op("v", lambda: V.tensor_reduce(T.row15[:], T.wb[:, 0:8, 15], AxisListType.X, Op.add), ["wb"], ["row15"])
-    op("v", lambda: V.tensor_scalar(T.rows[:], T.row15[:], -1.0, 1.0, Op.mult, Op.add), ["row15"], ["rows"])
-    op("v", lambda: V.tensor_scalar(T.z15[:], T.zb[:], T.row15[:], None, Op.mult), ["zb", "row15"], ["z15"])
-    wait("y", ("sentq", count["sentq"], {}, None))
-    for p in range(4):
-        dma("y", "lb", T.bs[:, 0, p, :], T.ke[32 * p + 15:32 * p + 32:16, :], (), ["b0"])
-    dma("y", "lu", T.uw[:], T.ue[:], (), ["uw"])
-    dma("y", "lv", T.vw[:], T.ve[:], (), ["vw"])
-    dma("y", "lx", T.xb[:], T.x0[:], (), ["xb", "mb"])
-    dma("y", "lx", T.mb[:], T.mm[:], (), ["xb", "mb"])
-    op("t", lambda: PE.matmul(T.pN[:, 0:256], identh, T.nmh[:], True, True), ["wh", "nmh"], ["N"], ["N"])
-    op("s", lambda: S.activation(T.n0[:], T.pN[:, 0:64], Act.Copy), ["N"], ["n0"], ["N"])
-
-    def span(h):
-        return {"a": (0, 4), "l": (loc0, 2), "r": (rem0, 2), "o": (rank, 1), "m": (mate, 1)}[h]
-
-    def rs(name, r0, n):
-        return ["%s%d" % (name, r) for r in range(r0, r0 + n)]
-
-    def tok(r0, n=1):
-        return slice(256 * r0, 256 * (r0 + n))
-
-    def tags(name, h):
-        return rs(name + "_", *span(h))
-
-    def gather(c, h, fixed=False):
-        r0, n = span(h)
-        a, k = c * 1024 + r0 * 256, c * 64 + r0 * 16
-        win = T.kw0 if fixed else T.kw
-        op("v", lambda: V.tensor_tensor(T.prod[:, a:a + 256 * n], win[:].indirect(T.off[:, k:k + 16 * n]), T.qall[:, tok(r0, n)], Op.mult),
-           ["kw0" if fixed else "kw", "off"] + rs("q", r0, n), tags("prod%d" % c, h))
-
-    def held(c, h):
-        if h == "m":
-            b, j = ("pX", "pM")[c // 2], c % 2
-            return b, T[b][:, tok(j)]
-        b = ("pD0", "pD1", "pX", "pM")[c]
-        return b, T[b][:]
-
-    def owners(b):
-        return {"pX": ["X"], "pM": ["M"], "pD0": rs("D", loc0, 2), "pD1": rs("D", rem0, 2)}[b]
-
-    def raw(q, c, h):
-        r0, n = span(h)
-        a, k = c * 1024 + r0 * 256, c * 64 + r0 * 16
-        out, src = T.rawk[:, a:a + 256 * n], T.kw[:].indirect(T.off[:, k:k + 16 * n])
-        op(q, (lambda: V.tensor_copy(out, src)) if q == "v" else (lambda: S.activation(out, src, Act.Copy)), ["kw", "off"], tags("raw%d" % c, h))
-
-    def hold(c, h):
-        r0, n = span(h)
-        a = c * 1024 + r0 * 256
-        b, place = held(c, h)
-        op("t", lambda: PE.matmul(place, ident, T.rawk[:, a:a + 256 * n], True, True), ["wb"] + tags("raw%d" % c, h), owners(b), [b])
-
-    def times_q(c, h):
-        r0, n = span(h)
-        a = c * 1024 + r0 * 256
-        b, place = held(c, h)
-        op("v", lambda: V.tensor_tensor(T.prod[:, a:a + 256 * n], place, T.qall[:, tok(r0, n)], Op.mult),
-           owners(b) + rs("q", r0, n), tags("prod%d" % c, h), [b])
-
-    def to_list(out, z, src, a, n):
-        return [lambda i=i: PE.matmul(out, z[:, 15 - i:143 - i], src[:, a + i:a + n:16], i == 0, i == 15) for i in range(16)]
-
-    def score(c, h):
-        r0, n = span(h)
-        cols = slice(r0 * 16, (r0 + n) * 16)
-        b, out = [("H", T.pH[:, cols]), ("pA", T.pA[:, 0, cols]), ("pA", T.pA[:, 1, cols]), ("pB", T.pB[:, 1, cols])][c]
-        op("t", to_list(out, T.zh, T.prod, c * 1024 + r0 * 256, 256 * n), ["zh"] + tags("prod%d" % c, h), tags("S%d" % c, h), [b])
-
-    def first():
-        op("s", lambda: S.activation(T.s0[:], T.pH[:, 0:64], Act.Copy), tags("S0", "a"), ["s0"], ["H"])
-
-    def bias_pick():
-        op("s", lambda: S.activation(T.bg[:], T.kw[:].indirect(T.off[:, 0:64]), Act.Copy), ["kw", "off"], ["bg"])
-
-    def bias_list():
-        op("t", to_list(T.pH[:, 64:128], T.z15, T.bg, 0, 1024), ["z15", "bg"], ["Bc"], ["H"])
-
-    def bias_add():
-        op("v", lambda: V.tensor_tensor(T.bq[:], T.pH[:, 64:128], T.q15[:], Op.mult), ["Bc", "q15"], ["bq"], ["H"])
-        op("v", lambda: V.tensor_tensor(T.s0[:], T.pH[:, 0:64], T.bq[:], Op.add), tags("S0", "a") + ["bq"], ["s0"], ["H"])
-
-    def select(l, h):
-        r0, n = span(h)
-        a, b = r0 * 16, (r0 + n) * 16
-        A, B = T.pA, T.pB
-
-        def tt(out, x, y, o, reads, writes, banks):
-            op("v", lambda: V.tensor_tensor(out, x, y, o), reads, writes, banks)
-
-        def nm(c):
-            return T.pN[:, c * 64 + a:c * 64 + b]
-        tt(T.dn[:, 0, a:b], nm(1), T.n0[:, a:b], Op.subtract, ["N", "n0"], ["dn1"], ["N"])
-        tt(A[:, 2, a:b], A[:, 0, a:b], T.s0[:, a:b], Op.is_gt, tags("S1", h) + ["s0"], ["g1"], ["pA"])
-        tt(T.m1[:, a:b], A[:, 0, a:b], T.s0[:, a:b], Op.max, tags("S1", h) + ["s0"], ["m1"], ["pA"])
-        tt(A[:, 3, a:b], A[:, 2, a:b], T.dn[:, 0, a:b], Op.mult, ["g1", "dn1"], ["t1"], ["pA"])
-        tt(A[:, 2, 64 + a:64 + b], A[:, 1, a:b], T.m1[:, a:b], Op.is_gt, tags("S2", h) + ["m1"], ["g2"], ["pA"])
-        tt(T.n1[:, a:b], A[:, 3, a:b], T.n0[:, a:b], Op.add, ["t1", "n0"], ["n1"], ["pA"])
-        tt(T.m2[:, a:b], A[:, 1, a:b], T.m1[:, a:b], Op.max, tags("S2", h) + ["m1"], ["m2"], ["pA"])
-        tt(T.dn[:, 1, a:b], nm(2), T.n1[:, a:b], Op.subtract, ["N", "n1"], ["dn2"], ["N"])
-        tt(A[:, 3, 64 + a:64 + b], A[:, 2, 64 + a:64 + b], T.dn[:, 1, a:b], Op.mult, ["g2", "dn2"], ["t2"], ["pA"])
-        tt(T.n2[:, a:b], A[:, 3, 64 + a:64 + b], T.n1[:, a:b], Op.add, ["t2", "n1"], ["n2"], ["pA"])
-        tt(T.dn[:, 2, a:b], nm(3), T.n2[:, a:b], Op.subtract, ["N", "n2"], ["dn3"], ["N"])
-        tt(B[:, 2, a:b], B[:, 1, a:b], T.m2[:, a:b], Op.is_gt, tags("S3", h) + ["m2"], ["g3"], ["pB"])
-        tt(B[:, 3, a:b], B[:, 2, a:b], T.dn[:, 2, a:b], Op.mult, ["g3", "dn3"], ["t3"], ["pB"])
-        w0 = (2 * l + 1) * 64
-        tt(T.w16[:, w0 + a:w0 + b], B[:, 3, a:b], T.n2[:, a:b], Op.add, ["t3", "n2", "wz"], tags("w%d" % l, h), ["pB"])
-
-    def offsets(l, h):
-        r0, n = span(h)
-        a, b = r0 * 16, (r0 + n) * 16
-        w0 = (2 * l + 1) * 64
-        op("v", lambda: V.tensor_copy(T.wu[:, l, a:b], T.w16[:, w0 + a:w0 + b]), tags("w%d" % l, h), tags("wu%d" % l, h))
-
-    def send_w(l):
-        w0 = (2 * l + 1) * 64
-        src, dst, sem = T.w16[:, w0:w0 + 64], T.wr[:, l, rank, :], "aw%d" % l
-        send([(rem[0], part(e_off, 0, 2), sem, src, dst), (rem[1], part(e_off, 1, 2), sem, src, dst),
-              (mate, mask(e_on), sem, src, dst)], tags("w%d" % l, "a"))
-        lands(sem, len(e_off) + len(e_on), ["wr%d" % l])
-
-    def name_sum(l, bankname, out):
-        w0 = (2 * l + 1) * 64
-        fns = [lambda: PE.matmul(out[:, 0:256], identh, T.nmh[:], True, False)]
-        if bankname == "N":
-            fns.append(lambda: PE.matmul(out[:, 0:256], ident, T.cbig[:], False, False))
-        fns += [lambda c=c: PE.matmul(out[:, c * 64:c * 64 + 64], shifth, T.w16[:, w0:w0 + 64], False, False) for c in range(4)]
-        op("t", fns, ["wh", "wb", "nmh", "cbig"] + tags("w%d" % l, "a"), [bankname], [bankname])
-
-    def name_rest(l, bankname, out):
-        others = [r for r in range(N) if r != rank]
-        pairs = [(r, c) for r in others for c in range(4)]
-        op("t", [lambda r=r, c=c: PE.matmul(out[:, c * 64:c * 64 + 64], shifth, T.wr[:, l, r, :], False,
-                                             bankname == "H" and (r, c) == pairs[-1]) for r, c in pairs],
-           ["wh", "wr%d" % l], [bankname], [bankname])
-
-    def name_floor():
-        op("s", lambda: S.activation(T.hb[:], T.pH[:, 0:256], Act.Identity, bias=-(ROUND2048 - 1023.5), scale=-1.0), ["H"], ["hb"], ["H"])
-
-    def name_mod():
-        op("t", lambda: PE.matmul(T.pN[:, 0:256], ident, T.hb[:], False, True), ["wb", "hb"], ["N"], ["N"])
-
-    def name_off():
-        op("v", lambda: V.tensor_copy(T.off[:], T.pN[:, 0:256]), ["N"], ["off"], ["N"])
-
-    def name_first():
-        op("s", lambda: S.activation(T.n0[:], T.pN[:, 0:64], Act.Copy), ["N"], ["n0"], ["N"])
-
-    WT = T.pB[:, 0, 64:128]
-
-    def turn(l):
-        w0 = (2 * l + 1) * 64
-        op("t", [lambda: PE.matmul(WT, ident, T.cmid[:], True, False),
-                 lambda: PE.matmul(WT, T.w16[:, w0:w0 + 128], T.wh[:, 0:8, 0:8], False, False),
-                 lambda: PE.matmul(WT, T.w16[:, w0 - 64:w0 + 64], T.wh[:, 0:8, 8:16], False, True)],
-           ["wb", "wh", "cmid", "wz"] + tags("w%d" % l, "a"), ["WT"], ["pB"])
-
-    def digits():
-        op("v", lambda: V.tensor_scalar(T.dv[:, :, 0:8], WT, ROUND32, -ROUND32, Op.add, Op.add), ["WT"], ["d0"], ["pB"])
-        op("v", lambda: V.tensor_tensor(T.ev[:, :, 0, :], WT, T.dv[:, :, 0:8], Op.subtract), ["WT", "d0"], ["e0"], ["pB"])
-        op("v", lambda: V.tensor_scalar(T.dv[:, :, 8:16], T.dv[:, :, 0:8], -32.0, None, Op.add), ["d0"], ["d1"])
-        op("s", lambda: S.activation(T.ev[:, :, 1, :], T.ev[:, :, 0, :], Act.Identity, bias=-8.0), ["e0"], ["e1"])
-        op("v", lambda: V.tensor_scalar(T.dv[:, :, 16:32], T.dv[:, :, 0:16], -64.0, None, Op.add), ["d0", "d1"], ["d2"])
-        op("s", lambda: S.activation(T.ev[:, :, 2:4, :], T.ev[:, :, 0:2, :], Act.Identity, bias=-16.0), ["e0", "e1"], ["e2"])
-        op("v", lambda: V.tensor_scalar(T.dv[:, :, 32:64], T.dv[:, :, 0:32], -128.0, None, Op.add), ["d0", "d1", "d2"], ["d3"])
-
-    def onehot(k, us=range(8)):
-        op("v", [lambda u=u: V.tensor_scalar(T.oh[:, 4 * k:4 * k + 4, u, :], T.dv[:, 4 * k:4 * k + 4, :], 256.0 * u, 0.5, Op.is_equal, Op.mult)
-                 for u in us], ["d0", "d1", "d2", "d3"], ["oh%d%d" % (k, u) for u in us])
-
-    def steps(k):
-        op("s", [lambda u=u: S.activation(T.th[:, 4 * k:4 * k + 4, u:32:8, :], T.ev[:, 4 * k:4 * k + 4, :, :], Act.Sign, bias=16.0 - u)
-                 for u in range(8)], ["e0", "e1", "e2"], ["th%d" % k])
-
-    def counts(k):
-        b = "pA" if k == 0 else "pB"
-        op("t", [lambda pp=pp, i=i: PE.matmul(T[b][:, pp, 0:66], T.oh[:, 4 * k + 2 * pp:4 * k + 2 * pp + 2, :, i::8],
-                                               T.th[:, 4 * k + 2 * pp:4 * k + 2 * pp + 2, :, i], i == 0, i == 7)
-                 for pp in range(2) for i in range(8)],
-           ["th32", "th%d" % k] + ["oh%d%d" % (k, u) for u in range(8)], ["C%d" % k], [b])
-
-    def bias_ends(l):
-        last = l == NL - 1
-        if last:
-            op("s", lambda: S.activation(T.bhi[:], T.bs[:, l], Act.Identity, bias=float(NL)), ["b%d" % l], ["bhi"])
-        op("s", lambda: S.activation(T.blo[:, l], T.bs[:, l], Act.Identity, bias=float(NL - 2) if last else -2.0), ["b%d" % l], ["blo%d" % l])
-
-    def bias(l, k):
-        b = "pA" if k == 0 else "pB"
-        C, last, pp = T[b], l == NL - 1, slice(2 * k, 2 * k + 2)
-        for par in range(2):
-            rows = slice(64 * par, 64 * par + 64)
-            old = T.bhi[rows, pp, :] if last else T.bs[rows, l, pp, :]
-            op("v", lambda: V.tensor_tensor(T.t1[rows, pp, :], old, C[rows, 0:2, 33 * par:33 * par + 32], Op.subtract),
-               ["C%d" % k, "bhi" if last else "b%d" % l], ["u%d%d" % (k, par)], [b])
-        for par in range(2):
-            rows = slice(64 * par, 64 * par + 64)
-            op("v", lambda: V.tensor_tensor(C[rows, 2:4, 0:32], C[rows, 0:2, 33 * par + 1:33 * par + 33], T.t1[rows, pp, :], Op.add),
-               ["C%d" % k, "u%d%d" % (k, par)], ["v%d%d" % (k, par)], [b])
-        new = T.bout[:, pp, :] if last else T.bs[:, l + 1, pp, :]
-        op("v", lambda: V.tensor_tensor(new, C[:, 2:4, 0:32], T.blo[:, l, pp, :], Op.max),
-           ["v%d0" % k, "v%d1" % k, "blo%d" % l], ["nb%d%d" % (l, k)] + (["b%d" % (l + 1)] if k == 1 else []), [b])
-        for p in range(2 * k, 2 * k + 2):
-            if last:
-                dma("y", "oyb", T.yb[2 * p:2 * p + 2, :], T.bout[:, p, :], ["nb%d%d" % (l, k)], ["yb"])
-            else:
-                dma("y", "bias%d" % l, T.kw[32 * p + 15:32 * p + 32:16, :], T.bs[:, l + 1, p, :], ["nb%d%d" % (l, k)], ["kw"])
-
-    def pick(q, kind, l, r0, n):
-        win, to = (T.uw, T.ur if r0 == rank else T.us) if kind == "u" else (T.vw, T.vr if r0 == rank else T.vs)
-        src = win[:].indirect(T.wu[:, l, 16 * r0:16 * (r0 + n)])
-        out = to[:, l, tok(r0, n)]
-        name = ("%sr%d%d" if r0 == rank else "%ss%d%d") % (kind, l, r0)
-        op(q, (lambda: V.tensor_copy(out, src)) if q == "v" else (lambda: S.activation(out, src, Act.Copy)),
-           [kind + "w"] + rs("wu%d_" % l, r0, n), [name])
-
-    def send_far(l):
-        sem = "ar%d" % l
-        send([(rem[0], part(e_off, 0, 4), sem, T.us[:, l, tok(rem[0])], T.ur[:, l, tok(rank)]),
-              (rem[1], part(e_off, 1, 4), sem, T.us[:, l, tok(rem[1])], T.ur[:, l, tok(rank)]),
-              (rem[0], part(e_off, 2, 4), sem, T.vs[:, l, tok(rem[0])], T.vr[:, l, tok(rank)]),
-              (rem[1], part(e_off, 3, 4), sem, T.vs[:, l, tok(rem[1])], T.vr[:, l, tok(rank)])],
-             ["us%d%d" % (l, rem0), "vs%d%d" % (l, rem0)])
-        lands(sem, len(e_off), ["%sr%d%d" % (k, l, r) for k in "uv" for r in rem])
-
-    def send_near(l):
-        sem = "am%d" % l
-        send([(mate, part(e_on, 0, 2), sem, T.us[:, l, tok(mate)], T.ur[:, l, tok(rank)]),
-              (mate, part(e_on, 1, 2), sem, T.vs[:, l, tok(mate)], T.vr[:, l, tok(rank)])],
-             ["us%d%d" % (l, mate), "vs%d%d" % (l, mate)])
-        lands(sem, len(e_on), ["ur%d%d" % (l, mate), "vr%d%d" % (l, mate)])
-
-    def dplace(r0, n):
-        b = "pD1" if r0 in rem else "pD0"
-        j = r0 - (rem0 if r0 in rem else loc0)
-        return b, T[b][:, tok(j, n)]
-
-    def mul_u(l, r0, n):
-        for r in range(r0, r0 + n):
-            op("v", lambda: V.tensor_tensor(T.pu[:, tok(r)], T.pX[:, 0:256], T.ur[:, l, tok(r)], Op.mult),
-               ["X", "ur%d%d" % (l, r)], ["pu%d" % r], ["pX"])
-
-    def dsum(r0, n):
-        b, D = dplace(r0, n)
-        op("t", lambda: PE.matmul(D, T.bd[:], T.pu[:, tok(r0, n)], True, True), ["bd"] + rs("pu", r0, n), rs("D", r0, n), [b])
-
-    def act(l, r0, n):
-        b, D = dplace(r0, n)
-        sg = T.sg[:, tok(r0, n)]
-        if FORM[l] == "silu":
-            op("s", lambda: S.activation(D, D, Act.Silu), rs("D", r0, n), rs("D", r0, n), [b])
-        else:
-            op("s", lambda: S.activation(sg, D, Act.Tanh, scale=0.5), rs("D", r0, n), rs("sg", r0, n), [b])
-            op("s", lambda: S.activation(sg, sg, Act.Identity, bias=0.5, scale=0.5), rs("sg", r0, n), rs("sg", r0, n))
-
-    def mul_v(l, r0, n):
-        b, D = dplace(r0, n)
-        if FORM[l] != "silu":
-            op("v", lambda: V.tensor_tensor(D, D, T.sg[:, tok(r0, n)], Op.mult), rs("D", r0, n) + rs("sg", r0, n), rs("D", r0, n), [b])
-        op("v", lambda: V.tensor_tensor(T.yy[:, tok(r0, n)], D, T.vr[:, l, tok(r0, n)], Op.mult),
-           rs("D", r0, n) + rs("vr%d" % l, r0, n), rs("y", r0, n), [b])
-
-    def mix_x():
-        op("t", lambda: PE.matmul(T.pM[:, 0:256], T.m32[:], T.xs2[:], True, False), ["m32", "xs2"], ["M"], ["pM"])
-
-    def mix(r0, n, end):
-        op("t", [lambda r=r: PE.matmul(T.pM[:, 0:256], T.m32[:], T.yy[:, tok(r)], False, end and r == r0 + n - 1)
-                 for r in range(r0, r0 + n)], ["m32"] + rs("y", r0, n), ["M"], ["pM"])
-
-    def new_x(l):
-        if l == NL - 1:
-            op("s", lambda: S.activation(T.xo[:], T.pM[:, 0:256], Act.Tanh, scale=0.25), ["M"], ["xo"], ["pM"])
-            dma("s", "oyx", T.yx[:], T.xo[:], ["xo"], ["yx"])
-        else:
-            op("s", lambda: S.activation(T.pX[:, 0:256], T.pM[:, 0:256], Act.Tanh, scale=0.25), ["M"], ["X"], ["pM", "pX"])
-            op("s", lambda: S.activation(T.xs2[:], T.pX[:, 0:256], Act.Identity, scale=2.0), ["X"], ["xs2"], ["pX"])
-
-    def fixed_keys():
-        op("s", lambda: S.activation(T.kw0[:], T.kw[:], Act.Identity, scale=T.rows[:]), ["kw", "rows"], ["kw0"])
-
-    def query_list():
-        op("t", to_list(T.pH[:, 128:192], T.z15, T.qall, 0, 1024), ["z15"] + rs("q", 0, 4), ["qc"], ["H"])
-
-    def query_keep():
-        op("s", lambda: S.activation(T.q15[:], T.pH[:, 128:192], Act.Copy), ["qc"], ["q15"], ["H"])
-
-    def start_m():
-        op("s", lambda: S.activation(T.m32[:], T.mb[:], Act.Copy), ["mb"], ["m32"])
-
-    def start_x():
-        op("s", lambda: S.activation(T.pX[:, 0:256], T.xb[:], Act.Copy), ["xb"], ["X"], ["pX"])
-        op("s", lambda: S.activation(T.xs2[:], T.xb[:], Act.Identity, scale=2.0), ["xb"], ["xs2"])
-
-    nb = {"H": T.pH, "N": T.pN}
-    do = {"raw": raw, "hold": hold, "times_q": times_q, "gather": gather, "score": score, "first": first,
-          "bias_pick": bias_pick, "bias_list": bias_list, "bias_add": bias_add,
-          "select": select, "offsets": offsets, "send_w": send_w, "name_floor": name_floor, "name_mod": name_mod,
-          "name_sum": lambda l, b: name_sum(l, b, nb[b]), "name_rest": lambda l, b: name_rest(l, b, nb[b]),
-          "name_off": name_off, "name_first": name_first, "turn": turn, "digits": digits, "steps": steps, "counts": counts,
-          "onehot": lambda k, a, b: onehot(k, range(a, b)), "bias_ends": bias_ends, "bias": bias,
-          "pick": lambda q, kind, l, h: pick(q, kind, l, *span(h)), "send_far": send_far, "send_near": send_near,
-          "mul_u": lambda l, h: mul_u(l, *span(h)), "dsum": lambda h: dsum(*span(h)), "act": lambda l, h: act(l, *span(h)),
-          "mul_v": lambda l, h: mul_v(l, *span(h)), "mix_x": mix_x, "mix": lambda h, end: mix(*span(h), end), "new_x": new_x,
-          "fixed_keys": fixed_keys, "query_list": query_list, "query_keep": query_keep, "start_m": start_m, "start_x": start_x}
-    for step in STEPS:
-        do[step[0]](*step[1:])
-
-    for sem in count:
-        if sem not in ("oyx", "oyb"):
-            wait("g", (sem, count[sem], {}, None))
-    wait("g", ("oyx", count["oyx"], {}, None))
-    wait("g", ("oyb", count["oyb"], {}, None))
+    for sem in sorted(count, key=lambda s: s in ("oyx", "oyb")):
+        wait("g", (sem, count[sem], {}, None))

@@ -5,49 +5,148 @@ from concourse.mybir import AluOpType as Op, ActivationFunctionType as Act
 NL = 3
 BF, F32, F16, I32, U16 = "bfloat16", "float32", "float16", "int32", "uint16"
 SCRATCH = {
-    "qall": ("sbuf", [128, 1024], BF), "nmi": ("sbuf", [128, 4, 64], I32), "nmh": ("sbuf", [128, 256], F16),
+    "qall": ("sbuf", [128, 1024], BF), "nmi": ("sbuf", [128, 4, 64], I32), "nmh": ("sbuf", [128, 256], F16), "nmn": ("sbuf", [128, 4, 64], F16),
     "off": ("sbuf", [128, 256], U16), "kw": ("sbuf", [128, 2048], BF), "uw": ("sbuf", [128, 2048], BF),
     "vw": ("sbuf", [128, 2048], BF), "xb": ("sbuf", [128, 256], BF), "mb": ("sbuf", [128, 128], BF),
-    "m32": ("sbuf", [128, 128], F32), "xs2": ("sbuf", [128, 256], F32), "xo": ("sbuf", [128, 256], F32), "sx": ("sbuf", [128, 256], F32),
-    "rawk": ("sbuf", [128, 4, 1024], BF), "prod": ("sbuf", [128, 4, 1024], F16),
-    "zb": ("sbuf", [128, 144], BF), "zh": ("sbuf", [128, 144], F16),
-    "wb": ("sbuf", [128, 16, 16], BF), "wh": ("sbuf", [128, 16, 16], F16), "neg": ("sbuf", [128, 8, 16], BF),
-    "bd": ("sbuf", [128, 128], F32), "bdb": ("sbuf", [128, 128], BF),
-    "sel": ("sbuf", [128, 8, 4, 16], F16), "c1": ("sbuf", [128, 128], BF), "c2": ("sbuf", [128, 128], BF),
-    "c3": ("sbuf", [128, 128], BF), "zero": ("sbuf", [128, 66], BF), "cbig": ("sbuf", [128, 256], BF), "hb": ("sbuf", [128, 256], BF),
+    "m32": ("sbuf", [128, 128], F32), "m4": ("sbuf", [128, 128], F32), "less": ("sbuf", [128, 2], F32), "minus": ("sbuf", [128, 2], BF),
+    "xo": ("sbuf", [128, 256], F32), "sx": ("sbuf", [128, 256], F32),
+    "rawk": ("sbuf", [128, 4, 1024], BF), "prod": ("sbuf", [128, 4, 1024], F16), "zh": ("sbuf", [128, 144], F16),
+    "wb": ("sbuf", [128, 16, 16], BF), "wh": ("sbuf", [128, 16, 16], F16), "neg": ("sbuf", [128, 8, 16], BF), "negh": ("sbuf", [128, 8, 16], F16),
+    "bd": ("sbuf", [128, 128], F32), "bdb": ("sbuf", [128, 128], BF), "fold": ("sbuf", [128, 120], F32), "wide": ("sbuf", [128, 64, 16], F32),
+    "sel": ("sbuf", [128, 8, 4, 16], F16), "c1": ("sbuf", [128, 128], BF), "c2": ("sbuf", [128, 128], F16), "c3": ("sbuf", [128, 128], BF),
+    "zero": ("sbuf", [128, 66], BF), "cbig": ("sbuf", [128, 256], BF), "hb": ("sbuf", [128, 256], BF),
     "sl": ("sbuf", [128, 2, 64], F32), "nl": ("sbuf", [128, 2, 64], F32), "dn": ("sbuf", [128, 2, 64], F32),
     "mx": ("sbuf", [128, 2, 64], F32), "nx": ("sbuf", [128, 2, 64], F32), "px": ("sbuf", [128, 2, 64], F32),
     "w16": ("sbuf", [128, NL, 64], F16), "wu": ("sbuf", [128, NL, 64], U16), "wr": ("sbuf", [128, 2, 4, 64], F16),
     "dv": ("sbuf", [128, 2, 8, 16], BF), "oh": ("sbuf", [128, 16, 8, 16], BF), "th": ("sbuf", [128, 16, 32, 4], BF),
-    "bs": ("sbuf", [128, NL + 1, 2, 72], BF), "blo": ("sbuf", [128, NL, 2, 64], BF), "bout": ("sbuf", [128, 2, 64], F32),
-    "i2": ("sbuf", [128, 2, 33], F32), "im": ("sbuf", [128, 2, 33], F32), "ee": ("sbuf", [128, 2, 33], F32),
-    "uvs": ("sbuf", [128, NL * 4, 2, 256], BF), "uvr": ("sbuf", [128, NL * 4, 2, 256], BF),
-    "pu": ("sbuf", [128, 1024], F32), "yy": ("sbuf", [128, 1024], F32), "sg": ("sbuf", [128, 1024], F32),
+    "bs": ("sbuf", [128, NL + 1, 2, 64], BF), "blo": ("sbuf", [128, NL, 2, 64], BF), "bout": ("sbuf", [128, 2, 64], F32),
+    "i2": ("sbuf", [128, 2, 33], F32), "up": ("sbuf", [128, 2, 33], F16), "ee": ("sbuf", [128, 2, 33], F16),
+    "wideb": ("sbuf", [128, 64, 16], BF), "sp": ("sbuf", [128, 4, 2, 64], BF),
+    "near": ("sbuf", [128, NL * 2, 768], BF), "away": ("sbuf", [128, NL * 2, 512], BF), "came": ("sbuf", [128, NL * 2, 2, 256], BF),
+    "pu": ("sbuf", [128, 4, 256], F32), "yy": ("sbuf", [128, 4, 256], F32), "sg": ("sbuf", [128, 4, 256], F32),
+    "sc": ("sbuf", [128, 4, 64], F32), "sn": ("sbuf", [128, 4, 64], F32),
     "pA": ("psum", [128, 8, 64], F32), "pB": ("psum", [128, 8, 64], F32), "pW": ("psum", [128, 8, 64], F32),
-    "pF": ("psum", [128, 8, 64], F32), "pX": ("psum", [128, 8, 64], F32), "pM": ("psum", [128, 8, 64], F32),
-    "pD0": ("psum", [128, 8, 64], F32), "pD1": ("psum", [128, 8, 64], F32),
+    "pF": ("psum", [128, 8, 64], F32), "pD": ("psum", [128, 8, 64], F32), "pM": ("psum", [128, 8, 64], F32),
+    "pE": ("psum", [128, 8, 64], F32), "pQ": ("psum", [128, 8, 64], F32),
 }
 SEMAPHORES = (["cv", "cs", "ct", "cg", "sent", "lq", "lnm", "lke", "lb", "lx", "lm", "lu", "lv", "aqm", "aqr", "oyx", "oyb"]
               + ["aw%d" % l for l in range(2)] + ["bias%d" % l for l in range(2)]
-              + ["a%d%s%s" % (l, k, h) for l in range(NL) for k in ("u", "v", "uv") for h in ("m", "ra", "rb")])
+              + ["a%d%s%s" % (l, k, h) for l in range(NL) for k in "uv" for h in "rm"])
 ROUND64 = 1.5 * 2.0 ** 13
 ROUND2048 = 1.5 * 2.0 ** 18
-ROUND1 = 1.5 * 2.0 ** 23
 ROUND4096 = 1.5 * 2.0 ** 35
 EDGE = math.log(4095.0)
 
+KEYS = ["", "r,fWfF l,qqqq", "r,fWfF l,qqqq"]
 PLAN = [
-    "judge,l,pA count,0,l,pA judge,r,pB tell count,1,r,pB biases names send,u,ra+rb,vv send,uv,m,vv send,v,ra+rb,ss send,uv,o,ss",
-    "judge,r,pA send,u,ra+rb,SS count,0,r,pA judge,l,pB tell count,1,l,pB biases names send,v,ra+rb,ss send,uv,m,ss send,uv,o,ss",
-    "judge,r,pA send,u,ra+rb,vS send,v,ra+rb,SS count,0,r,pA judge,l,pB send,uv,m,vs send,uv,o,vs count,1,l,pB biases",
+    "judge,l,pA count,0,l,pA,pW judge,r,pB tell far,u,v count,1,r,pB,pA biases names far,v,v,b1 pair,vs expert,o,n,pE,0 expert,r,c,pE,0 expert,m,n,pE,0",
+    "judge,r,pA far,u,s far,v,s count,0,r,pA,pW judge,l,pB tell count,1,l,pB,pA biases names pair,vv expert,r,c,pE,0 expert,l,n,pE,0",
+    "judge,r,pA far,u,s far,v,s count,0,r,pA,pW judge,l,pB pair,vs count,1,l,pB,pA biases expert,r,c,pE,0 expert,o,n,pB,0 expert,m,n,pQ,0",
 ]
-PLAN = [[tuple(int(x) if x.isdigit() else x for x in step.split(",")) for step in layer.split()] for layer in PLAN]
-HELD = {0: "pW", 2: "pF"}
-DUE = (20, 10)
-CYCLE = {"v": 0.9e-3, "s": 0.9e-3, "t": 0.45e-3, "g": 1.8e-3}
-CALL = {"v": 0.03, "s": 0.065, "t": 0.0, "g": 0.17}
-GATHER, HOP, LOCAL, ISSUE = 1.4, 0.13, 2.1, 0.6
-FLIGHT, FIRST, PORT, WAKE = 1.5, 3.6, 1.1, 0.8
+ORDER = {
+    "v": ["fill k0m k2m k1m k3m f0o f2o f1o f3o x2m x1m x3m x2r x1r wl*3 x3r wl oh0*4 wr*6 oh0*2 wr*1 oh0 wr Ur oh1 Vr Ul post off dn puo smo yyo pur",
+          "f0r f1r x2r x3r -smr x0l wr*3 x2l wr*4 x1l wr x3l oh0*6 wl*6 oh0*1 wl*1 oh0 wl Ul Vl -yyr oh1 -pum post*3 -smm post -yym off dn pur",
+          "f0r f1r x2r x3r -smr x0l wr*3 x2l wr*4 x1l wr x3l oh0*6 wl*6 oh0*1 wl*1 oh0 wl Ul -pul -yyr oh1 -sml -yyl post pur puo smr smo pum yyo smm yyr yym"],
+    "s": ["fill k0r k2r k1r k3r prep blo sll slr dv0 th0 dv1 th1 Vl hb nl sgo",
+          "k2r k3r k0l k2l slr -sgr k1l k3l sll Ur Vr dv0 th0 dv1 th1 blo -sgm hb nl -new",
+          "k2r k3r k0l k2l slr -sgr k1l k3l sll Ur Vr dv0 th0 Vl dv1 -sgl th1 blo -new sgr sgo sgm new"],
+    "t": ["h2m h1m h3m h2r h1r h3r prep s0l s1l s0r s1r hi0 lo0 ng0 q hi1 lo1 ng1 sum0 mixx nB Tb sum1 Tu Te nA nBr nAr nb Do",
+          "-mixo h2r h3r -Dr s0r s1r -Er hi0 s0l lo0 ng0 s1l sum0 hi1 lo1 ng1 nB -mixr -Dm Tb sum1 Tu Te nA nBr nAr nb -mixm",
+          "-mixx h2r h3r -Dr s0r s1r -Er hi0 s0l lo0 ng0 s1l sum0 hi1 lo1 ng1 -Dl -mixr Tb sum1 Tu Te -mixl mixx Dr Do Er Dm mixo mixr mixm"],
+    "g": ["fill q late tell Ur Vr pair", "Ur Vr tell pair", "Ur Vr pair"],
+    "y": ["load bias", "bias", "bias"],
+}
+PLAN = [
+    "judge,l,pA,pB judge,r,pB,pF count,0,l,pA,pW tell far,u,v count,1,r,pB,pA biases names heard far,v,s,b1 windows,b1 home,o,vs home,m,ss expert,o,n,pE,0 expert,r,h,pE,0 expert,m,n,pE,4",
+    "judge,r,pA,pB judge,l,pB,pF far,u,s count,0,r,pA,pW tell count,1,l,pB,pA biases names heard far,v,s,b2 home,o,vs home,m,ss expert,o,n,pE,0 expert,r,h,pE,0 expert,m,n,pE,4",
+    "judge,r,pA,pB judge,l,pB,pF far,u,s far,v,s count,0,r,pA,pW heard count,1,l,pB,pA biases expert,r,n,pE,0 expert,o,f,pB,0 expert,m,f,pQ,0",
+]
+ORDER = {
+    "v": ["fill k1m f2o k3m k0m f3o k2m f0o f1o x2m x1m x3m wl*4 x2r x3r x1r wl*4 wr Ur oh1*1 wl oh0*1 oh1*1 oh0 oh1 Uo post wm puo off smo dn yyo",
+          "f0r f1r x3r x2r -pur wr x2l x0l x3l x1l -smr oh0*2 -sdr wl*8 -yyr oh0*5 -pum oh0 oh1 wl Uo -smm post*3 -yym post wm pur off",
+          "f0r f1r x3r x2r -puo -dn -smr x0l wr*6 -sdr wr -smo x2l -yyo -pum x1l x3l -yyr oh0*2 wl*7 oh0*1 -smm wl*1 -yym wl oh0*2 oh1*5 oh0 oh1*1 pur oh1 puo pum smr smo yyo yyr smm yym post"],
+    "s": ["fill k2r k1r blo prep*2 k0r k3r sll slr prep*1 dv0 th0*4 dv1 th0 th1 Vr Vo",
+          "blo -hb -prep -sgo -nl k3r k2r k0l k2l slr k1l k3l Ur -sgr dv0 sll -shr -Um th0*6 dv1 th0 th1 -sgm -Vm Vr Vo -new -newp hb Um",
+          "k3r k2r -sgr -nl k0l k2l slr -shr -sgo k1l Ur k3l dv0 sll Vr -Vm -sgm blo*1 th0*5 dv1 th0*1 -new th0*1 -newp -news th1*1 th0 th1*4 sgr sgo th1 sgm blo new"],
+    "t": ["h1m h2m prep h3m h2r s0l s1l h3r h1r s0r s1r hi0 lo0 ng0 hi1 Tb lo1 nB ng1 sum0 sum1 nA Tu Te nBr nAr Do nb",
+          "h3r -q h2r s1r s0r -mixo -Dr*1 hi0 -Dr lo0 -mixx s0l s1l ng0 -Er hi1 lo1 ng1 -mixr*1 -Dm -mixr sum0 sum1 Tb nA Tu Te -mixm nB nBr nAr nb Dr mixx",
+          "h3r h2r s1r s0r -Do lo0 hi0 s0l -Er -mixo ng0 s1l -Dm -mixr hi1 -mixm Tb lo1 ng1 mixx Dr Do Dm sum0 sum1 mixo mixr mixm Tu Te"],
+    "g": ["fill q late tell Ur win Vr", "Ur tell Vr", "Ur Vr tell"],
+    "y": ["load bias", "bias", "bias"],
+}
+PLAN = [
+    "judge,l,pA,pB judge,r,pB,pF count,0,l,pA,pW tell count,1,r,pB,pA biases names pick,u,r,v pick,v,r,s pick,u,l,v pick,v,l,s give,u,r give,uv,m,kw1 give,v,r,kw1 expert,o,n,pE,0 expert,r,h,pE,0 expert,m,n,pE,4",
+    "judge,r,pA,pB judge,l,pB,pF count,0,r,pA,pW tell count,1,l,pB,pA biases names pick,u,r,s pick,v,r,s pick,u,l,v pick,v,l,s give,u,r give,uv,m,kw2 give,v,r,kw2 expert,o,n,pE,0 expert,r,h,pE,0 expert,m,n,pE,4",
+    "judge,r,pA,pB judge,l,pB,pF count,0,r,pA,pW count,1,l,pB,pA biases pick,u,r,s pick,v,r,s pick,u,m,v pick,v,m,s give,u,r give,v,r give,u,m give,v,m expert,r,n,pE,0 expert,o,f,pB,0 expert,m,n,pQ,0",
+]
+ORDER = {
+    "v": ["fill k2m k0m k1m f1o k3m f0o f2o f3o x2m x1m x3m x2r x1r x3r wl*8 wr Ur oh0 oh1 wl Ul post puo off pur dn",
+          "f0r f1r x3r x2r x0l x2l wr*7 -smr wr*1 x3l x1l -smo -sdr -yyo wl*8 wr -pum -yyr oh1*3 oh0 -smm oh1*2 -yym wl oh1 Ul post puo pur off dn",
+          "f1r f0r x2r -smr x3r x0l x2l wr*8 -smo wr -yyo x1l -sdr x3l -pum -yyr oh0*2 wl*7 -smm wl*1 -yym wl Um oh0 oh1*4 pur puo oh1 pum smr yyr smo post*2 yyo smm post*1 yym post"],
+    "s": ["fill k0r k1r k2r k3r sll slr dv0 blo th0*3 dv1 th0 th1 prep*1 Vr prep*2 hb Vl nl",
+          "blo k3r k2r k0l k2l -sgr slr k3l k1l -sgo dv0 -shr -prep sll th0 dv1 Ur th1*1 -sgm th1 Vr Vl -new -newp hb nl",
+          "k2r k3r -sgr k0l k2l slr -sgo k1l -shr k3l Ur blo*1 sll dv0 Vr th0*3 -sgm th0 dv1 -new th1*1 -newp -news Vm th1*4 sgr th1 sgo sgm blo new"],
+    "t": ["h1r h1m h2m h3m h2r s0l h3r s1l s0r s1r hi0 lo0 ng0 hi1 lo1 q ng1 nA prep nB sum0 sum1 Tb Tu Te nBr nAr nb Do mixx Dr",
+          "h3r h2r s1r s0r s0l hi0 lo0 ng0 s1l -Er hi1 Tb lo1 ng1 -Dm -mixr sum0 nB sum1 -mixm Tu Te -mixo nBr nA nAr nb Dr Do",
+          "h2r h3r -mixx s0r s1r s0l hi0 lo0 -mixo -Er ng0 s1l -Dm -mixr hi1 -mixm lo1 ng1 mixx sum0 Dr Tb Do Dm sum1 mixr Tu mixo Te mixm"],
+    "g": ["fill q late tell Ur Vr UVm", "tell Ur UVm Vr", "Ur Vr Um Vm"],
+    "y": ["load bias", "bias", "bias"],
+}
+NEW, DN = True, "t"
+KEYS = ["", "r,fffq l,qqqq", "r,fffq l,qqqq"]
+PLAN = [
+    "judge,l,pA,pB judge,r,pB,pF count,0,l,pA,pW tell count,1,r,pB,pA biases names pick,u,r,v pick,v,r,v pick,u,l,v pick,v,l,s give,u,r give,uv,m give,v,r,kw1 expert,o,x,pE,0 expert,r,j,pE,0 expert,m,n,pE,4",
+    "judge,r,pA,pB judge,l,pB,pF count,0,r,pA,pW tell count,1,l,pB,pA biases names pick,u,r,s pick,v,r,s pick,u,l,v pick,v,l,s give,u,r give,v,r give,uv,m,kw2 expert,o,x,pE,0 expert,r,j,pE,0 expert,m,n,pE,4",
+    "judge,r,pA,pB judge,l,pB,pF count,0,r,pA,pW count,1,l,pB,pA biases pick,u,r,s pick,v,r,s pick,u,m,v pick,v,m,s give,u,r give,v,r give,u,m give,v,m expert,r,x,pE,0 expert,o,f,pB,0 expert,m,n,pQ,0",
+]
+ORDER = {
+    "v": ["fill k2m k0m k3m f3o k1m f2o f0o f1o x2m x3m x1m x2r x1r x3r wl*8 wr*8 oh0*6 wr oh0 Ur wl oh1 Vr post Ul nn off puo",
+          "f0r f2r x3r f1r x2l x0l x3l x1l wr*8 -smo wl*7 oh0*1 wl*1 -yyo oh0*2 wl -ado -pur oh0 oh1 Ul wr -pum -smr post*3 -yyr*1 post -yyr -adr nn off -smm",
+          "f0r --yym f2r x3r f1r -puo -pur wr*8 -smo -yyo -ado wr x3l -pum x0l x2l -smr -yyr -adr x1l oh0*6 -smm wl*2 -yym wl Um pur*1 oh0*1 oh1*1 pur puo oh0 oh1 pum smr yyr smo adr post*2 yyo smm post*1 yym post"],
+    "s": ["fill k0r k1r k3r k2r blo sll slr dv0 th0*5 dv1 th0 th1 Vl x hb",
+          "k3r k3l k2l k0l k1l slr sll -prep -sgo blo -less dv0 th0*4 dv1 th1*3 th0 th1 -sgr Vr Ur hb -sgm",
+          "k3r k0l --new --newp -Vl slr k2l -sgo k3l Ur dv0 -sgr k1l th0*7 blo*1 sll -sgm th0 Vr -new -newp dv1 -news th1*4 Vm blo sgr th1 sgo sgm new"],
+    "t": ["h2m h3m h1r h1m h3r h2r s0l s1l s0r s1r hi0 lo0 ng0 hi1 lo1 ng1 q sum0 Tb sum1 nA Tu Te nAr less qr dn Do",
+          "s0r s1r s0l s1l hi0 lo0 ng0 hi1 lo1 ng1 -Dr sum0 sum1 Tb Tu Te nA nAr -Dm dn -mixr -mixo -mixm",
+          "s0r s1r -Do lo0 hi0 -Dr -mixo s0l ng0 -Dm s1l -mixr -mixm Tb hi1 lo1 ng1 Dr Do sum0 sum1 Dm mixr Tu mixo Te mixm"],
+    "g": ["fill q late tell Ur UVm Vr", "tell Ur Vr UVm", "Ur Vr Um Vm"],
+    "y": ["load bias", "bias", "bias"],
+}
+ORDER = {
+    "v": ["fill k0m k2m k3m k1m f3o f1o f0o x3m x1m f2o x2m x2r x1r x3r wl*8 wr*8 oh0*7 wr oh0 Ur oh1*2 wl oh1 Vr post Ul puo nn off",
+          "f2r f0r x3r x2l x0l f1r x1l x3l wr*8 wl*7 -smo wl*1 oh0*1 -yyo -ado -pur oh0 wr oh1 wl -pum -smr post -yyr -adr Ul nn -smm off -yym",
+          "f2r f0r f1r x3r -puo -pur wr*7 -smo wr*1 -yyo -ado wr -pum x3l x2l x0l -smr -yyr -adr x1l oh0*6 -smm wl*2 -yym wl Um pur oh1*3 puo oh1 oh0 smr pum yyr adr*1 smo adr yyo smm yym post"],
+    "s": ["fill k3r k0r k1r k2r sll slr dv0 th0*6 dv1 th0 th1 x prep blo Vl hb",
+          "k3r k2l k0l k1l k3l slr sll -sgo blo dv0 th0*5 dv1 th1*3 th0 th1 -sgr Vr Ur Vl hb -sgm -less",
+          "k1l k3r --new --newp slr k0l k2l -sgo k3l dv0 Ur -sgr blo*1 th0*3 sll Vr -sgm th0*4 -new -newp dv1 -news Vm th0 sgr th1 sgo sgm blo new"],
+    "t": ["h2m h3m h3r h1m h1r h2r s1l s0l s0r s1r hi0 lo0 ng0 hi1 lo1 ng1 qr Tb sum0 sum1 Tu Te nA nAr Do dn q",
+          "s0r s0l s1r s1l hi0 lo0 ng0 hi1 lo1 ng1 -Dr sum0 sum1 Tb Tu Te -less nA nAr -Dm dn -mixr -mixm -mixo",
+          "s0r s1r -Do hi0 -Dr lo0 ng0 -mixo s0l -Dm s1l -mixr -mixm lo1 hi1 Dr ng1 Do Tb sum0 Dm sum1 mixr mixo mixm Tu Te"],
+    "g": ["fill late q tell Ur UVm Vr", "tell Ur Vr UVm", "Ur Vr Um Vm"],
+    "y": ["load bias", "bias", "bias"],
+}
+PLAN = [
+    "judge,l,pA,pB judge,r,pB,pF count,0,l,pA,pW tell count,1,r,pB,pA biases names pick,u,r,v pick,v,r,v pick,u,l,s pick,v,l,s give,u,r give,uv,m,kw1 give,v,r,kw1 expert,o,n,pE,0 expert,r,n,pE,0 expert,m,n,pE,4",
+    "judge,r,pA,pB judge,l,pB,pF count,0,r,pA,pW tell count,1,l,pB,pA biases names pick,u,r,s pick,v,r,s pick,u,l,s pick,v,l,s give,u,r give,uv,m,kw2 give,v,r,kw2 expert,o,n,pE,0 expert,r,n,pE,0 expert,m,n,pE,4",
+    "judge,r,pA,pB judge,l,pB,pF count,0,r,pA,pW count,1,l,pB,pA biases pick,u,r,s pick,v,r,s pick,u,m,v pick,v,m,s give,u,r give,v,r give,u,m give,v,m expert,r,n,pE,0 expert,o,f,pB,0 expert,m,n,pQ,0",
+]
+ORDER = {
+    "v": ["fill k2m k1m k0m k3m f2o f0o f1o f3o x2m x3m x1m x1r x2r x3r wl*7 wr*1 wl*1 wr wl oh0*1 Ur oh1*1 oh0 oh1 Vr post puo nn pur*1 off pur",
+          "f2r f0r x2l f1r x3r x0l x3l -smo x1l wr*2 -yyo wr*5 wl*1 wr*1 wl*5 -pum wl -smr -yyr oh1*3 oh0 oh1*4 -smm oh1 wr -yym post puo nn off",
+          "f0r f2r x3r f1r -smo -pur*1 -yyo -pum wr*2 -pur wr*4 x0l wr*1 x2l wr*1 x1l wr x3l -smr -yyr wl*8 -smm wl -yym Um pur oh0*2 oh1*1 oh0*4 puo oh1*5 oh0*1 pum oh1*1 oh0 oh1 smr yyr smm smo yym yyo post"],
+    "s": ["fill k0r k1r k3r k2r sll slr blo dv0 th0*3 dv1 th0 th1 x Ul less hb prep*1 Vl prep",
+          "k2l k3r k0l k3l -sgo k1l blo slr sll -sgr dv0 th0*4 dv1 th0 th1*4 -sgm th1 Ul Vl -new Ur -newp hb",
+          "blo*1 -Vr k3r k2l -sgo k0l slr k1l blo k3l -sgr Ur sll dv0 -sgm Vr th0*5 -new -newp dv1 -news Vm th0*2 th1*4 sgr th1*1 th0 th1 sgm sgo new"],
+    "t": ["h2m h3m h1m h3r h1r h2r s0l s1l s0r s1r hi0 lo0 ng0 hi1 lo1 q ng1 qr less sum0 Tb sum1 nA nAr Tu Te Do",
+          "s0r -mixx s1r -dn s0l s1l -Dr hi0 -mixo lo0 ng0 hi1 lo1 ng1 -Dm -mixr Tb sum0 sum1 -mixm Tu Te nA nAr Do",
+          "s0r s1r -dn -Dr -mixx s0l lo0 -mixo s1l hi0 -Dm ng0 -mixr -mixm lo1 hi1 ng1 Dr Tb mixx Do Dm sum0 sum1 mixr mixm mixo Tu Te"],
+    "g": ["fill q late tell Ur UVm Vr", "tell Ur UVm Vr", "Ur Vr Um Vm"],
+    "y": ["load bias", "bias", "bias"],
+}
+CYCLE = {"v": 0.85e-3, "s": 0.85e-3, "t": 0.42e-3, "g": 1.7e-3}
+CALL = {"v": 0.015, "s": 0.03, "t": 0.0, "g": 0.17}
+GATHER, HOP, LOCAL, ISSUE = 1.4, 0.24, 1.6, 0.3
+FLIGHT, FIRST, PORT, WAKE = 1.0, 2.2, 1.0, 0.4
 
 
 def rank_program(g, core, T, topo):
@@ -55,9 +154,9 @@ def rank_program(g, core, T, topo):
     if rank is None:
         return
     N = len(T.cores)
-    near = topo.cores_of(core)
-    mate = [r for r in range(N) if r != rank and T.cores[r] in near][0]
-    rem = [r for r in range(N) if T.cores[r] not in near]
+    here = topo.cores_of(core)
+    mate = [r for r in range(N) if r != rank and T.cores[r] in here][0]
+    rem = [r for r in range(N) if T.cores[r] not in here]
     loc0, rem0 = min(rank, mate), min(rem)
     assert abs(rank - mate) == 1 and rem == [rem0, rem0 + 1]
     e_off = topo.engines(core, T.cores[rem0])
@@ -67,23 +166,23 @@ def rank_program(g, core, T, topo):
         k = len(es) // n
         return sum(1 << e for e in es[i * k:(i + 1) * k])
 
-    calls = []
+    calls, layer = [], [0]
 
-    def op(q, fns, cycles, reads, writes, banks=(), line=None):
+    def op(q, name, fns, cycles, reads, writes, banks=()):
         fns = fns if isinstance(fns, list) else [fns]
         busy = len(fns) * (CALL[q] + max(cycles, 32 if q == "t" else 64) * CYCLE[q])
-        calls.append(dict(kind="op", q=q, fns=fns, reads=reads, writes=writes, banks=banks, busy=busy, late=HOP, line=line))
+        calls.append(dict(kind="op", q=q, name=(layer[0], name), fns=fns, reads=reads, writes=writes, banks=banks, busy=busy, late=HOP, cycles=cycles))
 
-    def dma(q, sem, pairs, reads, writes, late=LOCAL, line=None):
-        calls.append(dict(kind="dma", q=q, sem=sem, pairs=pairs, reads=reads, writes=writes, banks=(), busy=0.05 * len(pairs), late=late, line=line))
+    def dma(q, name, sem, pairs, reads, writes, late=LOCAL):
+        calls.append(dict(kind="dma", q=q, name=(layer[0], name), sem=sem, pairs=pairs, reads=reads, writes=writes, banks=(), busy=0.05 * len(pairs), late=late))
 
-    def send(items, reads, lands, flight=FLIGHT):
-        calls.append(dict(kind="send", q="g", items=items, local="sent", reads=reads, writes=[], banks=(), busy=ISSUE, late=0.0, line="sends"))
+    def send(name, items, reads, lands, flight=FLIGHT):
+        calls.append(dict(kind="send", q="g", name=(layer[0], name), items=items, local="sent", reads=reads, writes=[], banks=(), busy=ISSUE, late=0.0))
         me = len(calls) - 1
         for sem, writes, pieces in lands:
             n = sum(bin(m).count("1") for _r, m, s, _a, _b in items if s == sem)
-            calls.append(dict(kind="land", q="port" if pieces else None, sem=sem, n=n, reads=[], writes=writes, banks=(),
-                              busy=max(pieces, 1.1) * PORT, late=WAKE if pieces else 0.3, flight=flight, after=me, line="port" if pieces else None))
+            calls.append(dict(kind="land", q=None, sem=sem, n=n, reads=[], writes=writes, banks=(),
+                              busy=flight + max(pieces, 1.1) * PORT, late=WAKE if pieces else 0.3, after=me))
 
     V, S, PE = g.vector, g.scalar, g.tensor
     ident, identh, shifth = T.wb[:, 0:8, :], T.wh[:, 0:8, :], T.wh[:, 7:15, :]
@@ -92,8 +191,7 @@ def rank_program(g, core, T, topo):
         return t[64 * half + 15:64 * half + 64:16, :]
 
     def span(h):
-        return {"a": (0, 4), "l": (loc0, 2), "r": (rem0, 2), "o": (rank, 1), "m": (mate, 1),
-                "ra": (rem0 + rank - loc0, 1), "rb": (rem0 + mate - loc0, 1)}[h]
+        return {"a": (0, 4), "l": (loc0, 2), "r": (rem0, 2), "o": (rank, 1), "m": (mate, 1)}[h]
 
     def rs(name, r0, n):
         return ["%s%d" % (name, r) for r in range(r0, r0 + n)]
@@ -108,239 +206,357 @@ def rank_program(g, core, T, topo):
     def tags(name, h):
         return rs(name + "_", *span(h))
 
+    blk = rs
+
     mine = T.qall[:, tok(rank)]
-    dma("y", "lq", [(mine, T.rq[:])], [], ["q%d" % rank], 2.0, "load")
-    dma("y", "lnm", [(T.nmi[:], T.nm[:])], [], ["nmi"], 2.6, "load")
-    dma("y", "lke", [(T.kw[:], T.ke[:])], [], ["kw"], 4.3, "load")
-    dma("y", "lb", [(T.bs[:, 0, half, 8:72], bias_rows(T.ke, half)) for half in range(2)], [], ["b0"], 5.0, "load")
-    op("v", lambda: V.memset(T.wb[:], 1.0), 128, [], ["wb"])
-    op("v", lambda: V.memset(T.zb[:], 0.0), 72, [], ["zb"])
-    op("v", lambda: V.memset(T.bdb[:], 1.0), 64, [], ["bdb"])
-    op("v", lambda: V.memset(T.zb[:, 15::16], 1.0), 9, ["zb"], ["zb"])
-    op("v", lambda: V.memset(T.bs[:, :, :, 0:8], 0.0), 32, [], ["pad"])
-    op("v", lambda: V.memset(T.cbig[:], ROUND2048), 128, [], ["cbig"])
-    op("v", lambda: V.memset(T.c3[:], -31.5), 64, [], ["c3"])
-    op("v", lambda: V.memset(T.zero[:], 0.0), 64, [], ["zero"])
-    op("g", lambda: g.affine_select(T.wb[:], T.wb[:], [[0, 2], [-1, 128]], Op.is_equal, 0.0, 0, 1), 256, ["wb"], ["wb"])
-    op("g", lambda: g.affine_select(T.zb[:, 15::16], T.zb[:, 15::16], [[-16, 9]], Op.is_ge, 0.0, 0, 1), 9, ["zb"], ["zb"])
-    op("g", lambda: g.affine_select(T.zb[:, 15::16], T.zb[:, 15::16], [[16, 9]], Op.is_ge, 0.0, 15, -1), 9, ["zb"], ["zb"])
-    send([(rem[0], part(e_off, 0, 2), "aqr", mine, mine), (rem[1], part(e_off, 1, 2), "aqr", mine, mine), (mate, part(e_on, 0, 1), "aqm", mine, mine)],
-         ["q%d" % rank], [("aqm", ["q%d" % mate], 0), ("aqr", rs("q", rem0, 2) + ["qgone"], 2)], FLIGHT + FIRST)
-    op("g", lambda: g.iota(T.c1[:], [[0, 8], [-64, 4], [0, 4]], int(ROUND64), 0, allow_small_or_imprecise_dtypes=True), 128, [], ["c1"])
-    op("g", lambda: g.iota(T.c2[:], [[0, 8], [-16, 4], [0, 4]], 0, 0, allow_small_or_imprecise_dtypes=True), 128, [], ["c2"])
-    op("g", lambda: g.affine_select(T.bdb[:], T.bdb[:], [[-16, 8], [0, 16]], Op.is_ge, 0.0, 0, 1), 128, ["bdb"], ["bdb"])
-    op("g", lambda: g.affine_select(T.bdb[:], T.bdb[:], [[16, 8], [0, 16]], Op.is_ge, 0.0, 15, -1), 128, ["bdb"], ["bdb"])
-    op("v", lambda: V.tensor_copy(T.wh[:], T.wb[:]), 128, ["wb"], ["wh"])
-    op("v", lambda: V.tensor_copy(T.zh[:], T.zb[:]), 72, ["zb"], ["zh"])
-    op("v", lambda: V.tensor_scalar(T.neg[:], ident, -1.0, None, Op.mult), 64, ["wb"], ["neg"])
-    op("v", [lambda k=k: V.tensor_copy(T.sel[:, :, k, :], ident) for k in range(4)], 64, ["wb"], ["sel"])
-    op("v", lambda: V.tensor_copy(T.off[:], T.nmi[:]), 256, ["nmi"], ["off"])
-    op("v", lambda: V.tensor_copy(T.nmh[:], T.nmi[:]), 256, ["nmi"], ["nmh"])
-    op("v", lambda: V.tensor_copy(T.nl[:], T.nmi[:, 0::2, :]), 128, ["nmi"], ["nl"])
-    op("v", lambda: V.tensor_tensor(T.dn[:], T.nmi[:, 1::2, :], T.nmi[:, 0::2, :], Op.subtract), 256, ["nmi"], ["dn"])
-    dma("y", "lu", [(T.uw[:], T.ue[:])], ["qgone"], ["uw"], 4.0, "load")
-    dma("y", "lv", [(T.vw[:], T.ve[:])], ["qgone"], ["vw"], 6.0, "load")
-    dma("y", "lx", [(T.xb[:], T.x0[:])], ["qgone"], ["xb"], 6.5, "load")
-    dma("y", "lm", [(T.mb[:], T.mm[:])], ["qgone"], ["mb"], 6.5, "load")
+    WIDE = T.wide[0:64] if ",c," in " ".join(PLAN) else T.wideb[0:64]
+    dma("y", "load", "lq", [(mine, T.rq[:])], [], ["q%d" % rank], 2.0)
+    dma("y", "load", "lnm", [(T.nmi[:], T.nm[:])], [], ["nmi"], 2.6)
+    dma("y", "load", "lke", [(T.kw[:], T.ke[:])], [], ["kw"], 4.0)
+    for ap, value, n, tag in [(T.bdb[:], 1.0, 64, "bdb"), (T.wb[:], 1.0, 128, "wb"), (T.fold[:], 0.0, 120, "fold"), (T.cbig[:], ROUND2048, 128, "cbig"),
+                              (T.zero[:], 0.0, 64, "zero"), (T.minus[:], -1.0, 64, "minus"), (T.c3[:], -31.5, 64, "c3"), (T.sl[:, 0, :], 0.0, 64, "slpB"),
+                              (WIDE, 1.0, 1024 if ",c," in " ".join(PLAN) else 512, "wide")]:
+        if not (NEW and tag in ("wide", "fold")):
+            op("v", "fill", lambda ap=ap, value=value: V.memset(ap, value), n, [], [tag])
+    op("g", "fill", lambda: g.affine_select(T.bdb[:], T.bdb[:], [[-16, 8], [0, 16]], Op.is_ge, 0.0, 0, 1), 128, ["bdb"], ["bdb"])
+    op("g", "fill", lambda: g.affine_select(T.bdb[:], T.bdb[:], [[16, 8], [0, 16]], Op.is_ge, 0.0, 15, -1), 128, ["bdb"], ["bdb"])
+    op("g", "fill", lambda: g.affine_select(T.wb[:], T.wb[:], [[0, 2], [-1, 128]], Op.is_equal, 0.0, 0, 1), 256, ["wb"], ["wb"])
+    send("q", [(rem[0], part(e_off, 0, 2), "aqr", mine, mine), (rem[1], part(e_off, 1, 2), "aqr", mine, mine), (mate, part(e_on, 0, 1), "aqm", mine, mine)],
+         ["q%d" % rank], [("aqm", ["q%d" % mate], 0), ("aqr", rs("q", rem0, 2), 2)], FLIGHT + FIRST)
+    dma("y", "load", "lb", [(T.bs[:, 0, half, :], bias_rows(T.ke, half)) for half in range(2)], ["q%d" % mate], ["b0"], 2.4)
+    dma("y", "load", "lu", [(T.uw[:], T.ue[:])], [], ["uw"], 4.4)
+    dma("y", "load", "lx", [(T.xb[:], T.x0[:])], [], ["xb"], 4.8)
+    dma("y", "load", "lm", [(T.mb[:], T.mm[:])], [], ["mb"], 5.1)
+    dma("y", "load", "lv", [(T.vw[:], T.ve[:])], [], ["vw"], 7.0)
+    op("g", "late", lambda: g.iota(T.c1[:], [[0, 8], [-64, 4], [0, 4]], int(ROUND64), 0, allow_small_or_imprecise_dtypes=True), 128, [], ["c1"])
+    if not NEW:
+      op("g", "late", lambda: g.affine_select(WIDE, WIDE, [[-1, 64], [0, 16]], Op.is_equal, 0.0, 0, 1), 1024, ["wide"], ["wide"])
+    op("s", "fill", lambda: S.activation(T.bd[:], T.bdb[:], Act.Sigmoid, bias=-128.0, scale=256.0), 1600, ["bdb"], ["bd"])
+    if NEW:
+        op("s", "fill", lambda: S.activation(T.bd[:], T.bd[:], Act.Identity, scale=0.25), 128, ["bd"], ["bd"])
+    for fn, n, reads, tag in [
+            (lambda: V.tensor_scalar(T.prod[:, 0, tok(mate)], T.cbig[:], 0.0, None, Op.mult), 128, ["cbig"], "prod0_%d" % mate),
+            (lambda: V.tensor_scalar(T.zh[:], T.cbig[:, 0:144], 0.0, None, Op.mult), 72, ["cbig"], "zh"),
+            (lambda: V.tensor_copy(T.fold[:, 56:64], T.bdb[:, 0::16]), 64, ["bdb"], "fold"),
+            (lambda: V.tensor_copy(T.wh[:], T.wb[:]), 128, ["wb"], "wh"),
+            (lambda: V.tensor_copy(T.zh[:, 15:143:16], T.bdb[:, 0::16]), 64, ["bdb"], "zh"),
+            (lambda: V.tensor_scalar(T.neg[:], ident, -1.0, None, Op.mult), 64, ["wb"], "neg"),
+            (lambda: V.tensor_scalar(T.negh[:], ident, -1.0, None, Op.mult), 64, ["wb"], "negh"),
+            ([lambda k=k: V.tensor_copy(T.sel[:, :, k, :], ident) for k in range(4)], 64, ["wb"], "sel"),
+            (lambda: V.tensor_copy(T.off[:], T.nmi[:]), 256, ["nmi"], "off"),
+            (lambda: V.tensor_copy(T.nl[:], T.nmi[:, 0::2, :]), 128, ["nmi"], "nl"),
+            (lambda: V.tensor_tensor(T.dn[:], T.nmi[:, 1::2, :], T.nmi[:, 0::2, :], Op.subtract), 256, ["nmi"], "dn"),
+            (lambda: V.tensor_copy(T.nmh[:], T.nmi[:]), 256, ["nmi"], "nmh"),
+            (lambda: V.tensor_scalar(T.c2[:], T.c1[:], 1.25, -0.25 * ROUND64, Op.mult, Op.add), 64, ["c1"], "c2")]:
+        if not (NEW and tag == "fold"):
+            op("v", "fill", fn, n, reads, [tag])
 
-    def names_of(c, h):
+    def keys(c, h):
         r0, n = span(h)
-        return T.off[:, c * 64 + r0 * 16:c * 64 + (r0 + n) * 16]
+        return T.kw[:].indirect(T.off[:, c * 64 + r0 * 16:c * 64 + (r0 + n) * 16])
 
-    def gather(c, h):
+    def fused(c, h):
         r0, n = span(h)
-        op("v", lambda: V.tensor_tensor(T.prod[:, c, tok(r0, n)], T.kw[:].indirect(names_of(c, h)), T.qall[:, tok(r0, n)], Op.mult),
-           256 * n * GATHER, ["kw", "off"] + rs("q", r0, n), tags("prod%d" % c, h), line="keys")
+        op("v", "f%d%s" % (c, h), lambda: V.tensor_tensor(T.prod[:, c, tok(r0, n)], keys(c, h), T.qall[:, tok(r0, n)], Op.mult),
+           256 * n * GATHER, ["kw", "off"] + rs("q", r0, n), tags("prod%d" % c, h))
 
-    def owners(b):
-        return {"pX": ["X"], "pM": rs("M", 0, 5), "pD0": rs("D", loc0, 2), "pD1": rs("D", rem0, 2), "pW": ["accpW", "L0", "L1"],
-                "pF": ["F", "Fs", "Ft", "Fu", "Fa"]}[b]
-
-    def hold(q, c, h, b, j):
+    def raw(q, c, h):
         r0, n = span(h)
-        out, src = T.rawk[:, c, tok(r0, n)], T.kw[:].indirect(names_of(c, h))
-        op(q, (lambda: V.tensor_copy(out, src)) if q == "v" else (lambda: S.activation(out, src, Act.Copy)), 256 * n * GATHER,
-           ["kw", "off"], tags("raw%d" % c, h), line="keys" if q == "v" else "steps")
-        op("t", lambda: PE.matmul(T[b][:, 4 * j:4 * (j + n), :], ident, out, True, True), 256 * n, ["wb"] + tags("raw%d" % c, h),
-           tags("held%d" % c, h) + (owners(b) if j == 0 else []), [b])
+        out = T.rawk[:, c, tok(r0, n)]
+        op(q, "k%d%s" % (c, h), (lambda: V.tensor_copy(out, keys(c, h))) if q == "v" else (lambda: S.activation(out, keys(c, h), Act.Copy)),
+           256 * n * GATHER, ["kw", "off"], tags("raw%d" % c, h))
 
-    def times(c, h, b, j):
+    def held(c, h, b, j=0, base=None):
         r0, n = span(h)
-        op("v", lambda: V.tensor_tensor(T.prod[:, c, tok(r0, n)], T[b][:, 4 * j:4 * (j + n), :], T.qall[:, tok(r0, n)], Op.mult), 256 * n,
-           tags("held%d" % c, h) + owners(b) + rs("q", r0, n), tags("prod%d" % c, h), [b], "keys")
+        P = T[b][:, j:j + 4 * n, :]
+        op("t", "h%d%s" % (c, h), [lambda: PE.matmul(P, ident, T.rawk[:, c, tok(r0, n)], True, base is None)]
+           + ([] if base is None else [lambda: PE.matmul(P, T.neg[:], T.rawk[:, base, tok(r0, n)], False, True)]), 256 * n,
+           ["wb", "neg"] + tags("raw%d" % c, h) + ([] if base is None else tags("raw%d" % base, h)), blk(b, j, 4 * n) + ["acc" + b], [b])
+        op("v", "x%d%s" % (c, h), lambda: V.tensor_tensor(T.prod[:, c, tok(r0, n)], P, T.qall[:, tok(r0, n)], Op.mult), 256 * n,
+           blk(b, j, 4 * n) + rs("q", r0, n), tags("prod%d" % c, h), [b])
 
-    def score(j, h, b):
+    def times(c, h):
         r0, n = span(h)
-        op("t", [lambda i=i: PE.matmul(T[b][:, j, 0:32 * n], T.zh[:, 15 - i:143 - i], T.prod[:, j::2, 256 * r0 + i:256 * (r0 + n):16], i == 0, i == 15)
-                 for i in range(16)], 64, ["zh"] + tags("prod%d" % j, h) + tags("prod%d" % (j + 2), h), ["S%d%s" % (j, b), "acc" + b] + (["h" + b] if j == 0 else []), [b])
+        b, j = ("pD", 0) if h == "r" else ("pQ", 4 * (r0 - loc0))
+        op("v", "x%d%s" % (c, h), lambda: V.tensor_tensor(T.prod[:, c, tok(r0, n)], T[b][:, j:j + 4 * n, :], T.rawk[:, c, tok(r0, n)], Op.mult), 256 * n,
+           blk(b, j, 4 * n) + tags("raw%d" % c, h), tags("prod%d" % c, h), [b])
 
-    def winners(l, h, b):
+    def winners(l, h, b, b2):
         cs, P = col(h), T[b]
-        w = 16 * span(h)[1]
-        score(0, h, b)
-        op("s", lambda: S.activation(T.sl[:, :, cs], P[:, 0, 0:2 * w], Act.Copy), 2 * w, ["S0" + b], ["sl" + b], [b])
-        score(1, h, b)
+        r0, n = span(h)
+        w = 16 * n
+        c0 = 1 if (l, h) == (0, "r") else 0
+
+        def score(j, k, b, at):
+            op("t", "s%d%s" % (j, h),
+               [lambda i=i: PE.matmul(T[b][:, at, k * w:2 * w], T.zh[:, 15 - i:143 - i], T.prod[:, j + 2 * k::2, 256 * r0 + i:256 * (r0 + n):16], i == 0, i == 15)
+                for i in range(16)], 64, ["zh"] + [t for c in range(j + 2 * k, 4, 2) for t in tags("prod%d" % c, h)], [b + str(at), "acc" + b], [b])
+        score(0, c0, b2, 7)
+        op("s", "sl" + h, lambda: S.activation(T.sl[:, c0:2, cs], T[b2][:, 7, c0 * w:2 * w], Act.Copy), 2 * w, [b2 + "7", "sl" + b], ["sl" + b], [b2])
+        score(1, 0, b, 1)
         right, g1, t1 = P[:, 1, 0:2 * w], P[:, 2, 0:2 * w], P[:, 3, 0:2 * w]
+        nl = T.nmn[:, 0::2, cs] if NEW and l else T.nl[:, :, cs]
+        far_dn = NEW and l and DN == "t"
+        if far_dn:
+            g1 = T.px[:, :, cs]
         for out, x, y, o, reads, writes, banks in [
-                (g1, right, T.sl[:, :, cs], Op.is_gt, ["S1" + b, "sl" + b], ["g" + b], [b]),
-                (T.mx[:, :, cs], right, T.sl[:, :, cs], Op.max, ["S1" + b, "sl" + b], ["mx" + b], [b]),
-                (t1, g1, T.dn[:, :, cs], Op.mult, ["g" + b, "dn"], ["t" + b], [b]),
-                (P[:, 0, 0:w], T.mx[:, 0, cs], T.mx[:, 1, cs], Op.is_ge, ["mx" + b], ["S0" + b], [b]),
-                (P[:, 0, w:2 * w], T.mx[:, 1, cs], T.mx[:, 0, cs], Op.is_gt, ["mx" + b], ["h" + b], [b]),
-                (T.nx[:, :, cs], t1, T.nl[:, :, cs], Op.add, ["t" + b, "nl"], ["nx" + b], [b]),
-                (T.px[:, :, cs], P[:, 0, 0:2 * w], T.nx[:, :, cs], Op.mult, ["S0" + b, "h" + b, "nx" + b], ["px" + b], [b]),
+                (g1, right, T.sl[:, :, cs], Op.is_gt, [b + "1", "sl" + b], ["px" + b if far_dn else b + "2"], [b]),
+                (T.mx[:, :, cs], right, T.sl[:, :, cs], Op.max, [b + "1", "sl" + b], ["mx" + b], [b]),
+                (t1, T.pF[:, 4:6, cs], g1, Op.mult, ["px" + b] + blk("pF", 4, 2), [b + "3"], [b, "pF"]) if far_dn else
+                (t1, g1, T.dn[:, :, cs], Op.mult, [b + "2", "dn"], [b + "3"], [b]),
+                (P[:, 0, 0:w], T.mx[:, 0, cs], T.mx[:, 1, cs], Op.is_ge, ["mx" + b], [b + "0"], [b]),
+                (P[:, 0, w:2 * w], T.mx[:, 1, cs], T.mx[:, 0, cs], Op.is_gt, ["mx" + b, "sl" + b], ["h" + b], [b]),
+                (T.nx[:, :, cs], t1, nl, Op.add, [b + "3", "nl"], ["nx" + b], [b]),
+                (T.px[:, :, cs], P[:, 0, 0:2 * w], T.nx[:, :, cs], Op.mult, [b + "0", "h" + b, "nx" + b], ["px" + b], [b]),
                 (T.w16[:, l, cs], T.px[:, 0, cs], T.px[:, 1, cs], Op.add, ["px" + b], tags("w%d" % l, h), [])]:
-            op("v", lambda out=out, x=x, y=y, o=o: V.tensor_tensor(out, x, y, o), 64, reads, writes, banks)
-        op("v", lambda: V.tensor_copy(T.wu[:, l, cs], T.w16[:, l, cs]), 64, tags("w%d" % l, h), tags("wu%d" % l, h))
+            op("v", "w" + h, lambda out=out, x=x, y=y, o=o: V.tensor_tensor(out, x, y, o), 64, reads, writes, banks)
+        op("v", "w" + h, lambda: V.tensor_copy(T.wu[:, l, cs], T.w16[:, l, cs]), 64, tags("w%d" % l, h), tags("wu%d" % l, h))
 
     def tell(l):
         src, dst, sem = T.w16[:, l, :], T.wr[:, l, rank, :], "aw%d" % l
-        send([(rem[0], part(e_off, 0, 2), sem, src, dst), (rem[1], part(e_off, 1, 2), sem, src, dst), (mate, part(e_on, 0, 1), sem, src, dst)],
+        send("tell", [(rem[0], part(e_off, 0, 2), sem, src, dst), (rem[1], part(e_off, 1, 2), sem, src, dst), (mate, part(e_on, 0, 1), sem, src, dst)],
              tags("w%d" % l, "a"), [(sem, ["wr%d" % l], 0.5)])
+
+    def steps_apart(nm):
+        if DN == "v":
+            op("v", "dn", lambda: V.tensor_tensor(T.dn[:], nm[:, 1::2, :], nm[:, 0::2, :], Op.subtract), 256, ["nl"], ["dn"])
+        else:
+            op("t", "dn", [lambda: PE.matmul(T.pF[:, 4:6, :], identh, nm[:, 1::2, :], True, False), lambda: PE.matmul(T.pF[:, 4:6, :], T.negh[:], nm[:, 0::2, :], False, True)],
+               128, ["wh", "negh", "nl"], blk("pF", 4, 2) + ["accpF"], ["pF"])
 
     def names(l):
         NP = T.pA[:, 4:8, :]
         pairs = [(r, c) for r in range(N) if r != rank for c in range(4)]
-        for b, tag in (("pB", "H"), ("pA", "N")):
-            op("t", [lambda b=b: PE.matmul(T[b][:, 4:8, :], identh, T.nmh[:], True, False)]
-               + ([lambda: PE.matmul(NP, ident, T.cbig[:], False, False)] if tag == "N" else [])
+        if NEW:
+            nb = blk("pA", 4, 4)
+            op("t", "nA", [lambda: PE.matmul(NP, identh, T.nmh[:], True, False), lambda: PE.matmul(NP, ident, T.cbig[:], False, False)]
+               + [lambda c=c: PE.matmul(T.pA[:, 4 + c, :], shifth, T.w16[:, l, :], False, False) for c in range(4)], 128,
+               ["wh", "wb", "nmh", "cbig"] + tags("w%d" % l, "a"), nb + ["accpA"], ["pA"])
+            op("t", "nAr", [lambda r=r, c=c: PE.matmul(T.pA[:, 4 + c, :], shifth, T.wr[:, l, r, :], False, (r, c) == pairs[-1]) for r, c in pairs],
+               64, ["wh", "wr%d" % l], nb + ["accpA"], ["pA"])
+            op("s", "hb", lambda: S.activation(T.hb[:], NP, Act.Identity, bias=1023.5, scale=-1.0), 256, nb, ["hb"], ["pA"])
+            op("v", "nn", lambda: V.tensor_tensor(T.nmn[:], NP, T.hb[:], Op.add), 256, nb + ["hb"], ["nl"], ["pA"])
+            op("v", "off", lambda: V.tensor_copy(T.off[:], T.nmn[:]), 128, ["nl"], ["off"])
+            steps_apart(T.nmn)
+            return
+        for b in ("pB", "pA"):
+            op("t", "n" + b[1], [lambda b=b: PE.matmul(T[b][:, 4:8, :], identh, T.nmh[:], True, False)]
+               + ([lambda: PE.matmul(NP, ident, T.cbig[:], False, False)] if b == "pA" else [])
                + [lambda b=b, c=c: PE.matmul(T[b][:, 4 + c, :], shifth, T.w16[:, l, :], False, False) for c in range(4)], 128,
-               ["wh", "wb", "nmh", "cbig"] + tags("w%d" % l, "a"), [tag, "W" + b, "acc" + b], [b])
-        for b, tag in (("pB", "H"), ("pA", "N")):
-            op("t", [lambda b=b, r=r, c=c, end=tag == "H" and (r, c) == pairs[-1]: PE.matmul(T[b][:, 4 + c, :], shifth, T.wr[:, l, r, :], False, end)
-                     for r, c in pairs], 64, ["wh", "wr%d" % l], [tag, "acc" + b], [b], "names")
-        op("s", lambda: S.activation(T.hb[:], T.pB[:, 4:8, :], Act.Identity, bias=1023.5 - ROUND2048, scale=-1.0), 256, ["H"], ["hb"], ["pB"])
-        op("t", lambda: PE.matmul(NP, ident, T.hb[:], False, True), 256, ["wb", "hb"], ["N", "accpA"], ["pA"])
-        op("v", lambda: V.tensor_copy(T.off[:], NP), 256, ["N"], ["off"], ["pA"])
-        op("s", lambda: S.activation(T.nl[:], T.pA[:, 4::2, :], Act.Copy), 128, ["N"], ["nl"], ["pA"])
-        op("v", lambda: V.tensor_tensor(T.dn[:], T.pA[:, 5::2, :], T.nl[:], Op.subtract), 128, ["N", "nl"], ["dn"], ["pA"])
+               ["wh", "wb", "nmh", "cbig"] + tags("w%d" % l, "a"), blk(b, 4, 4) + ["acc" + b], [b])
+        for b in ("pB", "pA"):
+            op("t", "n%sr" % b[1],
+               [lambda b=b, r=r, c=c, end=b == "pB" and (r, c) == pairs[-1]: PE.matmul(T[b][:, 4 + c, :], shifth, T.wr[:, l, r, :], False, end)
+                for r, c in pairs], 64, ["wh", "wr%d" % l], blk(b, 4, 4) + ["acc" + b], [b])
+        op("s", "hb", lambda: S.activation(T.hb[:], T.pB[:, 4:8, :], Act.Identity, bias=1023.5 - ROUND2048, scale=-1.0), 256, blk("pB", 4, 4), ["hb"], ["pB"])
+        op("t", "nb", lambda: PE.matmul(NP, ident, T.hb[:], False, True), 256, ["wb", "hb"], blk("pA", 4, 4) + ["accpA"], ["pA"])
+        op("v", "off", lambda: V.tensor_copy(T.off[:], NP), 256, blk("pA", 4, 4), ["off"], ["pA"])
+        op("s", "nl", lambda: S.activation(T.nl[:], T.pA[:, 4::2, :], Act.Copy), 128, blk("pA", 4, 4), ["nl"], ["pA"])
+        op("v", "dn", lambda: V.tensor_tensor(T.dn[:], T.pA[:, 5::2, :], T.nl[:], Op.subtract), 128, blk("pA", 4, 4) + ["nl"], ["dn"], ["pA"])
 
-    F, FS, FT, FA = T.pF[:, 0:2, 0:33], T.pF[:, 2:4, 0:32], T.pF[:, 4:6, :], T.pF[:, 6:8, 0:32]
+    tj = 2 if NEW else 4
+    F, FT = T.pF[:, 0:2, 0:33], T.pW[:, tj:tj + 2, :]
 
-    def count_start(l):
-        last = l == NL - 1
-        j = NL if last else l
-        if last:
-            op("s", lambda: S.activation(T.bs[:, NL, :, 8:72], T.bs[:, l, :, 8:72], Act.Identity, bias=float(NL)), 128, ["b%d" % l], ["b%d" % NL])
-        op("s", lambda: S.activation(T.blo[:, l], T.bs[:, l, :, 8:72], Act.Identity, bias=float(NL - 2) if last else -2.0), 128, ["b%d" % l], ["blo%d" % l])
-        op("t", [lambda: PE.matmul(FS, ident, T.bs[:, j, :, 8:72:2], True, False), lambda: PE.matmul(FS, ident, T.bs[:, j, :, 7:71:2], False, True),
-                 lambda: PE.matmul(F, ident, T.bs[:, j, :, 7:72:2], True, False)], 64, ["wb", "pad", "b%d" % j], ["F", "Fs", "Ft"], ["pF"])
-
-    def count(l, k, h, b):
-        def turn(b, cols):
-            return [lambda: PE.matmul(T[b][:, cols, :], ident, T.c1[:], True, False)] + [
-                lambda j=j: PE.matmul(T[b][32 * j:32 * j + 32, cols, :], T.w16[:, l, col(h)], T.sel[:, :, :, 4 * j:4 * j + 4], False, False) for j in range(4)]
-        high, low = T[b][:, 4:6, :], T.pW[:, 2 * k:2 * k + 2, :]
-        op("t", turn(b, slice(4, 6)) + [lambda: PE.matmul(high, ident, T.c3[:], False, True)], 128,
-           ["wb", "c1", "c3", "sel"] + tags("w%d" % l, h), ["W" + b, "acc" + b, {"pA": "N", "pB": "H"}[b]], [b], "turn")
-        op("t", turn("pW", slice(2 * k, 2 * k + 2)) + [lambda: PE.matmul(low, ident, T.c2[:], False, False)], 128,
-           ["wb", "c1", "c2", "sel"] + tags("w%d" % l, h), ["L%d" % k, "accpW"], ["pW"], "turn")
-        op("s", lambda: S.activation(T.dv[:, k], high, Act.Copy), 128, ["W" + b], ["dv%d" % k], [b], "steps")
-        op("t", lambda: PE.matmul(low, T.neg[:], T.dv[:, k], False, True), 128, ["neg", "dv%d" % k], ["L%d" % k, "accpW"], ["pW"])
+    def count(l, k, h, b, b2):
+        def turn(b, cols, eye, const):
+            rows = [lambda j=j: PE.matmul(T[b][32 * j:32 * j + 32, cols, :], T.w16[:, l, col(h)], T.sel[:, :, :, 4 * j:4 * j + 4], False, False) for j in range(4)]
+            return [lambda: PE.matmul(T[b][:, cols, :], eye, const, True, False)] + rows
+        name, k = k, int(k)
+        high, low = T[b][:, 4:6, :], T[b2][:, 0:2, :]
+        op("t", "hi" + name, turn(b, slice(4, 6), ident, T.c1[:]) + [lambda: PE.matmul(high, ident, T.c3[:], False, True)], 128,
+           ["wb", "c1", "c3", "sel"] + tags("w%d" % l, h), blk(b, 4, 2) + ["acc" + b], [b])
+        op("t", "lo" + name, turn(b2, slice(0, 2), identh, T.c2[:]), 128,
+           ["wh", "c2", "sel"] + tags("w%d" % l, h), blk(b2, 0, 2) + ["acc" + b2, "h" + b2], [b2])
+        op("s", "dv" + name, lambda: S.activation(T.dv[:, k], high, Act.Copy), 128, blk(b, 4, 2), ["dv%d" % k], [b])
+        op("t", "ng" + name, lambda: PE.matmul(low, T.neg[:], T.dv[:, k], False, True), 128, ["neg", "dv%d" % k], blk(b2, 0, 2) + ["acc" + b2], [b2])
         for u in range(8):
-            op("v", lambda u=u: V.tensor_scalar(T.oh[:, 8 * k:8 * k + 8, u, :], T.dv[:, k], ROUND64 + 256.0 * u, 4096.0, Op.is_equal, Op.mult), 64,
-               ["dv%d" % k], ["oh%d%d" % (k, u)], line="hot")
-            op("s", lambda u=u: S.activation(T.th[:, 8 * k:8 * k + 8, u::8, :], low, Act.Sigmoid, bias=-256.0 * u - EDGE, scale=128.0), 128,
-               ["L%d" % k], ["th%d%d" % (k, u)], ["pW"], "steps")
-        op("t", [lambda gr=gr, i=i: PE.matmul(T.pF[32 * (gr % 4):32 * (gr % 4) + 32, gr // 4, 0:32], T.oh[:, 8 * k + gr, :, i::4], T.th[:, 8 * k + gr, :, i],
-                                               False, False) for gr in range(8) for i in range(4)]
-           + ([lambda: PE.matmul(F, ident, T.zero[:], False, True)] if k == 1 else []), 32,
-           ["wb", "zero"] + ["%s%d%d" % (x, k, u) for x in ("oh", "th") for u in range(8)], ["F"], ["pF"])
+            op("v", "oh" + name, lambda u=u: V.tensor_scalar(T.oh[:, 8 * k:8 * k + 8, u, :], T.dv[:, k], ROUND64 + 256.0 * u, 4096.0, Op.is_equal, Op.mult), 64,
+               ["dv%d" % k], ["oh%d%d" % (k, u)])
+            op("s", "th" + name, lambda u=u: S.activation(T.th[:, 8 * k:8 * k + 8, u::8, :], low, Act.Sigmoid, bias=-256.0 * u - EDGE, scale=128.0), 128,
+               blk(b2, 0, 2), ["th%d%d" % (k, u)], [b2])
+        ends = [lambda: PE.matmul(F, ident, T.zero[:], k == 0, k == 1)]
+        sums = [lambda gr=gr, i=i: PE.matmul(T.pF[32 * (gr % 4):32 * (gr % 4) + 32, gr // 4, 0:32], T.oh[:, 8 * k + gr, :, i::4], T.th[:, 8 * k + gr, :, i],
+                                              False, False) for gr in range(8) for i in range(4)]
+        op("t", "sum" + name, ends + sums if k == 0 else sums + ends, 32,
+           ["wb", "zero"] + ["%s%d%d" % (x, k, u) for x in ("oh", "th") for u in range(8)], blk("pF", 0, 2) + ["accpF"], ["pF"])
 
     def biases(l):
         last = l == NL - 1
-        new = T.bout[:] if last else T.bs[:, l + 1, :, 8:72]
-        for fn, n, reads, writes in [
-                (lambda: V.tensor_scalar(T.i2[:], F, ROUND4096, -ROUND4096, Op.add, Op.add), 66, ["F"], ["i2"]),
-                (lambda: V.tensor_scalar(T.im[:], F, 2.0 ** -12, ROUND1, Op.mult, Op.add), 66, ["F"], ["im"]),
-                (lambda: V.tensor_tensor(T.ee[:], F, T.i2[:], Op.subtract), 66, ["F", "i2"], ["ee"]),
-                (lambda: V.tensor_tensor(FA, T.im[:, :, 1:33], T.im[:, :, 0:32], Op.subtract), 128, ["im"], ["Fa"]),
-                (lambda: V.tensor_tensor(T.pF[:, 4:6, 0::2], FS, T.ee[:, :, 0:32], Op.subtract), 64, ["Fs", "ee"], ["Ft"]),
-                (lambda: V.tensor_tensor(T.pF[:, 4:6, 1::2], FA, T.ee[:, :, 1:33], Op.add), 64, ["Fa", "ee"], ["Fu"]),
-                (lambda: V.tensor_tensor(new, FT, T.blo[:, l], Op.max), 128, ["Ft", "Fu", "blo%d" % l], ["bout" if last else "b%d" % (l + 1)])]:
-            op("v", fn, n, reads, writes, ["pF"])
+        j = NL if last else l
         if last:
-            dma("y", "oyb", [(T.yb[4 * half:4 * half + 4, :], T.bout[:, half, :]) for half in range(2)], ["bout"], ["yb"])
+            op("s", "blo", lambda: S.activation(T.bs[:, NL], T.bs[:, l], Act.Identity, bias=float(NL)), 128, ["b%d" % l], ["b%d" % NL])
+        op("s", "blo", lambda: S.activation(T.blo[:, l], T.bs[:, l], Act.Identity, bias=float(NL - 2) if last else -2.0), 128, ["b%d" % l], ["blo%d" % l])
+        new = T.bout[:] if last else T.bs[:, l + 1]
+        even, odd = T.pW[:, tj:tj + 2, 0::2], T.pW[:, tj:tj + 2, 1::2]
+        fb, tb = blk("pF", 0, 2), blk("pW", tj, 2) + ["accpW"]
+        op("t", "Tb", lambda: PE.matmul(FT, ident, T.bs[:, j], True, False), 128, ["wb", "b%d" % j], tb, ["pW"])
+        op("v", "post", lambda: V.tensor_scalar(T.i2[:], F, ROUND4096, -ROUND4096, Op.add, Op.add), 66, fb, ["i2"], ["pF"])
+        op("v", "post", lambda: V.tensor_scalar(T.up[:], F, 2.0 ** -12, 1024.0, Op.mult, Op.add), 66, fb, ["up"], ["pF"])
+        op("v", "post", lambda: V.tensor_tensor(T.ee[:], F, T.i2[:], Op.subtract), 66, fb + ["i2"], ["ee"], ["pF"])
+        op("t", "Tu", [lambda: PE.matmul(odd, T.negh[:], T.up[:, :, 0:32], False, False), lambda: PE.matmul(odd, identh, T.up[:, :, 1:33], False, False)],
+           64, ["wh", "negh", "up"], tb, ["pW"])
+        op("t", "Te", [lambda: PE.matmul(odd, identh, T.ee[:, :, 1:33], False, False), lambda: PE.matmul(even, T.negh[:], T.ee[:, :, 0:32], False, True)],
+           64, ["wh", "negh", "ee"], tb, ["pW"])
+        op("v", "post", lambda: V.tensor_tensor(new, FT, T.blo[:, l], Op.max), 128, tb + ["blo%d" % l], ["bout" if last else "b%d" % (l + 1)], ["pW"])
+        if last:
+            dma("y", "bias", "oyb", [(T.yb[4 * half:4 * half + 4, :], T.bout[:, half, :]) for half in range(2)], ["bout"], ["yb"])
         else:
-            dma("y", "bias%d" % l, [(bias_rows(T.kw, half), T.bs[:, l + 1, half, 8:72]) for half in range(2)], ["b%d" % (l + 1)], ["kw", "kw%d" % l])
+            dma("y", "bias", "bias%d" % l, [(bias_rows(T.kw, half), T.bs[:, l + 1, half, :]) for half in range(2)], ["b%d" % (l + 1)], ["kw", "kw%d" % (l + 1)])
+
+    out_j, in_j = (2, 0) if rank < mate else (0, 2)
+
+    def chosen(l, k, h):
+        return (T.uw, T.vw)[k][:].indirect(T.wu[:, l, col(h)]), ["uv"[k] + "w"] + tags("wu%d" % l, h)
 
     def pick(l, kind, h, q):
-        r = span(h)[0]
-        src = (T.uw if kind == "u" else T.vw)[:].indirect(T.wu[:, l, col(h)])
-        out = (T.uvr if r == rank else T.uvs)[:, 4 * l + r, "uv".index(kind), :]
-        op(q.lower(), (lambda: V.tensor_copy(out, src)) if q == "v" else (lambda: S.activation(out, src, Act.Copy)),
-           256 * GATHER, [kind + "w", "wu%d_%d" % (l, r)], ["%s%s%d%d" % (kind, "r" if r == rank else "s", l, r)], line="steps" if q == "S" else None)
+        k = "uv".index(kind)
+        src, reads = chosen(l, k, h)
+        out = T.away[:, 2 * l + k] if h == "r" else T.near[:, 2 * l + k, {"l": tok(min(1, out_j), 2), "m": tok(out_j), "o": tok(1)}[h]]
+        op(q, "UV"[k] + h, (lambda: V.tensor_copy(out, src)) if q == "v" else (lambda: S.activation(out, src, Act.Copy)),
+           256 * span(h)[1] * GATHER, reads, tags("%s%dp" % (kind, l), h))
 
-    def parcel(l, kinds, hs, qs):
-        to = [span(h)[0] for h in hs.split("+")]
-        for (kind, h), q in zip([(kind, h) for kind in kinds for h in hs.split("+")], qs):
-            pick(l, kind, h, q)
-        if to != [rank]:
-            sem, k = "a%d%s%s" % (l, kinds, hs[0:2]), slice("uv".index(kinds[0]), "uv".index(kinds[-1]) + 1)
-            send([(r, part(e_on if r == mate else e_off, i, len(to)), sem, T.uvs[:, 4 * l + r, k], T.uvr[:, 4 * l + rank, k]) for i, r in enumerate(to)],
-                 ["%ss%d%d" % (kind, l, r) for kind in kinds for r in to],
-                 [(sem, ["%sr%d%d" % (kind, l, r) for kind in kinds for r in to], 0 if to == [mate] else len(to) * len(kinds))])
+    def give(l, kinds, to, *behind):
+        items, reads, lands = [], list(behind), []
+        for i, kind in enumerate(kinds):
+            k = 2 * l + "uv".index(kind)
+            for h in to:
+                sem = "a%d%s%s" % (l, kind, h)
+                if h == "r":
+                    items += [(r, part(e_off, j, 2), sem, T.away[:, k, tok(j)], T.came[:, k, rank - loc0]) for j, r in enumerate(rem)]
+                else:
+                    items += [(mate, part(e_on, i, len(kinds)), sem, T.near[:, k, tok(out_j)], T.near[:, k, tok(out_j)])]
+                reads += tags("%s%dp" % (kind, l), h)
+                lands += [(sem, tags("%s%dc" % (kind, l), h), 2 if h == "r" else 0)]
+        send(kinds.upper() + to, items, reads, lands)
 
-    X, M = T.pX[:, 0:4, :], T.pM[:, 0:4, :]
-    mixed = [0]
+    xb_, xj = ("pW", 4) if NEW else ("pD", 0)
+    X, M = T[xb_][:, xj:xj + 4, :], T.pM[:, 0:4, :]
+    mixes, mixed = [0] * NL, [0] * NL
 
-    def mix(rhs):
-        mixed[0] += 1
-        return PE.matmul(M, T.m32[:], rhs, mixed[0] % 5 == 1, mixed[0] % 5 == 0)
+    def mix(l, name, m, rhs, reads):
+        def fn():
+            mixed[l] += 1
+            return PE.matmul(M, m, rhs, mixed[l] == 1, mixed[l] == mixes[l])
+        op("t", name, fn, 1024, reads, ["pM%d" % mixes[l]], ["pM"])
+        mixes[l] += 1
 
-    def expert(l, h):
-        r = span(h)[0]
-        b, j = ("pD1", r - rem0) if r in rem else ("pD0", r - loc0)
-        D = T[b][:, 4 * j:4 * j + 4, :]
-        op("v", lambda: V.tensor_tensor(T.pu[:, tok(r)], X, T.uvr[:, 4 * l + r, 0, :], Op.mult), 256, ["X", "ur%d%d" % (l, r)], ["pu%d" % r], ["pX"])
-        op("t", lambda: PE.matmul(D, T.bd[:], T.pu[:, tok(r)], True, True), 1024, ["bd", "pu%d" % r], ["D%d" % r], [b])
-        op("s", lambda: S.activation(T.sg[:, tok(r)], D, Act.Sigmoid), 256, ["D%d" % r], ["sg%d" % r], [b])
-        op("v", lambda: V.tensor_tensor(D, D, T.sg[:, tok(r)], Op.mult), 256, ["D%d" % r, "sg%d" % r], ["D%d" % r], [b])
-        op("v", lambda: V.tensor_tensor(T.yy[:, tok(r)], D, T.uvr[:, 4 * l + r, 1, :], Op.mult), 256, ["D%d" % r, "vr%d%d" % (l, r)], ["y%d" % r], [b])
-        op("t", lambda: mix(T.yy[:, tok(r)]), 1024, ["m32", "y%d" % r], ["M%d" % r], ["pM"])
+    def expert(l, h, form, b, b0):
+        b0 = int(b0)
+        if h == "r":
+            n, y0, ranks = 2, 2, rem
+            src = lambda k, i, m: T.came[:, 2 * l + k, i:i + m]
+        else:
+            j0 = {"l": min(1, in_j), "m": in_j, "o": 1}[h]
+            n, y0 = span(h)[1], j0 - min(1, in_j)
+            ranks = [rank if j == 1 else mate for j in range(j0, j0 + n)]
+            src = lambda k, i, m: T.near[:, 2 * l + k, tok(j0 + i, m)]
+        have = lambda kind, r: "%s%d%s_%d" % (kind, l, "p" if r == rank else "c", r)
+        order = sorted(range(n), key=lambda i: ranks[i] != rank)
+        E, eb = T[b][:, b0:b0 + 4 * n, :], blk(b, b0, 4 * n)
+        if form == "f":
+            (u, ur), (v, vr) = chosen(l, 0, h), chosen(l, 1, h)
+            op("v", "pu" + h, lambda: V.tensor_tensor(T.pu[:, y0], u, T.xo[:], Op.mult), 256 * GATHER, ["xo"] + ur, ["pu%d" % y0])
+        for i in order if form != "f" else ():
+            op("v", "pu" + h, lambda i=i: V.tensor_tensor(T.pu[:, y0 + i], X, src(0, i, 1), Op.mult), 256,
+               blk(xb_, xj, 4) + [have("u", ranks[i])], ["pu%d" % (y0 + i)], [xb_])
+        if form not in "ch":
+            for i in order:
+                op("t", "D" + h, lambda i=i: PE.matmul(T[b][:, b0 + 4 * i:b0 + 4 * i + 4, :], T.bd[:], T.pu[:, y0 + i], True, True), 1024,
+                   ["bd", "pu%d" % (y0 + i)], blk(b, b0 + 4 * i, 4) + ["acc" + b], [b])
+            op("s", "sg" + h, lambda: S.activation(T.sg[:, y0:y0 + n], E, Act.Sigmoid, scale=4.0 if NEW else 1.0), 256 * n, eb, rs("sg", y0, n), [b])
+            if form == "f":
+                op("v", "sm" + h, lambda: V.tensor_tensor(T.sg[:, y0], E, T.sg[:, y0], Op.mult), 256, eb + ["sg%d" % y0], ["sg%d" % y0], [b])
+                op("v", "yy" + h, lambda: V.tensor_tensor(T.yy[:, y0], v, T.sg[:, y0], Op.mult), 256 * GATHER, ["sg%d" % y0] + vr, ["y%d" % y0])
+            else:
+                op("v", "sm" + h, lambda: V.tensor_tensor(E, E, T.sg[:, y0:y0 + n], Op.mult), 256 * n, eb + rs("sg", y0, n), eb, [b])
+        else:
+            D, db = T.pD[0:32 * n, 4 + y0, :], blk("pD", 4 + y0, 1)
+            for i in order:
+                op("t", "D" + h,
+                   [lambda i=i, j=j: PE.matmul(D, T.fold[:, 56 - 32 * i - 8 * j:56 - 32 * i - 8 * j + 32 * n], T.pu[:, y0 + i, 64 * j:64 * j + 64],
+                                               i == order[0] and j == 0, i == order[-1] and j == 3) for j in range(4)],
+                   256, ["fold", "pu%d" % (y0 + i)], db + ["accpD"], ["pD"])
+            op("s", "sg" + h, lambda: S.activation(T.sn[0:32 * n, y0], D, Act.Sigmoid), 64, db, ["sn%d" % y0], ["pD"])
+            op("v", "sm" + h, lambda: V.tensor_tensor(T.sc[0:32 * n, y0], D, T.sn[0:32 * n, y0], Op.mult), 64, db + ["sn%d" % y0], ["sc%d" % y0], ["pD"])
+            if form == "h":
+                op("s", "sh" + h, lambda: S.activation(T.sp[0:32 * n, y0, 0], T.sc[0:32 * n, y0], Act.Copy), 64, ["sc%d" % y0], ["sh%d" % y0])
+                op("v", "sd" + h, lambda: V.tensor_tensor(T.sp[0:32 * n, y0, 1], T.sc[0:32 * n, y0], T.sp[0:32 * n, y0, 0], Op.subtract), 128,
+                   ["sc%d" % y0, "sh%d" % y0], ["sd%d" % y0])
+                op("t", "E" + h, [lambda k=k, j=j: PE.matmul(T[b][:, b0 + k, :], T.wideb[0:32 * n, 8 * k:8 * k + 8, :], T.sp[0:32 * n, y0, j], j == 0, j == 1)
+                                  for k in range(4 * n) for j in range(2)], 64, ["wide", "sh%d" % y0, "sd%d" % y0], eb + ["acc" + b], [b])
+            for i in range(n) if form == "c" else ():
+                op("t", "E" + h, [lambda k=k: PE.matmul(T[b][:, b0 + k, :], T.wide[0:32 * n, 8 * k:8 * k + 8, :], T.sc[0:32 * n, y0], True, True)
+                                  for k in range(4 * i, 4 * i + 4)], 256, ["wide", "sc%d" % y0], blk(b, b0 + 4 * i, 4) + ["acc" + b], [b])
+        vs = [have("v", r) for r in ranks]
+        if form in "jx":
+            keep = int(form == "j")
+            P = T[b][:, b0 + 4 * keep:b0 + 4 * n, :]
+            if keep:
+                op("v", "yy" + h, lambda: V.tensor_tensor(T.yy[:, y0], T[b][:, b0:b0 + 4, :], src(1, 0, 1), Op.mult), 256, eb + vs, ["y%d" % y0], [b])
+            op("v", "yy" + h, lambda: V.tensor_tensor(P, P, src(1, keep, n - keep), Op.mult), 256 * (n - keep), eb + vs, eb, [b])
+            for i in range(keep, n):
+                op("v", "ad" + h, lambda i=i: V.tensor_tensor(T.yy[:, y0], T[b][:, b0 + 4 * i:b0 + 4 * i + 4, :], T.yy[:, y0] if i else T.sx[:], Op.add), 256,
+                   eb + ["y%d" % y0, "sx"], ["y%d" % y0], [b])
+        elif form != "f":
+            op("v", "yy" + h, lambda: V.tensor_tensor(T.yy[:, y0:y0 + n], E, src(1, 0, n), Op.mult), 256 * n, eb + vs, rs("y", y0, n), [b])
+        for i in range(1 if form in "jx" else n):
+            mix(l, "mix" + h, T.m32[:] if NEW else T.m4[:], T.yy[:, y0 + i], ["m32" if NEW else "m4", "y%d" % (y0 + i)])
 
     def tokens(l):
-        op("t", lambda: mix(T.xs2[:]), 1024, ["m32", "xs2"], ["M4"], ["pM"])
-        op("s", lambda: S.activation(T.sx[:], M, Act.Sigmoid, scale=0.5), 256, rs("M", 0, 5), ["sx"], ["pM"])
+        if ",x," not in PLAN[l]:
+            mix(l, "mixx", T.m32[:], T.sx[:], ["m32", "sx"])
+        op("s", "new", lambda: S.activation(T.sx[:], M, Act.Sigmoid, bias=T.less[:, 0:1], scale=2.0), 256, blk("pM", 0, 5) + ["less"], ["sx"], ["pM"])
         if l == NL - 1:
-            op("s", lambda: S.activation(T.xo[:], T.sx[:], Act.Identity, bias=-1.0, scale=2.0), 256, ["sx"], ["xo"])
-            dma("s", "oyx", [(T.yx[:], T.xo[:])], ["xo"], ["yx"])
+            op("s", "new", lambda: S.activation(T.xo[:], T.sx[:], Act.Identity, bias=-1.0, scale=2.0), 256, ["sx"], ["xo"])
+            dma("s", "new", "oyx", [(T.yx[:], T.xo[:])], ["xo"], ["yx"])
         else:
-            op("s", lambda: S.activation(X, T.sx[:], Act.Identity, bias=-1.0, scale=2.0), 256, ["sx"], ["X"], ["pX"])
-            calls[-1]["due"] = DUE[l]
-            op("s", lambda: S.activation(T.xs2[:], T.sx[:], Act.Identity, bias=-2.0, scale=4.0), 256, ["sx"], ["xs2"])
+            op("s", "newp", lambda: S.activation(X, T.sx[:], Act.Identity, bias=-1.0, scale=2.0), 256, ["sx"], blk(xb_, xj, 4), [xb_])
+            if ",f," in PLAN[l + 1]:
+                op("s", "news", lambda: S.activation(T.xo[:], T.sx[:], Act.Identity, bias=-1.0, scale=2.0), 256, ["sx"], ["xo"])
 
+    turns = (0, 2, 1, 3)
     for l in range(NL):
-        turns = (0, 2, 1, 3)
+        layer[0] = l
         if l == 0:
+            for h, q in (("m", "v"), ("r", "s")):
+                for c in turns:
+                    raw(q, c, h)
             for c in turns:
-                hold("v", c, "m", ("pW", "pF")[c % 2], c // 2)
-                hold("s", c, "r", ("pD0", "pD1", "pX", "pM")[c], 0)
-            for c in turns:
-                gather(c, "o")
-            for c in turns:
-                times(c, "m", ("pW", "pF")[c % 2], c // 2)
-            for c in turns:
-                times(c, "r", ("pD0", "pD1", "pX", "pM")[c], 0)
+                fused(c, "o")
+            for c, b, j in zip(turns[1:], ("pW", "pF", "pW"), (0, 0, 4)):
+                held(c, "m", b, j, 0)
+            for c, b in zip(turns[1:], ("pE", "pM", "pQ")):
+                held(c, "r", b, 0, 0)
+            op("t", "q", lambda: PE.matmul(T.pQ[:], ident, T.qall[:, tok(loc0, 2)], True, True), 512, ["wb"] + rs("q", loc0, 2), blk("pQ", 0, 8) + ["accpQ"], ["pQ"])
+            if NEW:
+                if "q" in "".join(w for k in KEYS for w in k.split() if w[0] == "r"):
+                    op("t", "qr", lambda: PE.matmul(T.pD[:], ident, T.qall[:, tok(rem0, 2)], True, True), 512, ["wb"] + rs("q", rem0, 2), blk("pD", 0, 8) + ["accpD"], ["pD"])
+                op("t", "less", lambda: PE.matmul(T.pM[:, 7, 0:2], T.mb[:], T.minus[:], True, True), 64, ["mb", "minus"], blk("pM", 0, 8), ["pM"])
+                op("s", "less", lambda: S.activation(T.less[:], T.pM[:, 7, 0:2], Act.Copy), 64, blk("pM", 0, 8), ["less"], ["pM"])
+                op("s", "x", lambda: S.activation(X, T.xb[:], Act.Copy), 256, ["xb"], blk(xb_, xj, 4), [xb_])
+            else:
+                op("t", "prep", [lambda: PE.matmul(T.pD[:, 7, 0:2], T.mb[:], T.minus[:], True, True), lambda: PE.matmul(X, ident, T.xb[:], True, True)], 160,
+                   ["wb", "xb", "mb", "minus"], blk("pD", 0, 4) + ["pD7", "accpD"], ["pD"])
+            op("s", "prep", lambda: S.activation(T.m32[:], T.mb[:], Act.Copy), 128, ["mb"], ["m32"])
+            if not NEW:
+                op("s", "prep", lambda: S.activation(T.m4[:], T.mb[:], Act.Identity, scale=0.25), 128, ["mb"], ["m4"])
+            op("s", "prep", lambda: S.activation(T.sx[:], T.xb[:], Act.Identity, bias=0.5, scale=0.5), 256, ["xb"], ["sx"])
+            if not NEW:
+                op("s", "prep", lambda: S.activation(T.less[:], T.pD[:, 7, 0:2], Act.Copy), 64, ["pD7"], ["less"], ["pD"])
         else:
-            for c in HELD:
-                hold("s", c, "l", HELD[c], 0)
-            for step in PLAN[l]:
-                for c in turns if step[0] == "judge" else ():
-                    if c in HELD and step[1] in "lmo":
-                        times(c, step[1], HELD[c], span(step[1])[0] - loc0)
+            for h, how in (word.split(",") for word in KEYS[l].split()):
+                for c, x in zip(turns, how):
+                    if x == "f":
+                        fused(c, h)
+                        continue
+                    raw("s", c, h)
+                    if x == "q":
+                        times(c, h)
                     else:
-                        gather(c, step[1])
-        if l == 0:
-            op("s", lambda: S.activation(T.bd[:], T.bdb[:], Act.Sigmoid, bias=-128.0, scale=256.0), 1500, ["bdb"] + tags("raw3", "r"), ["bd", "wide"])
-            op("s", lambda: S.activation(T.m32[:], T.mb[:], Act.Copy), 128, ["mb"], ["m32"])
-            op("s", lambda: S.activation(X, T.xb[:], Act.Copy), 256, ["xb"], ["X"], ["pX"])
-            op("s", lambda: S.activation(T.xs2[:], T.xb[:], Act.Identity, scale=2.0), 256, ["xb"], ["xs2"])
-        count_start(l)
-        for step in PLAN[l]:
-            {"judge": winners, "count": count, "send": parcel, "tell": tell, "names": names, "biases": biases}[step[0]](l, *step[1:])
-        for h in ("o", "m", "ra", "rb"):
-            expert(l, h)
+                        held(c, h, "p" + x)
+        for step in PLAN[l].split():
+            name, *args = step.split(",")
+            {"judge": winners, "count": count, "pick": pick, "give": give, "tell": tell, "names": names, "biases": biases, "expert": expert}[name](l, *args)
         tokens(l)
 
     issue(g, T, topo, core, calls)
@@ -359,50 +575,41 @@ def arrange(calls):
             readers.setdefault(r, []).append(i)
         for r in c["writes"]:
             lastw[r], readers[r] = i, []
-        if c["kind"] == "send":
-            lastw[c["local"]] = i
-    behind, last = {}, {}
+    steps, lines = {}, []
     for i, c in enumerate(calls):
-        if c.get("line"):
-            if c["line"] in last:
-                behind[i] = last[c["line"]]
-            last[c["line"]] = i
-    n = len(calls)
-    edges = [(j, i, calls[j]["late"] + (calls[i]["flight"] if calls[i].get("after") == j else 0.0)) for i in range(n) for j in before[i]]
-    edges += [(j, i, 0.0) for i, j in behind.items()]
-    busy = [c["busy"] + 1e-4 for c in calls]
-
-    def place(order, back):
-        need = [[] for _ in calls]
-        for j, i, lag in edges:
-            need[j if back else i].append((i if back else j, lag))
-        start, taken = {}, {}
-        for i in order:
-            c = calls[i]
-            t = max([c["late"] if back else 0.0] + [start[j] + busy[j] + lag for j, lag in need[i]])
-            spans = [(a, b) for a, b, _q in taken.get(c["q"], []) if b > t]
-            spans += [(a - HOP, b + HOP) for k in c["banks"] for a, b, q in taken.get(k, []) if q != c["q"] and b + HOP > t]
-            for a, b in sorted(spans):
-                if a >= t + busy[i]:
-                    break
-                t = max(t, b)
-            start[i] = t
-            for k in ([c["q"]] if c["q"] else []) + list(c["banks"]):
-                taken.setdefault(k, []).append((t, t + busy[i], c["q"]))
-        return start
-    way = [max(busy[i] + calls[i]["late"], calls[i].get("due", 0)) for i in range(n)]
-    for j, i, lag in sorted(edges, key=lambda e: -e[1]):
-        way[j] = max(way[j], busy[j] + lag + way[i])
-    start = place(sorted(range(n), key=lambda i: -way[i]), False)
-    for _ in range(ROUNDS):
-        back = place(sorted(range(n), key=lambda i: -start[i] - busy[i]), True)
-        start = place(sorted(range(n), key=lambda i: -back[i] - busy[i]), False)
-        LOG.append(max(start[i] + busy[i] + calls[i]["late"] for i in range(n)))
-    return [calls[i] for i in sorted(range(n), key=lambda i: start[i])]
-
-
-ROUNDS = 1
-LOG = []
+        if c["q"]:
+            steps.setdefault((c["q"],) + c["name"], []).append(i)
+        else:
+            lines.append([i])
+    for q in ORDER:
+        line = []
+        for l, words in enumerate(ORDER[q]):
+            for word in words.split():
+                name, _, n = word.partition("*")
+                rest = steps[(q, l - name.count("-"), name.lstrip("-"))]
+                line += [rest.pop(0) for _ in range(int(n) if n else len(rest))]
+        lines.append(line)
+    assert not any(steps.values()), [k for k in steps if steps[k]]
+    end, free, bank, order = {}, {}, {}, []
+    while any(lines):
+        best = None
+        for line in lines:
+            if line and all(j in end for j in before[line[0]]):
+                c = calls[line[0]]
+                t = max([free.get(c["q"], 0.0)] + [end[j] + calls[j]["late"] for j in before[line[0]]]
+                        + [e + HOP for b in c["banks"] for q, e in bank.get(b, {}).items() if q != c["q"]])
+                if best is None or t < best[0]:
+                    best = (t, line)
+        assert best, [calls[line[0]].get("name") for line in lines if line]
+        t, i = best[0], best[1].pop(0)
+        c = calls[i]
+        end[i] = t + c["busy"]
+        if c["q"]:
+            free[c["q"]] = end[i]
+        for b in c["banks"]:
+            bank.setdefault(b, {})[c["q"]] = end[i]
+        order.append(c)
+    return order
 
 
 def issue(g, T, topo, core, calls):

@@ -5,148 +5,89 @@ from concourse.mybir import AluOpType as Op, ActivationFunctionType as Act
 NL = 3
 BF, F32, F16, I32, U16 = "bfloat16", "float32", "float16", "int32", "uint16"
 SCRATCH = {
-    "qall": ("sbuf", [128, 1024], BF), "nmi": ("sbuf", [128, 4, 64], I32), "nmh": ("sbuf", [128, 256], F16), "nmn": ("sbuf", [128, 4, 64], F16),
-    "off": ("sbuf", [128, 256], U16), "kw": ("sbuf", [128, 2048], BF), "uw": ("sbuf", [128, 2048], BF),
-    "vw": ("sbuf", [128, 2048], BF), "xb": ("sbuf", [128, 256], BF), "mb": ("sbuf", [128, 128], BF),
-    "m32": ("sbuf", [128, 128], F32), "m4": ("sbuf", [128, 128], F32), "less": ("sbuf", [128, 2], F32), "minus": ("sbuf", [128, 2], BF),
+    "qall": ("sbuf", [128, 1024], BF), "qt": ("sbuf", [128, 1024], BF), "nmi": ("sbuf", [128, 256], I32),
+    "nmh": ("sbuf", [128, 4, 64], F16), "nmn": ("sbuf", [128, 4, 64], F16), "off": ("sbuf", [128, 256], U16),
+    "kw": ("sbuf", [128, 2048], BF), "uw": ("sbuf", [128, 2048], BF), "vw": ("sbuf", [128, 2048], BF),
+    "xb": ("sbuf", [128, 256], BF), "mb": ("sbuf", [128, 128], BF), "m32": ("sbuf", [128, 128], F32),
+    "less": ("sbuf", [128, 2], F32), "minus": ("sbuf", [128, 66], BF), "four": ("sbuf", [128, 64], BF),
     "xo": ("sbuf", [128, 256], F32), "sx": ("sbuf", [128, 256], F32),
-    "rawk": ("sbuf", [128, 4, 1024], BF), "prod": ("sbuf", [128, 4, 1024], F16), "zh": ("sbuf", [128, 144], F16),
-    "wb": ("sbuf", [128, 16, 16], BF), "wh": ("sbuf", [128, 16, 16], F16), "neg": ("sbuf", [128, 8, 16], BF), "negh": ("sbuf", [128, 8, 16], F16),
-    "bd": ("sbuf", [128, 128], F32), "bdb": ("sbuf", [128, 128], BF), "fold": ("sbuf", [128, 120], F32), "wide": ("sbuf", [128, 64, 16], F32),
-    "sel": ("sbuf", [128, 8, 4, 16], F16), "c1": ("sbuf", [128, 128], BF), "c2": ("sbuf", [128, 128], F16), "c3": ("sbuf", [128, 128], BF),
-    "zero": ("sbuf", [128, 66], BF), "cbig": ("sbuf", [128, 256], BF), "hb": ("sbuf", [128, 256], BF),
-    "sl": ("sbuf", [128, 2, 64], F32), "nl": ("sbuf", [128, 2, 64], F32), "dn": ("sbuf", [128, 2, 64], F32),
-    "mx": ("sbuf", [128, 2, 64], F32), "nx": ("sbuf", [128, 2, 64], F32), "px": ("sbuf", [128, 2, 64], F32),
+    "rawk": ("sbuf", [128, 4, 1024], BF), "prod": ("sbuf", [128, 1024, 4], F16), "quick": ("sbuf", [128, 64, 4, 16], F16), "zh": ("sbuf", [128, 144], F16),
+    "wb": ("sbuf", [128, 16, 16], BF), "wh": ("sbuf", [128, 16, 16], F16), "selb": ("sbuf", [128, 8, 4, 16], BF), "seln": ("sbuf", [128, 8, 4, 16], BF),
+    "half": ("sbuf", [128, 8], BF), "bdn": ("sbuf", [128, 128], BF), "bd": ("sbuf", [128, 128], F32), "hw": ("sbuf", [128, 2, 32], BF), "sg": ("sbuf", [128, 4, 256], F32),
+    "negh": ("sbuf", [128, 8, 16], F16),
+    "bdb": ("sbuf", [128, 128], BF), "fold": ("sbuf", [128, 8], F32), "wide": ("sbuf", [128, 32, 16], BF),
+    "sel": ("sbuf", [128, 8, 4, 16], F16), "c1": ("sbuf", [128, 128], BF), "c2": ("sbuf", [128, 128], F16),
+    "cbig": ("sbuf", [128, 256], BF), "hb": ("sbuf", [128, 256], BF),
+    "ramp": ("sbuf", [128, 64], BF), "none": ("sbuf", [128, 128], F32), "top": ("sbuf", [128, 256], F32), "keep": ("sbuf", [128, 256], F32), "run": ("sbuf", [128, 256], F16),
     "w16": ("sbuf", [128, NL, 64], F16), "wu": ("sbuf", [128, NL, 64], U16), "wr": ("sbuf", [128, 2, 4, 64], F16),
     "dv": ("sbuf", [128, 2, 8, 16], BF), "oh": ("sbuf", [128, 16, 8, 16], BF), "th": ("sbuf", [128, 16, 32, 4], BF),
-    "bs": ("sbuf", [128, NL + 1, 2, 64], BF), "blo": ("sbuf", [128, NL, 2, 64], BF), "bout": ("sbuf", [128, 2, 64], F32),
+    "bs": ("sbuf", [128, NL + 1, 2, 64], BF), "bout": ("sbuf", [128, 2, 64], F32),
     "i2": ("sbuf", [128, 2, 33], F32), "up": ("sbuf", [128, 2, 33], F16), "ee": ("sbuf", [128, 2, 33], F16),
-    "wideb": ("sbuf", [128, 64, 16], BF), "sp": ("sbuf", [128, 4, 2, 64], BF),
     "near": ("sbuf", [128, NL * 2, 768], BF), "away": ("sbuf", [128, NL * 2, 512], BF), "came": ("sbuf", [128, NL * 2, 2, 256], BF),
-    "pu": ("sbuf", [128, 4, 256], F32), "yy": ("sbuf", [128, 4, 256], F32), "sg": ("sbuf", [128, 4, 256], F32),
-    "sc": ("sbuf", [128, 4, 64], F32), "sn": ("sbuf", [128, 4, 64], F32),
-    "pA": ("psum", [128, 8, 64], F32), "pB": ("psum", [128, 8, 64], F32), "pW": ("psum", [128, 8, 64], F32),
-    "pF": ("psum", [128, 8, 64], F32), "pD": ("psum", [128, 8, 64], F32), "pM": ("psum", [128, 8, 64], F32),
-    "pE": ("psum", [128, 8, 64], F32), "pQ": ("psum", [128, 8, 64], F32),
+    "pu": ("sbuf", [128, 4, 256], F32), "yy": ("sbuf", [128, 4, 256], F32),
+    "sn": ("sbuf", [128, 2, 32], F32), "sq": ("sbuf", [128, 2, 128], BF), "sp": ("sbuf", [128, 2, 64], BF),
+    "pA": ("psum", [128, 512], F32), "pB": ("psum", [128, 512], F32), "pF": ("psum", [128, 8, 64], F32),
+    "pX": ("psum", [128, 512], F32), "pM": ("psum", [128, 512], F32), "pE": ("psum", [128, 512], F32),
+    "pG": ("psum", [128, 512], F32), "pQ": ("psum", [128, 1024], BF),
 }
-SEMAPHORES = (["cv", "cs", "ct", "cg", "sent", "lq", "lnm", "lke", "lb", "lx", "lm", "lu", "lv", "aqm", "aqr", "oyx", "oyb"]
+SEMAPHORES = (["cv", "cs", "ct", "cg", "sent", "lq", "lnm", "lke", "lb", "lx", "lm", "lu", "lv", "aqm", "aqa", "aqb", "oyx", "oyb"]
               + ["aw%d" % l for l in range(2)] + ["bias%d" % l for l in range(2)]
-              + ["a%d%s%s" % (l, k, h) for l in range(NL) for k in "uv" for h in "rm"])
+              + ["a%d%s%s" % (l, k, h) for l in range(NL) for k in "uv" for h in "abm"])
 ROUND64 = 1.5 * 2.0 ** 13
 ROUND2048 = 1.5 * 2.0 ** 18
 ROUND4096 = 1.5 * 2.0 ** 35
 EDGE = math.log(4095.0)
 
-KEYS = ["", "r,fWfF l,qqqq", "r,fWfF l,qqqq"]
-PLAN = [
-    "judge,l,pA count,0,l,pA,pW judge,r,pB tell far,u,v count,1,r,pB,pA biases names far,v,v,b1 pair,vs expert,o,n,pE,0 expert,r,c,pE,0 expert,m,n,pE,0",
-    "judge,r,pA far,u,s far,v,s count,0,r,pA,pW judge,l,pB tell count,1,l,pB,pA biases names pair,vv expert,r,c,pE,0 expert,l,n,pE,0",
-    "judge,r,pA far,u,s far,v,s count,0,r,pA,pW judge,l,pB pair,vs count,1,l,pB,pA biases expert,r,c,pE,0 expert,o,n,pB,0 expert,m,n,pQ,0",
-]
-ORDER = {
-    "v": ["fill k0m k2m k1m k3m f0o f2o f1o f3o x2m x1m x3m x2r x1r wl*3 x3r wl oh0*4 wr*6 oh0*2 wr*1 oh0 wr Ur oh1 Vr Ul post off dn puo smo yyo pur",
-          "f0r f1r x2r x3r -smr x0l wr*3 x2l wr*4 x1l wr x3l oh0*6 wl*6 oh0*1 wl*1 oh0 wl Ul Vl -yyr oh1 -pum post*3 -smm post -yym off dn pur",
-          "f0r f1r x2r x3r -smr x0l wr*3 x2l wr*4 x1l wr x3l oh0*6 wl*6 oh0*1 wl*1 oh0 wl Ul -pul -yyr oh1 -sml -yyl post pur puo smr smo pum yyo smm yyr yym"],
-    "s": ["fill k0r k2r k1r k3r prep blo sll slr dv0 th0 dv1 th1 Vl hb nl sgo",
-          "k2r k3r k0l k2l slr -sgr k1l k3l sll Ur Vr dv0 th0 dv1 th1 blo -sgm hb nl -new",
-          "k2r k3r k0l k2l slr -sgr k1l k3l sll Ur Vr dv0 th0 Vl dv1 -sgl th1 blo -new sgr sgo sgm new"],
-    "t": ["h2m h1m h3m h2r h1r h3r prep s0l s1l s0r s1r hi0 lo0 ng0 q hi1 lo1 ng1 sum0 mixx nB Tb sum1 Tu Te nA nBr nAr nb Do",
-          "-mixo h2r h3r -Dr s0r s1r -Er hi0 s0l lo0 ng0 s1l sum0 hi1 lo1 ng1 nB -mixr -Dm Tb sum1 Tu Te nA nBr nAr nb -mixm",
-          "-mixx h2r h3r -Dr s0r s1r -Er hi0 s0l lo0 ng0 s1l sum0 hi1 lo1 ng1 -Dl -mixr Tb sum1 Tu Te -mixl mixx Dr Do Er Dm mixo mixr mixm"],
-    "g": ["fill q late tell Ur Vr pair", "Ur Vr tell pair", "Ur Vr pair"],
-    "y": ["load bias", "bias", "bias"],
+KEYS = ["r,qqqq l,ffff", "r,fqfq l,fqfq", "r,fqfq l,fqfq"]
+EARLY, MEET = "r,svsv m,ssss", "m,qqqq a,qqqq b,dddd"
+QS = "a b.m"
+TURNED, COPIES, FORMS = "sss", ["vv", "vv", "vv"], ["nn", "nn", "ww"]
+PICKS = ["ur,s vr,s ul,v vl,s", "ur,s vr,s ul,v vl,s", "ur,s vr,s um,v uo,v vm,s vo,s"]
+GIVES = ["ua.ub.um va.vb.vm+", "ua.ub.um va.vb.vm+", "ua ub um.vm va vb"]
+ADDS = ["", "", "p"]
+ROUGH = dict(cycle=0.9e-3, tensor=0.46e-3, v=0.03, s=0.05, gather=1.5, hop=0.2, local=1.6, issue=0.35, flight=1.1, first=2.2, port=1.0, wake=0.35)
+BOOST, PASSES, PLANNED = {}, 1, [0.0]
+KINDS = {
+    "S": "load qa qb qm fill",
+    "R": "dn k0r k1r k2r k3r f0r f1r f2r f3r h1r h2r h3r x0r x1r x2r x3r x1a x2a x3a x1b x2b x3b s0r s2r w1r w2r w3r w5r",
+    "L": "k0m k1m k2m k3m f0o f1o f2o f3o h1m h2m h3m x1m x2m x3m k0l k1l k2l k3l f0l f1l f2l f3l x0l x1l x2l x3l s0l s2l w1l w2l w3l w5l",
+    "C": "hi0 dv0 ng0 oh0 th0 sum0", "D": "hi1 dv1 ng1 oh1 th1 sum1 blo Tb post Tu Te bias",
+    "N": "w4l w4r tell nA nB hb nn off q1l q2l q3l q1r q2r q3r",
+    "U": "Ur Ua Ub ua ub ua.ub", "V": "Vr Va Vb va vb va.vb", "M": "Ul Um Uo Vl Vm Vo um vm um.vm um.vm.va.vb+ um.vm+ va.vb+",
+    "X": "late less x prep mixx pur Dr sgr smr sdr Er yyr adr mixr", "Y": "pul Dl sgl sml sdl El yyl adl mixl new newp",
 }
-PLAN = [
-    "judge,l,pA,pB judge,r,pB,pF count,0,l,pA,pW tell far,u,v count,1,r,pB,pA biases names heard far,v,s,b1 windows,b1 home,o,vs home,m,ss expert,o,n,pE,0 expert,r,h,pE,0 expert,m,n,pE,4",
-    "judge,r,pA,pB judge,l,pB,pF far,u,s count,0,r,pA,pW tell count,1,l,pB,pA biases names heard far,v,s,b2 home,o,vs home,m,ss expert,o,n,pE,0 expert,r,h,pE,0 expert,m,n,pE,4",
-    "judge,r,pA,pB judge,l,pB,pF far,u,s far,v,s count,0,r,pA,pW heard count,1,l,pB,pA biases expert,r,n,pE,0 expert,o,f,pB,0 expert,m,f,pQ,0",
-]
-ORDER = {
-    "v": ["fill k1m f2o k3m k0m f3o k2m f0o f1o x2m x1m x3m wl*4 x2r x3r x1r wl*4 wr Ur oh1*1 wl oh0*1 oh1*1 oh0 oh1 Uo post wm puo off smo dn yyo",
-          "f0r f1r x3r x2r -pur wr x2l x0l x3l x1l -smr oh0*2 -sdr wl*8 -yyr oh0*5 -pum oh0 oh1 wl Uo -smm post*3 -yym post wm pur off",
-          "f0r f1r x3r x2r -puo -dn -smr x0l wr*6 -sdr wr -smo x2l -yyo -pum x1l x3l -yyr oh0*2 wl*7 oh0*1 -smm wl*1 -yym wl oh0*2 oh1*5 oh0 oh1*1 pur oh1 puo pum smr smo yyo yyr smm yym post"],
-    "s": ["fill k2r k1r blo prep*2 k0r k3r sll slr prep*1 dv0 th0*4 dv1 th0 th1 Vr Vo",
-          "blo -hb -prep -sgo -nl k3r k2r k0l k2l slr k1l k3l Ur -sgr dv0 sll -shr -Um th0*6 dv1 th0 th1 -sgm -Vm Vr Vo -new -newp hb Um",
-          "k3r k2r -sgr -nl k0l k2l slr -shr -sgo k1l Ur k3l dv0 sll Vr -Vm -sgm blo*1 th0*5 dv1 th0*1 -new th0*1 -newp -news th1*1 th0 th1*4 sgr sgo th1 sgm blo new"],
-    "t": ["h1m h2m prep h3m h2r s0l s1l h3r h1r s0r s1r hi0 lo0 ng0 hi1 Tb lo1 nB ng1 sum0 sum1 nA Tu Te nBr nAr Do nb",
-          "h3r -q h2r s1r s0r -mixo -Dr*1 hi0 -Dr lo0 -mixx s0l s1l ng0 -Er hi1 lo1 ng1 -mixr*1 -Dm -mixr sum0 sum1 Tb nA Tu Te -mixm nB nBr nAr nb Dr mixx",
-          "h3r h2r s1r s0r -Do lo0 hi0 s0l -Er -mixo ng0 s1l -Dm -mixr hi1 -mixm Tb lo1 ng1 mixx Dr Do Dm sum0 sum1 mixo mixr mixm Tu Te"],
-    "g": ["fill q late tell Ur win Vr", "Ur tell Vr", "Ur Vr tell"],
-    "y": ["load bias", "bias", "bias"],
-}
-PLAN = [
-    "judge,l,pA,pB judge,r,pB,pF count,0,l,pA,pW tell count,1,r,pB,pA biases names pick,u,r,v pick,v,r,s pick,u,l,v pick,v,l,s give,u,r give,uv,m,kw1 give,v,r,kw1 expert,o,n,pE,0 expert,r,h,pE,0 expert,m,n,pE,4",
-    "judge,r,pA,pB judge,l,pB,pF count,0,r,pA,pW tell count,1,l,pB,pA biases names pick,u,r,s pick,v,r,s pick,u,l,v pick,v,l,s give,u,r give,uv,m,kw2 give,v,r,kw2 expert,o,n,pE,0 expert,r,h,pE,0 expert,m,n,pE,4",
-    "judge,r,pA,pB judge,l,pB,pF count,0,r,pA,pW count,1,l,pB,pA biases pick,u,r,s pick,v,r,s pick,u,m,v pick,v,m,s give,u,r give,v,r give,u,m give,v,m expert,r,n,pE,0 expert,o,f,pB,0 expert,m,n,pQ,0",
-]
-ORDER = {
-    "v": ["fill k2m k0m k1m f1o k3m f0o f2o f3o x2m x1m x3m x2r x1r x3r wl*8 wr Ur oh0 oh1 wl Ul post puo off pur dn",
-          "f0r f1r x3r x2r x0l x2l wr*7 -smr wr*1 x3l x1l -smo -sdr -yyo wl*8 wr -pum -yyr oh1*3 oh0 -smm oh1*2 -yym wl oh1 Ul post puo pur off dn",
-          "f1r f0r x2r -smr x3r x0l x2l wr*8 -smo wr -yyo x1l -sdr x3l -pum -yyr oh0*2 wl*7 -smm wl*1 -yym wl Um oh0 oh1*4 pur puo oh1 pum smr yyr smo post*2 yyo smm post*1 yym post"],
-    "s": ["fill k0r k1r k2r k3r sll slr dv0 blo th0*3 dv1 th0 th1 prep*1 Vr prep*2 hb Vl nl",
-          "blo k3r k2r k0l k2l -sgr slr k3l k1l -sgo dv0 -shr -prep sll th0 dv1 Ur th1*1 -sgm th1 Vr Vl -new -newp hb nl",
-          "k2r k3r -sgr k0l k2l slr -sgo k1l -shr k3l Ur blo*1 sll dv0 Vr th0*3 -sgm th0 dv1 -new th1*1 -newp -news Vm th1*4 sgr th1 sgo sgm blo new"],
-    "t": ["h1r h1m h2m h3m h2r s0l h3r s1l s0r s1r hi0 lo0 ng0 hi1 lo1 q ng1 nA prep nB sum0 sum1 Tb Tu Te nBr nAr nb Do mixx Dr",
-          "h3r h2r s1r s0r s0l hi0 lo0 ng0 s1l -Er hi1 Tb lo1 ng1 -Dm -mixr sum0 nB sum1 -mixm Tu Te -mixo nBr nA nAr nb Dr Do",
-          "h2r h3r -mixx s0r s1r s0l hi0 lo0 -mixo -Er ng0 s1l -Dm -mixr hi1 -mixm lo1 ng1 mixx sum0 Dr Tb Do Dm sum1 mixr Tu mixo Te mixm"],
-    "g": ["fill q late tell Ur Vr UVm", "tell Ur UVm Vr", "Ur Vr Um Vm"],
-    "y": ["load bias", "bias", "bias"],
-}
-NEW, DN = True, "t"
-KEYS = ["", "r,fffq l,qqqq", "r,fffq l,qqqq"]
-PLAN = [
-    "judge,l,pA,pB judge,r,pB,pF count,0,l,pA,pW tell count,1,r,pB,pA biases names pick,u,r,v pick,v,r,v pick,u,l,v pick,v,l,s give,u,r give,uv,m give,v,r,kw1 expert,o,x,pE,0 expert,r,j,pE,0 expert,m,n,pE,4",
-    "judge,r,pA,pB judge,l,pB,pF count,0,r,pA,pW tell count,1,l,pB,pA biases names pick,u,r,s pick,v,r,s pick,u,l,v pick,v,l,s give,u,r give,v,r give,uv,m,kw2 expert,o,x,pE,0 expert,r,j,pE,0 expert,m,n,pE,4",
-    "judge,r,pA,pB judge,l,pB,pF count,0,r,pA,pW count,1,l,pB,pA biases pick,u,r,s pick,v,r,s pick,u,m,v pick,v,m,s give,u,r give,v,r give,u,m give,v,m expert,r,x,pE,0 expert,o,f,pB,0 expert,m,n,pQ,0",
-]
-ORDER = {
-    "v": ["fill k2m k0m k3m f3o k1m f2o f0o f1o x2m x3m x1m x2r x1r x3r wl*8 wr*8 oh0*6 wr oh0 Ur wl oh1 Vr post Ul nn off puo",
-          "f0r f2r x3r f1r x2l x0l x3l x1l wr*8 -smo wl*7 oh0*1 wl*1 -yyo oh0*2 wl -ado -pur oh0 oh1 Ul wr -pum -smr post*3 -yyr*1 post -yyr -adr nn off -smm",
-          "f0r --yym f2r x3r f1r -puo -pur wr*8 -smo -yyo -ado wr x3l -pum x0l x2l -smr -yyr -adr x1l oh0*6 -smm wl*2 -yym wl Um pur*1 oh0*1 oh1*1 pur puo oh0 oh1 pum smr yyr smo adr post*2 yyo smm post*1 yym post"],
-    "s": ["fill k0r k1r k3r k2r blo sll slr dv0 th0*5 dv1 th0 th1 Vl x hb",
-          "k3r k3l k2l k0l k1l slr sll -prep -sgo blo -less dv0 th0*4 dv1 th1*3 th0 th1 -sgr Vr Ur hb -sgm",
-          "k3r k0l --new --newp -Vl slr k2l -sgo k3l Ur dv0 -sgr k1l th0*7 blo*1 sll -sgm th0 Vr -new -newp dv1 -news th1*4 Vm blo sgr th1 sgo sgm new"],
-    "t": ["h2m h3m h1r h1m h3r h2r s0l s1l s0r s1r hi0 lo0 ng0 hi1 lo1 ng1 q sum0 Tb sum1 nA Tu Te nAr less qr dn Do",
-          "s0r s1r s0l s1l hi0 lo0 ng0 hi1 lo1 ng1 -Dr sum0 sum1 Tb Tu Te nA nAr -Dm dn -mixr -mixo -mixm",
-          "s0r s1r -Do lo0 hi0 -Dr -mixo s0l ng0 -Dm s1l -mixr -mixm Tb hi1 lo1 ng1 Dr Do sum0 sum1 Dm mixr Tu mixo Te mixm"],
-    "g": ["fill q late tell Ur UVm Vr", "tell Ur Vr UVm", "Ur Vr Um Vm"],
-    "y": ["load bias", "bias", "bias"],
-}
-ORDER = {
-    "v": ["fill k0m k2m k3m k1m f3o f1o f0o x3m x1m f2o x2m x2r x1r x3r wl*8 wr*8 oh0*7 wr oh0 Ur oh1*2 wl oh1 Vr post Ul puo nn off",
-          "f2r f0r x3r x2l x0l f1r x1l x3l wr*8 wl*7 -smo wl*1 oh0*1 -yyo -ado -pur oh0 wr oh1 wl -pum -smr post -yyr -adr Ul nn -smm off -yym",
-          "f2r f0r f1r x3r -puo -pur wr*7 -smo wr*1 -yyo -ado wr -pum x3l x2l x0l -smr -yyr -adr x1l oh0*6 -smm wl*2 -yym wl Um pur oh1*3 puo oh1 oh0 smr pum yyr adr*1 smo adr yyo smm yym post"],
-    "s": ["fill k3r k0r k1r k2r sll slr dv0 th0*6 dv1 th0 th1 x prep blo Vl hb",
-          "k3r k2l k0l k1l k3l slr sll -sgo blo dv0 th0*5 dv1 th1*3 th0 th1 -sgr Vr Ur Vl hb -sgm -less",
-          "k1l k3r --new --newp slr k0l k2l -sgo k3l dv0 Ur -sgr blo*1 th0*3 sll Vr -sgm th0*4 -new -newp dv1 -news Vm th0 sgr th1 sgo sgm blo new"],
-    "t": ["h2m h3m h3r h1m h1r h2r s1l s0l s0r s1r hi0 lo0 ng0 hi1 lo1 ng1 qr Tb sum0 sum1 Tu Te nA nAr Do dn q",
-          "s0r s0l s1r s1l hi0 lo0 ng0 hi1 lo1 ng1 -Dr sum0 sum1 Tb Tu Te -less nA nAr -Dm dn -mixr -mixm -mixo",
-          "s0r s1r -Do hi0 -Dr lo0 ng0 -mixo s0l -Dm s1l -mixr -mixm lo1 hi1 Dr ng1 Do Tb sum0 Dm sum1 mixr mixo mixm Tu Te"],
-    "g": ["fill late q tell Ur UVm Vr", "tell Ur Vr UVm", "Ur Vr Um Vm"],
-    "y": ["load bias", "bias", "bias"],
-}
-PLAN = [
-    "judge,l,pA,pB judge,r,pB,pF count,0,l,pA,pW tell count,1,r,pB,pA biases names pick,u,r,v pick,v,r,v pick,u,l,s pick,v,l,s give,u,r give,uv,m,kw1 give,v,r,kw1 expert,o,n,pE,0 expert,r,n,pE,0 expert,m,n,pE,4",
-    "judge,r,pA,pB judge,l,pB,pF count,0,r,pA,pW tell count,1,l,pB,pA biases names pick,u,r,s pick,v,r,s pick,u,l,s pick,v,l,s give,u,r give,uv,m,kw2 give,v,r,kw2 expert,o,n,pE,0 expert,r,n,pE,0 expert,m,n,pE,4",
-    "judge,r,pA,pB judge,l,pB,pF count,0,r,pA,pW count,1,l,pB,pA biases pick,u,r,s pick,v,r,s pick,u,m,v pick,v,m,s give,u,r give,v,r give,u,m give,v,m expert,r,n,pE,0 expert,o,f,pB,0 expert,m,n,pQ,0",
-]
-ORDER = {
-    "v": ["fill k2m k1m k0m k3m f2o f0o f1o f3o x2m x3m x1m x1r x2r x3r wl*7 wr*1 wl*1 wr wl oh0*1 Ur oh1*1 oh0 oh1 Vr post puo nn pur*1 off pur",
-          "f2r f0r x2l f1r x3r x0l x3l -smo x1l wr*2 -yyo wr*5 wl*1 wr*1 wl*5 -pum wl -smr -yyr oh1*3 oh0 oh1*4 -smm oh1 wr -yym post puo nn off",
-          "f0r f2r x3r f1r -smo -pur*1 -yyo -pum wr*2 -pur wr*4 x0l wr*1 x2l wr*1 x1l wr x3l -smr -yyr wl*8 -smm wl -yym Um pur oh0*2 oh1*1 oh0*4 puo oh1*5 oh0*1 pum oh1*1 oh0 oh1 smr yyr smm smo yym yyo post"],
-    "s": ["fill k0r k1r k3r k2r sll slr blo dv0 th0*3 dv1 th0 th1 x Ul less hb prep*1 Vl prep",
-          "k2l k3r k0l k3l -sgo k1l blo slr sll -sgr dv0 th0*4 dv1 th0 th1*4 -sgm th1 Ul Vl -new Ur -newp hb",
-          "blo*1 -Vr k3r k2l -sgo k0l slr k1l blo k3l -sgr Ur sll dv0 -sgm Vr th0*5 -new -newp dv1 -news Vm th0*2 th1*4 sgr th1*1 th0 th1 sgm sgo new"],
-    "t": ["h2m h3m h1m h3r h1r h2r s0l s1l s0r s1r hi0 lo0 ng0 hi1 lo1 q ng1 qr less sum0 Tb sum1 nA nAr Tu Te Do",
-          "s0r -mixx s1r -dn s0l s1l -Dr hi0 -mixo lo0 ng0 hi1 lo1 ng1 -Dm -mixr Tb sum0 sum1 -mixm Tu Te nA nAr Do",
-          "s0r s1r -dn -Dr -mixx s0l lo0 -mixo s1l hi0 -Dm ng0 -mixr -mixm lo1 hi1 ng1 Dr Tb mixx Do Dm sum0 sum1 mixr mixm mixo Tu Te"],
-    "g": ["fill q late tell Ur UVm Vr", "tell Ur UVm Vr", "Ur Vr Um Vm"],
-    "y": ["load bias", "bias", "bias"],
-}
-CYCLE = {"v": 0.85e-3, "s": 0.85e-3, "t": 0.42e-3, "g": 1.7e-3}
-CALL = {"v": 0.015, "s": 0.03, "t": 0.0, "g": 0.17}
-GATHER, HOP, LOCAL, ISSUE = 1.4, 0.24, 1.6, 0.3
-FLIGHT, FIRST, PORT, WAKE = 1.0, 2.2, 1.0, 0.4
+ORDER = """
+y0load*1 v0fill*1 g0late*1 y0load*1 v0fill*1 y0load*1 v0fill*1 g0fill*1 v0fill*2 g0fill*1 v0fill*5 g0fill v0fill*2 g0qa v0fill*1 s0fill*1 v0fill*3 g0qb v0fill*1 g0qm v0fill t0dn v0k1m s0k1r v0k0m s0k0r v0k2m t0h1m v0f0o t0h2m s0k3r v0k3m t0h1r v0f3o t0h3m s0k2r v0f1o t0h3r v0f2o y0load*1 g0late*1 t0q1l s0fill y0load*3 v0x1m t0h2r y0load v0x3m v0x2m t0s0l v0x3a v0q2l t0s2l v0x1a t0q1r v0x1b t0q3l v0x3b s0x g0late t0s0r v0w1l s0prep*1 v0x2a s0prep v0x2b v0w2l t0s2r v0w3l v0q2r t0hi0 v0w5l v0w1r t0less v0w4l s0dv0 v0w2r s0less v0w3r t0ng0 v0oh0*1 t0q3r v0oh0*2 s0th0*1 v0oh0*1 t0hi1 v0w4r s0th0*1 v0oh0*2 s0th0*1 v0oh0*1 g0tell t0mixx v0w5r s0th0*1 v0oh0 v0Ul s0th0*1 s0dv1 s0th0*2 t0ng1 t0Tb s0th0 v0oh1*2 s0Ur v0oh1*2 t0sum0 v0oh1 v0pul*1 t0nA s0th1*2 g0ua.ub.um s0th1 s0Vr t0sum1 t0nB v0post*3 t0Tu s0hb t0Te s0Vl v0post v0pul y0bias v0nn v0off t1dn v0pur t0Dr g0va.vb.vm+ s1k3r v1f1r t0Dl*1 v1f0r s1k3l t0Dl v1x3r s0sgr t1s0r s0sgl v1f2r s1k1l v0sml*1 s1k0l v0sml v0smr*1 t1s2r v0smr v1x3l v0sdl v0sdr s1k2l v1x1l t0Er v1w1r v1x0l t0El v1w2r t1s0l v1w3r v1x2l t1hi0 v0yyl t1s2l s1dv0 v1w5r v1w4r v0yyr s1Ur t0mixl*1 v1w1l t1ng0 v1oh0*2 t0mixl v1w2l s1th0*1 v1oh0*2 s1th0*1 v1w3l s1th0*1 t0mixr*1 v1oh0*2 s1th0*1 v1w4l v1w5l s1th0*1 v1oh0 g1tell s1th0*1 t1hi1 v1Ul s1th0*1 t0mixr s1dv1 s1th0 t1ng1 v1oh1*2 g1ua.ub.um v1oh1*1 t1nA s0new v1oh1*3 s1th1*1 v1oh1 s1th1*1 t1mixx s1th1*3 t1sum0 s1th1 s0newp t1sum1 s1Vl v1pul*1 t1Tb t1nB v1post*3 t1Tu v1pul s1hb t1Te v1post s1Vr v1nn y1bias s2blo v1pur*1 v1off v1pur t1Dr g1va.vb.vm+ v2f1r s2k1l t2dn v2f0r s1sgr s2k3r t1Dl*1 v2f2r t1Dl s2k2l t2s0r v2x3r s1sgl s2k0l v2x1l t2s2r v2x2l v1sml v1smr*1 s2k3l v1smr v1sdl v2w1r v1sdr t1El v2x0l t1Er v2w2r v2x3l t2s0l v2w3r t2s2l v2w5r v1yyl s2Ur t2hi0 v2w1l t1mixl*1 v2w2l s2dv0 s2Vr g2ua v2w3l t2ng0 v1yyr t1mixl g2ub v2w5l s2th0*1 v2oh0*1 t2hi1 v2oh0*1 s2th0*1 g2va v2Um s2th0*1 t1mixr*1 s2Vm g2vb v2oh0*4 t1mixr s2dv1 v2oh0 s2th0*1 g2um.vm s2th0*1 v2oh1*2 t2ng1 s2th0*1 v2oh1*2 s2th0*1 v2oh1*2 s2th0 v2oh1 s1new v2Uo t2sum0 s2th1*3 t2mixx s2th1 s1newp t2Tb t2sum1 s2Vo v2pur t2Dr*1 v2pul*1 t2Dr v2pul t2Dl s2sgr s2sgl v2smr v2sml v2sdr v2post*2 v2sdl t2Er v2post*1 t2Tu t2El v2yyr*1 t2Te v2yyr v2yyl v2adr v2post v2adl t2mixr y2bias t2mixl s2new
+"""
+
+
+ORDER = """
+y0load*1 v0fill*1 g0late*1 y0load*2 v0fill*2 g0fill*1 v0fill*5 g0fill*1 v0fill*3 g0fill v0fill*3 g0qa s0fill*1 v0fill*2 g0qb v0fill*2 g0qm v0fill t0dn s0k0r v0k0m v0k1m s0fill v0k2m s0k3r t0h1m v0f1o t0h2m v0k3m s0k1r t0h3r v0f3o t0h3m s0k2r v0f2o t0h1r v0f0o y0load*1 g0late*1 t0q1l y0load*3 v0x1m y0load t0h2r v0x2m v0x3m t0s0l v0x3a v0q2l t0s2l v0x1a v0x2a t0q3l v0x1b t0q1r s0x g0late v0w1l s0prep*1 v0x2b t0s0r s0prep v0x3b v0w2l t0s2r v0w3l v0q2r t0hi0 v0w4l v0w5l v0w1r t0less t0q3r s0dv0 v0w2r s0less v0w3r t0ng0 v0oh0*1 t0mixx v0oh0*2 s0th0*1 v0oh0*1 v0w4r s0th0*1 v0oh0*2 s0th0*1 t0hi1 v0w5r g0tell v0oh0*1 s0th0*1 v0oh0 v0Ul s0th0*2 s0dv1 s0th0 t0ng1 v0oh1*1 t0Tb v0oh1*1 s0Ur v0oh1*2 t0nA v0oh1 v0pul*1 t0sum0 s0th1*2 g0ua.ub.um s0th1 s0Vr t0sum1 t0nB v0post*3 t0Tu s0hb t0Te s0Vl v0post v0pul y0bias v0nn v0off t1dn v0pur t0Dr g0va.vb.vm+ s1k3r v1f0r t0Dl*1 v1f1r s1k1l t0Dl v1x3r s0sgr t1s0r s0sgl v1f2r s1k3l v0sml*1 s1k0l v0smr t1s2r v0sml v1x1l v0sdr v0sdl s1k2l v1x3l v1x0l t0El v1w1r t0Er t1s0l v1w2r v1w3r v1x2l t1hi0 v1w5r v0yyl t1s2l s1dv0 s1Ur v1w4r t1ng0 t0mixl*1 v1w1l v0yyr s1th0*1 t0mixl s1th0*1 v1w2l s1th0*1 v1oh0*2 s1th0*1 v1w3l t0mixr*1 s1th0*1 v1oh0*2 s1th0*1 v1w4l v1oh0*1 s1th0*1 v1w5l t1hi1 v1oh0*1 g1tell s1th0 v1oh0 v1Ul t0mixr s1dv1 t1ng1 t1nA s0new v1oh1*3 g1ua.ub.um v1oh1*1 s1th1*1 t1sum0 v1oh1*2 s1th1*1 v1oh1 s1th1*2 t1mixx s1th1 s0newp t1sum1 s1Vl v1pul*1 t1Tb t1nB v1post*3 t1Tu s1hb t1Te v1post s1Vr v1pul y1bias v1nn s2blo v1off t2dn v1pur t1Dr s2k3r g1va.vb.vm+ v2f1r t1Dl*1 v2f0r s2k2l t1Dl v2x3r s2k1l t2s0r v2f2r s1sgl s1sgr s2k0l v2x2l t2s2r v1smr v1sml v2x1l s2k3l v1sdr v2x0l t1Er v2w1r t2s0l v1sdl v2w2r v2x3l t1El v2w3r t2s2l v2w5r v1yyl s2Ur t2hi0 v2w1l t1mixl*1 v2w2l s2dv0 s2Vr v2w3l g2ua t1mixl v2oh0*2 v2w5l g2ub v1yyr t2ng0 t2hi1 s2Vm v2Um g2va t1mixr*1 s2th0*1 v2oh0*1 s2dv1 v2oh0*2 g2um.vm s2th0*1 v2oh0*1 t1mixr v2oh0*1 s2th0*1 v2oh0 v2oh1*1 s2th0*1 g2vb v2oh1*3 t2ng1 v2oh1*2 t2Tb s1new v2oh1 v2Uo s2th0*1 s1newp t2mixx s2th0*2 v2pur*1 s2th0 v2pul*1 s2th1*2 t2Dr*1 s2th1*3 v2pur s2th1 t2Dr s2Vo t2Dl*1 v2pul t2Dl t2sum0 s2sgl s2sgr t2sum1 v2smr v2sml v2sdr v2sdl t2Er v2post*2 t2El v2post*1 v2yyr*1 t2Tu t2Te v2yyr v2yyl v2adr v2post v2adl t2mixr y2bias t2mixl s2new
+"""
+
+
+ORDER = """
+y0load*1 v0fill*1 g0ramp y0load*1 v0fill*1 y0load*1 v0fill*1 g0fill*1 v0fill*3 v0ramp g0late*1 v0fill*3 g0fill*1 v0fill*4 s0fill*1 v0fill*1 g0fill g0qa v0fill*2 g0qb v0fill*2 g0qm v0fill*1 s0fill v0fill t0dn v0k1m s0k0r v0k0m s0k3r v0k3m t0h1m v0k2m t0h3m s0k1r v0f1o t0h3r v0f3o t0h2m s0k2r v0f2o t0h1r v0f0o y0load*1 g0late*1 t0q1l y0load*3 v0x2m t0h2r y0load v0x3m v0x1m t0s0l v0q2l v0x1a t0s1l v0x2a v0x3a t0q1r v0x2b s0x t0q3l g0late v0w1l s0prep*1 v0x3b t0s0r s0prep v0x1b v0w2l t0less t0s1r s0less v0w3l v0q2r t0hi0 v0w4l v0w5l v0w1r t0q3r s0dv0 v0w2r v0oh0*1 t0ng0 v0oh0*1 t0mixx v0w3r v0oh0*1 s0th0*1 v0oh0*2 s0th0*1 v0w4r v0w5r s0th0*1 t0hi1 v0oh0*2 s0th0*1 g0tell v0oh0 v0Ul s0th0*2 s0dv1 s0Ur t0ng1 v0oh1*1 t0Tb v0oh1*6 s0th0*1 v0oh1 v0pul*1 s0th0 g0ua.ub.um s0th1*2 t0nA s0th1*2 t0sum0 s0th1 s0Vr t0sum1 t0nB v0post*3 t0Tu s0hb t0Te s0Vl v0post v0nn y0bias v0pul v0off v0pur t0Dr g0va.vb.vm+ s1k3r v1f2r t0Dl v1f0r s1k1l t1dn v1x3r s0sgl s0sgr t1s0r s1k3l v1f1r s1k0l v0smr v0sml*1 t1s1r v0sml v1x1l v0sdr v0sdl s1k2l v1x3l t0Er v1w1r t0El v1x0l v1x2l v1w2r t1s0l v1w3r v1w5r t1s1l v1w4r v0yyl s1Ur t1hi0 v1w1l t0mixl*1 s1dv0 v1w2l v0yyr t1ng0 t0mixl s1th0*1 v1w3l s1th0*1 v1oh0*2 s1th0*1 v1w4l t1hi1 v1oh0*1 s1th0*1 v1w5l v1oh0*1 g1tell s1th0*1 t0mixr*1 v1oh0*2 s1th0*1 v1oh0 s1dv1 v1Ul s1th0*1 t0mixr s1th0 t1ng1 v1oh1*1 t1nA v1oh1*1 s0new v1oh1*1 g1ua.ub.um v1oh1*2 s1th1*1 v1oh1*1 t1sum0 v1oh1*1 s1th1*1 v1oh1 s1th1*2 t1mixx s1th1 s0newp t1sum1 s1Vl v1pul*1 t1Tb t1nB v1post*3 t1Tu s1hb t1Te v1post s1Vr v1pul y1bias v1nn s2blo v1off t2dn v1pur t1Dr s2k3r g1va.vb.vm+ v2f2r t1Dl v2f0r s2k2l v2x3r s2k1l t2s0r v2f1r s1sgl s1sgr s2k0l v2x2l t2s1r v1smr v1sml v2x1l s2k3l v1sdr v2x0l t1Er v2w1r v1sdl t2s0l v2w2r v2x3l t1El v2w3r t2s1l v2w5r v1yyl s2Ur t2hi0 v2w1l t1mixl*1 v2w2l s2dv0 s2Vr g2ua v2w3l t2ng0 v2oh0*2 t1mixl g2ub v2w5l v1yyr s2th0*1 t2hi1 s2Vm g2va v2Um t1mixr*1 s2dv1 v2oh0*2 s2th0*1 v2oh0*1 g2um.vm v2oh0*1 t1mixr s2th0*1 v2oh0 s2th0*1 v2oh1*1 g2vb v2oh1*3 t2ng1 v2oh1*2 t2Tb s1new v2oh1 v2Uo s2th0*1 s1newp t2mixx s2th0*2 v2pur*1 s2th0 v2pul*1 s2th1*2 t2Dr*1 s2th1*3 v2pur s2th1 t2Dr s2Vo t2Dl*1 v2pul t2Dl t2sum0 s2sgl s2sgr t2sum1 v2smr v2sml v2sdr v2sdl t2Er v2post*2 t2El v2post*1 v2yyr*1 t2Tu t2Te v2yyr v2yyl v2adr v2post v2adl t2mixr y2bias t2mixl s2new
+"""
+
+
+ORDER = """
+y0load*1 v0fill*1 g0late*1 y0load*1 v0fill*1 y0load*1 v0fill*1 g0fill*1 v0fill*4 g0fill*1 v0fill*2 g0fill v0fill*6 g0qb s0fill*1 v0fill*2 g0qa v0fill*1 g0ramp v0fill*1 g0qm v0fill v0ramp t0dn v0k0m s0k1r v0k1m s0k0r v0k3m t0h1m v0k2m t0h3m s0k3r v0f1o t0h2m v0f0o t0h1r s0k2r v0f3o t0h3r v0f2o y0load*1 g0late*1 t0q1l s0fill y0load*3 v0x2m t0h2r y0load v0x3m v0x1m t0s0l v0x1b v0q2l t0s1l v0x2b v0x2a t0q3l v0x1a s0prep*1 t0q1r g0late v0x3a t0s0r s0x v0w1l s0prep v0x3b v0w2l v0q2r t0less t0s1r s0less v0w3l v0w4l t0hi0 v0w5l v0w1r t0lo0 v0w2r s0dv0 v0w3r t0ng0 t0q3r v0oh0*2 s0th0*1 v0oh0*1 t0hi1 v0oh0*1 s0th0*1 v0w4r v0oh0*1 s0th0*1 v0w5r v0oh0*1 t0lo1 g0tell s0th0*1 v0oh0*1 v0Ul s0th0*1 t0mixx s0dv1 s0Ur t0ng1 t0Tb v0oh1*3 v0oh0 v0oh1*2 s0th0*1 v0oh1*2 s0th1*1 g0ua.ub.um v0oh1 v0pul*1 s0th0 s0th1*2 t0sum0 s0th1 s0Vr t0sum1 t0nA v0post*3 t0Tu v0pul t0Te t0nB v0post y0bias s0hb s0Vl v0nn v0pur*1 v0off v0pur t0Dr t0Dl*1 g0va.vb.vm+ s1k3r v1f2r t0Dl v1f0r s1k1l t1dn v1f1r s0sgl s0sgr t1s0r s1k0l v1x3r s1k2l v0sml v0smr*1 t1s1r v0smr v1x1l v0sdr v0sdl s1k3l v1x0l t0El v1x2l t0Er v1w1r t1s0l v1x3l v1w2r t1s1l v1w3r v0yyl t1hi0 v1w1l t1lo0 v1w5r s1dv0 v1w2l t0mixl*1 s1Ur v1w4r v1w3l v1oh0*2 t1ng0 v1w4l t1hi1 v1oh0*2 s1th0*1 v1oh0*1 g1tell v1w5l t0mixl s1th0*1 v1oh0*2 s1th0*1 v0yyr s1dv1 t1lo1 s1th0*2 v1Ul t1ng1 s1th0*1 t1Tb t0mixr*1 s1th0 s1th1*1 v1oh0 s1th1*1 t0mixr v1oh1*2 s1th1*1 g1ua.ub.um v1oh1*2 s1th1*1 v1oh1*2 s1th1*1 t1sum0 v1oh1 s1th1 s0new t1sum1 s1Vr t1nA v1post*2 s0newp v1post*1 t1Tu t1Te t1nB v1post v1pul*1 t1mixx y1bias s1hb v1pul s1Vl v1nn v1off s2blo v1pur t1Dr*1 g1va.vb.vm+ s2k3r v2f2r t2dn t1Dr v2f0r s2k2l t1Dl v2x3r s2k1l v2f1r t2s0r s1sgr s1sgl s2k0l v2x2l t2s1r v1smr v1sml v2x1l s2k3l v1sdr v2x0l t1Er v2w1r v1sdl t2s0l v2w2r v2x3l t1El v2w3r t2s1l v2w5r v1yyl s2Ur t2hi0 v2w1l t2lo0 v2w2l s2dv0 t1mixl*1 s2Vr g2ua v2w3l v2oh0*2 g2ub v2oh0*1 t2ng0 v2oh0*1 t1mixl v2w5l v1yyr s2th0*1 s2Vm g2va t2hi1 v2Um g2vb t2lo1 s2dv1 v2oh0*2 t1mixr*1 s2th0*1 g2um.vm s2th0*1 v2oh1*2 s2th0*1 v2oh1*2 t2ng1 v2oh1*1 t2Tb v2oh1*1 t1mixr v2oh1*1 s2th1*1 v2Uo s2th1*2 v2oh0*1 s2th1*1 v2oh0 v2oh1 s1new s2th1*1 t2mixx s1newp s2th1*2 v2pur*1 s2th1 v2pul*1 s2th0*2 t2Dr*1 v2pur s2th0 s2Vo t2Dr t2Dl*1 v2pul t2Dl t2sum0 s2sgl s2sgr t2sum1 v2smr v2sml v2sdr v2sdl t2Er v2post*2 t2El v2post*1 v2yyr*1 t2Tu t2Te v2yyr v2yyl v2adr v2post v2adl t2mixr y2bias t2mixl s2new
+"""
+
+
+KEYS = ["r,qqqq l,ffff", "r,fqfq l,fqqq", "r,fqfq l,fqqq"]
+PICKS = ["ur,v vr,s ul,v vl,s", "ur,s vr,v ul,v vl,s", "ua,s ub,s vr,s um,v uo,v vm,s vo,s"]
+GIVES = ["ua.ub.um va.vb.vm+", "ua.ub va.vb.um vm", "ua ub um va vb vm"]
+ADDS = ["", "", ""]
+ORDER = """
+y0lq v0minus g0ramp y0lnm v0keep y0lke v0bdb v0wb g0late*1 v0wide v0cbig g0wb v0ramp v0c2 v0none v0four v0zh*1 g0bdb*1 v0neg v0wh v0negh v0sel g0qa t0q1o g0bdb v0nm0 g0qb.m v0off*1 s0fold t0dn v0q2o v0zh t0q3o s0k3m v0f0o v0f1o s0k2m v0f3o s0k0m v0k1r s0k0r v0k3r s0k2r t0q1a s0k1m g0late*1 t0q1m y0lm y0lx y0lb y0lu y0lv v0q2m v0f2o t0q3m v0x0m v0x2m g0late v0q2a v0x2b t0q3a v0x0b t0s0l v0x3m s0prep*1 v0x1m v0x0a t0less v0x1a t0s1l v0x2a s0prep v0x3b s0x v0x1b t0s0r s0less v0x3a v0w1l t0s1r v0w2l v0w3l t0q1b v0w1r t0hi0 v0q2b v0w2r t0lo0 v0w5l s0dv0 v0w3r t0q3b t0ng0 v0w4 t0hi1 v0oh0*1 s0th0*1 v0w5r g0tell v0Ul t0Tb t0lo1 s0th0*1 s0dv1 s0th0*1 v0Ur t0ng1 t0mixx s0th0 s0th1*1 v0oh0*1 s0th1*1 v0oh0*1 g0ua.ub.um v0oh0 s0th1*1 v0oh1*2 t0sum0 s0th1 v0oh1 s0Vl v0pul*1 t0sum1 t0nA s0Vr v0post*3 t0Tu t0Te t0nB v0post t0Dl*1 y0bias v0pul s0hb t0Dl v0nn s0sgl t1dn v0sml v0off v0sdl v0pur*1 t0Wl v0pur s0sql t0Dr*1 g0va.vb.vm+ v1f0r s1k1r t0Dr t0El v1f2r s1k3r v1x1r s0sgr s1k2l t1s0r v1x3r v1f0l t1s1r s1k1l v1x2l v1w1r s1k3l v0smr*1 t1s0l v0smr v1w2r v0sdr v1w3r t0Wr v1x1l t1hi0 s0sqr v1w5r v1x3l s1Ur t0Er v0yyl t1s1l v0yyr s1dv0 t1lo0 g1ua.ub t1ng0 v1w1l t0mixl*1 v1oh0*1 s1th0*1 v1w2l v1oh0*1 s1th0*1 t0mixl v1w3l v1oh0*1 s1th0*1 v1w4 v1w5l t1hi1 v1Vr s1th0 g1tell t1lo1 s1dv1 v1Ul t1ng1 t0mixr*1 s1th1*2 t0mixr v1oh0 v1oh1*1 g1va.vb.um s1th1*1 v1oh1*1 t1Tb t1sum0 v1oh1*1 s0new v1oh1 s1th1 s0newp t1sum1 s1Vl v1pur t1Dr*1 v1post*2 v1pul*1 t1Dr g1vm t1nA v1post*1 s1sgr t1Tu t1Te t1nB v1pul v1post t1Dl*1 v1smr s1hb y1bias t1Dl v1sdr s2blo t1Wr v1nn s1sgl t1mixx s1sqr v1sml v1off t1Er v1sdl t1Wl t2dn s1sql v1yyr t1El s2k1r v2f0r t1mixr v2f2r s2k3r v2x1r s2k2l t2s0r v2x3r v1yyl t2s1r s2k3l v2x2l t1mixl*1 v2w1r s2k1l v2w2r t1mixl v2w3r v2w5r t2hi0 v2f0l s2Ua t2lo0 s1new v2x1l g2ua s2dv0 t2s0l v2x3l s1newp v2oh0*1 s2Ub v2oh0*1 t2s1l v2oh0 s2Vr g2ub t2ng0 t2mixx v2w1l v2w2l s2th0*1 g2va v2w3l s2th0*1 g2vb v2w5l t2hi1 v2Um s2Vm t2Tb t2lo1 s2dv1 v2pur*1 g2um s2th0*1 v2Uo t2ng1 s2th0 t2Dr*1 g2vm s2th1*2 v2pur v2oh1*2 t2Dr v2pul*1 t2sum0 v2oh1*1 s2sgr s2th1*1 v2smr t2Dl*1 s2Vo v2sdr s2th1 t2Wr v2pul s2sqr v2oh1 t2Dl t2Er s2sgl t2sum1 v2sml v2yyr*1 v2sdl v2post*2 v2yyr t2Wl t2mixr*1 s2sql v2post*1 t2El t2Tu t2Te t2mixr v2yyl*1 v2post v2yyl t2mixl*1 y2bias t2mixl s2new
+"""
+
+
+ORDER = """
+y0lq g0ramp v0wb y0lnm y0lke v0minus v0four v0keep v0none g0wb v0cbig v0bdb v0ramp v0wide v0zh*1 g0bdb*1 v0negh v0wh v0sel t0q1o g0qa g0bdb v0q2o v0nm0 g0qb.m t0q3o v0off*1 s0fold v0seln t0dn g0late*1 v0bd v0bdn v0zh v0half v0selb v0c2 v0f0o s0k1m v0f2o v0f3o s0k3m v0f1o s0k0m v0k3r s0k2m s0k2r t0q1a g0late*1 t0q1m y0lm y0lx y0lb s0k0r y0lu y0lv v0q2m v0q2a v0k1r t0q3a t0q3m g0late v0x0m t0less s0prep*1 v0x2m v0x1m v0x3m s0x v0x1a t0s0l v0x2b s0less s0prep v0x0a v0x2a t0s1l v0x0b v0x3a v0x3b t0s0r v0x1b v0w1l t0s1r v0w2l t0q1b v0w3l v0w1r v0up0 t0lo0 v0q2b v0w2r t0hi0 v0w5l v0w3r t0ng0 v0dv0 t0q3b v0w4 v0up1 s0th0*1 v0w5r v0Ul t0lo1 g0tell s0th0*1 t0ng1 s0th0*1 t0hi1 v0Ur s0th0 t0Tb t0mixx s0th1*2 v0oh0*1 v0dv1 s0th1*1 g0ua.ub.um v0oh0*2 s0th1 v0oh0 v0oh1*1 s0Vl v0oh1*1 t0sum0 v0oh1 v0pul*1 s0Vr t0sum1 t0nA v0post*2 t0nB v0post*1 v0pul t0Tu t0Te s0hb t0Dl*1 v0post t0Dl v0nn y0bias s0sgl v0off t1dn v0sml v0sdl v0pur t0Wl t0Dr*1 s1k1r g0va.vb.vm+ v1f2r t0Dr v1f0r s1k3r v1x1r s0sgr s1k2l t1s0r v1x3r v1f0l t1s1r s1k1l v1x2l s1k3l v1w1r v0smr*1 t1s0l v0smr v1w2r v1x1l s0sql v0sdr v1w3r v1x3l t0Wr t0El v1w5r v1up0 s0sqr t1s1l s1Ur v0yyl t1hi0 v1w1l t0Er g1ua.ub t1lo0 v1w2l v1dv0 t1ng0 v1w3l t0mixl*1 v0yyr s1th0*1 t1lo1 v1up1 s1th0*1 v1w5l v1w4 v1oh0*1 s1th0*1 t1ng1 v1oh0*1 g1tell v1Vr s1th0 t1hi1 s1th1*1 t0mixr*1 s1th1*1 v1dv1 v1oh0*1 t0mixr s1th1*1 v1oh0 v1oh1*1 s1th1 v1oh1*1 t0mixl v1oh1 v1Ul t1sum0 s0newp t1sum1 s1Vl v1pur*1 g1va.vb.um t1Tb t1nA s0new v1post*2 t1nB g1vm v1post*1 v1pur t1Tu v1pul*1 t1Te t1Dr*1 s1hb v1post t1Dr v1nn t1Dl*1 y1bias s2blo s1sgr t1mixx v1pul v1smr v1off t1Dl v1sdr t2dn t1Wr s1sgl s1sqr v1sml s2k1r v2f2r t1Er s2k3r v1sdl v1yyr t1Wl v2f0r s1sql t1mixr*1 s2k2l v2x1r t1El v2x3r t2s0r s2k1l v1yyl t2s1r v2f0l s2k3l t1mixr v2w1r t1mixl*1 v2x2l v2w2r t1mixl v2x1l v2w3r v2x3l t2s0l v2w5r s1newp v2up0 t2s1l s2Ua s2Ub t2hi0 g2ua v2w1l t2lo0 s2Vr g2ub t2ng0 v2w2l v2dv0 v2w3l s1new v2oh0*1 s2th0*1 g2va v2w5l t2lo1 v2up1 v2oh0*1 s2th0*1 g2vb v2Uo t2hi1 s2th0*1 s2Vm v2Um t2Tb t2ng1 t2mixx v2pul*1 s2th0 v2dv1 g2um s2Vo v2oh0*1 t2Do v2oh0 g2vm v2pur*1 v2oh1*2 t2Da v2oh1*1 v2pur s2sgo v2oh1 s2th1*1 t2Db v2smo s2th1*2 v2pul t2sum0 s2th1 v2yyo s2sgb s2sga t2Dm v2sma t2sum1 v2smb s2sgm v2yya t2mixo v2yyb v2post*1 v2smm t2mixa v2post*2 v2yym t2mixb t2Tu t2Te t2mixm v2post y2bias s2new
+"""
 
 
 def rank_program(g, core, T, topo):
@@ -159,8 +100,11 @@ def rank_program(g, core, T, topo):
     rem = [r for r in range(N) if T.cores[r] not in here]
     loc0, rem0 = min(rank, mate), min(rem)
     assert abs(rank - mate) == 1 and rem == [rem0, rem0 + 1]
+    far_a, far_b = sorted(rem, key=lambda r: topo.die(T.cores[r]) != topo.die(core))
+    assert topo.die(T.cores[far_a]) == topo.die(core) != topo.die(T.cores[far_b])
     e_off = topo.engines(core, T.cores[rem0])
     e_on = [e for e in topo.engines(core, T.cores[mate]) if e not in e_off]
+    R = ROUGH
 
     def part(es, i, n):
         k = len(es) // n
@@ -168,21 +112,30 @@ def rank_program(g, core, T, topo):
 
     calls, layer = [], [0]
 
+    def note(**c):
+        calls.append(dict(c, name=(layer[0], c["name"])))
+
     def op(q, name, fns, cycles, reads, writes, banks=()):
         fns = fns if isinstance(fns, list) else [fns]
-        busy = len(fns) * (CALL[q] + max(cycles, 32 if q == "t" else 64) * CYCLE[q])
-        calls.append(dict(kind="op", q=q, name=(layer[0], name), fns=fns, reads=reads, writes=writes, banks=banks, busy=busy, late=HOP, cycles=cycles))
+        name = writes[0].split("_")[0] if name == "fill" else name
+        if q == "t":
+            busy = len(fns) * cycles * R["tensor"]
+        elif q == "g":
+            busy = len(fns) * (0.17 + 2 * cycles * R["cycle"])
+        else:
+            busy = len(fns) * (R[q] + max(cycles, 64) * R["cycle"])
+        note(kind="op", q=q, name=name, fns=fns, reads=reads, writes=writes, banks=banks, busy=busy, late=R["hop"])
 
-    def dma(q, name, sem, pairs, reads, writes, late=LOCAL):
-        calls.append(dict(kind="dma", q=q, name=(layer[0], name), sem=sem, pairs=pairs, reads=reads, writes=writes, banks=(), busy=0.05 * len(pairs), late=late))
+    def dma(q, name, sem, pairs, reads, writes, late):
+        note(kind="dma", q=q, name=sem if name == "load" else name, sem=sem, pairs=pairs, reads=reads, writes=writes, banks=(), busy=0.05 * len(pairs), late=late)
 
-    def send(name, items, reads, lands, flight=FLIGHT):
-        calls.append(dict(kind="send", q="g", name=(layer[0], name), items=items, local="sent", reads=reads, writes=[], banks=(), busy=ISSUE, late=0.0))
+    def send(name, items, reads, lands, flight=0.0):
+        note(kind="send", q="g", name=name, items=items, reads=reads, writes=[], banks=(), busy=R["issue"], late=R["flight"] + flight)
         me = len(calls) - 1
-        for sem, writes, pieces in lands:
+        for sem, writes, pieces, far in lands:
             n = sum(bin(m).count("1") for _r, m, s, _a, _b in items if s == sem)
-            calls.append(dict(kind="land", q=None, sem=sem, n=n, reads=[], writes=writes, banks=(),
-                              busy=flight + max(pieces, 1.1) * PORT, late=WAKE if pieces else 0.3, after=me))
+            note(kind="land", q="port" if far else "chip", name=name, sem=sem, n=n, reads=[], writes=writes, banks=(),
+                 busy=pieces * R["port"], late=R["wake"], after=me)
 
     V, S, PE = g.vector, g.scalar, g.tensor
     ident, identh, shifth = T.wb[:, 0:8, :], T.wh[:, 0:8, :], T.wh[:, 7:15, :]
@@ -191,7 +144,7 @@ def rank_program(g, core, T, topo):
         return t[64 * half + 15:64 * half + 64:16, :]
 
     def span(h):
-        return {"a": (0, 4), "l": (loc0, 2), "r": (rem0, 2), "o": (rank, 1), "m": (mate, 1)}[h]
+        return {"*": (0, 4), "l": (loc0, 2), "r": (rem0, 2), "o": (rank, 1), "m": (mate, 1), "a": (far_a, 1), "b": (far_b, 1)}[h]
 
     def rs(name, r0, n):
         return ["%s%d" % (name, r) for r in range(r0, r0 + n)]
@@ -206,50 +159,52 @@ def rank_program(g, core, T, topo):
     def tags(name, h):
         return rs(name + "_", *span(h))
 
+    def at(b, j, n):
+        return T[b][:, j:j + n, :] if b == "pF" else T[b][:, 64 * j:64 * (j + n)]
+
     blk = rs
 
     mine = T.qall[:, tok(rank)]
-    WIDE = T.wide[0:64] if ",c," in " ".join(PLAN) else T.wideb[0:64]
-    dma("y", "load", "lq", [(mine, T.rq[:])], [], ["q%d" % rank], 2.0)
-    dma("y", "load", "lnm", [(T.nmi[:], T.nm[:])], [], ["nmi"], 2.6)
-    dma("y", "load", "lke", [(T.kw[:], T.ke[:])], [], ["kw"], 4.0)
-    for ap, value, n, tag in [(T.bdb[:], 1.0, 64, "bdb"), (T.wb[:], 1.0, 128, "wb"), (T.fold[:], 0.0, 120, "fold"), (T.cbig[:], ROUND2048, 128, "cbig"),
-                              (T.zero[:], 0.0, 64, "zero"), (T.minus[:], -1.0, 64, "minus"), (T.c3[:], -31.5, 64, "c3"), (T.sl[:, 0, :], 0.0, 64, "slpB"),
-                              (WIDE, 1.0, 1024 if ",c," in " ".join(PLAN) else 512, "wide")]:
-        if not (NEW and tag in ("wide", "fold")):
-            op("v", "fill", lambda ap=ap, value=value: V.memset(ap, value), n, [], [tag])
+    dma("y", "load", "lq", [(mine, T.rq[:])], [], ["q%d" % rank], 1.7)
+    dma("y", "load", "lnm", [(T.nmi[:], T.nm[:])], [], ["nmi"], 2.2)
+    dma("y", "load", "lke", [(T.kw[:], T.ke[:])], [], ["kw"], 3.7)
+    for ap, value, n, tag in [(T.bdb[:], 1.0, 64, "bdb"), (T.wb[:], 1.0, 128, "wb"), (T.cbig[:], ROUND2048, 128, "cbig"),
+                              (T.minus[:], -1.0, 64, "minus"), (T.four[:], 4.0, 64, "four"), (T.none[:], 0.0, 128, "none"),
+                              (T.keep[:, 0::128], 0.0, 64, "keep"), (T.wide[:], 0.5, 256, "wide")]:
+        op("v", "fill", lambda ap=ap, value=value: V.memset(ap, value), n, [], [tag])
     op("g", "fill", lambda: g.affine_select(T.bdb[:], T.bdb[:], [[-16, 8], [0, 16]], Op.is_ge, 0.0, 0, 1), 128, ["bdb"], ["bdb"])
     op("g", "fill", lambda: g.affine_select(T.bdb[:], T.bdb[:], [[16, 8], [0, 16]], Op.is_ge, 0.0, 15, -1), 128, ["bdb"], ["bdb"])
     op("g", "fill", lambda: g.affine_select(T.wb[:], T.wb[:], [[0, 2], [-1, 128]], Op.is_equal, 0.0, 0, 1), 256, ["wb"], ["wb"])
-    send("q", [(rem[0], part(e_off, 0, 2), "aqr", mine, mine), (rem[1], part(e_off, 1, 2), "aqr", mine, mine), (mate, part(e_on, 0, 1), "aqm", mine, mine)],
-         ["q%d" % rank], [("aqm", ["q%d" % mate], 0), ("aqr", rs("q", rem0, 2), 2)], FLIGHT + FIRST)
-    dma("y", "load", "lb", [(T.bs[:, 0, half, :], bias_rows(T.ke, half)) for half in range(2)], ["q%d" % mate], ["b0"], 2.4)
-    dma("y", "load", "lu", [(T.uw[:], T.ue[:])], [], ["uw"], 4.4)
-    dma("y", "load", "lx", [(T.xb[:], T.x0[:])], [], ["xb"], 4.8)
-    dma("y", "load", "lm", [(T.mb[:], T.mm[:])], [], ["mb"], 5.1)
-    dma("y", "load", "lv", [(T.vw[:], T.ve[:])], [], ["vw"], 7.0)
-    op("g", "late", lambda: g.iota(T.c1[:], [[0, 8], [-64, 4], [0, 4]], int(ROUND64), 0, allow_small_or_imprecise_dtypes=True), 128, [], ["c1"])
-    if not NEW:
-      op("g", "late", lambda: g.affine_select(WIDE, WIDE, [[-1, 64], [0, 16]], Op.is_equal, 0.0, 0, 1), 1024, ["wide"], ["wide"])
-    op("s", "fill", lambda: S.activation(T.bd[:], T.bdb[:], Act.Sigmoid, bias=-128.0, scale=256.0), 1600, ["bdb"], ["bd"])
-    if NEW:
-        op("s", "fill", lambda: S.activation(T.bd[:], T.bd[:], Act.Identity, scale=0.25), 128, ["bd"], ["bd"])
-    for fn, n, reads, tag in [
-            (lambda: V.tensor_scalar(T.prod[:, 0, tok(mate)], T.cbig[:], 0.0, None, Op.mult), 128, ["cbig"], "prod0_%d" % mate),
-            (lambda: V.tensor_scalar(T.zh[:], T.cbig[:, 0:144], 0.0, None, Op.mult), 72, ["cbig"], "zh"),
-            (lambda: V.tensor_copy(T.fold[:, 56:64], T.bdb[:, 0::16]), 64, ["bdb"], "fold"),
-            (lambda: V.tensor_copy(T.wh[:], T.wb[:]), 128, ["wb"], "wh"),
-            (lambda: V.tensor_copy(T.zh[:, 15:143:16], T.bdb[:, 0::16]), 64, ["bdb"], "zh"),
-            (lambda: V.tensor_scalar(T.neg[:], ident, -1.0, None, Op.mult), 64, ["wb"], "neg"),
-            (lambda: V.tensor_scalar(T.negh[:], ident, -1.0, None, Op.mult), 64, ["wb"], "negh"),
-            ([lambda k=k: V.tensor_copy(T.sel[:, :, k, :], ident) for k in range(4)], 64, ["wb"], "sel"),
-            (lambda: V.tensor_copy(T.off[:], T.nmi[:]), 256, ["nmi"], "off"),
-            (lambda: V.tensor_copy(T.nl[:], T.nmi[:, 0::2, :]), 128, ["nmi"], "nl"),
-            (lambda: V.tensor_tensor(T.dn[:], T.nmi[:, 1::2, :], T.nmi[:, 0::2, :], Op.subtract), 256, ["nmi"], "dn"),
-            (lambda: V.tensor_copy(T.nmh[:], T.nmi[:]), 256, ["nmi"], "nmh"),
-            (lambda: V.tensor_scalar(T.c2[:], T.c1[:], 1.25, -0.25 * ROUND64, Op.mult, Op.add), 64, ["c1"], "c2")]:
-        if not (NEW and tag == "fold"):
-            op("v", "fill", fn, n, reads, [tag])
+    for word in QS.split():
+        hs = word.split(".")
+        far = [h for h in hs if h != "m"]
+        send("q" + word, [(span(h)[0], part(e_on, 0, 1) if h == "m" else part(e_off, far.index(h), len(far)), "aq" + h, mine, mine) for h in hs],
+             ["q%d" % rank], [("aq" + h, ["q%d" % span(h)[0]], 1, h != "m") for h in hs])
+    dma("y", "load", "lb", [(T.bs[:, 0, half, :], bias_rows(T.ke, half)) for half in range(2)], ["q%d" % mate], ["b0", "y1"], 1.7)
+    for sem, out, in_, tag, late in [("lu", T.uw, T.ue, "uw", 3.2), ("lx", T.xb, T.x0, "xb", 3.5), ("lm", T.mb, T.mm, "mb", 3.7), ("lv", T.vw, T.ve, "vw", 5.2)]:
+        dma("y", "load", sem, [(out[:], in_[:])], ["q%d" % mate], [tag], late)
+    op("g", "late", lambda: g.iota(T.c1[:], [[0, 8], [-64, 4], [0, 4]], 0, 0, allow_small_or_imprecise_dtypes=True), 128, [], ["c1"])
+    op("g", "ramp", lambda: g.iota(T.ramp[:], [[1, 32], [0, 2]], 0, 0, allow_small_or_imprecise_dtypes=True), 64, [], ["ramp"])
+    op("v", "ramp", lambda: V.tensor_scalar(T.ramp[:], T.ramp[:], 65536.0, None, Op.mult), 64, ["ramp"], ["ramp"])
+    for half in range(2):
+        ap = T.wide[32 * half:32 * half + 32]
+        op("g", "late", lambda ap=ap: g.affine_select(ap, ap, [[-1, 32], [0, 16]], Op.is_equal, 0.0, 0, 1), 512, ["wide", "q%d" % mate], ["wide%d" % half])
+    op("s", "fill", lambda: S.activation(T.fold[:], T.bdb[:, 0::16], Act.Sigmoid, bias=-128.0, scale=256.0), 1500, ["bdb"], ["fold"])
+    for fn, n, reads, writes in [
+            (lambda: V.tensor_copy(T.off[:], T.nmi[:]), 256, ["nmi"], ["off"]),
+            ([lambda k=k: V.tensor_copy(T.sel[:, :, k, :], ident) for k in range(4)], 64, ["wb"], ["sel"]),
+            (lambda: V.tensor_scalar(T.zh[:], T.cbig[:, 0:144], 0.0, None, Op.mult), 72, ["cbig"], ["zh"]),
+            (lambda: V.tensor_copy(T.wh[:], T.wb[:]), 128, ["wb"], ["wh"]),
+            (lambda: V.tensor_copy(T.zh[:, 15:143:16], T.bdb[:, 0::16]), 64, ["bdb"], ["zh"]),
+            (lambda: V.tensor_copy(T.selb[:], T.sel[:]), 256, ["sel"], ["selb"]),
+            (lambda: V.tensor_scalar(T.seln[:], T.sel[:], -1.0, None, Op.mult), 256, ["sel"], ["seln"]),
+            (lambda: V.tensor_scalar(T.half[:], T.bdb[:, 0::16], -0.5, None, Op.mult), 64, ["bdb"], ["half"]),
+            (lambda: V.tensor_scalar(T.bdn[:], T.bdb[:], -0.25, None, Op.mult), 64, ["bdb"], ["bdn"]),
+            (lambda: V.tensor_scalar(T.bd[:], T.bdb[:], 0.5, None, Op.mult), 128, ["bdb"], ["bd"]),
+            (lambda: V.tensor_scalar(T.negh[:], ident, -1.0, None, Op.mult), 64, ["wb"], ["negh"]),
+            (lambda: V.tensor_copy(T.nmh[:], T.nmi[:]), 256, ["nmi"], ["nm0"]),
+            (lambda: V.tensor_scalar(T.c2[:], T.c1[:], 0.25, ROUND64, Op.mult, Op.add), 64, ["c1"], ["c2"])]:
+        op("v", "fill", fn, n, reads, writes)
 
     def keys(c, h):
         r0, n = span(h)
@@ -257,306 +212,294 @@ def rank_program(g, core, T, topo):
 
     def fused(c, h):
         r0, n = span(h)
-        op("v", "f%d%s" % (c, h), lambda: V.tensor_tensor(T.prod[:, c, tok(r0, n)], keys(c, h), T.qall[:, tok(r0, n)], Op.mult),
-           256 * n * GATHER, ["kw", "off"] + rs("q", r0, n), tags("prod%d" % c, h))
+        op("v", "f%d%s" % (c, h), lambda: V.tensor_tensor(T.prod[:, tok(r0, n), c], keys(c, h), T.qall[:, tok(r0, n)], Op.mult),
+           256 * n * R["gather"], ["kw", "off"] + rs("q", r0, n), tags("prod%d" % c, h))
 
     def raw(q, c, h):
         r0, n = span(h)
         out = T.rawk[:, c, tok(r0, n)]
         op(q, "k%d%s" % (c, h), (lambda: V.tensor_copy(out, keys(c, h))) if q == "v" else (lambda: S.activation(out, keys(c, h), Act.Copy)),
-           256 * n * GATHER, ["kw", "off"], tags("raw%d" % c, h))
+           256 * n * R["gather"], ["kw", "off"], tags("raw%d" % c, h))
 
-    def held(c, h, b, j=0, base=None):
+    def held(c, h, b, j, parts):
         r0, n = span(h)
-        P = T[b][:, j:j + 4 * n, :]
-        op("t", "h%d%s" % (c, h), [lambda: PE.matmul(P, ident, T.rawk[:, c, tok(r0, n)], True, base is None)]
-           + ([] if base is None else [lambda: PE.matmul(P, T.neg[:], T.rawk[:, base, tok(r0, n)], False, True)]), 256 * n,
-           ["wb", "neg"] + tags("raw%d" % c, h) + ([] if base is None else tags("raw%d" % base, h)), blk(b, j, 4 * n) + ["acc" + b], [b])
-        op("v", "x%d%s" % (c, h), lambda: V.tensor_tensor(T.prod[:, c, tok(r0, n)], P, T.qall[:, tok(r0, n)], Op.mult), 256 * n,
-           blk(b, j, 4 * n) + rs("q", r0, n), tags("prod%d" % c, h), [b])
+        op("t", "h%d%s" % (c, h), [lambda: PE.matmul(at(b, j, 4 * n), ident, T.rawk[:, c, tok(r0, n)], True, False),
+                                   lambda: PE.matmul(at(b, j, 4 * n), T.neg[:], T.rawk[:, 0, tok(r0, n)], False, True)], 256 * n,
+           ["wb", "neg"] + tags("raw%d" % c, h) + tags("raw0", h), blk(b, j, 4 * n) + ["acc" + b], [b])
+        for p in parts:
+            r = span(p)[0]
+            k = j + 4 * (r - r0)
+            op("v", "x%d%s" % (c, p), lambda p=p, r=r, k=k: V.tensor_tensor(T.prod[:, tok(r), c], at(b, k, 4), T.qall[:, tok(r)], Op.mult), 256,
+               blk(b, k, 4) + ["q%d" % r], tags("prod%d" % c, p), [b])
 
-    def times(c, h):
+    def times(c, h, pair, how="q"):
         r0, n = span(h)
-        b, j = ("pD", 0) if h == "r" else ("pQ", 4 * (r0 - loc0))
-        op("v", "x%d%s" % (c, h), lambda: V.tensor_tensor(T.prod[:, c, tok(r0, n)], T[b][:, j:j + 4 * n, :], T.rawk[:, c, tok(r0, n)], Op.mult), 256 * n,
-           blk(b, j, 4 * n) + tags("raw%d" % c, h), tags("prod%d" % c, h), [b])
+        out = T.quick[:, col(h), c, :] if pair == "qq" else T.prod[:, tok(r0, n), c]
+        src, tag = (T.pQ, "pQ") if how == "q" else (T.qall, "q")
+        op("v", "x%d%s" % (c, h), lambda: V.tensor_tensor(out, src[:, tok(r0, n)], T.rawk[:, c, tok(r0, n)], Op.mult), 128 * n,
+           rs(tag, r0, n) + tags("raw%d" % c, h), tags("prod%d" % c, h), ["pQ"] if how == "q" else [])
 
-    def winners(l, h, b, b2):
-        cs, P = col(h), T[b]
+    def stand(h):
         r0, n = span(h)
-        w = 16 * n
-        c0 = 1 if (l, h) == (0, "r") else 0
+        pieces = [slice(c, c + 128) for c in range(256 * r0, 256 * (r0 + n), 128)]
+        op("t", "q1" + h, [lambda s=s: PE.transpose(T.pQ[:, s], T.qall[:, s], ident) for s in pieces], 128, ["wb"] + rs("q", r0, n), rs("pQ", r0, n), ["pQ"])
+        op("v", "q2" + h, lambda: V.tensor_copy(T.qt[:, tok(r0, n)], T.pQ[:, tok(r0, n)]), 128 * n, rs("pQ", r0, n), rs("qt", r0, n), ["pQ"])
+        op("t", "q3" + h, [lambda s=s: PE.transpose(T.pQ[:, s], T.qt[:, s], ident) for s in pieces], 128, ["wb"] + rs("qt", r0, n), rs("pQ", r0, n), ["pQ"])
 
-        def score(j, k, b, at):
-            op("t", "s%d%s" % (j, h),
-               [lambda i=i: PE.matmul(T[b][:, at, k * w:2 * w], T.zh[:, 15 - i:143 - i], T.prod[:, j + 2 * k::2, 256 * r0 + i:256 * (r0 + n):16], i == 0, i == 15)
-                for i in range(16)], 64, ["zh"] + [t for c in range(j + 2 * k, 4, 2) for t in tags("prod%d" % c, h)], [b + str(at), "acc" + b], [b])
-        score(0, c0, b2, 7)
-        op("s", "sl" + h, lambda: S.activation(T.sl[:, c0:2, cs], T[b2][:, 7, c0 * w:2 * w], Act.Copy), 2 * w, [b2 + "7", "sl" + b], ["sl" + b], [b2])
-        score(1, 0, b, 1)
-        right, g1, t1 = P[:, 1, 0:2 * w], P[:, 2, 0:2 * w], P[:, 3, 0:2 * w]
-        nl = T.nmn[:, 0::2, cs] if NEW and l else T.nl[:, :, cs]
-        far_dn = NEW and l and DN == "t"
-        if far_dn:
-            g1 = T.px[:, :, cs]
-        for out, x, y, o, reads, writes, banks in [
-                (g1, right, T.sl[:, :, cs], Op.is_gt, [b + "1", "sl" + b], ["px" + b if far_dn else b + "2"], [b]),
-                (T.mx[:, :, cs], right, T.sl[:, :, cs], Op.max, [b + "1", "sl" + b], ["mx" + b], [b]),
-                (t1, T.pF[:, 4:6, cs], g1, Op.mult, ["px" + b] + blk("pF", 4, 2), [b + "3"], [b, "pF"]) if far_dn else
-                (t1, g1, T.dn[:, :, cs], Op.mult, [b + "2", "dn"], [b + "3"], [b]),
-                (P[:, 0, 0:w], T.mx[:, 0, cs], T.mx[:, 1, cs], Op.is_ge, ["mx" + b], [b + "0"], [b]),
-                (P[:, 0, w:2 * w], T.mx[:, 1, cs], T.mx[:, 0, cs], Op.is_gt, ["mx" + b, "sl" + b], ["h" + b], [b]),
-                (T.nx[:, :, cs], t1, nl, Op.add, [b + "3", "nl"], ["nx" + b], [b]),
-                (T.px[:, :, cs], P[:, 0, 0:2 * w], T.nx[:, :, cs], Op.mult, [b + "0", "h" + b, "nx" + b], ["px" + b], [b]),
-                (T.w16[:, l, cs], T.px[:, 0, cs], T.px[:, 1, cs], Op.add, ["px" + b], tags("w%d" % l, h), [])]:
-            op("v", "w" + h, lambda out=out, x=x, y=y, o=o: V.tensor_tensor(out, x, y, o), 64, reads, writes, banks)
-        op("v", "w" + h, lambda: V.tensor_copy(T.wu[:, l, cs], T.w16[:, l, cs]), 64, tags("w%d" % l, h), tags("wu%d" % l, h))
+    def steps(l):
+        nm = T.nmn if l else T.nmh
+        op("t", "dn", [lambda c=c: PE.matmul(T.pX[:, 256 + c::4], identh, nm[:, c, :], c == 0, False) for c in range(4)]
+           + [lambda c=c: PE.matmul(T.pX[:, 256 + c::4], T.negh[:], nm[:, c + 1, :], False, c == 2) for c in range(3)], 64,
+           ["wh", "negh", "nm%d" % l], blk("pX", 4, 4) + ["accpX"], ["pX"])
 
-    def tell(l):
-        src, dst, sem = T.w16[:, l, :], T.wr[:, l, rank, :], "aw%d" % l
-        send("tell", [(rem[0], part(e_off, 0, 2), sem, src, dst), (rem[1], part(e_off, 1, 2), sem, src, dst), (mate, part(e_on, 0, 1), sem, src, dst)],
-             tags("w%d" % l, "a"), [(sem, ["wr%d" % l], 0.5)])
+    def winners(l, h, b):
+        cs = col(h)
+        a, P = 4 * cs.start, T[b]
+        how = dict(word.split(",") for word in KEYS[l].split()).get(h, "ffff")
+        for c in (0, 1):
+            rhs = [T.quick[:, cs, c::2, i] if how[c::2] == "qq" else T.prod[:, 16 * cs.start + i:16 * cs.stop:16, c::2] for i in range(16)]
+            op("t", "s%d%s" % (c, h), [lambda c=c: PE.matmul(P[:, c:128:2], ident, T.ramp[:], True, False)]
+               + [lambda i=i, c=c, rhs=rhs: PE.matmul(P[:, c:128:2], T.zh[:, 15 - i:143 - i], rhs[i], False, i == 15) for i in range(16)], 64,
+               ["zh", "wb", "ramp"] + tags("prod%d" % c, h) + tags("prod%d" % (c + 2), h), [b + "0" if c else b + "1", "acc" + b], [b])
+        both = blk(b, 0, 2)
+        op("v", "w1" + h, lambda: V.tensor_tensor_scan(T.top[:, a:a + 128], T.none[:], P[:, 0:128], -65536.0, Op.add, Op.max), 128, both + ["none"], ["top" + b], [b])
+        op("v", "w2" + h, lambda: V.tensor_tensor(T.keep[:, a + 1:a + 128], P[:, 1:128], T.top[:, a:a + 127], Op.is_le), 127, both + ["top" + b, "keep"], ["keep" + b], [b])
+        op("v", "w3" + h, lambda: V.tensor_tensor_scan(T.run[:, a:a + 128], T.keep[:, a:a + 128], T.pX[:, 256 + a:384 + a], 0.0, Op.mult, Op.add), 128,
+           ["keep" + b] + blk("pX", 4, 4), tags("run", h), ["pX"])
+        op("v", "w5" + h, lambda: V.tensor_copy(T.wu[:, l, cs], won(h)), 64, tags("run", h), tags("wu%d" % l, h))
 
-    def steps_apart(nm):
-        if DN == "v":
-            op("v", "dn", lambda: V.tensor_tensor(T.dn[:], nm[:, 1::2, :], nm[:, 0::2, :], Op.subtract), 256, ["nl"], ["dn"])
-        else:
-            op("t", "dn", [lambda: PE.matmul(T.pF[:, 4:6, :], identh, nm[:, 1::2, :], True, False), lambda: PE.matmul(T.pF[:, 4:6, :], T.negh[:], nm[:, 0::2, :], False, True)],
-               128, ["wh", "negh", "nl"], blk("pF", 4, 2) + ["accpF"], ["pF"])
+    def won(h):
+        return T.run[:, 4 * col(h).start + 3:4 * col(h).stop:4]
 
     def names(l):
-        NP = T.pA[:, 4:8, :]
+        src, dst, sem = T.w16[:, l, :], T.wr[:, l, rank, :], "aw%d" % l
+        op("v", "w4", lambda: V.tensor_copy(src, won("*")), 64, tags("run", "*"), tags("w%d" % l, "*"))
+        send("tell", [(far_a, part(e_off, 0, 2), sem, src, dst), (far_b, part(e_off, 1, 2), sem, src, dst), (mate, part(e_on, 0, 1), sem, src, dst)],
+             tags("w%d" % l, "*"), [(sem, ["wr%d" % l], 0.5, True)])
+        NP, nb = at("pA", 4, 4), blk("pA", 4, 4)
         pairs = [(r, c) for r in range(N) if r != rank for c in range(4)]
-        if NEW:
-            nb = blk("pA", 4, 4)
-            op("t", "nA", [lambda: PE.matmul(NP, identh, T.nmh[:], True, False), lambda: PE.matmul(NP, ident, T.cbig[:], False, False)]
-               + [lambda c=c: PE.matmul(T.pA[:, 4 + c, :], shifth, T.w16[:, l, :], False, False) for c in range(4)], 128,
-               ["wh", "wb", "nmh", "cbig"] + tags("w%d" % l, "a"), nb + ["accpA"], ["pA"])
-            op("t", "nAr", [lambda r=r, c=c: PE.matmul(T.pA[:, 4 + c, :], shifth, T.wr[:, l, r, :], False, (r, c) == pairs[-1]) for r, c in pairs],
-               64, ["wh", "wr%d" % l], nb + ["accpA"], ["pA"])
-            op("s", "hb", lambda: S.activation(T.hb[:], NP, Act.Identity, bias=1023.5, scale=-1.0), 256, nb, ["hb"], ["pA"])
-            op("v", "nn", lambda: V.tensor_tensor(T.nmn[:], NP, T.hb[:], Op.add), 256, nb + ["hb"], ["nl"], ["pA"])
-            op("v", "off", lambda: V.tensor_copy(T.off[:], T.nmn[:]), 128, ["nl"], ["off"])
-            steps_apart(T.nmn)
-            return
-        for b in ("pB", "pA"):
-            op("t", "n" + b[1], [lambda b=b: PE.matmul(T[b][:, 4:8, :], identh, T.nmh[:], True, False)]
-               + ([lambda: PE.matmul(NP, ident, T.cbig[:], False, False)] if b == "pA" else [])
-               + [lambda b=b, c=c: PE.matmul(T[b][:, 4 + c, :], shifth, T.w16[:, l, :], False, False) for c in range(4)], 128,
-               ["wh", "wb", "nmh", "cbig"] + tags("w%d" % l, "a"), blk(b, 4, 4) + ["acc" + b], [b])
-        for b in ("pB", "pA"):
-            op("t", "n%sr" % b[1],
-               [lambda b=b, r=r, c=c, end=b == "pB" and (r, c) == pairs[-1]: PE.matmul(T[b][:, 4 + c, :], shifth, T.wr[:, l, r, :], False, end)
-                for r, c in pairs], 64, ["wh", "wr%d" % l], blk(b, 4, 4) + ["acc" + b], [b])
-        op("s", "hb", lambda: S.activation(T.hb[:], T.pB[:, 4:8, :], Act.Identity, bias=1023.5 - ROUND2048, scale=-1.0), 256, blk("pB", 4, 4), ["hb"], ["pB"])
-        op("t", "nb", lambda: PE.matmul(NP, ident, T.hb[:], False, True), 256, ["wb", "hb"], blk("pA", 4, 4) + ["accpA"], ["pA"])
-        op("v", "off", lambda: V.tensor_copy(T.off[:], NP), 256, blk("pA", 4, 4), ["off"], ["pA"])
-        op("s", "nl", lambda: S.activation(T.nl[:], T.pA[:, 4::2, :], Act.Copy), 128, blk("pA", 4, 4), ["nl"], ["pA"])
-        op("v", "dn", lambda: V.tensor_tensor(T.dn[:], T.pA[:, 5::2, :], T.nl[:], Op.subtract), 128, blk("pA", 4, 4) + ["nl"], ["dn"], ["pA"])
+        op("t", "nA", [lambda: PE.matmul(NP, identh, T.nmh[:], True, False), lambda: PE.matmul(NP, ident, T.cbig[:], False, False)]
+           + [lambda c=c: PE.matmul(at("pA", 4 + c, 1), shifth, T.w16[:, l, :], False, False) for c in range(4)], 128,
+           ["wh", "wb", "nm0", "cbig"] + tags("w%d" % l, "*"), nb + ["accpA"], ["pA"])
+        op("t", "nB", [lambda r=r, c=c: PE.matmul(at("pA", 4 + c, 1), shifth, T.wr[:, l, r, :], False, (r, c) == pairs[-1]) for r, c in pairs],
+           64, ["wh", "wr%d" % l], nb + ["accpA"], ["pA"])
+        op("s", "hb", lambda: S.activation(T.hb[:], NP, Act.Identity, bias=1023.5, scale=-1.0), 256, nb, ["hb"], ["pA"])
+        op("v", "nn", lambda: V.tensor_tensor(T.nmn[:], NP, T.hb[:], Op.add), 256, nb + ["hb"], ["nmn", "nm%d" % (l + 1)], ["pA"])
+        op("v", "off", lambda: V.tensor_copy(T.off[:], T.nmn[:]), 128, ["nmn"], ["off"])
 
-    tj = 2 if NEW else 4
-    F, FT = T.pF[:, 0:2, 0:33], T.pW[:, tj:tj + 2, :]
+    F = T.pF[:, 0:2, 0:33]
 
-    def count(l, k, h, b, b2):
-        def turn(b, cols, eye, const):
-            rows = [lambda j=j: PE.matmul(T[b][32 * j:32 * j + 32, cols, :], T.w16[:, l, col(h)], T.sel[:, :, :, 4 * j:4 * j + 4], False, False) for j in range(4)]
-            return [lambda: PE.matmul(T[b][:, cols, :], eye, const, True, False)] + rows
-        name, k = k, int(k)
-        high, low = T[b][:, 4:6, :], T[b2][:, 0:2, :]
-        op("t", "hi" + name, turn(b, slice(4, 6), ident, T.c1[:]) + [lambda: PE.matmul(high, ident, T.c3[:], False, True)], 128,
-           ["wb", "c1", "c3", "sel"] + tags("w%d" % l, h), blk(b, 4, 2) + ["acc" + b], [b])
-        op("t", "lo" + name, turn(b2, slice(0, 2), identh, T.c2[:]), 128,
-           ["wh", "c2", "sel"] + tags("w%d" % l, h), blk(b2, 0, 2) + ["acc" + b2, "h" + b2], [b2])
-        op("s", "dv" + name, lambda: S.activation(T.dv[:, k], high, Act.Copy), 128, blk(b, 4, 2), ["dv%d" % k], [b])
-        op("t", "ng" + name, lambda: PE.matmul(low, T.neg[:], T.dv[:, k], False, True), 128, ["neg", "dv%d" % k], blk(b2, 0, 2) + ["acc" + b2], [b2])
-        for u in range(8):
-            op("v", "oh" + name, lambda u=u: V.tensor_scalar(T.oh[:, 8 * k:8 * k + 8, u, :], T.dv[:, k], ROUND64 + 256.0 * u, 4096.0, Op.is_equal, Op.mult), 64,
-               ["dv%d" % k], ["oh%d%d" % (k, u)])
-            op("s", "th" + name, lambda u=u: S.activation(T.th[:, 8 * k:8 * k + 8, u::8, :], low, Act.Sigmoid, bias=-256.0 * u - EDGE, scale=128.0), 128,
-               blk(b2, 0, 2), ["th%d%d" % (k, u)], [b2])
-        ends = [lambda: PE.matmul(F, ident, T.zero[:], k == 0, k == 1)]
+    def count(l, k, h, b):
+        high(l, k, h, b)
+        low(l, k, h)
+
+    def high(l, k, h, b):
+        H, hb = at(b, 2, 2), blk(b, 2, 2)
+        op("v", "up%d" % k, lambda: V.tensor_scalar(T.hw[:, k], won(h), ROUND64 - 31.5, None, Op.add), 64, tags("run", h), ["hw%d" % k])
+        op("t", "hi%d" % k, [lambda: PE.matmul(H, ident, T.c1[:], True, False)] + turn(H, T.hw[:, k], T.selb) + [close(H)], 128,
+           ["wb", "wh", "zh", "c1", "selb", "hw%d" % k], hb + ["acc" + b], [b])
+        q = COPIES[l][k]
+        op(q, "dv%d" % k, (lambda: V.tensor_copy(T.dv[:, k], H)) if q == "v" else (lambda: S.activation(T.dv[:, k], H, Act.Copy)), 128, hb, ["dv%d" % k], [b])
+
+    def turn(H, w, sel):
+        return [lambda j=j: PE.matmul(H[32 * j:32 * j + 32], w, sel[:, :, :, 4 * j:4 * j + 4], False, False) for j in range(4)]
+
+    def close(H):
+        return lambda: PE.matmul(H[:, 0, 0:2] if len(H.shape) > 2 else H[:, 0:2], identh, T.zh[:, 0:2], False, True)
+
+    def low(l, k, h):
+        b = ("pF", "pA")[k]
+        H, hb = at(b, 4, 2), blk(b, 4, 2)
+        op("t", "lo%d" % k, [lambda: PE.matmul(H, identh, T.c2[:], True, False)] + turn(H, won(h), T.sel), 128,
+           ["wh", "c2", "sel"] + tags("run", h), hb + ["acc" + b], [b])
+        op("t", "ng%d" % k, turn(H, T.hw[:, k], T.seln) + [close(H)], 128, ["seln", "wh", "zh", "hw%d" % k], hb + ["acc" + b], [b])
+        for u0 in range(0, 8, 2):
+            op("v", "oh%d" % k, [lambda u=u: V.tensor_scalar(T.oh[:, 8 * k:8 * k + 8, u, :], T.dv[:, k], ROUND64 + 256.0 * u, 4096.0, Op.is_equal, Op.mult)
+                                 for u in (u0, u0 + 1)], 64, ["dv%d" % k], ["oh%d%d" % (k, u0)])
+            op("s", "th%d" % k, [lambda u=u: S.activation(T.th[:, 8 * k:8 * k + 8, u::8, :], H, Act.Sigmoid, bias=-256.0 * u - EDGE, scale=128.0)
+                                 for u in (u0, u0 + 1)], 128, hb, ["th%d%d" % (k, u0)], [b])
+        ends = [lambda: PE.matmul(F, ident, T.minus[:], k == 0, k == 1)]
         sums = [lambda gr=gr, i=i: PE.matmul(T.pF[32 * (gr % 4):32 * (gr % 4) + 32, gr // 4, 0:32], T.oh[:, 8 * k + gr, :, i::4], T.th[:, 8 * k + gr, :, i],
                                               False, False) for gr in range(8) for i in range(4)]
-        op("t", "sum" + name, ends + sums if k == 0 else sums + ends, 32,
-           ["wb", "zero"] + ["%s%d%d" % (x, k, u) for x in ("oh", "th") for u in range(8)], blk("pF", 0, 2) + ["accpF"], ["pF"])
+        op("t", "sum%d" % k, ends + sums if k == 0 else sums + ends, 33,
+           ["wb", "minus"] + ["%s%d%d" % (x, k, u) for x in ("oh", "th") for u in range(8)], blk("pF", 0, 2) + ["accpF"], ["pF"])
 
     def biases(l):
         last = l == NL - 1
         j = NL if last else l
         if last:
-            op("s", "blo", lambda: S.activation(T.bs[:, NL], T.bs[:, l], Act.Identity, bias=float(NL)), 128, ["b%d" % l], ["b%d" % NL])
-        op("s", "blo", lambda: S.activation(T.blo[:, l], T.bs[:, l], Act.Identity, bias=float(NL - 2) if last else -2.0), 128, ["b%d" % l], ["blo%d" % l])
+            op("s", "blo", lambda: S.activation(T.bs[:, NL], T.bs[:, l], Act.Identity, bias=-float(NL)), 128, ["b%d" % l], ["b%d" % NL])
         new = T.bout[:] if last else T.bs[:, l + 1]
-        even, odd = T.pW[:, tj:tj + 2, 0::2], T.pW[:, tj:tj + 2, 1::2]
-        fb, tb = blk("pF", 0, 2), blk("pW", tj, 2) + ["accpW"]
-        op("t", "Tb", lambda: PE.matmul(FT, ident, T.bs[:, j], True, False), 128, ["wb", "b%d" % j], tb, ["pW"])
+        FT, even, odd = at("pB", 4, 2), T.pB[:, 256:384:2], T.pB[:, 257:384:2]
+        fb, tb = blk("pF", 0, 2), blk("pB", 4, 2) + ["accpB"]
+        op("t", "Tb", [lambda: PE.matmul(FT, ident, T.bs[:, j], True, False), lambda: PE.matmul(odd, ident, T.four[:], False, False)], 96,
+           ["wb", "four", "b%d" % j], tb, ["pB"])
         op("v", "post", lambda: V.tensor_scalar(T.i2[:], F, ROUND4096, -ROUND4096, Op.add, Op.add), 66, fb, ["i2"], ["pF"])
         op("v", "post", lambda: V.tensor_scalar(T.up[:], F, 2.0 ** -12, 1024.0, Op.mult, Op.add), 66, fb, ["up"], ["pF"])
         op("v", "post", lambda: V.tensor_tensor(T.ee[:], F, T.i2[:], Op.subtract), 66, fb + ["i2"], ["ee"], ["pF"])
         op("t", "Tu", [lambda: PE.matmul(odd, T.negh[:], T.up[:, :, 0:32], False, False), lambda: PE.matmul(odd, identh, T.up[:, :, 1:33], False, False)],
-           64, ["wh", "negh", "up"], tb, ["pW"])
+           64, ["wh", "negh", "up"], tb, ["pB"])
         op("t", "Te", [lambda: PE.matmul(odd, identh, T.ee[:, :, 1:33], False, False), lambda: PE.matmul(even, T.negh[:], T.ee[:, :, 0:32], False, True)],
-           64, ["wh", "negh", "ee"], tb, ["pW"])
-        op("v", "post", lambda: V.tensor_tensor(new, FT, T.blo[:, l], Op.max), 128, tb + ["blo%d" % l], ["bout" if last else "b%d" % (l + 1)], ["pW"])
+           64, ["wh", "negh", "ee"], tb, ["pB"])
+        op("v", "post", lambda: V.tensor_tensor(new, FT, T.bs[:, j], Op.max), 128, tb + ["b%d" % j], ["bout" if last else "b%d" % (l + 1)], ["pB"])
         if last:
-            dma("y", "bias", "oyb", [(T.yb[4 * half:4 * half + 4, :], T.bout[:, half, :]) for half in range(2)], ["bout"], ["yb"])
+            dma("y", "bias", "oyb", [(T.yb[4 * half:4 * half + 4, :], T.bout[:, half, :]) for half in range(2)], ["bout"], ["yb"], R["local"])
         else:
-            dma("y", "bias", "bias%d" % l, [(bias_rows(T.kw, half), T.bs[:, l + 1, half, :]) for half in range(2)], ["b%d" % (l + 1)], ["kw", "kw%d" % (l + 1)])
+            dma("y", "bias", "bias%d" % l, [(bias_rows(T.kw, half), T.bs[:, l + 1, half, :]) for half in range(2)], ["b%d" % (l + 1)],
+                ["kw", "kw%d" % (l + 1)], R["local"])
 
     out_j, in_j = (2, 0) if rank < mate else (0, 2)
 
-    def chosen(l, k, h):
-        return (T.uw, T.vw)[k][:].indirect(T.wu[:, l, col(h)]), ["uv"[k] + "w"] + tags("wu%d" % l, h)
-
-    def pick(l, kind, h, q):
+    def pick(l, what, q):
+        kind, h = what
         k = "uv".index(kind)
-        src, reads = chosen(l, k, h)
-        out = T.away[:, 2 * l + k] if h == "r" else T.near[:, 2 * l + k, {"l": tok(min(1, out_j), 2), "m": tok(out_j), "o": tok(1)}[h]]
-        op(q, "UV"[k] + h, (lambda: V.tensor_copy(out, src)) if q == "v" else (lambda: S.activation(out, src, Act.Copy)),
-           256 * span(h)[1] * GATHER, reads, tags("%s%dp" % (kind, l), h))
+        src = (T.uw, T.vw)[k][:].indirect(T.wu[:, l, col(h)])
+        r0, n = span(h)
+        out = T.away[:, 2 * l + k, tok(r0 - rem0, n)] if h in "rab" else T.near[:, 2 * l + k, {"l": tok(min(1, out_j), 2), "m": tok(out_j), "o": tok(1)}[h]]
+        op(q, kind.upper() + h, (lambda: V.tensor_copy(out, src)) if q == "v" else (lambda: S.activation(out, src, Act.Copy)),
+           256 * n * R["gather"], [kind + "w"] + tags("wu%d" % l, h), tags("%s%dp" % (kind, l), h))
 
-    def give(l, kinds, to, *behind):
-        items, reads, lands = [], list(behind), []
-        for i, kind in enumerate(kinds):
+    def give(l, word):
+        what = word.rstrip("+").split(".")
+        items, reads, lands = [], ["kw%d" % (l + 1)] if word[-1] == "+" else [], []
+        for kind, h in what:
             k = 2 * l + "uv".index(kind)
-            for h in to:
-                sem = "a%d%s%s" % (l, kind, h)
-                if h == "r":
-                    items += [(r, part(e_off, j, 2), sem, T.away[:, k, tok(j)], T.came[:, k, rank - loc0]) for j, r in enumerate(rem)]
-                else:
-                    items += [(mate, part(e_on, i, len(kinds)), sem, T.near[:, k, tok(out_j)], T.near[:, k, tok(out_j)])]
-                reads += tags("%s%dp" % (kind, l), h)
-                lands += [(sem, tags("%s%dc" % (kind, l), h), 2 if h == "r" else 0)]
-        send(kinds.upper() + to, items, reads, lands)
+            like = [w for w in what if (w[1] == "m") == (h == "m")]
+            i, sem, r = like.index(kind + h), "a%d%s%s" % (l, kind, h), span(h)[0]
+            if h == "m":
+                items.append((r, part(e_on, i, len(like)), sem, T.near[:, k, tok(out_j)], T.near[:, k, tok(out_j)]))
+            else:
+                items.append((r, part(e_off, i, len(like)), sem, T.away[:, k, tok(r - rem0)], T.came[:, k, rank - loc0]))
+            reads += tags("%s%dp" % (kind, l), h)
+            lands.append((sem, tags("%s%dc" % (kind, l), h), 0.7 if h == "m" else 1, h != "m"))
+        send(word, items, reads, lands)
 
-    xb_, xj = ("pW", 4) if NEW else ("pD", 0)
-    X, M = T[xb_][:, xj:xj + 4, :], T.pM[:, 0:4, :]
+    X, xb, M = at("pX", 0, 4), blk("pX", 0, 4), at("pM", 0, 4)
     mixes, mixed = [0] * NL, [0] * NL
 
-    def mix(l, name, m, rhs, reads):
+    def mix(l, name, rhs, reads):
         def fn():
             mixed[l] += 1
-            return PE.matmul(M, m, rhs, mixed[l] == 1, mixed[l] == mixes[l])
-        op("t", name, fn, 1024, reads, ["pM%d" % mixes[l]], ["pM"])
+            return PE.matmul(M, T.m32[:], rhs, mixed[l] == 1, mixed[l] == mixes[l])
+        op("t", name, fn, 1024, ["m32", "mix%d" % l, "mixp%d" % l] + reads, ["pM_%d" % mixes[l]], ["pM"])
         mixes[l] += 1
 
-    def expert(l, h, form, b, b0):
-        b0 = int(b0)
+    def expert(l, h, b):
+        n = int(h == "l")
         if h == "r":
-            n, y0, ranks = 2, 2, rem
-            src = lambda k, i, m: T.came[:, 2 * l + k, i:i + m]
+            ranks, src = [rem0, rem0 + 1], lambda k, i, m: T.came[:, 2 * l + k, i:i + m]
+            order = [far_a - rem0, far_b - rem0]
+            piece = lambda i, j: T.came[:, 2 * l, i, 128 * j:128 * j + 128]
         else:
-            j0 = {"l": min(1, in_j), "m": in_j, "o": 1}[h]
-            n, y0 = span(h)[1], j0 - min(1, in_j)
-            ranks = [rank if j == 1 else mate for j in range(j0, j0 + n)]
-            src = lambda k, i, m: T.near[:, 2 * l + k, tok(j0 + i, m)]
+            j0 = min(1, in_j)
+            piece = lambda i, j: T.near[:, 2 * l, 256 * (j0 + i) + 128 * j:256 * (j0 + i) + 128 * j + 128]
+            ranks, src = [rank if j == 1 else mate for j in (j0, j0 + 1)], lambda k, i, m: T.near[:, 2 * l + k, tok(j0 + i, m)]
+            order = [ranks.index(rank), ranks.index(mate)]
         have = lambda kind, r: "%s%d%s_%d" % (kind, l, "p" if r == rank else "c", r)
-        order = sorted(range(n), key=lambda i: ranks[i] != rank)
-        E, eb = T[b][:, b0:b0 + 4 * n, :], blk(b, b0, 4 * n)
-        if form == "f":
-            (u, ur), (v, vr) = chosen(l, 0, h), chosen(l, 1, h)
-            op("v", "pu" + h, lambda: V.tensor_tensor(T.pu[:, y0], u, T.xo[:], Op.mult), 256 * GATHER, ["xo"] + ur, ["pu%d" % y0])
-        for i in order if form != "f" else ():
-            op("v", "pu" + h, lambda i=i: V.tensor_tensor(T.pu[:, y0 + i], X, src(0, i, 1), Op.mult), 256,
-               blk(xb_, xj, 4) + [have("u", ranks[i])], ["pu%d" % (y0 + i)], [xb_])
-        if form not in "ch":
-            for i in order:
-                op("t", "D" + h, lambda i=i: PE.matmul(T[b][:, b0 + 4 * i:b0 + 4 * i + 4, :], T.bd[:], T.pu[:, y0 + i], True, True), 1024,
-                   ["bd", "pu%d" % (y0 + i)], blk(b, b0 + 4 * i, 4) + ["acc" + b], [b])
-            op("s", "sg" + h, lambda: S.activation(T.sg[:, y0:y0 + n], E, Act.Sigmoid, scale=4.0 if NEW else 1.0), 256 * n, eb, rs("sg", y0, n), [b])
-            if form == "f":
-                op("v", "sm" + h, lambda: V.tensor_tensor(T.sg[:, y0], E, T.sg[:, y0], Op.mult), 256, eb + ["sg%d" % y0], ["sg%d" % y0], [b])
-                op("v", "yy" + h, lambda: V.tensor_tensor(T.yy[:, y0], v, T.sg[:, y0], Op.mult), 256 * GATHER, ["sg%d" % y0] + vr, ["y%d" % y0])
-            else:
-                op("v", "sm" + h, lambda: V.tensor_tensor(E, E, T.sg[:, y0:y0 + n], Op.mult), 256 * n, eb + rs("sg", y0, n), eb, [b])
-        else:
-            D, db = T.pD[0:32 * n, 4 + y0, :], blk("pD", 4 + y0, 1)
-            for i in order:
-                op("t", "D" + h,
-                   [lambda i=i, j=j: PE.matmul(D, T.fold[:, 56 - 32 * i - 8 * j:56 - 32 * i - 8 * j + 32 * n], T.pu[:, y0 + i, 64 * j:64 * j + 64],
-                                               i == order[0] and j == 0, i == order[-1] and j == 3) for j in range(4)],
-                   256, ["fold", "pu%d" % (y0 + i)], db + ["accpD"], ["pD"])
-            op("s", "sg" + h, lambda: S.activation(T.sn[0:32 * n, y0], D, Act.Sigmoid), 64, db, ["sn%d" % y0], ["pD"])
-            op("v", "sm" + h, lambda: V.tensor_tensor(T.sc[0:32 * n, y0], D, T.sn[0:32 * n, y0], Op.mult), 64, db + ["sn%d" % y0], ["sc%d" % y0], ["pD"])
-            if form == "h":
-                op("s", "sh" + h, lambda: S.activation(T.sp[0:32 * n, y0, 0], T.sc[0:32 * n, y0], Act.Copy), 64, ["sc%d" % y0], ["sh%d" % y0])
-                op("v", "sd" + h, lambda: V.tensor_tensor(T.sp[0:32 * n, y0, 1], T.sc[0:32 * n, y0], T.sp[0:32 * n, y0, 0], Op.subtract), 128,
-                   ["sc%d" % y0, "sh%d" % y0], ["sd%d" % y0])
-                op("t", "E" + h, [lambda k=k, j=j: PE.matmul(T[b][:, b0 + k, :], T.wideb[0:32 * n, 8 * k:8 * k + 8, :], T.sp[0:32 * n, y0, j], j == 0, j == 1)
-                                  for k in range(4 * n) for j in range(2)], 64, ["wide", "sh%d" % y0, "sd%d" % y0], eb + ["acc" + b], [b])
-            for i in range(n) if form == "c" else ():
-                op("t", "E" + h, [lambda k=k: PE.matmul(T[b][:, b0 + k, :], T.wide[0:32 * n, 8 * k:8 * k + 8, :], T.sc[0:32 * n, y0], True, True)
-                                  for k in range(4 * i, 4 * i + 4)], 256, ["wide", "sc%d" % y0], blk(b, b0 + 4 * i, 4) + ["acc" + b], [b])
+        D, C, W = T[b][:, 0:32], T[b][:, 64:96], T[b][0:64, 128:256]
+        for i in order:
+            y = 2 * n + i
+            op("v", "pu" + h, lambda i=i, y=y: V.tensor_tensor(T.pu[:, y], X, src(0, i, 1), Op.mult), 256, xb + [have("u", ranks[i])], ["pu%d" % y], ["pX"])
+            if FORMS[l][n] == "w":
+                p, E, eb = "ab"[order.index(i)] if h == "r" else "om"[order.index(i)], at(b, 4 * i, 4), blk(b, 4 * i, 4)
+                op("t", "D" + p, [lambda i=i, E=E: PE.matmul(E, T.bdn[:], src(0, i, 1), True, False), lambda y=y, E=E: PE.matmul(E, T.bd[:], T.pu[:, y], False, True)],
+                   640, ["bd", "bdn", "pu%d" % y], eb, [b])
+                op("s", "sg" + p, lambda y=y, E=E: S.activation(T.sg[:, y], E, Act.Sigmoid, scale=4.0), 256, eb, ["sg%d" % y], [b])
+                op("v", "sm" + p, lambda y=y, E=E: V.tensor_tensor(E, E, T.sg[:, y], Op.mult), 256, ["sg%d" % y], eb, [b])
+                op("v", "yy" + p, lambda i=i, y=y, E=E: V.tensor_tensor(T.yy[:, y], E, src(1, i, 1), Op.mult), 256, eb + [have("v", ranks[i])], ["y%d" % y], [b])
+                mix(l, "mix" + p, T.yy[:, y], ["y%d" % y])
+                continue
+            op("t", "D" + h, [fn for j in range(2) for fn in (
+                lambda i=i, j=j: PE.matmul(D[:, 16 * i + 8 * j:16 * i + 8 * j + 8], piece(i, j), T.half[:], True, False),
+                lambda i=i, y=y, j=j: PE.matmul(D[:, 16 * i + 8 * j:16 * i + 8 * j + 8], T.pu[:, y, 128 * j:128 * j + 128], T.fold[:], False, True))],
+               160, ["fold", "half", "pu%d" % y], [b + "0"], [b])
+        if FORMS[l][n] == "w":
+            return
+        op("s", "sg" + h, lambda: S.activation(T.sn[:, n], D, Act.Sigmoid, scale=2.0), 64, [b + "0"], ["sn" + h], [b])
+        op("v", "sm" + h, lambda: V.tensor_tensor(T.sp[:, n, 0:32], D, T.sn[:, n], Op.mult), 64, [b + "0", "sn" + h], ["sp" + h], [b])
+        op("v", "sm" + h, lambda: V.tensor_tensor(C, D, T.sn[:, n], Op.mult), 64, [b + "0", "sn" + h], [b + "1"], [b])
+        op("v", "sd" + h, lambda: V.tensor_tensor(T.sp[:, n, 32:64], C, T.sp[:, n, 0:32], Op.subtract), 64, [b + "1", "sp" + h], ["sl" + h], [b])
+        op("t", "W" + h, lambda: PE.matmul(W, T.sp[:, n], ident, True, True), 128, ["wb", "sp" + h, "sl" + h], blk(b, 2, 2), [b])
+        q = TURNED[l]
+        op(q, "sq" + h, (lambda: V.tensor_copy(T.sq[0:64, n], W)) if q == "v" else (lambda: S.activation(T.sq[0:64, n], W, Act.Copy)), 128,
+           blk(b, 2, 2), ["sq" + h], [b])
+        op("t", "E" + h, [lambda k=k: PE.matmul(at(b, 2 * k, 2), T.wide[0:64, 8 * k:8 * k + 8, :], T.sq[0:64, n], True, True) for k in range(4)], 128,
+           ["wide0", "wide1", "sq" + h], blk(b, 0, 8), [b])
         vs = [have("v", r) for r in ranks]
-        if form in "jx":
-            keep = int(form == "j")
-            P = T[b][:, b0 + 4 * keep:b0 + 4 * n, :]
-            if keep:
-                op("v", "yy" + h, lambda: V.tensor_tensor(T.yy[:, y0], T[b][:, b0:b0 + 4, :], src(1, 0, 1), Op.mult), 256, eb + vs, ["y%d" % y0], [b])
-            op("v", "yy" + h, lambda: V.tensor_tensor(P, P, src(1, keep, n - keep), Op.mult), 256 * (n - keep), eb + vs, eb, [b])
-            for i in range(keep, n):
-                op("v", "ad" + h, lambda i=i: V.tensor_tensor(T.yy[:, y0], T[b][:, b0 + 4 * i:b0 + 4 * i + 4, :], T.yy[:, y0] if i else T.sx[:], Op.add), 256,
-                   eb + ["y%d" % y0, "sx"], ["y%d" % y0], [b])
-        elif form != "f":
-            op("v", "yy" + h, lambda: V.tensor_tensor(T.yy[:, y0:y0 + n], E, src(1, 0, n), Op.mult), 256 * n, eb + vs, rs("y", y0, n), [b])
-        for i in range(1 if form in "jx" else n):
-            mix(l, "mix" + h, T.m32[:] if NEW else T.m4[:], T.yy[:, y0 + i], ["m32" if NEW else "m4", "y%d" % (y0 + i)])
+        own = "x" in ADDS[l] and h == "l"
+        if "p" in ADDS[l] or own:
+            first, second = order
+            P = at(b, 4 * first, 4)
+            op("v", "yy" + h, lambda: V.tensor_tensor(P, P, src(1, first, 1), Op.mult), 256, [vs[first]], blk(b, 4 * first, 4), [b])
+            op("v", "yy" + h, lambda: V.tensor_tensor(T.yy[:, 2 * n + 1], at(b, 4 * second, 4), src(1, second, 1), Op.mult), 256,
+               [vs[second]] + blk(b, 4 * second, 4), ["y%d" % (2 * n + 1)], [b])
+            if own and "p" in ADDS[l]:
+                op("v", "ad" + h, lambda: V.tensor_tensor(P, P, T.sx[:], Op.add), 256, ["sx"], blk(b, 4 * first, 4), [b])
+            if "p" in ADDS[l]:
+                op("v", "ad" + h, lambda: V.tensor_tensor(T.yy[:, 2 * n + 1], P, T.yy[:, 2 * n + 1], Op.add), 256, blk(b, 4 * first, 4), ["y%d" % (2 * n + 1)], [b])
+            else:
+                op("v", "ad" + h, lambda: V.tensor_tensor(T.yy[:, 2 * n], P, T.sx[:], Op.add), 256, blk(b, 4 * first, 4) + ["sx"], ["y%d" % (2 * n)], [b])
+                mix(l, "mix" + h, T.yy[:, 2 * n], ["y%d" % (2 * n)])
+            mix(l, "mix" + h, T.yy[:, 2 * n + 1], ["y%d" % (2 * n + 1)])
+            return
+        for i0, m in [(i, 1) for i in order] if l == NL - 1 else [(0, 2)]:
+            y = 2 * n + i0
+            op("v", "yy" + h, lambda i0=i0, m=m, y=y: V.tensor_tensor(T.yy[:, y:y + m], at(b, 4 * i0, 4 * m), src(1, i0, m), Op.mult), 256 * m,
+               blk(b, 4 * i0, 4 * m) + vs[i0:i0 + m], rs("y", y, m), [b])
+        for i in order:
+            mix(l, "mix" + h, T.yy[:, 2 * n + i], ["y%d" % (2 * n + i)])
 
     def tokens(l):
-        if ",x," not in PLAN[l]:
-            mix(l, "mixx", T.m32[:], T.sx[:], ["m32", "sx"])
-        op("s", "new", lambda: S.activation(T.sx[:], M, Act.Sigmoid, bias=T.less[:, 0:1], scale=2.0), 256, blk("pM", 0, 5) + ["less"], ["sx"], ["pM"])
+        if "x" not in ADDS[l]:
+            mix(l, "mixx", T.sx[:], ["sx"])
+        op("s", "new", lambda: S.activation(T.sx[:], M, Act.Sigmoid, bias=T.less[:, 0:1], scale=2.0), 256, rs("pM_", 0, 5) + ["less"], ["sx", "mix%d" % (l + 1)], ["pM"])
         if l == NL - 1:
             op("s", "new", lambda: S.activation(T.xo[:], T.sx[:], Act.Identity, bias=-1.0, scale=2.0), 256, ["sx"], ["xo"])
-            dma("s", "new", "oyx", [(T.yx[:], T.xo[:])], ["xo"], ["yx"])
+            dma("s", "new", "oyx", [(T.yx[:], T.xo[:])], ["xo"], ["yx"], R["local"] + 0.4)
         else:
-            op("s", "newp", lambda: S.activation(X, T.sx[:], Act.Identity, bias=-1.0, scale=2.0), 256, ["sx"], blk(xb_, xj, 4), [xb_])
-            if ",f," in PLAN[l + 1]:
-                op("s", "news", lambda: S.activation(T.xo[:], T.sx[:], Act.Identity, bias=-1.0, scale=2.0), 256, ["sx"], ["xo"])
+            op("s", "newp", lambda: S.activation(X, M, Act.Sigmoid, bias=T.less[:, 0:1], scale=2.0), 256, rs("pM_", 0, 5) + ["less"], xb + ["mixp%d" % (l + 1)], ["pM", "pX"])
 
-    turns = (0, 2, 1, 3)
     for l in range(NL):
         layer[0] = l
+        steps(l)
         if l == 0:
-            for h, q in (("m", "v"), ("r", "s")):
-                for c in turns:
+            for h in "omab":
+                stand(h)
+            for h, how in (word.split(",") for word in EARLY.split()):
+                for c, q in enumerate(how):
                     raw(q, c, h)
-            for c in turns:
+            for c in range(4):
                 fused(c, "o")
-            for c, b, j in zip(turns[1:], ("pW", "pF", "pW"), (0, 0, 4)):
-                held(c, "m", b, j, 0)
-            for c, b in zip(turns[1:], ("pE", "pM", "pQ")):
-                held(c, "r", b, 0, 0)
-            op("t", "q", lambda: PE.matmul(T.pQ[:], ident, T.qall[:, tok(loc0, 2)], True, True), 512, ["wb"] + rs("q", loc0, 2), blk("pQ", 0, 8) + ["accpQ"], ["pQ"])
-            if NEW:
-                if "q" in "".join(w for k in KEYS for w in k.split() if w[0] == "r"):
-                    op("t", "qr", lambda: PE.matmul(T.pD[:], ident, T.qall[:, tok(rem0, 2)], True, True), 512, ["wb"] + rs("q", rem0, 2), blk("pD", 0, 8) + ["accpD"], ["pD"])
-                op("t", "less", lambda: PE.matmul(T.pM[:, 7, 0:2], T.mb[:], T.minus[:], True, True), 64, ["mb", "minus"], blk("pM", 0, 8), ["pM"])
-                op("s", "less", lambda: S.activation(T.less[:], T.pM[:, 7, 0:2], Act.Copy), 64, blk("pM", 0, 8), ["less"], ["pM"])
-                op("s", "x", lambda: S.activation(X, T.xb[:], Act.Copy), 256, ["xb"], blk(xb_, xj, 4), [xb_])
-            else:
-                op("t", "prep", [lambda: PE.matmul(T.pD[:, 7, 0:2], T.mb[:], T.minus[:], True, True), lambda: PE.matmul(X, ident, T.xb[:], True, True)], 160,
-                   ["wb", "xb", "mb", "minus"], blk("pD", 0, 4) + ["pD7", "accpD"], ["pD"])
+            for h, how in (word.split(",") for word in MEET.split()):
+                for c, x in enumerate(how):
+                    times(c, h, "ff" if h == "m" else "qq", x)
+            op("t", "less", lambda: PE.matmul(T.pM[:, 510:512], T.mb[:], T.minus[:, 0:2], True, True), 64, ["mb", "minus"], blk("pM", 0, 8), ["pM"])
+            op("s", "less", lambda: S.activation(T.less[:], T.pM[:, 510:512], Act.Copy), 64, blk("pM", 0, 8), ["less", "mix0"], ["pM"])
+            op("s", "x", lambda: S.activation(X, T.xb[:], Act.Identity, bias=0.5, scale=0.5), 256, ["xb"], xb, ["pX"])
             op("s", "prep", lambda: S.activation(T.m32[:], T.mb[:], Act.Copy), 128, ["mb"], ["m32"])
-            if not NEW:
-                op("s", "prep", lambda: S.activation(T.m4[:], T.mb[:], Act.Identity, scale=0.25), 128, ["mb"], ["m4"])
             op("s", "prep", lambda: S.activation(T.sx[:], T.xb[:], Act.Identity, bias=0.5, scale=0.5), 256, ["xb"], ["sx"])
-            if not NEW:
-                op("s", "prep", lambda: S.activation(T.less[:], T.pD[:, 7, 0:2], Act.Copy), 64, ["pD7"], ["less"], ["pD"])
         else:
             for h, how in (word.split(",") for word in KEYS[l].split()):
-                for c, x in zip(turns, how):
+                for c, x in enumerate(how):
                     if x == "f":
                         fused(c, h)
-                        continue
-                    raw("s", c, h)
-                    if x == "q":
-                        times(c, h)
                     else:
-                        held(c, h, "p" + x)
-        for step in PLAN[l].split():
-            name, *args = step.split(",")
-            {"judge": winners, "count": count, "pick": pick, "give": give, "tell": tell, "names": names, "biases": biases, "expert": expert}[name](l, *args)
+                        raw("s", c, h)
+                        times(c, h, how[c & 1::2])
+        halves = "rl" if l else "lr"
+        for h, b in zip(halves, ("pA", "pB")):
+            winners(l, h, b)
+        for k, (h, b) in enumerate(zip(halves, ("pA", "pB"))):
+            count(l, k, h, b)
+        if l < NL - 1:
+            names(l)
+        biases(l)
+        for word in PICKS[l].split():
+            pick(l, *word.split(","))
+        for word in GIVES[l].split():
+            give(l, word)
+        expert(l, "r", "pE")
+        expert(l, "l", "pG")
         tokens(l)
 
     issue(g, T, topo, core, calls)
@@ -565,7 +508,7 @@ def rank_program(g, core, T, topo):
 def arrange(calls):
     lastw, readers, before = {}, {}, []
     for i, c in enumerate(calls):
-        need = {lastw[r] for r in list(c["reads"]) + list(c["writes"]) if r in lastw}
+        need = {lastw[r] for r in list(c["reads"]) + list(c["writes"]) + c.get("behind", []) if r in lastw}
         for r in c["writes"]:
             need.update(readers.get(r, []))
         if "after" in c:
@@ -575,40 +518,27 @@ def arrange(calls):
             readers.setdefault(r, []).append(i)
         for r in c["writes"]:
             lastw[r], readers[r] = i, []
-    steps, lines = {}, []
+    steps, order, done = {}, [], set()
     for i, c in enumerate(calls):
-        if c["q"]:
-            steps.setdefault((c["q"],) + c["name"], []).append(i)
-        else:
-            lines.append([i])
-    for q in ORDER:
-        line = []
-        for l, words in enumerate(ORDER[q]):
-            for word in words.split():
-                name, _, n = word.partition("*")
-                rest = steps[(q, l - name.count("-"), name.lstrip("-"))]
-                line += [rest.pop(0) for _ in range(int(n) if n else len(rest))]
-        lines.append(line)
-    assert not any(steps.values()), [k for k in steps if steps[k]]
-    end, free, bank, order = {}, {}, {}, []
-    while any(lines):
-        best = None
-        for line in lines:
-            if line and all(j in end for j in before[line[0]]):
-                c = calls[line[0]]
-                t = max([free.get(c["q"], 0.0)] + [end[j] + calls[j]["late"] for j in before[line[0]]]
-                        + [e + HOP for b in c["banks"] for q, e in bank.get(b, {}).items() if q != c["q"]])
-                if best is None or t < best[0]:
-                    best = (t, line)
-        assert best, [calls[line[0]].get("name") for line in lines if line]
-        t, i = best[0], best[1].pop(0)
-        c = calls[i]
-        end[i] = t + c["busy"]
-        if c["q"]:
-            free[c["q"]] = end[i]
-        for b in c["banks"]:
-            bank.setdefault(b, {})[c["q"]] = end[i]
-        order.append(c)
+        if c["kind"] != "land":
+            steps.setdefault("%s%d%s" % (c["q"], *c["name"]), []).append(i)
+
+    def put(i):
+        if i not in done:
+            done.add(i)
+            for j in sorted(before[i]):
+                put(j)
+            order.append(calls[i])
+            for j, c in enumerate(calls):
+                if c.get("after") == i:
+                    put(j)
+    for word in ORDER.split():
+        name, _, n = word.partition("*")
+        rest = steps.get(name, [])
+        for _ in range(min(int(n or 99), len(rest))):
+            put(rest.pop(0))
+    for i in range(len(calls)):
+        put(i)
     return order
 
 
@@ -639,6 +569,8 @@ def issue(g, T, topo, core, calls):
                 need += [ev for ev in [lastw.get(r)] + readers.get(r, []) if ev and (ev[3], src) != ("t", "t")]
             for b in c["banks"]:
                 need += [ev for o, ev in bank.get(b, {}).items() if o != q]
+            if c["name"][1] == "late" and "cg" in count:
+                need.append(("cg", count["cg"], {}, "g"))
             for ev in sorted(need, key=lambda ev: -ev[1]):
                 wait(q, ev)
             if kind == "op":
@@ -653,7 +585,7 @@ def issue(g, T, topo, core, calls):
                     Q[q].dma_start(out, in_).then_inc(T.sem[sem], 16)
                 count[sem] = 16 * len(c["pairs"])
             else:
-                sem, tr = c["local"], []
+                sem, tr = "sent", []
                 for r, m, s, a, b in c["items"]:
                     rid, pid = topo.addr(T.cores[r], core)
                     tr.append(RemoteDMATransfer(dst_ids=[DstId(rid=rid, pnc=pid)], dma_engine_mask=m, remote_sem=T.sem[s], src=a, dst=b))

@@ -11,82 +11,62 @@ SCRATCH = {
     "xb": ("sbuf", [128, 256], BF), "mb": ("sbuf", [128, 128], BF), "m32": ("sbuf", [128, 128], F32),
     "less": ("sbuf", [128, 2], F32), "minus": ("sbuf", [128, 66], BF), "four": ("sbuf", [128, 64], BF),
     "xo": ("sbuf", [128, 256], F32), "sx": ("sbuf", [128, 256], F32),
-    "rawk": ("sbuf", [128, 4, 1024], BF), "prod": ("sbuf", [128, 1024, 4], F16), "quick": ("sbuf", [128, 64, 4, 16], F16), "zh": ("sbuf", [128, 144], F16),
-    "wb": ("sbuf", [128, 16, 16], BF), "wh": ("sbuf", [128, 16, 16], F16), "selb": ("sbuf", [128, 8, 4, 16], BF), "seln": ("sbuf", [128, 8, 4, 16], BF),
-    "half": ("sbuf", [128, 8], BF), "bdn": ("sbuf", [128, 128], BF), "bd": ("sbuf", [128, 128], F32), "hw": ("sbuf", [128, 2, 32], BF), "sg": ("sbuf", [128, 4, 256], F32),
-    "negh": ("sbuf", [128, 8, 16], F16),
-    "bdb": ("sbuf", [128, 128], BF), "fold": ("sbuf", [128, 8], F32), "wide": ("sbuf", [128, 32, 16], BF),
-    "sel": ("sbuf", [128, 8, 4, 16], F16), "c1": ("sbuf", [128, 128], BF), "c2": ("sbuf", [128, 128], F16),
-    "cbig": ("sbuf", [128, 256], BF), "hb": ("sbuf", [128, 256], BF),
-    "ramp": ("sbuf", [128, 64], BF), "none": ("sbuf", [128, 128], F32), "top": ("sbuf", [128, 256], F32), "keep": ("sbuf", [128, 256], F32), "run": ("sbuf", [128, 256], F16),
-    "w16": ("sbuf", [128, NL, 64], F16), "wu": ("sbuf", [128, NL, 64], U16), "wr": ("sbuf", [128, 2, 4, 64], F16),
+    "rawk": ("sbuf", [128, 4, 1024], BF), "prod": ("sbuf", [128, 1024, 4], F16), "quick": ("sbuf", [128, 64, 4, 16], F16),
+    "zh": ("sbuf", [128, 144], F16), "wb": ("sbuf", [128, 16, 16], BF), "wh": ("sbuf", [128, 16, 16], F16), "negh": ("sbuf", [128, 8, 16], F16),
+    "sel": ("sbuf", [128, 8, 4, 16], F16), "selb": ("sbuf", [128, 8, 4, 16], BF), "seln": ("sbuf", [128, 8, 4, 16], BF),
+    "bdb": ("sbuf", [128, 128], BF), "bd": ("sbuf", [128, 128], F32), "fold": ("sbuf", [128, 8], F32), "half": ("sbuf", [128, 8], BF),
+    "wide": ("sbuf", [128, 32, 16], BF), "c1": ("sbuf", [128, 128], BF), "c2": ("sbuf", [128, 128], F16),
+    "cbig": ("sbuf", [128, 256], BF), "hb": ("sbuf", [128, 256], BF), "ramp": ("sbuf", [128, 64], BF), "none": ("sbuf", [128, 128], F32),
+    "top": ("sbuf", [128, 256], F32), "keep": ("sbuf", [128, 256], F32), "run": ("sbuf", [128, 256], F16),
+    "w16": ("sbuf", [128, 2, 64], F16), "wu": ("sbuf", [128, NL, 64], U16), "wr": ("sbuf", [128, 2, 4, 64], F16), "hw": ("sbuf", [128, 2, 32], BF),
     "dv": ("sbuf", [128, 2, 8, 16], BF), "oh": ("sbuf", [128, 16, 8, 16], BF), "th": ("sbuf", [128, 16, 32, 4], BF),
     "bs": ("sbuf", [128, NL + 1, 2, 64], BF), "bout": ("sbuf", [128, 2, 64], F32),
     "i2": ("sbuf", [128, 2, 33], F32), "up": ("sbuf", [128, 2, 33], F16), "ee": ("sbuf", [128, 2, 33], F16),
     "near": ("sbuf", [128, NL * 2, 768], BF), "away": ("sbuf", [128, NL * 2, 512], BF), "came": ("sbuf", [128, NL * 2, 2, 256], BF),
-    "pu": ("sbuf", [128, 4, 256], F32), "yy": ("sbuf", [128, 4, 256], F32),
-    "sn": ("sbuf", [128, 2, 32], F32), "sq": ("sbuf", [128, 2, 128], BF), "sp": ("sbuf", [128, 2, 64], BF),
+    "pu": ("sbuf", [128, 4, 256], F32), "yy": ("sbuf", [128, 4, 256], F32), "sg": ("sbuf", [128, 4, 256], F32),
+    "sn": ("sbuf", [128, 2, 32], F32), "sp": ("sbuf", [128, 2, 64], BF), "sq": ("sbuf", [128, 2, 128], BF),
     "pA": ("psum", [128, 512], F32), "pB": ("psum", [128, 512], F32), "pF": ("psum", [128, 8, 64], F32),
     "pX": ("psum", [128, 512], F32), "pM": ("psum", [128, 512], F32), "pE": ("psum", [128, 512], F32),
     "pG": ("psum", [128, 512], F32), "pQ": ("psum", [128, 1024], BF),
 }
-SEMAPHORES = (["cv", "cs", "ct", "cg", "sent", "lq", "lnm", "lke", "lb", "lx", "lm", "lu", "lv", "aqm", "aqa", "aqb", "oyx", "oyb"]
+SEMAPHORES = (["cv", "cs", "ct", "cg", "sent", "lq", "lnm", "lke", "lb", "lx", "lm", "lu", "lv", "aqm", "aqa", "aqb", "oyx0", "oyx1", "oyb"]
               + ["aw%d" % l for l in range(2)] + ["bias%d" % l for l in range(2)]
               + ["a%d%s%s" % (l, k, h) for l in range(NL) for k in "uv" for h in "abm"])
 ROUND64 = 1.5 * 2.0 ** 13
 ROUND2048 = 1.5 * 2.0 ** 18
 ROUND4096 = 1.5 * 2.0 ** 35
 EDGE = math.log(4095.0)
+RISE = 65536.0
 
-KEYS = ["r,qqqq l,ffff", "r,fqfq l,fqfq", "r,fqfq l,fqfq"]
-EARLY, MEET = "r,svsv m,ssss", "m,qqqq a,qqqq b,dddd"
-QS = "a b.m"
-TURNED, COPIES, FORMS = "sss", ["vv", "vv", "vv"], ["nn", "nn", "ww"]
-PICKS = ["ur,s vr,s ul,v vl,s", "ur,s vr,s ul,v vl,s", "ur,s vr,s um,v uo,v vm,s vo,s"]
-GIVES = ["ua.ub.um va.vb.vm+", "ua.ub.um va.vb.vm+", "ua ub um.vm va vb"]
-ADDS = ["", "", "p"]
-ROUGH = dict(cycle=0.9e-3, tensor=0.46e-3, v=0.03, s=0.05, gather=1.5, hop=0.2, local=1.6, issue=0.35, flight=1.1, first=2.2, port=1.0, wake=0.35)
-BOOST, PASSES, PLANNED = {}, 1, [0.0]
-KINDS = {
-    "S": "load qa qb qm fill",
-    "R": "dn k0r k1r k2r k3r f0r f1r f2r f3r h1r h2r h3r x0r x1r x2r x3r x1a x2a x3a x1b x2b x3b s0r s2r w1r w2r w3r w5r",
-    "L": "k0m k1m k2m k3m f0o f1o f2o f3o h1m h2m h3m x1m x2m x3m k0l k1l k2l k3l f0l f1l f2l f3l x0l x1l x2l x3l s0l s2l w1l w2l w3l w5l",
-    "C": "hi0 dv0 ng0 oh0 th0 sum0", "D": "hi1 dv1 ng1 oh1 th1 sum1 blo Tb post Tu Te bias",
-    "N": "w4l w4r tell nA nB hb nn off q1l q2l q3l q1r q2r q3r",
-    "U": "Ur Ua Ub ua ub ua.ub", "V": "Vr Va Vb va vb va.vb", "M": "Ul Um Uo Vl Vm Vo um vm um.vm um.vm.va.vb+ um.vm+ va.vb+",
-    "X": "late less x prep mixx pur Dr sgr smr sdr Er yyr adr mixr", "Y": "pul Dl sgl sml sdl El yyl adl mixl new newp",
-}
-ORDER = """
-y0load*1 v0fill*1 g0late*1 y0load*1 v0fill*1 y0load*1 v0fill*1 g0fill*1 v0fill*2 g0fill*1 v0fill*5 g0fill v0fill*2 g0qa v0fill*1 s0fill*1 v0fill*3 g0qb v0fill*1 g0qm v0fill t0dn v0k1m s0k1r v0k0m s0k0r v0k2m t0h1m v0f0o t0h2m s0k3r v0k3m t0h1r v0f3o t0h3m s0k2r v0f1o t0h3r v0f2o y0load*1 g0late*1 t0q1l s0fill y0load*3 v0x1m t0h2r y0load v0x3m v0x2m t0s0l v0x3a v0q2l t0s2l v0x1a t0q1r v0x1b t0q3l v0x3b s0x g0late t0s0r v0w1l s0prep*1 v0x2a s0prep v0x2b v0w2l t0s2r v0w3l v0q2r t0hi0 v0w5l v0w1r t0less v0w4l s0dv0 v0w2r s0less v0w3r t0ng0 v0oh0*1 t0q3r v0oh0*2 s0th0*1 v0oh0*1 t0hi1 v0w4r s0th0*1 v0oh0*2 s0th0*1 v0oh0*1 g0tell t0mixx v0w5r s0th0*1 v0oh0 v0Ul s0th0*1 s0dv1 s0th0*2 t0ng1 t0Tb s0th0 v0oh1*2 s0Ur v0oh1*2 t0sum0 v0oh1 v0pul*1 t0nA s0th1*2 g0ua.ub.um s0th1 s0Vr t0sum1 t0nB v0post*3 t0Tu s0hb t0Te s0Vl v0post v0pul y0bias v0nn v0off t1dn v0pur t0Dr g0va.vb.vm+ s1k3r v1f1r t0Dl*1 v1f0r s1k3l t0Dl v1x3r s0sgr t1s0r s0sgl v1f2r s1k1l v0sml*1 s1k0l v0sml v0smr*1 t1s2r v0smr v1x3l v0sdl v0sdr s1k2l v1x1l t0Er v1w1r v1x0l t0El v1w2r t1s0l v1w3r v1x2l t1hi0 v0yyl t1s2l s1dv0 v1w5r v1w4r v0yyr s1Ur t0mixl*1 v1w1l t1ng0 v1oh0*2 t0mixl v1w2l s1th0*1 v1oh0*2 s1th0*1 v1w3l s1th0*1 t0mixr*1 v1oh0*2 s1th0*1 v1w4l v1w5l s1th0*1 v1oh0 g1tell s1th0*1 t1hi1 v1Ul s1th0*1 t0mixr s1dv1 s1th0 t1ng1 v1oh1*2 g1ua.ub.um v1oh1*1 t1nA s0new v1oh1*3 s1th1*1 v1oh1 s1th1*1 t1mixx s1th1*3 t1sum0 s1th1 s0newp t1sum1 s1Vl v1pul*1 t1Tb t1nB v1post*3 t1Tu v1pul s1hb t1Te v1post s1Vr v1nn y1bias s2blo v1pur*1 v1off v1pur t1Dr g1va.vb.vm+ v2f1r s2k1l t2dn v2f0r s1sgr s2k3r t1Dl*1 v2f2r t1Dl s2k2l t2s0r v2x3r s1sgl s2k0l v2x1l t2s2r v2x2l v1sml v1smr*1 s2k3l v1smr v1sdl v2w1r v1sdr t1El v2x0l t1Er v2w2r v2x3l t2s0l v2w3r t2s2l v2w5r v1yyl s2Ur t2hi0 v2w1l t1mixl*1 v2w2l s2dv0 s2Vr g2ua v2w3l t2ng0 v1yyr t1mixl g2ub v2w5l s2th0*1 v2oh0*1 t2hi1 v2oh0*1 s2th0*1 g2va v2Um s2th0*1 t1mixr*1 s2Vm g2vb v2oh0*4 t1mixr s2dv1 v2oh0 s2th0*1 g2um.vm s2th0*1 v2oh1*2 t2ng1 s2th0*1 v2oh1*2 s2th0*1 v2oh1*2 s2th0 v2oh1 s1new v2Uo t2sum0 s2th1*3 t2mixx s2th1 s1newp t2Tb t2sum1 s2Vo v2pur t2Dr*1 v2pul*1 t2Dr v2pul t2Dl s2sgr s2sgl v2smr v2sml v2sdr v2post*2 v2sdl t2Er v2post*1 t2Tu t2El v2yyr*1 t2Te v2yyr v2yyl v2adr v2post v2adl t2mixr y2bias t2mixl s2new
-"""
-
-
-ORDER = """
-y0load*1 v0fill*1 g0late*1 y0load*2 v0fill*2 g0fill*1 v0fill*5 g0fill*1 v0fill*3 g0fill v0fill*3 g0qa s0fill*1 v0fill*2 g0qb v0fill*2 g0qm v0fill t0dn s0k0r v0k0m v0k1m s0fill v0k2m s0k3r t0h1m v0f1o t0h2m v0k3m s0k1r t0h3r v0f3o t0h3m s0k2r v0f2o t0h1r v0f0o y0load*1 g0late*1 t0q1l y0load*3 v0x1m y0load t0h2r v0x2m v0x3m t0s0l v0x3a v0q2l t0s2l v0x1a v0x2a t0q3l v0x1b t0q1r s0x g0late v0w1l s0prep*1 v0x2b t0s0r s0prep v0x3b v0w2l t0s2r v0w3l v0q2r t0hi0 v0w4l v0w5l v0w1r t0less t0q3r s0dv0 v0w2r s0less v0w3r t0ng0 v0oh0*1 t0mixx v0oh0*2 s0th0*1 v0oh0*1 v0w4r s0th0*1 v0oh0*2 s0th0*1 t0hi1 v0w5r g0tell v0oh0*1 s0th0*1 v0oh0 v0Ul s0th0*2 s0dv1 s0th0 t0ng1 v0oh1*1 t0Tb v0oh1*1 s0Ur v0oh1*2 t0nA v0oh1 v0pul*1 t0sum0 s0th1*2 g0ua.ub.um s0th1 s0Vr t0sum1 t0nB v0post*3 t0Tu s0hb t0Te s0Vl v0post v0pul y0bias v0nn v0off t1dn v0pur t0Dr g0va.vb.vm+ s1k3r v1f0r t0Dl*1 v1f1r s1k1l t0Dl v1x3r s0sgr t1s0r s0sgl v1f2r s1k3l v0sml*1 s1k0l v0smr t1s2r v0sml v1x1l v0sdr v0sdl s1k2l v1x3l v1x0l t0El v1w1r t0Er t1s0l v1w2r v1w3r v1x2l t1hi0 v1w5r v0yyl t1s2l s1dv0 s1Ur v1w4r t1ng0 t0mixl*1 v1w1l v0yyr s1th0*1 t0mixl s1th0*1 v1w2l s1th0*1 v1oh0*2 s1th0*1 v1w3l t0mixr*1 s1th0*1 v1oh0*2 s1th0*1 v1w4l v1oh0*1 s1th0*1 v1w5l t1hi1 v1oh0*1 g1tell s1th0 v1oh0 v1Ul t0mixr s1dv1 t1ng1 t1nA s0new v1oh1*3 g1ua.ub.um v1oh1*1 s1th1*1 t1sum0 v1oh1*2 s1th1*1 v1oh1 s1th1*2 t1mixx s1th1 s0newp t1sum1 s1Vl v1pul*1 t1Tb t1nB v1post*3 t1Tu s1hb t1Te v1post s1Vr v1pul y1bias v1nn s2blo v1off t2dn v1pur t1Dr s2k3r g1va.vb.vm+ v2f1r t1Dl*1 v2f0r s2k2l t1Dl v2x3r s2k1l t2s0r v2f2r s1sgl s1sgr s2k0l v2x2l t2s2r v1smr v1sml v2x1l s2k3l v1sdr v2x0l t1Er v2w1r t2s0l v1sdl v2w2r v2x3l t1El v2w3r t2s2l v2w5r v1yyl s2Ur t2hi0 v2w1l t1mixl*1 v2w2l s2dv0 s2Vr v2w3l g2ua t1mixl v2oh0*2 v2w5l g2ub v1yyr t2ng0 t2hi1 s2Vm v2Um g2va t1mixr*1 s2th0*1 v2oh0*1 s2dv1 v2oh0*2 g2um.vm s2th0*1 v2oh0*1 t1mixr v2oh0*1 s2th0*1 v2oh0 v2oh1*1 s2th0*1 g2vb v2oh1*3 t2ng1 v2oh1*2 t2Tb s1new v2oh1 v2Uo s2th0*1 s1newp t2mixx s2th0*2 v2pur*1 s2th0 v2pul*1 s2th1*2 t2Dr*1 s2th1*3 v2pur s2th1 t2Dr s2Vo t2Dl*1 v2pul t2Dl t2sum0 s2sgl s2sgr t2sum1 v2smr v2sml v2sdr v2sdl t2Er v2post*2 t2El v2post*1 v2yyr*1 t2Tu t2Te v2yyr v2yyl v2adr v2post v2adl t2mixr y2bias t2mixl s2new
-"""
-
-
-ORDER = """
-y0load*1 v0fill*1 g0ramp y0load*1 v0fill*1 y0load*1 v0fill*1 g0fill*1 v0fill*3 v0ramp g0late*1 v0fill*3 g0fill*1 v0fill*4 s0fill*1 v0fill*1 g0fill g0qa v0fill*2 g0qb v0fill*2 g0qm v0fill*1 s0fill v0fill t0dn v0k1m s0k0r v0k0m s0k3r v0k3m t0h1m v0k2m t0h3m s0k1r v0f1o t0h3r v0f3o t0h2m s0k2r v0f2o t0h1r v0f0o y0load*1 g0late*1 t0q1l y0load*3 v0x2m t0h2r y0load v0x3m v0x1m t0s0l v0q2l v0x1a t0s1l v0x2a v0x3a t0q1r v0x2b s0x t0q3l g0late v0w1l s0prep*1 v0x3b t0s0r s0prep v0x1b v0w2l t0less t0s1r s0less v0w3l v0q2r t0hi0 v0w4l v0w5l v0w1r t0q3r s0dv0 v0w2r v0oh0*1 t0ng0 v0oh0*1 t0mixx v0w3r v0oh0*1 s0th0*1 v0oh0*2 s0th0*1 v0w4r v0w5r s0th0*1 t0hi1 v0oh0*2 s0th0*1 g0tell v0oh0 v0Ul s0th0*2 s0dv1 s0Ur t0ng1 v0oh1*1 t0Tb v0oh1*6 s0th0*1 v0oh1 v0pul*1 s0th0 g0ua.ub.um s0th1*2 t0nA s0th1*2 t0sum0 s0th1 s0Vr t0sum1 t0nB v0post*3 t0Tu s0hb t0Te s0Vl v0post v0nn y0bias v0pul v0off v0pur t0Dr g0va.vb.vm+ s1k3r v1f2r t0Dl v1f0r s1k1l t1dn v1x3r s0sgl s0sgr t1s0r s1k3l v1f1r s1k0l v0smr v0sml*1 t1s1r v0sml v1x1l v0sdr v0sdl s1k2l v1x3l t0Er v1w1r t0El v1x0l v1x2l v1w2r t1s0l v1w3r v1w5r t1s1l v1w4r v0yyl s1Ur t1hi0 v1w1l t0mixl*1 s1dv0 v1w2l v0yyr t1ng0 t0mixl s1th0*1 v1w3l s1th0*1 v1oh0*2 s1th0*1 v1w4l t1hi1 v1oh0*1 s1th0*1 v1w5l v1oh0*1 g1tell s1th0*1 t0mixr*1 v1oh0*2 s1th0*1 v1oh0 s1dv1 v1Ul s1th0*1 t0mixr s1th0 t1ng1 v1oh1*1 t1nA v1oh1*1 s0new v1oh1*1 g1ua.ub.um v1oh1*2 s1th1*1 v1oh1*1 t1sum0 v1oh1*1 s1th1*1 v1oh1 s1th1*2 t1mixx s1th1 s0newp t1sum1 s1Vl v1pul*1 t1Tb t1nB v1post*3 t1Tu s1hb t1Te v1post s1Vr v1pul y1bias v1nn s2blo v1off t2dn v1pur t1Dr s2k3r g1va.vb.vm+ v2f2r t1Dl v2f0r s2k2l v2x3r s2k1l t2s0r v2f1r s1sgl s1sgr s2k0l v2x2l t2s1r v1smr v1sml v2x1l s2k3l v1sdr v2x0l t1Er v2w1r v1sdl t2s0l v2w2r v2x3l t1El v2w3r t2s1l v2w5r v1yyl s2Ur t2hi0 v2w1l t1mixl*1 v2w2l s2dv0 s2Vr g2ua v2w3l t2ng0 v2oh0*2 t1mixl g2ub v2w5l v1yyr s2th0*1 t2hi1 s2Vm g2va v2Um t1mixr*1 s2dv1 v2oh0*2 s2th0*1 v2oh0*1 g2um.vm v2oh0*1 t1mixr s2th0*1 v2oh0 s2th0*1 v2oh1*1 g2vb v2oh1*3 t2ng1 v2oh1*2 t2Tb s1new v2oh1 v2Uo s2th0*1 s1newp t2mixx s2th0*2 v2pur*1 s2th0 v2pul*1 s2th1*2 t2Dr*1 s2th1*3 v2pur s2th1 t2Dr s2Vo t2Dl*1 v2pul t2Dl t2sum0 s2sgl s2sgr t2sum1 v2smr v2sml v2sdr v2sdl t2Er v2post*2 t2El v2post*1 v2yyr*1 t2Tu t2Te v2yyr v2yyl v2adr v2post v2adl t2mixr y2bias t2mixl s2new
-"""
-
-
-ORDER = """
-y0load*1 v0fill*1 g0late*1 y0load*1 v0fill*1 y0load*1 v0fill*1 g0fill*1 v0fill*4 g0fill*1 v0fill*2 g0fill v0fill*6 g0qb s0fill*1 v0fill*2 g0qa v0fill*1 g0ramp v0fill*1 g0qm v0fill v0ramp t0dn v0k0m s0k1r v0k1m s0k0r v0k3m t0h1m v0k2m t0h3m s0k3r v0f1o t0h2m v0f0o t0h1r s0k2r v0f3o t0h3r v0f2o y0load*1 g0late*1 t0q1l s0fill y0load*3 v0x2m t0h2r y0load v0x3m v0x1m t0s0l v0x1b v0q2l t0s1l v0x2b v0x2a t0q3l v0x1a s0prep*1 t0q1r g0late v0x3a t0s0r s0x v0w1l s0prep v0x3b v0w2l v0q2r t0less t0s1r s0less v0w3l v0w4l t0hi0 v0w5l v0w1r t0lo0 v0w2r s0dv0 v0w3r t0ng0 t0q3r v0oh0*2 s0th0*1 v0oh0*1 t0hi1 v0oh0*1 s0th0*1 v0w4r v0oh0*1 s0th0*1 v0w5r v0oh0*1 t0lo1 g0tell s0th0*1 v0oh0*1 v0Ul s0th0*1 t0mixx s0dv1 s0Ur t0ng1 t0Tb v0oh1*3 v0oh0 v0oh1*2 s0th0*1 v0oh1*2 s0th1*1 g0ua.ub.um v0oh1 v0pul*1 s0th0 s0th1*2 t0sum0 s0th1 s0Vr t0sum1 t0nA v0post*3 t0Tu v0pul t0Te t0nB v0post y0bias s0hb s0Vl v0nn v0pur*1 v0off v0pur t0Dr t0Dl*1 g0va.vb.vm+ s1k3r v1f2r t0Dl v1f0r s1k1l t1dn v1f1r s0sgl s0sgr t1s0r s1k0l v1x3r s1k2l v0sml v0smr*1 t1s1r v0smr v1x1l v0sdr v0sdl s1k3l v1x0l t0El v1x2l t0Er v1w1r t1s0l v1x3l v1w2r t1s1l v1w3r v0yyl t1hi0 v1w1l t1lo0 v1w5r s1dv0 v1w2l t0mixl*1 s1Ur v1w4r v1w3l v1oh0*2 t1ng0 v1w4l t1hi1 v1oh0*2 s1th0*1 v1oh0*1 g1tell v1w5l t0mixl s1th0*1 v1oh0*2 s1th0*1 v0yyr s1dv1 t1lo1 s1th0*2 v1Ul t1ng1 s1th0*1 t1Tb t0mixr*1 s1th0 s1th1*1 v1oh0 s1th1*1 t0mixr v1oh1*2 s1th1*1 g1ua.ub.um v1oh1*2 s1th1*1 v1oh1*2 s1th1*1 t1sum0 v1oh1 s1th1 s0new t1sum1 s1Vr t1nA v1post*2 s0newp v1post*1 t1Tu t1Te t1nB v1post v1pul*1 t1mixx y1bias s1hb v1pul s1Vl v1nn v1off s2blo v1pur t1Dr*1 g1va.vb.vm+ s2k3r v2f2r t2dn t1Dr v2f0r s2k2l t1Dl v2x3r s2k1l v2f1r t2s0r s1sgr s1sgl s2k0l v2x2l t2s1r v1smr v1sml v2x1l s2k3l v1sdr v2x0l t1Er v2w1r v1sdl t2s0l v2w2r v2x3l t1El v2w3r t2s1l v2w5r v1yyl s2Ur t2hi0 v2w1l t2lo0 v2w2l s2dv0 t1mixl*1 s2Vr g2ua v2w3l v2oh0*2 g2ub v2oh0*1 t2ng0 v2oh0*1 t1mixl v2w5l v1yyr s2th0*1 s2Vm g2va t2hi1 v2Um g2vb t2lo1 s2dv1 v2oh0*2 t1mixr*1 s2th0*1 g2um.vm s2th0*1 v2oh1*2 s2th0*1 v2oh1*2 t2ng1 v2oh1*1 t2Tb v2oh1*1 t1mixr v2oh1*1 s2th1*1 v2Uo s2th1*2 v2oh0*1 s2th1*1 v2oh0 v2oh1 s1new s2th1*1 t2mixx s1newp s2th1*2 v2pur*1 s2th1 v2pul*1 s2th0*2 t2Dr*1 v2pur s2th0 s2Vo t2Dr t2Dl*1 v2pul t2Dl t2sum0 s2sgl s2sgr t2sum1 v2smr v2sml v2sdr v2sdl t2Er v2post*2 t2El v2post*1 v2yyr*1 t2Tu t2Te v2yyr v2yyl v2adr v2post v2adl t2mixr y2bias t2mixl s2new
-"""
-
-
+QUERIES = "a b.m"
 KEYS = ["r,qqqq l,ffff", "r,fqfq l,fqqq", "r,fqfq l,fqqq"]
-PICKS = ["ur,v vr,s ul,v vl,s", "ur,s vr,v ul,v vl,s", "ua,s ub,s vr,s um,v uo,v vm,s vo,s"]
-GIVES = ["ua.ub.um va.vb.vm+", "ua.ub va.vb.um vm", "ua ub um va vb vm"]
-ADDS = ["", "", ""]
+EARLY, MEET = "r,ssss m,svsv", "m,dddd a,qqqq b,qqqq"
+PICKS = ["ur,v vr,s ul,s vl,s", "ur,s vr,s ul,v vl,s", "ua,s ub,s vr,s um,v vm,s"]
+GIVES = ["ua.ub.um va.vb.vm+", "ua.ub va.vb um vm", "ua ub um va vb vm"]
+PAIRED = (0,)
 ORDER = """
-y0lq v0minus g0ramp y0lnm v0keep y0lke v0bdb v0wb g0late*1 v0wide v0cbig g0wb v0ramp v0c2 v0none v0four v0zh*1 g0bdb*1 v0neg v0wh v0negh v0sel g0qa t0q1o g0bdb v0nm0 g0qb.m v0off*1 s0fold t0dn v0q2o v0zh t0q3o s0k3m v0f0o v0f1o s0k2m v0f3o s0k0m v0k1r s0k0r v0k3r s0k2r t0q1a s0k1m g0late*1 t0q1m y0lm y0lx y0lb y0lu y0lv v0q2m v0f2o t0q3m v0x0m v0x2m g0late v0q2a v0x2b t0q3a v0x0b t0s0l v0x3m s0prep*1 v0x1m v0x0a t0less v0x1a t0s1l v0x2a s0prep v0x3b s0x v0x1b t0s0r s0less v0x3a v0w1l t0s1r v0w2l v0w3l t0q1b v0w1r t0hi0 v0q2b v0w2r t0lo0 v0w5l s0dv0 v0w3r t0q3b t0ng0 v0w4 t0hi1 v0oh0*1 s0th0*1 v0w5r g0tell v0Ul t0Tb t0lo1 s0th0*1 s0dv1 s0th0*1 v0Ur t0ng1 t0mixx s0th0 s0th1*1 v0oh0*1 s0th1*1 v0oh0*1 g0ua.ub.um v0oh0 s0th1*1 v0oh1*2 t0sum0 s0th1 v0oh1 s0Vl v0pul*1 t0sum1 t0nA s0Vr v0post*3 t0Tu t0Te t0nB v0post t0Dl*1 y0bias v0pul s0hb t0Dl v0nn s0sgl t1dn v0sml v0off v0sdl v0pur*1 t0Wl v0pur s0sql t0Dr*1 g0va.vb.vm+ v1f0r s1k1r t0Dr t0El v1f2r s1k3r v1x1r s0sgr s1k2l t1s0r v1x3r v1f0l t1s1r s1k1l v1x2l v1w1r s1k3l v0smr*1 t1s0l v0smr v1w2r v0sdr v1w3r t0Wr v1x1l t1hi0 s0sqr v1w5r v1x3l s1Ur t0Er v0yyl t1s1l v0yyr s1dv0 t1lo0 g1ua.ub t1ng0 v1w1l t0mixl*1 v1oh0*1 s1th0*1 v1w2l v1oh0*1 s1th0*1 t0mixl v1w3l v1oh0*1 s1th0*1 v1w4 v1w5l t1hi1 v1Vr s1th0 g1tell t1lo1 s1dv1 v1Ul t1ng1 t0mixr*1 s1th1*2 t0mixr v1oh0 v1oh1*1 g1va.vb.um s1th1*1 v1oh1*1 t1Tb t1sum0 v1oh1*1 s0new v1oh1 s1th1 s0newp t1sum1 s1Vl v1pur t1Dr*1 v1post*2 v1pul*1 t1Dr g1vm t1nA v1post*1 s1sgr t1Tu t1Te t1nB v1pul v1post t1Dl*1 v1smr s1hb y1bias t1Dl v1sdr s2blo t1Wr v1nn s1sgl t1mixx s1sqr v1sml v1off t1Er v1sdl t1Wl t2dn s1sql v1yyr t1El s2k1r v2f0r t1mixr v2f2r s2k3r v2x1r s2k2l t2s0r v2x3r v1yyl t2s1r s2k3l v2x2l t1mixl*1 v2w1r s2k1l v2w2r t1mixl v2w3r v2w5r t2hi0 v2f0l s2Ua t2lo0 s1new v2x1l g2ua s2dv0 t2s0l v2x3l s1newp v2oh0*1 s2Ub v2oh0*1 t2s1l v2oh0 s2Vr g2ub t2ng0 t2mixx v2w1l v2w2l s2th0*1 g2va v2w3l s2th0*1 g2vb v2w5l t2hi1 v2Um s2Vm t2Tb t2lo1 s2dv1 v2pur*1 g2um s2th0*1 v2Uo t2ng1 s2th0 t2Dr*1 g2vm s2th1*2 v2pur v2oh1*2 t2Dr v2pul*1 t2sum0 v2oh1*1 s2sgr s2th1*1 v2smr t2Dl*1 s2Vo v2sdr s2th1 t2Wr v2pul s2sqr v2oh1 t2Dl t2Er s2sgl t2sum1 v2sml v2yyr*1 v2sdl v2post*2 v2yyr t2Wl t2mixr*1 s2sql v2post*1 t2El t2Tu t2Te t2mixr v2yyl*1 v2post v2yyl t2mixl*1 y2bias t2mixl s2new
-"""
+y0lq g0ramp v0wb y0lnm y0lke v0none v0cbig v0minus g0wb v0bdb v0four v0ramp v0zh*1 v0keep v0wide v0wh v0negh v0sel g0qa t0q1o
+g0bdb*1 v0nm0 v0off*1 g0bdb v0q2o t0dn v0selb v0seln t0q3o g0qb.m v0bd g0late*1 v0k3m s0k2m v0zh s0k0m v0f2o s0k0r v0f3o v0f0o
+s0k2r v0k1m t0q1a s0k3r v0q2a g0late*1 y0lm y0lx v0x2m y0lu y0lb y0lv v0x0m t0q3a t0q1b s0k1r v0x1m v0q2b v0x3m g0late v0f1o
+t0q3b t0s0l v0x2b v0x0a t0s1l v0x0b s0x v0x2a v0x3b s0prep*1 v0x1b s0fold t0less v0x1a t0s0r v0x3a v0w1l t0s1r v0w2l v0c2 v0w3l
+v0w1r s0prep v0up0 t0lo0 v0w5l v0w2r t0hi0 s0Ul t0ng0 v0w3r v0dv0 v0w4 v0w5r s0th0*1 v0up1 t0lo1 v0oh0*1 g0tell s0th0*1 v0Ur
+t0ng1 s0th0*1 t0hi1 s0th0 v0oh0*1 s0th1*1 v0dv1 g0ua.ub.um v0oh0*1 s0th1*1 v0oh0 t0Tb v0oh1*1 t0q1m s0th1*1 v0oh1*1 t0sum0
+v0oh1*1 s0th1 v0oh1 v0pul*1 s0less s0Vr v0half v0q2m t0sum1 t0Dl*1 s0Vl v0post*1 t0nA v0post*2 t0q3m v0pul t0Tu t0Te t0nB
+v0post t0Dl v0pur*1 s0hb v0pur y0bias t0Dr*1 s0sgl v0nn t0Dr v0sml v0off t1dn s0sgr v0sdl t0Wl t0mixx
 
+v1f2r s1k3r g0va.vb.vm+ v1f0r s1k1r v1x3r s0sql s1k2l t1s0r v1x1r v0smr v1f0l t1s1r s1k3l t0El v0sdr v1w1r s1k1l v1x2l t0Wr
+v1w2r v1x3l t1s0l s0sqr v1w3r v1x1l t0Er v1w5r v0yyl*1 t1s1l v0yyl s1Ur v1up0 v0yyr*1 t1lo0 v1w1l s1Vr t1hi0 v0adl t1ng0
+g1ua.ub v1w2l v0yyr t0mixl v1w3l s1th0*1 v1dv0 v0adr s1th0*1 v1up1 t1lo1 v1w4 s1th0*1 v1w5l v1oh0*1 t1ng1 v1oh0*1 s1th0 g1tell
+v1Ul t1hi1 g1va.vb t0mixr s1th1*2 v1dv1 v1oh0*1 s1th1*1 g1um v1oh0 t1Tb v1oh1*1 s0newp v1oh1*1 t1sum0 v1oh1*1 s1th1 v1oh1
+v1pul*1 s0new v1pur*1 t1sum1 v1pur t1Dr*1 v1post*1 t1Dr v1post*1 t1Dl*1 v1post*1 v1pul s1sgr t1Tu s1Vl t1Te t1nA v1post t1Dl
+v1smr t1nB y1bias v1sdr s1sgl g1vm s2blo t1Wr t1mixx v1sml*1 s1hb v1sml s1sqr v1sdl v1nn t1Er t1Wl v1off t2dn v1yyr s1sql
 
-ORDER = """
-y0lq g0ramp v0wb y0lnm y0lke v0minus v0four v0keep v0none g0wb v0cbig v0bdb v0ramp v0wide v0zh*1 g0bdb*1 v0negh v0wh v0sel t0q1o g0qa g0bdb v0q2o v0nm0 g0qb.m t0q3o v0off*1 s0fold v0seln t0dn g0late*1 v0bd v0bdn v0zh v0half v0selb v0c2 v0f0o s0k1m v0f2o v0f3o s0k3m v0f1o s0k0m v0k3r s0k2m s0k2r t0q1a g0late*1 t0q1m y0lm y0lx y0lb s0k0r y0lu y0lv v0q2m v0q2a v0k1r t0q3a t0q3m g0late v0x0m t0less s0prep*1 v0x2m v0x1m v0x3m s0x v0x1a t0s0l v0x2b s0less s0prep v0x0a v0x2a t0s1l v0x0b v0x3a v0x3b t0s0r v0x1b v0w1l t0s1r v0w2l t0q1b v0w3l v0w1r v0up0 t0lo0 v0q2b v0w2r t0hi0 v0w5l v0w3r t0ng0 v0dv0 t0q3b v0w4 v0up1 s0th0*1 v0w5r v0Ul t0lo1 g0tell s0th0*1 t0ng1 s0th0*1 t0hi1 v0Ur s0th0 t0Tb t0mixx s0th1*2 v0oh0*1 v0dv1 s0th1*1 g0ua.ub.um v0oh0*2 s0th1 v0oh0 v0oh1*1 s0Vl v0oh1*1 t0sum0 v0oh1 v0pul*1 s0Vr t0sum1 t0nA v0post*2 t0nB v0post*1 v0pul t0Tu t0Te s0hb t0Dl*1 v0post t0Dl v0nn y0bias s0sgl v0off t1dn v0sml v0sdl v0pur t0Wl t0Dr*1 s1k1r g0va.vb.vm+ v1f2r t0Dr v1f0r s1k3r v1x1r s0sgr s1k2l t1s0r v1x3r v1f0l t1s1r s1k1l v1x2l s1k3l v1w1r v0smr*1 t1s0l v0smr v1w2r v1x1l s0sql v0sdr v1w3r v1x3l t0Wr t0El v1w5r v1up0 s0sqr t1s1l s1Ur v0yyl t1hi0 v1w1l t0Er g1ua.ub t1lo0 v1w2l v1dv0 t1ng0 v1w3l t0mixl*1 v0yyr s1th0*1 t1lo1 v1up1 s1th0*1 v1w5l v1w4 v1oh0*1 s1th0*1 t1ng1 v1oh0*1 g1tell v1Vr s1th0 t1hi1 s1th1*1 t0mixr*1 s1th1*1 v1dv1 v1oh0*1 t0mixr s1th1*1 v1oh0 v1oh1*1 s1th1 v1oh1*1 t0mixl v1oh1 v1Ul t1sum0 s0newp t1sum1 s1Vl v1pur*1 g1va.vb.um t1Tb t1nA s0new v1post*2 t1nB g1vm v1post*1 v1pur t1Tu v1pul*1 t1Te t1Dr*1 s1hb v1post t1Dr v1nn t1Dl*1 y1bias s2blo s1sgr t1mixx v1pul v1smr v1off t1Dl v1sdr t2dn t1Wr s1sgl s1sqr v1sml s2k1r v2f2r t1Er s2k3r v1sdl v1yyr t1Wl v2f0r s1sql t1mixr*1 s2k2l v2x1r t1El v2x3r t2s0r s2k1l v1yyl t2s1r v2f0l s2k3l t1mixr v2w1r t1mixl*1 v2x2l v2w2r t1mixl v2x1l v2w3r v2x3l t2s0l v2w5r s1newp v2up0 t2s1l s2Ua s2Ub t2hi0 g2ua v2w1l t2lo0 s2Vr g2ub t2ng0 v2w2l v2dv0 v2w3l s1new v2oh0*1 s2th0*1 g2va v2w5l t2lo1 v2up1 v2oh0*1 s2th0*1 g2vb v2Uo t2hi1 s2th0*1 s2Vm v2Um t2Tb t2ng1 t2mixx v2pul*1 s2th0 v2dv1 g2um s2Vo v2oh0*1 t2Do v2oh0 g2vm v2pur*1 v2oh1*2 t2Da v2oh1*1 v2pur s2sgo v2oh1 s2th1*1 t2Db v2smo s2th1*2 v2pul t2sum0 s2th1 v2yyo s2sgb s2sga t2Dm v2sma t2sum1 v2smb s2sgm v2yya t2mixo v2yyb v2post*1 v2smm t2mixa v2post*2 v2yym t2mixb t2Tu t2Te t2mixm v2post y2bias s2new
+s2k3r t1El v2f2r t1mixr*1 s2k1r v2f0r t1mixr s2k2l v2x3r v2x1r t2s0r v1yyl s2k3l t2s1r v2f0l s2k1l t1mixl*1 v2w1r t1mixl v2x2l
+v2w2r v2x3l t2s0l v2w3r s1new v2x1l v2w5r v2up0 s1newp t2s1l s2Ua t2hi0 s2Ub t2lo0 v2w1l g2ua s1news t2ng0 v2w2l s2Vr g2ub
+v2dv0 t2mixx v2w3l v2oh0*1 s2th0*1 v2w5l t2lo1 v2up1 v2oh0*1 g2va s2th0*1 v2Um t2hi1 s2th0*1 g2vb t2ng1 v2puo s2Vm g2um v2dv1
+v2pua s2th1*1 t2Do v2oh1*1 g2vm s2th1*1 v2oh1*2 s2th0 v2pub t2Tb t2Da v2oh0 s2sgo t2Db s2th1*1 v2smo s2th1 t2sum0 v2pum s2sga
+v2oh1 v2yyo s2sgb t2Dm v2smb t2sum1 v2sma s2sgm v2yyb t2mixo v2yya v2post*1 t2mixb v2smm v2post*2 t2mixa v2yym t2Tu t2Te
+t2mixm v2post y2bias s2new0 s2new1 v2out0 s2out1*1 y2out0 s2out1
 """
 
 
@@ -104,7 +84,6 @@ def rank_program(g, core, T, topo):
     assert topo.die(T.cores[far_a]) == topo.die(core) != topo.die(T.cores[far_b])
     e_off = topo.engines(core, T.cores[rem0])
     e_on = [e for e in topo.engines(core, T.cores[mate]) if e not in e_off]
-    R = ROUGH
 
     def part(es, i, n):
         k = len(es) // n
@@ -112,33 +91,30 @@ def rank_program(g, core, T, topo):
 
     calls, layer = [], [0]
 
-    def note(**c):
-        calls.append(dict(c, name=(layer[0], c["name"])))
+    def note(kind, q, name, reads, writes, banks=(), **more):
+        calls.append(dict(more, kind=kind, q=q, name=(layer[0], name), reads=reads, writes=writes, banks=banks))
 
-    def op(q, name, fns, cycles, reads, writes, banks=()):
-        fns = fns if isinstance(fns, list) else [fns]
-        name = writes[0].split("_")[0] if name == "fill" else name
-        if q == "t":
-            busy = len(fns) * cycles * R["tensor"]
-        elif q == "g":
-            busy = len(fns) * (0.17 + 2 * cycles * R["cycle"])
-        else:
-            busy = len(fns) * (R[q] + max(cycles, 64) * R["cycle"])
-        note(kind="op", q=q, name=name, fns=fns, reads=reads, writes=writes, banks=banks, busy=busy, late=R["hop"])
+    def op(q, name, fns, reads, writes, banks=()):
+        note("op", q, name, reads, writes, banks, fns=fns if isinstance(fns, list) else [fns])
 
-    def dma(q, name, sem, pairs, reads, writes, late):
-        note(kind="dma", q=q, name=sem if name == "load" else name, sem=sem, pairs=pairs, reads=reads, writes=writes, banks=(), busy=0.05 * len(pairs), late=late)
+    def dma(q, name, sem, pairs, reads, writes):
+        note("dma", q, name, reads, writes, sem=sem, pairs=pairs)
 
-    def send(name, items, reads, lands, flight=0.0):
-        note(kind="send", q="g", name=name, items=items, reads=reads, writes=[], banks=(), busy=R["issue"], late=R["flight"] + flight)
+    def send(name, items, reads, lands):
+        note("send", "g", name, reads, [], items=items)
         me = len(calls) - 1
-        for sem, writes, pieces, far in lands:
-            n = sum(bin(m).count("1") for _r, m, s, _a, _b in items if s == sem)
-            note(kind="land", q="port" if far else "chip", name=name, sem=sem, n=n, reads=[], writes=writes, banks=(),
-                 busy=pieces * R["port"], late=R["wake"], after=me)
+        for sem, writes in lands:
+            note("land", "", name, [], writes, sem=sem, n=sum(bin(m).count("1") for _r, m, s, _a, _b in items if s == sem), after=me)
+
+    def parcels(hs):
+        far, near = [h for h in hs if h[-1] != "m"], [h for h in hs if h[-1] == "m"]
+        return [(span(h[-1])[0], part(e_on, near.index(h), len(near)) if h in near else part(e_off, far.index(h), len(far))) for h in hs]
 
     V, S, PE = g.vector, g.scalar, g.tensor
     ident, identh, shifth = T.wb[:, 0:8, :], T.wh[:, 0:8, :], T.wh[:, 7:15, :]
+
+    def copy(q, out, in_):
+        return (lambda: V.tensor_copy(out, in_)) if q == "v" else (lambda: S.activation(out, in_, Act.Copy))
 
     def bias_rows(t, half):
         return t[64 * half + 15:64 * half + 64:16, :]
@@ -165,46 +141,42 @@ def rank_program(g, core, T, topo):
     blk = rs
 
     mine = T.qall[:, tok(rank)]
-    dma("y", "load", "lq", [(mine, T.rq[:])], [], ["q%d" % rank], 1.7)
-    dma("y", "load", "lnm", [(T.nmi[:], T.nm[:])], [], ["nmi"], 2.2)
-    dma("y", "load", "lke", [(T.kw[:], T.ke[:])], [], ["kw"], 3.7)
-    for ap, value, n, tag in [(T.bdb[:], 1.0, 64, "bdb"), (T.wb[:], 1.0, 128, "wb"), (T.cbig[:], ROUND2048, 128, "cbig"),
-                              (T.minus[:], -1.0, 64, "minus"), (T.four[:], 4.0, 64, "four"), (T.none[:], 0.0, 128, "none"),
-                              (T.keep[:, 0::128], 0.0, 64, "keep"), (T.wide[:], 0.5, 256, "wide")]:
-        op("v", "fill", lambda ap=ap, value=value: V.memset(ap, value), n, [], [tag])
-    op("g", "fill", lambda: g.affine_select(T.bdb[:], T.bdb[:], [[-16, 8], [0, 16]], Op.is_ge, 0.0, 0, 1), 128, ["bdb"], ["bdb"])
-    op("g", "fill", lambda: g.affine_select(T.bdb[:], T.bdb[:], [[16, 8], [0, 16]], Op.is_ge, 0.0, 15, -1), 128, ["bdb"], ["bdb"])
-    op("g", "fill", lambda: g.affine_select(T.wb[:], T.wb[:], [[0, 2], [-1, 128]], Op.is_equal, 0.0, 0, 1), 256, ["wb"], ["wb"])
-    for word in QS.split():
+    dma("y", "lq", "lq", [(mine, T.rq[:])], [], ["q%d" % rank])
+    dma("y", "lnm", "lnm", [(T.nmi[:], T.nm[:])], [], ["nmi"])
+    dma("y", "lke", "lke", [(T.kw[:], T.ke[:])], [], ["kw"])
+    for ap, value, tag in [(T.bdb[:], 1.0, "bdb"), (T.wb[:], 1.0, "wb"), (T.cbig[:], ROUND2048, "cbig"), (T.minus[:], -1.0, "minus"),
+                           (T.four[:], 4.0, "four"), (T.none[:], 0.0, "none"), (T.keep[:, 0::128], 0.0, "keep"), (T.wide[:], 0.5, "wide")]:
+        op("v", tag, lambda ap=ap, value=value: V.memset(ap, value), [], [tag])
+    op("g", "bdb", lambda: g.affine_select(T.bdb[:], T.bdb[:], [[-16, 8], [0, 16]], Op.is_ge, 0.0, 0, 1), ["bdb"], ["bdb"])
+    op("g", "bdb", lambda: g.affine_select(T.bdb[:], T.bdb[:], [[16, 8], [0, 16]], Op.is_ge, 0.0, 15, -1), ["bdb"], ["bdb"])
+    op("g", "wb", lambda: g.affine_select(T.wb[:], T.wb[:], [[0, 2], [-1, 128]], Op.is_equal, 0.0, 0, 1), ["wb"], ["wb"])
+    for word in QUERIES.split():
         hs = word.split(".")
-        far = [h for h in hs if h != "m"]
-        send("q" + word, [(span(h)[0], part(e_on, 0, 1) if h == "m" else part(e_off, far.index(h), len(far)), "aq" + h, mine, mine) for h in hs],
-             ["q%d" % rank], [("aq" + h, ["q%d" % span(h)[0]], 1, h != "m") for h in hs])
-    dma("y", "load", "lb", [(T.bs[:, 0, half, :], bias_rows(T.ke, half)) for half in range(2)], ["q%d" % mate], ["b0", "y1"], 1.7)
-    for sem, out, in_, tag, late in [("lu", T.uw, T.ue, "uw", 3.2), ("lx", T.xb, T.x0, "xb", 3.5), ("lm", T.mb, T.mm, "mb", 3.7), ("lv", T.vw, T.ve, "vw", 5.2)]:
-        dma("y", "load", sem, [(out[:], in_[:])], ["q%d" % mate], [tag], late)
-    op("g", "late", lambda: g.iota(T.c1[:], [[0, 8], [-64, 4], [0, 4]], 0, 0, allow_small_or_imprecise_dtypes=True), 128, [], ["c1"])
-    op("g", "ramp", lambda: g.iota(T.ramp[:], [[1, 32], [0, 2]], 0, 0, allow_small_or_imprecise_dtypes=True), 64, [], ["ramp"])
-    op("v", "ramp", lambda: V.tensor_scalar(T.ramp[:], T.ramp[:], 65536.0, None, Op.mult), 64, ["ramp"], ["ramp"])
+        send("q" + word, [(r, m, "aq" + h, mine, mine) for h, (r, m) in zip(hs, parcels(hs))], ["q%d" % rank], [("aq" + h, ["q%d" % span(h)[0]]) for h in hs])
+    dma("y", "lb", "lb", [(T.bs[:, 0, half, :], bias_rows(T.ke, half)) for half in range(2)], ["q%d" % mate], ["b0"])
+    for sem, out, in_, tag in [("lu", T.uw, T.ue, "uw"), ("lx", T.xb, T.x0, "xb"), ("lm", T.mb, T.mm, "mb"), ("lv", T.vw, T.ve, "vw")]:
+        dma("y", sem, sem, [(out[:], in_[:])], ["q%d" % mate], [tag])
+    op("g", "late", lambda: g.iota(T.c1[:], [[0, 8], [-64, 4], [0, 4]], 0, 0, allow_small_or_imprecise_dtypes=True), [], ["c1"])
+    op("g", "ramp", lambda: g.iota(T.ramp[:], [[1, 32], [0, 2]], 0, 0, allow_small_or_imprecise_dtypes=True), [], ["ramp"])
+    op("v", "ramp", lambda: V.tensor_scalar(T.ramp[:], T.ramp[:], RISE, None, Op.mult), ["ramp"], ["ramp"])
     for half in range(2):
         ap = T.wide[32 * half:32 * half + 32]
-        op("g", "late", lambda ap=ap: g.affine_select(ap, ap, [[-1, 32], [0, 16]], Op.is_equal, 0.0, 0, 1), 512, ["wide", "q%d" % mate], ["wide%d" % half])
-    op("s", "fill", lambda: S.activation(T.fold[:], T.bdb[:, 0::16], Act.Sigmoid, bias=-128.0, scale=256.0), 1500, ["bdb"], ["fold"])
-    for fn, n, reads, writes in [
-            (lambda: V.tensor_copy(T.off[:], T.nmi[:]), 256, ["nmi"], ["off"]),
-            ([lambda k=k: V.tensor_copy(T.sel[:, :, k, :], ident) for k in range(4)], 64, ["wb"], ["sel"]),
-            (lambda: V.tensor_scalar(T.zh[:], T.cbig[:, 0:144], 0.0, None, Op.mult), 72, ["cbig"], ["zh"]),
-            (lambda: V.tensor_copy(T.wh[:], T.wb[:]), 128, ["wb"], ["wh"]),
-            (lambda: V.tensor_copy(T.zh[:, 15:143:16], T.bdb[:, 0::16]), 64, ["bdb"], ["zh"]),
-            (lambda: V.tensor_copy(T.selb[:], T.sel[:]), 256, ["sel"], ["selb"]),
-            (lambda: V.tensor_scalar(T.seln[:], T.sel[:], -1.0, None, Op.mult), 256, ["sel"], ["seln"]),
-            (lambda: V.tensor_scalar(T.half[:], T.bdb[:, 0::16], -0.5, None, Op.mult), 64, ["bdb"], ["half"]),
-            (lambda: V.tensor_scalar(T.bdn[:], T.bdb[:], -0.25, None, Op.mult), 64, ["bdb"], ["bdn"]),
-            (lambda: V.tensor_scalar(T.bd[:], T.bdb[:], 0.5, None, Op.mult), 128, ["bdb"], ["bd"]),
-            (lambda: V.tensor_scalar(T.negh[:], ident, -1.0, None, Op.mult), 64, ["wb"], ["negh"]),
-            (lambda: V.tensor_copy(T.nmh[:], T.nmi[:]), 256, ["nmi"], ["nm0"]),
-            (lambda: V.tensor_scalar(T.c2[:], T.c1[:], 0.25, ROUND64, Op.mult, Op.add), 64, ["c1"], ["c2"])]:
-        op("v", "fill", fn, n, reads, writes)
+        op("g", "late", lambda ap=ap: g.affine_select(ap, ap, [[-1, 32], [0, 16]], Op.is_equal, 0.0, 0, 1), ["wide", "q%d" % mate], ["wide%d" % half])
+    op("s", "fold", lambda: S.activation(T.fold[:], T.bdb[:, 0::16], Act.Sigmoid, bias=-128.0, scale=256.0), ["bdb"], ["fold"])
+    for fn, read, tag in [
+            (lambda: V.tensor_copy(T.off[:], T.nmi[:]), "nmi", "off"),
+            ([lambda k=k: V.tensor_copy(T.sel[:, :, k, :], ident) for k in range(4)], "wb", "sel"),
+            (lambda: V.tensor_scalar(T.zh[:], T.cbig[:, 0:144], 0.0, None, Op.mult), "cbig", "zh"),
+            (lambda: V.tensor_copy(T.wh[:], T.wb[:]), "wb", "wh"),
+            (lambda: V.tensor_copy(T.zh[:, 15:143:16], T.bdb[:, 0::16]), "bdb", "zh"),
+            (lambda: V.tensor_copy(T.selb[:], T.sel[:]), "sel", "selb"),
+            (lambda: V.tensor_scalar(T.seln[:], T.sel[:], -1.0, None, Op.mult), "sel", "seln"),
+            (lambda: V.tensor_scalar(T.half[:], T.bdb[:, 0::16], -0.5, None, Op.mult), "bdb", "half"),
+            (lambda: V.tensor_scalar(T.bd[:], T.bdb[:], 0.25, None, Op.mult), "bdb", "bd"),
+            (lambda: V.tensor_scalar(T.negh[:], ident, -1.0, None, Op.mult), "wb", "negh"),
+            (lambda: V.tensor_copy(T.nmh[:], T.nmi[:]), "nmi", "nm0"),
+            (lambda: V.tensor_scalar(T.c2[:], T.c1[:], 0.25, ROUND64, Op.mult, Op.add), "c1", "c2")]:
+        op("v", tag, fn, [read], [tag])
 
     def keys(c, h):
         r0, n = span(h)
@@ -213,165 +185,137 @@ def rank_program(g, core, T, topo):
     def fused(c, h):
         r0, n = span(h)
         op("v", "f%d%s" % (c, h), lambda: V.tensor_tensor(T.prod[:, tok(r0, n), c], keys(c, h), T.qall[:, tok(r0, n)], Op.mult),
-           256 * n * R["gather"], ["kw", "off"] + rs("q", r0, n), tags("prod%d" % c, h))
+           ["kw", "off"] + rs("q", r0, n), tags("prod%d" % c, h))
 
     def raw(q, c, h):
-        r0, n = span(h)
-        out = T.rawk[:, c, tok(r0, n)]
-        op(q, "k%d%s" % (c, h), (lambda: V.tensor_copy(out, keys(c, h))) if q == "v" else (lambda: S.activation(out, keys(c, h), Act.Copy)),
-           256 * n * R["gather"], ["kw", "off"], tags("raw%d" % c, h))
+        op(q, "k%d%s" % (c, h), copy(q, T.rawk[:, c, tok(*span(h))], keys(c, h)), ["kw", "off"], tags("raw%d" % c, h))
 
-    def held(c, h, b, j, parts):
+    def times(c, h, runs, how="q"):
         r0, n = span(h)
-        op("t", "h%d%s" % (c, h), [lambda: PE.matmul(at(b, j, 4 * n), ident, T.rawk[:, c, tok(r0, n)], True, False),
-                                   lambda: PE.matmul(at(b, j, 4 * n), T.neg[:], T.rawk[:, 0, tok(r0, n)], False, True)], 256 * n,
-           ["wb", "neg"] + tags("raw%d" % c, h) + tags("raw0", h), blk(b, j, 4 * n) + ["acc" + b], [b])
-        for p in parts:
-            r = span(p)[0]
-            k = j + 4 * (r - r0)
-            op("v", "x%d%s" % (c, p), lambda p=p, r=r, k=k: V.tensor_tensor(T.prod[:, tok(r), c], at(b, k, 4), T.qall[:, tok(r)], Op.mult), 256,
-               blk(b, k, 4) + ["q%d" % r], tags("prod%d" % c, p), [b])
-
-    def times(c, h, pair, how="q"):
-        r0, n = span(h)
-        out = T.quick[:, col(h), c, :] if pair == "qq" else T.prod[:, tok(r0, n), c]
+        out = T.quick[:, col(h), c, :] if runs else T.prod[:, tok(r0, n), c]
         src, tag = (T.pQ, "pQ") if how == "q" else (T.qall, "q")
-        op("v", "x%d%s" % (c, h), lambda: V.tensor_tensor(out, src[:, tok(r0, n)], T.rawk[:, c, tok(r0, n)], Op.mult), 128 * n,
+        op("v", "x%d%s" % (c, h), lambda: V.tensor_tensor(out, src[:, tok(r0, n)], T.rawk[:, c, tok(r0, n)], Op.mult),
            rs(tag, r0, n) + tags("raw%d" % c, h), tags("prod%d" % c, h), ["pQ"] if how == "q" else [])
 
     def stand(h):
         r0, n = span(h)
         pieces = [slice(c, c + 128) for c in range(256 * r0, 256 * (r0 + n), 128)]
-        op("t", "q1" + h, [lambda s=s: PE.transpose(T.pQ[:, s], T.qall[:, s], ident) for s in pieces], 128, ["wb"] + rs("q", r0, n), rs("pQ", r0, n), ["pQ"])
-        op("v", "q2" + h, lambda: V.tensor_copy(T.qt[:, tok(r0, n)], T.pQ[:, tok(r0, n)]), 128 * n, rs("pQ", r0, n), rs("qt", r0, n), ["pQ"])
-        op("t", "q3" + h, [lambda s=s: PE.transpose(T.pQ[:, s], T.qt[:, s], ident) for s in pieces], 128, ["wb"] + rs("qt", r0, n), rs("pQ", r0, n), ["pQ"])
+        op("t", "q1" + h, [lambda s=s: PE.transpose(T.pQ[:, s], T.qall[:, s], ident) for s in pieces], ["wb"] + rs("q", r0, n), rs("pQ", r0, n), ["pQ"])
+        op("v", "q2" + h, copy("v", T.qt[:, tok(r0, n)], T.pQ[:, tok(r0, n)]), rs("pQ", r0, n), rs("qt", r0, n), ["pQ"])
+        op("t", "q3" + h, [lambda s=s: PE.transpose(T.pQ[:, s], T.qt[:, s], ident) for s in pieces], ["wb"] + rs("qt", r0, n), rs("pQ", r0, n), ["pQ"])
 
     def steps(l):
         nm = T.nmn if l else T.nmh
         op("t", "dn", [lambda c=c: PE.matmul(T.pX[:, 256 + c::4], identh, nm[:, c, :], c == 0, False) for c in range(4)]
-           + [lambda c=c: PE.matmul(T.pX[:, 256 + c::4], T.negh[:], nm[:, c + 1, :], False, c == 2) for c in range(3)], 64,
+           + [lambda c=c: PE.matmul(T.pX[:, 256 + c::4], T.negh[:], nm[:, c + 1, :], False, c == 2) for c in range(3)],
            ["wh", "negh", "nm%d" % l], blk("pX", 4, 4) + ["accpX"], ["pX"])
 
     def winners(l, h, b):
         cs = col(h)
         a, P = 4 * cs.start, T[b]
-        how = dict(word.split(",") for word in KEYS[l].split()).get(h, "ffff")
+        how = dict(word.split(",") for word in KEYS[l].split())[h]
         for c in (0, 1):
             rhs = [T.quick[:, cs, c::2, i] if how[c::2] == "qq" else T.prod[:, 16 * cs.start + i:16 * cs.stop:16, c::2] for i in range(16)]
             op("t", "s%d%s" % (c, h), [lambda c=c: PE.matmul(P[:, c:128:2], ident, T.ramp[:], True, False)]
-               + [lambda i=i, c=c, rhs=rhs: PE.matmul(P[:, c:128:2], T.zh[:, 15 - i:143 - i], rhs[i], False, i == 15) for i in range(16)], 64,
+               + [lambda i=i, c=c, rhs=rhs: PE.matmul(P[:, c:128:2], T.zh[:, 15 - i:143 - i], rhs[i], False, i == 15) for i in range(16)],
                ["zh", "wb", "ramp"] + tags("prod%d" % c, h) + tags("prod%d" % (c + 2), h), [b + "0" if c else b + "1", "acc" + b], [b])
         both = blk(b, 0, 2)
-        op("v", "w1" + h, lambda: V.tensor_tensor_scan(T.top[:, a:a + 128], T.none[:], P[:, 0:128], -65536.0, Op.add, Op.max), 128, both + ["none"], ["top" + b], [b])
-        op("v", "w2" + h, lambda: V.tensor_tensor(T.keep[:, a + 1:a + 128], P[:, 1:128], T.top[:, a:a + 127], Op.is_le), 127, both + ["top" + b, "keep"], ["keep" + b], [b])
-        op("v", "w3" + h, lambda: V.tensor_tensor_scan(T.run[:, a:a + 128], T.keep[:, a:a + 128], T.pX[:, 256 + a:384 + a], 0.0, Op.mult, Op.add), 128,
+        op("v", "w1" + h, lambda: V.tensor_tensor_scan(T.top[:, a:a + 128], T.none[:], P[:, 0:128], -RISE, Op.add, Op.max), both + ["none"], ["top" + b], [b])
+        op("v", "w2" + h, lambda: V.tensor_tensor(T.keep[:, a + 1:a + 128], P[:, 1:128], T.top[:, a:a + 127], Op.is_le), both + ["top" + b, "keep"], ["keep" + b], [b])
+        op("v", "w3" + h, lambda: V.tensor_tensor_scan(T.run[:, a:a + 128], T.keep[:, a:a + 128], T.pX[:, 256 + a:384 + a], 0.0, Op.mult, Op.add),
            ["keep" + b] + blk("pX", 4, 4), tags("run", h), ["pX"])
-        op("v", "w5" + h, lambda: V.tensor_copy(T.wu[:, l, cs], won(h)), 64, tags("run", h), tags("wu%d" % l, h))
+        op("v", "w5" + h, copy("v", T.wu[:, l, cs], won(h)), tags("run", h), tags("wu%d" % l, h))
 
     def won(h):
         return T.run[:, 4 * col(h).start + 3:4 * col(h).stop:4]
 
     def names(l):
         src, dst, sem = T.w16[:, l, :], T.wr[:, l, rank, :], "aw%d" % l
-        op("v", "w4", lambda: V.tensor_copy(src, won("*")), 64, tags("run", "*"), tags("w%d" % l, "*"))
-        send("tell", [(far_a, part(e_off, 0, 2), sem, src, dst), (far_b, part(e_off, 1, 2), sem, src, dst), (mate, part(e_on, 0, 1), sem, src, dst)],
-             tags("w%d" % l, "*"), [(sem, ["wr%d" % l], 0.5, True)])
+        op("v", "w4", copy("v", src, won("*")), tags("run", "*"), tags("w%d" % l, "*"))
+        send("tell", [(r, m, sem, src, dst) for r, m in parcels(["a", "b", "m"])], tags("w%d" % l, "*"), [(sem, ["wr%d" % l])])
         NP, nb = at("pA", 4, 4), blk("pA", 4, 4)
         pairs = [(r, c) for r in range(N) if r != rank for c in range(4)]
         op("t", "nA", [lambda: PE.matmul(NP, identh, T.nmh[:], True, False), lambda: PE.matmul(NP, ident, T.cbig[:], False, False)]
-           + [lambda c=c: PE.matmul(at("pA", 4 + c, 1), shifth, T.w16[:, l, :], False, False) for c in range(4)], 128,
+           + [lambda c=c: PE.matmul(at("pA", 4 + c, 1), shifth, T.w16[:, l, :], False, False) for c in range(4)],
            ["wh", "wb", "nm0", "cbig"] + tags("w%d" % l, "*"), nb + ["accpA"], ["pA"])
         op("t", "nB", [lambda r=r, c=c: PE.matmul(at("pA", 4 + c, 1), shifth, T.wr[:, l, r, :], False, (r, c) == pairs[-1]) for r, c in pairs],
-           64, ["wh", "wr%d" % l], nb + ["accpA"], ["pA"])
-        op("s", "hb", lambda: S.activation(T.hb[:], NP, Act.Identity, bias=1023.5, scale=-1.0), 256, nb, ["hb"], ["pA"])
-        op("v", "nn", lambda: V.tensor_tensor(T.nmn[:], NP, T.hb[:], Op.add), 256, nb + ["hb"], ["nmn", "nm%d" % (l + 1)], ["pA"])
-        op("v", "off", lambda: V.tensor_copy(T.off[:], T.nmn[:]), 128, ["nmn"], ["off"])
+           ["wh", "wr%d" % l], nb + ["accpA"], ["pA"])
+        op("s", "hb", lambda: S.activation(T.hb[:], NP, Act.Identity, bias=1023.5, scale=-1.0), nb, ["hb"], ["pA"])
+        op("v", "nn", lambda: V.tensor_tensor(T.nmn[:], NP, T.hb[:], Op.add), nb + ["hb"], ["nmn", "nm%d" % (l + 1)], ["pA"])
+        op("v", "off", copy("v", T.off[:], T.nmn[:]), ["nmn"], ["off"])
 
     F = T.pF[:, 0:2, 0:33]
 
-    def count(l, k, h, b):
-        high(l, k, h, b)
-        low(l, k, h)
+    def turn(P, w, sel, alone=False):
+        return [lambda j=j: PE.matmul(P[32 * j:32 * j + 32], w, sel[:, :, :, 4 * j:4 * j + 4], alone, alone) for j in range(4)]
 
-    def high(l, k, h, b):
+    def count(k, h, b):
         H, hb = at(b, 2, 2), blk(b, 2, 2)
-        op("v", "up%d" % k, lambda: V.tensor_scalar(T.hw[:, k], won(h), ROUND64 - 31.5, None, Op.add), 64, tags("run", h), ["hw%d" % k])
-        op("t", "hi%d" % k, [lambda: PE.matmul(H, ident, T.c1[:], True, False)] + turn(H, T.hw[:, k], T.selb) + [close(H)], 128,
-           ["wb", "wh", "zh", "c1", "selb", "hw%d" % k], hb + ["acc" + b], [b])
-        q = COPIES[l][k]
-        op(q, "dv%d" % k, (lambda: V.tensor_copy(T.dv[:, k], H)) if q == "v" else (lambda: S.activation(T.dv[:, k], H, Act.Copy)), 128, hb, ["dv%d" % k], [b])
-
-    def turn(H, w, sel):
-        return [lambda j=j: PE.matmul(H[32 * j:32 * j + 32], w, sel[:, :, :, 4 * j:4 * j + 4], False, False) for j in range(4)]
-
-    def close(H):
-        return lambda: PE.matmul(H[:, 0, 0:2] if len(H.shape) > 2 else H[:, 0:2], identh, T.zh[:, 0:2], False, True)
-
-    def low(l, k, h):
+        op("v", "up%d" % k, lambda: V.tensor_scalar(T.hw[:, k], won(h), ROUND64 - 31.5, None, Op.add), tags("run", h), ["hw%d" % k])
+        op("t", "hi%d" % k, turn(H, T.hw[:, k], T.selb, True), ["selb", "hw%d" % k], hb + ["acc" + b], [b])
+        op("v", "dv%d" % k, lambda: V.tensor_tensor(T.dv[:, k], H, T.c1[:], Op.add), hb + ["c1"], ["dv%d" % k], [b])
         b = ("pF", "pA")[k]
-        H, hb = at(b, 4, 2), blk(b, 4, 2)
-        op("t", "lo%d" % k, [lambda: PE.matmul(H, identh, T.c2[:], True, False)] + turn(H, won(h), T.sel), 128,
-           ["wh", "c2", "sel"] + tags("run", h), hb + ["acc" + b], [b])
-        op("t", "ng%d" % k, turn(H, T.hw[:, k], T.seln) + [close(H)], 128, ["seln", "wh", "zh", "hw%d" % k], hb + ["acc" + b], [b])
+        L, lb = at(b, 4, 2), blk(b, 4, 2)
+        edge = T.pF[:, 4, 0:2] if k == 0 else T.pA[:, 256:258]
+        op("t", "lo%d" % k, [lambda: PE.matmul(L, identh, T.c2[:], True, False)] + turn(L, won(h), T.sel),
+           ["wh", "c2", "sel"] + tags("run", h), lb + ["acc" + b], [b])
+        op("t", "ng%d" % k, turn(L, T.hw[:, k], T.seln) + [lambda: PE.matmul(edge, identh, T.zh[:, 0:2], False, True)],
+           ["seln", "wh", "zh", "hw%d" % k], lb + ["acc" + b], [b])
         for u0 in range(0, 8, 2):
             op("v", "oh%d" % k, [lambda u=u: V.tensor_scalar(T.oh[:, 8 * k:8 * k + 8, u, :], T.dv[:, k], ROUND64 + 256.0 * u, 4096.0, Op.is_equal, Op.mult)
-                                 for u in (u0, u0 + 1)], 64, ["dv%d" % k], ["oh%d%d" % (k, u0)])
-            op("s", "th%d" % k, [lambda u=u: S.activation(T.th[:, 8 * k:8 * k + 8, u::8, :], H, Act.Sigmoid, bias=-256.0 * u - EDGE, scale=128.0)
-                                 for u in (u0, u0 + 1)], 128, hb, ["th%d%d" % (k, u0)], [b])
+                                 for u in (u0, u0 + 1)], ["dv%d" % k], ["oh%d%d" % (k, u0)])
+            op("s", "th%d" % k, [lambda u=u: S.activation(T.th[:, 8 * k:8 * k + 8, u::8, :], L, Act.Sigmoid, bias=-256.0 * u - EDGE, scale=128.0)
+                                 for u in (u0, u0 + 1)], lb, ["th%d%d" % (k, u0)], [b])
         ends = [lambda: PE.matmul(F, ident, T.minus[:], k == 0, k == 1)]
         sums = [lambda gr=gr, i=i: PE.matmul(T.pF[32 * (gr % 4):32 * (gr % 4) + 32, gr // 4, 0:32], T.oh[:, 8 * k + gr, :, i::4], T.th[:, 8 * k + gr, :, i],
                                               False, False) for gr in range(8) for i in range(4)]
-        op("t", "sum%d" % k, ends + sums if k == 0 else sums + ends, 33,
-           ["wb", "minus"] + ["%s%d%d" % (x, k, u) for x in ("oh", "th") for u in range(8)], blk("pF", 0, 2) + ["accpF"], ["pF"])
+        op("t", "sum%d" % k, ends + sums if k == 0 else sums + ends,
+           ["wb", "minus"] + ["%s%d%d" % (x, k, u) for x in ("oh", "th") for u in range(0, 8, 2)], blk("pF", 0, 2) + ["accpF"], ["pF"])
 
     def biases(l):
         last = l == NL - 1
         j = NL if last else l
         if last:
-            op("s", "blo", lambda: S.activation(T.bs[:, NL], T.bs[:, l], Act.Identity, bias=-float(NL)), 128, ["b%d" % l], ["b%d" % NL])
+            op("s", "blo", lambda: S.activation(T.bs[:, NL], T.bs[:, l], Act.Identity, bias=-float(NL)), ["b%d" % l], ["b%d" % NL])
         new = T.bout[:] if last else T.bs[:, l + 1]
         FT, even, odd = at("pB", 4, 2), T.pB[:, 256:384:2], T.pB[:, 257:384:2]
         fb, tb = blk("pF", 0, 2), blk("pB", 4, 2) + ["accpB"]
-        op("t", "Tb", [lambda: PE.matmul(FT, ident, T.bs[:, j], True, False), lambda: PE.matmul(odd, ident, T.four[:], False, False)], 96,
+        op("t", "Tb", [lambda: PE.matmul(FT, ident, T.bs[:, j], True, False), lambda: PE.matmul(odd, ident, T.four[:], False, False)],
            ["wb", "four", "b%d" % j], tb, ["pB"])
-        op("v", "post", lambda: V.tensor_scalar(T.i2[:], F, ROUND4096, -ROUND4096, Op.add, Op.add), 66, fb, ["i2"], ["pF"])
-        op("v", "post", lambda: V.tensor_scalar(T.up[:], F, 2.0 ** -12, 1024.0, Op.mult, Op.add), 66, fb, ["up"], ["pF"])
-        op("v", "post", lambda: V.tensor_tensor(T.ee[:], F, T.i2[:], Op.subtract), 66, fb + ["i2"], ["ee"], ["pF"])
+        op("v", "post", lambda: V.tensor_scalar(T.i2[:], F, ROUND4096, -ROUND4096, Op.add, Op.add), fb, ["i2"], ["pF"])
+        op("v", "post", lambda: V.tensor_scalar(T.up[:], F, 2.0 ** -12, 1024.0, Op.mult, Op.add), fb, ["up"], ["pF"])
+        op("v", "post", lambda: V.tensor_tensor(T.ee[:], F, T.i2[:], Op.subtract), fb + ["i2"], ["ee"], ["pF"])
         op("t", "Tu", [lambda: PE.matmul(odd, T.negh[:], T.up[:, :, 0:32], False, False), lambda: PE.matmul(odd, identh, T.up[:, :, 1:33], False, False)],
-           64, ["wh", "negh", "up"], tb, ["pB"])
+           ["wh", "negh", "up"], tb, ["pB"])
         op("t", "Te", [lambda: PE.matmul(odd, identh, T.ee[:, :, 1:33], False, False), lambda: PE.matmul(even, T.negh[:], T.ee[:, :, 0:32], False, True)],
-           64, ["wh", "negh", "ee"], tb, ["pB"])
-        op("v", "post", lambda: V.tensor_tensor(new, FT, T.bs[:, j], Op.max), 128, tb + ["b%d" % j], ["bout" if last else "b%d" % (l + 1)], ["pB"])
+           ["wh", "negh", "ee"], tb, ["pB"])
+        op("v", "post", lambda: V.tensor_tensor(new, FT, T.bs[:, j], Op.max), tb + ["b%d" % j], ["bout" if last else "b%d" % (l + 1)], ["pB"])
         if last:
-            dma("y", "bias", "oyb", [(T.yb[4 * half:4 * half + 4, :], T.bout[:, half, :]) for half in range(2)], ["bout"], ["yb"], R["local"])
+            dma("y", "bias", "oyb", [(T.yb[4 * half:4 * half + 4, :], T.bout[:, half, :]) for half in range(2)], ["bout"], ["yb"])
         else:
-            dma("y", "bias", "bias%d" % l, [(bias_rows(T.kw, half), T.bs[:, l + 1, half, :]) for half in range(2)], ["b%d" % (l + 1)],
-                ["kw", "kw%d" % (l + 1)], R["local"])
+            dma("y", "bias", "bias%d" % l, [(bias_rows(T.kw, half), T.bs[:, l + 1, half, :]) for half in range(2)], ["b%d" % (l + 1)], ["kw", "kw%d" % (l + 1)])
 
     out_j, in_j = (2, 0) if rank < mate else (0, 2)
+
+    def chosen(l, k, h):
+        return (T.uw, T.vw)[k][:].indirect(T.wu[:, l, col(h)])
 
     def pick(l, what, q):
         kind, h = what
         k = "uv".index(kind)
-        src = (T.uw, T.vw)[k][:].indirect(T.wu[:, l, col(h)])
         r0, n = span(h)
-        out = T.away[:, 2 * l + k, tok(r0 - rem0, n)] if h in "rab" else T.near[:, 2 * l + k, {"l": tok(min(1, out_j), 2), "m": tok(out_j), "o": tok(1)}[h]]
-        op(q, kind.upper() + h, (lambda: V.tensor_copy(out, src)) if q == "v" else (lambda: S.activation(out, src, Act.Copy)),
-           256 * n * R["gather"], [kind + "w"] + tags("wu%d" % l, h), tags("%s%dp" % (kind, l), h))
+        out = T.away[:, 2 * l + k, tok(r0 - rem0, n)] if h in "rab" else T.near[:, 2 * l + k, {"l": tok(min(1, out_j), 2), "m": tok(out_j)}[h]]
+        op(q, kind.upper() + h, copy(q, out, chosen(l, k, h)), [kind + "w"] + tags("wu%d" % l, h), tags("%s%dp" % (kind, l), h))
 
     def give(l, word):
         what = word.rstrip("+").split(".")
         items, reads, lands = [], ["kw%d" % (l + 1)] if word[-1] == "+" else [], []
-        for kind, h in what:
-            k = 2 * l + "uv".index(kind)
-            like = [w for w in what if (w[1] == "m") == (h == "m")]
-            i, sem, r = like.index(kind + h), "a%d%s%s" % (l, kind, h), span(h)[0]
-            if h == "m":
-                items.append((r, part(e_on, i, len(like)), sem, T.near[:, k, tok(out_j)], T.near[:, k, tok(out_j)]))
-            else:
-                items.append((r, part(e_off, i, len(like)), sem, T.away[:, k, tok(r - rem0)], T.came[:, k, rank - loc0]))
+        for (kind, h), (r, mask) in zip(what, parcels(what)):
+            k, sem = 2 * l + "uv".index(kind), "a%d%s%s" % (l, kind, h)
+            sides = (T.near[:, k, tok(out_j)],) * 2 if h == "m" else (T.away[:, k, tok(r - rem0)], T.came[:, k, rank - loc0])
+            items.append((r, mask, sem) + sides)
             reads += tags("%s%dp" % (kind, l), h)
-            lands.append((sem, tags("%s%dc" % (kind, l), h), 0.7 if h == "m" else 1, h != "m"))
+            lands.append((sem, tags("%s%dc" % (kind, l), h)))
         send(word, items, reads, lands)
 
     X, xb, M = at("pX", 0, 4), blk("pX", 0, 4), at("pM", 0, 4)
@@ -381,83 +325,93 @@ def rank_program(g, core, T, topo):
         def fn():
             mixed[l] += 1
             return PE.matmul(M, T.m32[:], rhs, mixed[l] == 1, mixed[l] == mixes[l])
-        op("t", name, fn, 1024, ["m32", "mix%d" % l, "mixp%d" % l] + reads, ["pM_%d" % mixes[l]], ["pM"])
+        op("t", name, fn, ["m32", "mix%d" % l, "mixp%d" % l] + reads, ["pM_%d" % mixes[l]], ["pM"])
         mixes[l] += 1
 
-    def expert(l, h, b):
-        n = int(h == "l")
+    def columns(l, h):
         if h == "r":
-            ranks, src = [rem0, rem0 + 1], lambda k, i, m: T.came[:, 2 * l + k, i:i + m]
-            order = [far_a - rem0, far_b - rem0]
-            piece = lambda i, j: T.came[:, 2 * l, i, 128 * j:128 * j + 128]
-        else:
-            j0 = min(1, in_j)
-            piece = lambda i, j: T.near[:, 2 * l, 256 * (j0 + i) + 128 * j:256 * (j0 + i) + 128 * j + 128]
-            ranks, src = [rank if j == 1 else mate for j in (j0, j0 + 1)], lambda k, i, m: T.near[:, 2 * l + k, tok(j0 + i, m)]
-            order = [ranks.index(rank), ranks.index(mate)]
-        have = lambda kind, r: "%s%d%s_%d" % (kind, l, "p" if r == rank else "c", r)
+            return [rem0, rem0 + 1], (lambda k, i, a=0, n=256: T.came[:, 2 * l + k, i, a:a + n] if n <= 256 else T.came[:, 2 * l + k]), [far_a - rem0, far_b - rem0]
+        j0 = min(1, in_j)
+        ranks = [rank if j == 1 else mate for j in (j0, j0 + 1)]
+        return ranks, (lambda k, i, a=0, n=256: T.near[:, 2 * l + k, 256 * (j0 + i) + a:256 * (j0 + i) + a + n]), [ranks.index(rank), ranks.index(mate)]
+
+    def have(l, kind, r):
+        return "%s%d%s_%d" % (kind, l, "p" if r == rank else "c", r)
+
+    def narrow(l, h, b):
+        n = int(h == "l")
+        ranks, src, order = columns(l, h)
         D, C, W = T[b][:, 0:32], T[b][:, 64:96], T[b][0:64, 128:256]
         for i in order:
             y = 2 * n + i
-            op("v", "pu" + h, lambda i=i, y=y: V.tensor_tensor(T.pu[:, y], X, src(0, i, 1), Op.mult), 256, xb + [have("u", ranks[i])], ["pu%d" % y], ["pX"])
-            if FORMS[l][n] == "w":
-                p, E, eb = "ab"[order.index(i)] if h == "r" else "om"[order.index(i)], at(b, 4 * i, 4), blk(b, 4 * i, 4)
-                op("t", "D" + p, [lambda i=i, E=E: PE.matmul(E, T.bdn[:], src(0, i, 1), True, False), lambda y=y, E=E: PE.matmul(E, T.bd[:], T.pu[:, y], False, True)],
-                   640, ["bd", "bdn", "pu%d" % y], eb, [b])
-                op("s", "sg" + p, lambda y=y, E=E: S.activation(T.sg[:, y], E, Act.Sigmoid, scale=4.0), 256, eb, ["sg%d" % y], [b])
-                op("v", "sm" + p, lambda y=y, E=E: V.tensor_tensor(E, E, T.sg[:, y], Op.mult), 256, ["sg%d" % y], eb, [b])
-                op("v", "yy" + p, lambda i=i, y=y, E=E: V.tensor_tensor(T.yy[:, y], E, src(1, i, 1), Op.mult), 256, eb + [have("v", ranks[i])], ["y%d" % y], [b])
-                mix(l, "mix" + p, T.yy[:, y], ["y%d" % y])
-                continue
+            op("v", "pu" + h, lambda i=i, y=y: V.tensor_tensor(T.pu[:, y], X, src(0, i), Op.mult), xb + [have(l, "u", ranks[i])], ["pu%d" % y], ["pX"])
             op("t", "D" + h, [fn for j in range(2) for fn in (
-                lambda i=i, j=j: PE.matmul(D[:, 16 * i + 8 * j:16 * i + 8 * j + 8], piece(i, j), T.half[:], True, False),
+                lambda i=i, j=j: PE.matmul(D[:, 16 * i + 8 * j:16 * i + 8 * j + 8], src(0, i, 128 * j, 128), T.half[:], True, False),
                 lambda i=i, y=y, j=j: PE.matmul(D[:, 16 * i + 8 * j:16 * i + 8 * j + 8], T.pu[:, y, 128 * j:128 * j + 128], T.fold[:], False, True))],
-               160, ["fold", "half", "pu%d" % y], [b + "0"], [b])
-        if FORMS[l][n] == "w":
-            return
-        op("s", "sg" + h, lambda: S.activation(T.sn[:, n], D, Act.Sigmoid, scale=2.0), 64, [b + "0"], ["sn" + h], [b])
-        op("v", "sm" + h, lambda: V.tensor_tensor(T.sp[:, n, 0:32], D, T.sn[:, n], Op.mult), 64, [b + "0", "sn" + h], ["sp" + h], [b])
-        op("v", "sm" + h, lambda: V.tensor_tensor(C, D, T.sn[:, n], Op.mult), 64, [b + "0", "sn" + h], [b + "1"], [b])
-        op("v", "sd" + h, lambda: V.tensor_tensor(T.sp[:, n, 32:64], C, T.sp[:, n, 0:32], Op.subtract), 64, [b + "1", "sp" + h], ["sl" + h], [b])
-        op("t", "W" + h, lambda: PE.matmul(W, T.sp[:, n], ident, True, True), 128, ["wb", "sp" + h, "sl" + h], blk(b, 2, 2), [b])
-        q = TURNED[l]
-        op(q, "sq" + h, (lambda: V.tensor_copy(T.sq[0:64, n], W)) if q == "v" else (lambda: S.activation(T.sq[0:64, n], W, Act.Copy)), 128,
-           blk(b, 2, 2), ["sq" + h], [b])
-        op("t", "E" + h, [lambda k=k: PE.matmul(at(b, 2 * k, 2), T.wide[0:64, 8 * k:8 * k + 8, :], T.sq[0:64, n], True, True) for k in range(4)], 128,
+               ["fold", "half", "pu%d" % y], [b + "0"], [b])
+        op("s", "sg" + h, lambda: S.activation(T.sn[:, n], D, Act.Sigmoid, scale=2.0), [b + "0"], ["sn" + h], [b])
+        op("v", "sm" + h, lambda: V.tensor_tensor(T.sp[:, n, 0:32], D, T.sn[:, n], Op.mult), [b + "0", "sn" + h], ["sp" + h], [b])
+        op("v", "sm" + h, lambda: V.tensor_tensor(C, D, T.sn[:, n], Op.mult), [b + "0", "sn" + h], [b + "1"], [b])
+        op("v", "sd" + h, lambda: V.tensor_tensor(T.sp[:, n, 32:64], C, T.sp[:, n, 0:32], Op.subtract), [b + "1", "sp" + h], ["sl" + h], [b])
+        op("t", "W" + h, lambda: PE.matmul(W, T.sp[:, n], ident, True, True), ["wb", "sp" + h, "sl" + h], blk(b, 2, 2), [b])
+        op("s", "sq" + h, copy("s", T.sq[0:64, n], W), blk(b, 2, 2), ["sq" + h], [b])
+        op("t", "E" + h, [lambda k=k: PE.matmul(at(b, 2 * k, 2), T.wide[0:64, 8 * k:8 * k + 8, :], T.sq[0:64, n], True, True) for k in range(4)],
            ["wide0", "wide1", "sq" + h], blk(b, 0, 8), [b])
-        vs = [have("v", r) for r in ranks]
-        own = "x" in ADDS[l] and h == "l"
-        if "p" in ADDS[l] or own:
+        vs = [have(l, "v", r) for r in ranks]
+        if l in PAIRED:
             first, second = order
-            P = at(b, 4 * first, 4)
-            op("v", "yy" + h, lambda: V.tensor_tensor(P, P, src(1, first, 1), Op.mult), 256, [vs[first]], blk(b, 4 * first, 4), [b])
-            op("v", "yy" + h, lambda: V.tensor_tensor(T.yy[:, 2 * n + 1], at(b, 4 * second, 4), src(1, second, 1), Op.mult), 256,
-               [vs[second]] + blk(b, 4 * second, 4), ["y%d" % (2 * n + 1)], [b])
-            if own and "p" in ADDS[l]:
-                op("v", "ad" + h, lambda: V.tensor_tensor(P, P, T.sx[:], Op.add), 256, ["sx"], blk(b, 4 * first, 4), [b])
-            if "p" in ADDS[l]:
-                op("v", "ad" + h, lambda: V.tensor_tensor(T.yy[:, 2 * n + 1], P, T.yy[:, 2 * n + 1], Op.add), 256, blk(b, 4 * first, 4), ["y%d" % (2 * n + 1)], [b])
-            else:
-                op("v", "ad" + h, lambda: V.tensor_tensor(T.yy[:, 2 * n], P, T.sx[:], Op.add), 256, blk(b, 4 * first, 4) + ["sx"], ["y%d" % (2 * n)], [b])
-                mix(l, "mix" + h, T.yy[:, 2 * n], ["y%d" % (2 * n)])
-            mix(l, "mix" + h, T.yy[:, 2 * n + 1], ["y%d" % (2 * n + 1)])
+            P, y = at(b, 4 * first, 4), 2 * n + 1
+            op("v", "yy" + h, lambda: V.tensor_tensor(P, P, src(1, first), Op.mult), [vs[first]], blk(b, 4 * first, 4), [b])
+            op("v", "yy" + h, lambda: V.tensor_tensor(T.yy[:, y], at(b, 4 * second, 4), src(1, second), Op.mult), [vs[second]] + blk(b, 4 * second, 4), ["y%d" % y], [b])
+            op("v", "ad" + h, lambda: V.tensor_tensor(T.yy[:, y], P, T.yy[:, y], Op.add), blk(b, 4 * first, 4), ["y%d" % y], [b])
+            mix(l, "mix" + h, T.yy[:, y], ["y%d" % y])
             return
-        for i0, m in [(i, 1) for i in order] if l == NL - 1 else [(0, 2)]:
-            y = 2 * n + i0
-            op("v", "yy" + h, lambda i0=i0, m=m, y=y: V.tensor_tensor(T.yy[:, y:y + m], at(b, 4 * i0, 4 * m), src(1, i0, m), Op.mult), 256 * m,
-               blk(b, 4 * i0, 4 * m) + vs[i0:i0 + m], rs("y", y, m), [b])
+        op("v", "yy" + h, lambda: V.tensor_tensor(T.yy[:, 2 * n:2 * n + 2], at(b, 0, 8), src(1, 0, 0, 512), Op.mult), blk(b, 0, 8) + vs, rs("y", 2 * n, 2), [b])
         for i in order:
             mix(l, "mix" + h, T.yy[:, 2 * n + i], ["y%d" % (2 * n + i)])
 
+    def full(l, h, bank):
+        ranks, src, order = columns(l, h)
+        for i, p in zip(order, "ab" if h == "r" else "om"):
+            y = 2 * int(h == "l") + i
+            b, j = ("pB", 0) if p == "o" else (bank, 4 * i)
+            E, eb = at(b, j, 4), blk(b, j, 4)
+            if p == "o":
+                op("v", "puo", lambda y=y: V.tensor_tensor(T.pu[:, y], chosen(l, 0, "o"), T.xo[:], Op.mult), ["xo", "uw"] + tags("wu%d" % l, "o"), ["pu%d" % y])
+            else:
+                op("v", "pu" + p, lambda i=i, y=y: V.tensor_tensor(T.pu[:, y], X, src(0, i), Op.mult), xb + [have(l, "u", ranks[i])], ["pu%d" % y], ["pX"])
+            op("t", "D" + p, lambda y=y, E=E: PE.matmul(E, T.bd[:], T.pu[:, y], True, True), ["bd", "pu%d" % y], eb + ["acc" + b], [b])
+            op("s", "sg" + p, lambda y=y, E=E: S.activation(T.sg[:, y], E, Act.Sigmoid, scale=4.0), eb, ["sg%d" % y], [b])
+            if p == "o":
+                op("v", "smo", lambda y=y, E=E: V.tensor_tensor(T.sg[:, y], E, T.sg[:, y], Op.mult), eb, ["sg%d" % y], [b])
+                op("v", "yyo", lambda y=y: V.tensor_tensor(T.yy[:, y], chosen(l, 1, "o"), T.sg[:, y], Op.mult), ["sg%d" % y, "vw"] + tags("wu%d" % l, "o"), ["y%d" % y])
+            else:
+                op("v", "sm" + p, lambda y=y, E=E: V.tensor_tensor(E, E, T.sg[:, y], Op.mult), ["sg%d" % y], eb, [b])
+                op("v", "yy" + p, lambda i=i, y=y, E=E: V.tensor_tensor(T.yy[:, y], E, src(1, i), Op.mult), eb + [have(l, "v", ranks[i])], ["y%d" % y], [b])
+            mix(l, "mix" + p, T.yy[:, y], ["y%d" % y])
+
     def tokens(l):
-        if "x" not in ADDS[l]:
-            mix(l, "mixx", T.sx[:], ["sx"])
-        op("s", "new", lambda: S.activation(T.sx[:], M, Act.Sigmoid, bias=T.less[:, 0:1], scale=2.0), 256, rs("pM_", 0, 5) + ["less"], ["sx", "mix%d" % (l + 1)], ["pM"])
+        mix(l, "mixx", T.sx[:], ["sx"])
+        done = rs("pM_", 0, 5) + ["less"]
+
+        def squash(out, s=slice(0, 256)):
+            return lambda: S.activation(out, T.pM[:, s], Act.Sigmoid, bias=T.less[:, 0:1], scale=2.0)
+
+        def stretch(out, s=slice(0, 256)):
+            return lambda: S.activation(out, T.sx[:, s], Act.Identity, bias=-1.0, scale=2.0)
         if l == NL - 1:
-            op("s", "new", lambda: S.activation(T.xo[:], T.sx[:], Act.Identity, bias=-1.0, scale=2.0), 256, ["sx"], ["xo"])
-            dma("s", "new", "oyx", [(T.yx[:], T.xo[:])], ["xo"], ["yx"], R["local"] + 0.4)
+            for k, s in enumerate((slice(0, 128), slice(128, 256))):
+                op("s", "new%d" % k, squash(T.sx[:, s], s), done + ["sx"], ["sx%d" % k], ["pM"])
+                op("vs"[k], "out%d" % k, stretch(T.xo[:, s], s) if k else (lambda s=s: V.tensor_scalar(T.xo[:, s], T.sx[:, s], 2.0, -1.0, Op.mult, Op.add)),
+                   ["sx%d" % k] + rs("pu", 0, 4), ["xo%d" % k])
+                dma("ys"[k], "out%d" % k, "oyx%d" % k, [(T.yx[:, s], T.xo[:, s])], ["xo%d" % k], ["yx%d" % k])
+            return
+        op("s", "new", squash(T.sx[:]), done, ["sx", "mix%d" % (l + 1)], ["pM"])
+        if l == NL - 2:
+            op("s", "newp", stretch(X), ["sx"], xb, ["pX"])
+            op("s", "news", stretch(T.xo[:]), ["sx"], ["xo"])
         else:
-            op("s", "newp", lambda: S.activation(X, M, Act.Sigmoid, bias=T.less[:, 0:1], scale=2.0), 256, rs("pM_", 0, 5) + ["less"], xb + ["mixp%d" % (l + 1)], ["pM", "pX"])
+            op("s", "newp", squash(X), done, xb + ["mixp%d" % (l + 1)], ["pM", "pX"])
 
     for l in range(NL):
         layer[0] = l
@@ -472,12 +426,12 @@ def rank_program(g, core, T, topo):
                 fused(c, "o")
             for h, how in (word.split(",") for word in MEET.split()):
                 for c, x in enumerate(how):
-                    times(c, h, "ff" if h == "m" else "qq", x)
-            op("t", "less", lambda: PE.matmul(T.pM[:, 510:512], T.mb[:], T.minus[:, 0:2], True, True), 64, ["mb", "minus"], blk("pM", 0, 8), ["pM"])
-            op("s", "less", lambda: S.activation(T.less[:], T.pM[:, 510:512], Act.Copy), 64, blk("pM", 0, 8), ["less", "mix0"], ["pM"])
-            op("s", "x", lambda: S.activation(X, T.xb[:], Act.Identity, bias=0.5, scale=0.5), 256, ["xb"], xb, ["pX"])
-            op("s", "prep", lambda: S.activation(T.m32[:], T.mb[:], Act.Copy), 128, ["mb"], ["m32"])
-            op("s", "prep", lambda: S.activation(T.sx[:], T.xb[:], Act.Identity, bias=0.5, scale=0.5), 256, ["xb"], ["sx"])
+                    times(c, h, h != "m", x)
+            op("t", "less", lambda: PE.matmul(T.pM[:, 510:512], T.mb[:], T.minus[:, 0:2], True, True), ["mb", "minus"], blk("pM", 0, 8), ["pM"])
+            op("s", "less", copy("s", T.less[:], T.pM[:, 510:512]), blk("pM", 0, 8), ["less", "mix0"], ["pM"])
+            op("s", "x", lambda: S.activation(X, T.xb[:], Act.Identity, bias=0.5, scale=0.5), ["xb"], xb, ["pX"])
+            op("s", "prep", copy("s", T.m32[:], T.mb[:]), ["mb"], ["m32"])
+            op("s", "prep", lambda: S.activation(T.sx[:], T.xb[:], Act.Identity, bias=0.5, scale=0.5), ["xb"], ["sx"])
         else:
             for h, how in (word.split(",") for word in KEYS[l].split()):
                 for c, x in enumerate(how):
@@ -485,21 +439,23 @@ def rank_program(g, core, T, topo):
                         fused(c, h)
                     else:
                         raw("s", c, h)
-                        times(c, h, how[c & 1::2])
-        halves = "rl" if l else "lr"
-        for h, b in zip(halves, ("pA", "pB")):
+                        times(c, h, how[c & 1::2] == "qq")
+        halves = list(zip("rl" if l else "lr", ("pA", "pB")))
+        for h, b in halves:
             winners(l, h, b)
-        for k, (h, b) in enumerate(zip(halves, ("pA", "pB"))):
-            count(l, k, h, b)
+        for k, (h, b) in enumerate(halves):
+            count(k, h, b)
         if l < NL - 1:
             names(l)
-        biases(l)
+            biases(l)
         for word in PICKS[l].split():
             pick(l, *word.split(","))
         for word in GIVES[l].split():
             give(l, word)
-        expert(l, "r", "pE")
-        expert(l, "l", "pG")
+        for h, b in (("r", "pE"), ("l", "pG")):
+            (narrow if l < NL - 1 else full)(l, h, b)
+        if l == NL - 1:
+            biases(l)
         tokens(l)
 
     issue(g, T, topo, core, calls)
@@ -508,7 +464,7 @@ def rank_program(g, core, T, topo):
 def arrange(calls):
     lastw, readers, before = {}, {}, []
     for i, c in enumerate(calls):
-        need = {lastw[r] for r in list(c["reads"]) + list(c["writes"]) + c.get("behind", []) if r in lastw}
+        need = {lastw[r] for r in list(c["reads"]) + list(c["writes"]) if r in lastw}
         for r in c["writes"]:
             need.update(readers.get(r, []))
         if "after" in c:
@@ -599,5 +555,5 @@ def issue(g, T, topo, core, calls):
             lastw[r], readers[r] = ev, []
         for b in c["banks"]:
             bank.setdefault(b, {})[q] = ev
-    for sem in sorted(count, key=lambda s: s in ("oyx", "oyb")):
+    for sem in sorted(count, key=lambda s: s[0] == "o"):
         wait("g", (sem, count[sem], {}, None))

import math
from concourse.bass import DstId, RemoteDMATransfer
from concourse.mybir import AluOpType as Op, ActivationFunctionType as Act

NL = 3
BF, F32, F16, I32, U16 = "bfloat16", "float32", "float16", "int32", "uint16"
SCRATCH = {
    "qall": ("sbuf", [128, 1024], BF), "qt": ("sbuf", [128, 1024], BF), "nmi": ("sbuf", [128, 256], I32),
    "nmh": ("sbuf", [128, 4, 64], F16), "nmn": ("sbuf", [128, 4, 64], F16), "off": ("sbuf", [128, 256], U16),
    "kw": ("sbuf", [128, 2048], BF), "uw": ("sbuf", [128, 2048], BF), "vw": ("sbuf", [128, 2048], BF),
    "xb": ("sbuf", [128, 256], BF), "mb": ("sbuf", [128, 128], BF), "m32": ("sbuf", [128, 128], F32),
    "less": ("sbuf", [128, 2], F32), "minus": ("sbuf", [128, 66], BF), "four": ("sbuf", [128, 64], BF),
    "xo": ("sbuf", [128, 256], F32), "sx": ("sbuf", [128, 256], F32),
    "rawk": ("sbuf", [128, 4, 1024], BF), "prod": ("sbuf", [128, 1024, 4], F16), "quick": ("sbuf", [128, 64, 4, 16], F16),
    "zh": ("sbuf", [128, 144], F16), "wb": ("sbuf", [128, 16, 16], BF), "wh": ("sbuf", [128, 16, 16], F16), "negh": ("sbuf", [128, 8, 16], F16),
    "sel": ("sbuf", [128, 8, 4, 16], F16), "selb": ("sbuf", [128, 8, 4, 16], BF), "seln": ("sbuf", [128, 8, 4, 16], BF),
    "bdb": ("sbuf", [128, 128], BF), "bd": ("sbuf", [128, 128], F32), "fold": ("sbuf", [128, 8], F32), "half": ("sbuf", [128, 8], BF),
    "wide": ("sbuf", [128, 32, 16], BF), "c1": ("sbuf", [128, 128], BF), "c2": ("sbuf", [128, 128], F16),
    "cbig": ("sbuf", [128, 256], BF), "hb": ("sbuf", [128, 256], BF), "ramp": ("sbuf", [128, 64], BF), "none": ("sbuf", [128, 128], F32),
    "top": ("sbuf", [128, 256], F32), "keep": ("sbuf", [128, 256], F32), "run": ("sbuf", [128, 256], F16),
    "w16": ("sbuf", [128, 2, 64], F16), "wu": ("sbuf", [128, NL, 64], U16), "wr": ("sbuf", [128, 2, 4, 64], F16), "hw": ("sbuf", [128, 2, 32], BF),
    "dv": ("sbuf", [128, 2, 8, 16], BF), "oh": ("sbuf", [128, 16, 8, 16], BF), "th": ("sbuf", [128, 16, 32, 4], BF),
    "bs": ("sbuf", [128, NL + 1, 2, 64], BF), "bout": ("sbuf", [128, 2, 64], F32),
    "i2": ("sbuf", [128, 2, 33], F32), "up": ("sbuf", [128, 2, 33], F16), "ee": ("sbuf", [128, 2, 33], F16),
    "near": ("sbuf", [128, NL * 2, 768], BF), "away": ("sbuf", [128, NL * 2, 512], BF), "came": ("sbuf", [128, NL * 2, 2, 256], BF),
    "pu": ("sbuf", [128, 4, 256], F32), "yy": ("sbuf", [128, 4, 256], F32), "sg": ("sbuf", [128, 4, 256], F32),
    "sn": ("sbuf", [128, 2, 32], F32), "sp": ("sbuf", [128, 2, 64], BF), "sq": ("sbuf", [128, 2, 128], BF),
    "pA": ("psum", [128, 512], F32), "pB": ("psum", [128, 512], F32), "pF": ("psum", [128, 8, 64], F32),
    "pX": ("psum", [128, 512], F32), "pM": ("psum", [128, 512], F32), "pE": ("psum", [128, 512], F32),
    "pG": ("psum", [128, 512], F32), "pQ": ("psum", [128, 1024], BF),
}
SEMAPHORES = (["cv", "cs", "ct", "cg", "sent", "lq", "lnm", "lke", "lb", "lx", "lm", "lu", "lv", "aqm", "aqa", "aqb", "oyx0", "oyx1", "oyb"]
              + ["aw%d" % l for l in range(2)] + ["bias%d" % l for l in range(2)]
              + ["a%d%s%s" % (l, k, h) for l in range(NL) for k in "uv" for h in "abm"])
ROUND64 = 1.5 * 2.0 ** 13
ROUND2048 = 1.5 * 2.0 ** 18
ROUND4096 = 1.5 * 2.0 ** 35
EDGE = math.log(4095.0)
RISE = 65536.0

QUERIES = "a b.m"
KEYS = ["r,qqqq l,ffff", "r,fqfq l,fqqq", "r,fqfq l,fqqq"]
EARLY, MEET = "r,ssss m,svsv", "m,dddd a,qqqq b,qqqq"
PICKS = ["ur,v vr,s ul,s vl,s", "ur,s vr,s ul,v vl,s", "ua,s ub,s vr,s um,v vm,s"]
GIVES = ["ua.ub.um va.vb.vm+", "ua.ub va.vb um vm", "ua ub um va vb vm"]
PAIRED = (0,)
ORDER = """
y0lq g0ramp v0wb y0lnm y0lke v0none v0cbig v0minus g0wb v0bdb v0four v0ramp v0zh*1 v0keep v0wide v0wh v0negh v0sel g0qa t0q1o
g0bdb*1 v0nm0 v0off*1 g0bdb v0q2o t0dn v0selb v0seln t0q3o g0qb.m v0bd g0late*1 v0k3m s0k2m v0zh s0k0m v0f2o s0k0r v0f3o v0f0o
s0k2r v0k1m t0q1a s0k3r v0q2a g0late*1 y0lm y0lx v0x2m y0lu y0lb y0lv v0x0m t0q3a t0q1b s0k1r v0x1m v0q2b v0x3m g0late v0f1o
t0q3b t0s0l v0x2b v0x0a t0s1l v0x0b s0x v0x2a v0x3b s0prep*1 v0x1b s0fold t0less v0x1a t0s0r v0x3a v0w1l t0s1r v0w2l v0c2 v0w3l
v0w1r s0prep v0up0 t0lo0 v0w5l v0w2r t0hi0 s0Ul t0ng0 v0w3r v0dv0 v0w4 v0w5r s0th0*1 v0up1 t0lo1 v0oh0*1 g0tell s0th0*1 v0Ur
t0ng1 s0th0*1 t0hi1 s0th0 v0oh0*1 s0th1*1 v0dv1 g0ua.ub.um v0oh0*1 s0th1*1 v0oh0 t0Tb v0oh1*1 t0q1m s0th1*1 v0oh1*1 t0sum0
v0oh1*1 s0th1 v0oh1 v0pul*1 s0less s0Vr v0half v0q2m t0sum1 t0Dl*1 s0Vl v0post*1 t0nA v0post*2 t0q3m v0pul t0Tu t0Te t0nB
v0post t0Dl v0pur*1 s0hb v0pur y0bias t0Dr*1 s0sgl v0nn t0Dr v0sml v0off t1dn s0sgr v0sdl t0Wl t0mixx

v1f2r s1k3r g0va.vb.vm+ v1f0r s1k1r v1x3r s0sql s1k2l t1s0r v1x1r v0smr v1f0l t1s1r s1k3l t0El v0sdr v1w1r s1k1l v1x2l t0Wr
v1w2r v1x3l t1s0l s0sqr v1w3r v1x1l t0Er v1w5r v0yyl*1 t1s1l v0yyl s1Ur v1up0 v0yyr*1 t1lo0 v1w1l s1Vr t1hi0 v0adl t1ng0
g1ua.ub v1w2l v0yyr t0mixl v1w3l s1th0*1 v1dv0 v0adr s1th0*1 v1up1 t1lo1 v1w4 s1th0*1 v1w5l v1oh0*1 t1ng1 v1oh0*1 s1th0 g1tell
v1Ul t1hi1 g1va.vb t0mixr s1th1*2 v1dv1 v1oh0*1 s1th1*1 g1um v1oh0 t1Tb v1oh1*1 s0newp v1oh1*1 t1sum0 v1oh1*1 s1th1 v1oh1
v1pul*1 s0new v1pur*1 t1sum1 v1pur t1Dr*1 v1post*1 t1Dr v1post*1 t1Dl*1 v1post*1 v1pul s1sgr t1Tu s1Vl t1Te t1nA v1post t1Dl
v1smr t1nB y1bias v1sdr s1sgl g1vm s2blo t1Wr t1mixx v1sml*1 s1hb v1sml s1sqr v1sdl v1nn t1Er t1Wl v1off t2dn v1yyr s1sql

s2k3r t1El v2f2r t1mixr*1 s2k1r v2f0r t1mixr s2k2l v2x3r v2x1r t2s0r v1yyl s2k3l t2s1r v2f0l s2k1l t1mixl*1 v2w1r t1mixl v2x2l
v2w2r v2x3l t2s0l v2w3r s1new v2x1l v2w5r v2up0 s1newp t2s1l s2Ua t2hi0 s2Ub t2lo0 v2w1l g2ua s1news t2ng0 v2w2l s2Vr g2ub
v2dv0 t2mixx v2w3l v2oh0*1 s2th0*1 v2w5l t2lo1 v2up1 v2oh0*1 g2va s2th0*1 v2Um t2hi1 s2th0*1 g2vb t2ng1 v2puo s2Vm g2um v2dv1
v2pua s2th1*1 t2Do v2oh1*1 g2vm s2th1*1 v2oh1*2 s2th0 v2pub t2Tb t2Da v2oh0 s2sgo t2Db s2th1*1 v2smo s2th1 t2sum0 v2pum s2sga
v2oh1 v2yyo s2sgb t2Dm v2smb t2sum1 v2sma s2sgm v2yyb t2mixo v2yya v2post*1 t2mixb v2smm v2post*2 t2mixa v2yym t2Tu t2Te
t2mixm v2post y2bias s2new0 s2new1 v2out0 s2out1*1 y2out0 s2out1
"""


def rank_program(g, core, T, topo):
    rank = T.rank_of(core)
    if rank is None:
        return
    N = len(T.cores)
    here = topo.cores_of(core)
    mate = [r for r in range(N) if r != rank and T.cores[r] in here][0]
    rem = [r for r in range(N) if T.cores[r] not in here]
    loc0, rem0 = min(rank, mate), min(rem)
    assert abs(rank - mate) == 1 and rem == [rem0, rem0 + 1]
    far_a, far_b = sorted(rem, key=lambda r: topo.die(T.cores[r]) != topo.die(core))
    assert topo.die(T.cores[far_a]) == topo.die(core) != topo.die(T.cores[far_b])
    e_off = topo.engines(core, T.cores[rem0])
    e_on = [e for e in topo.engines(core, T.cores[mate]) if e not in e_off]

    def part(es, i, n):
        k = len(es) // n
        return sum(1 << e for e in es[i * k:(i + 1) * k])

    calls, layer = [], [0]

    def note(kind, q, name, reads, writes, banks=(), **more):
        calls.append(dict(more, kind=kind, q=q, name=(layer[0], name), reads=reads, writes=writes, banks=banks))

    def op(q, name, fns, reads, writes, banks=()):
        note("op", q, name, reads, writes, banks, fns=fns if isinstance(fns, list) else [fns])

    def dma(q, name, sem, pairs, reads, writes):
        note("dma", q, name, reads, writes, sem=sem, pairs=pairs)

    def send(name, items, reads, lands):
        note("send", "g", name, reads, [], items=items)
        me = len(calls) - 1
        for sem, writes in lands:
            note("land", "", name, [], writes, sem=sem, n=sum(bin(m).count("1") for _r, m, s, _a, _b in items if s == sem), after=me)

    def parcels(hs):
        far, near = [h for h in hs if h[-1] != "m"], [h for h in hs if h[-1] == "m"]
        return [(span(h[-1])[0], part(e_on, near.index(h), len(near)) if h in near else part(e_off, far.index(h), len(far))) for h in hs]

    V, S, PE = g.vector, g.scalar, g.tensor
    ident, identh, shifth = T.wb[:, 0:8, :], T.wh[:, 0:8, :], T.wh[:, 7:15, :]

    def copy(q, out, in_):
        return (lambda: V.tensor_copy(out, in_)) if q == "v" else (lambda: S.activation(out, in_, Act.Copy))

    def bias_rows(t, half):
        return t[64 * half + 15:64 * half + 64:16, :]

    def span(h):
        return {"*": (0, 4), "l": (loc0, 2), "r": (rem0, 2), "o": (rank, 1), "m": (mate, 1), "a": (far_a, 1), "b": (far_b, 1)}[h]

    def rs(name, r0, n):
        return ["%s%d" % (name, r) for r in range(r0, r0 + n)]

    def tok(r0, n=1):
        return slice(256 * r0, 256 * (r0 + n))

    def col(h):
        r0, n = span(h)
        return slice(16 * r0, 16 * (r0 + n))

    def tags(name, h):
        return rs(name + "_", *span(h))

    def at(b, j, n):
        return T[b][:, j:j + n, :] if b == "pF" else T[b][:, 64 * j:64 * (j + n)]

    blk = rs

    mine = T.qall[:, tok(rank)]
    dma("y", "lq", "lq", [(mine, T.rq[:])], [], ["q%d" % rank])
    dma("y", "lnm", "lnm", [(T.nmi[:], T.nm[:])], [], ["nmi"])
    dma("y", "lke", "lke", [(T.kw[:], T.ke[:])], [], ["kw"])
    for ap, value, tag in [(T.bdb[:], 1.0, "bdb"), (T.wb[:], 1.0, "wb"), (T.cbig[:], ROUND2048, "cbig"), (T.minus[:], -1.0, "minus"),
                           (T.four[:], 4.0, "four"), (T.none[:], 0.0, "none"), (T.keep[:, 0::128], 0.0, "keep"), (T.wide[:], 0.5, "wide")]:
        op("v", tag, lambda ap=ap, value=value: V.memset(ap, value), [], [tag])
    op("g", "bdb", lambda: g.affine_select(T.bdb[:], T.bdb[:], [[-16, 8], [0, 16]], Op.is_ge, 0.0, 0, 1), ["bdb"], ["bdb"])
    op("g", "bdb", lambda: g.affine_select(T.bdb[:], T.bdb[:], [[16, 8], [0, 16]], Op.is_ge, 0.0, 15, -1), ["bdb"], ["bdb"])
    op("g", "wb", lambda: g.affine_select(T.wb[:], T.wb[:], [[0, 2], [-1, 128]], Op.is_equal, 0.0, 0, 1), ["wb"], ["wb"])
    for word in QUERIES.split():
        hs = word.split(".")
        send("q" + word, [(r, m, "aq" + h, mine, mine) for h, (r, m) in zip(hs, parcels(hs))], ["q%d" % rank], [("aq" + h, ["q%d" % span(h)[0]]) for h in hs])
    dma("y", "lb", "lb", [(T.bs[:, 0, half, :], bias_rows(T.ke, half)) for half in range(2)], ["q%d" % mate], ["b0"])
    for sem, out, in_, tag in [("lu", T.uw, T.ue, "uw"), ("lx", T.xb, T.x0, "xb"), ("lm", T.mb, T.mm, "mb"), ("lv", T.vw, T.ve, "vw")]:
        dma("y", sem, sem, [(out[:], in_[:])], ["q%d" % mate], [tag])
    op("g", "late", lambda: g.iota(T.c1[:], [[0, 8], [-64, 4], [0, 4]], 0, 0, allow_small_or_imprecise_dtypes=True), [], ["c1"])
    op("g", "ramp", lambda: g.iota(T.ramp[:], [[1, 32], [0, 2]], 0, 0, allow_small_or_imprecise_dtypes=True), [], ["ramp"])
    op("v", "ramp", lambda: V.tensor_scalar(T.ramp[:], T.ramp[:], RISE, None, Op.mult), ["ramp"], ["ramp"])
    for half in range(2):
        ap = T.wide[32 * half:32 * half + 32]
        op("g", "late", lambda ap=ap: g.affine_select(ap, ap, [[-1, 32], [0, 16]], Op.is_equal, 0.0, 0, 1), ["wide", "q%d" % mate], ["wide%d" % half])
    op("s", "fold", lambda: S.activation(T.fold[:], T.bdb[:, 0::16], Act.Sigmoid, bias=-128.0, scale=256.0), ["bdb"], ["fold"])
    for fn, read, tag in [
            (lambda: V.tensor_copy(T.off[:], T.nmi[:]), "nmi", "off"),
            ([lambda k=k: V.tensor_copy(T.sel[:, :, k, :], ident) for k in range(4)], "wb", "sel"),
            (lambda: V.tensor_scalar(T.zh[:], T.cbig[:, 0:144], 0.0, None, Op.mult), "cbig", "zh"),
            (lambda: V.tensor_copy(T.wh[:], T.wb[:]), "wb", "wh"),
            (lambda: V.tensor_copy(T.zh[:, 15:143:16], T.bdb[:, 0::16]), "bdb", "zh"),
            (lambda: V.tensor_copy(T.selb[:], T.sel[:]), "sel", "selb"),
            (lambda: V.tensor_scalar(T.seln[:], T.sel[:], -1.0, None, Op.mult), "sel", "seln"),
            (lambda: V.tensor_scalar(T.half[:], T.bdb[:, 0::16], -0.5, None, Op.mult), "bdb", "half"),
            (lambda: V.tensor_scalar(T.bd[:], T.bdb[:], 0.25, None, Op.mult), "bdb", "bd"),
            (lambda: V.tensor_scalar(T.negh[:], ident, -1.0, None, Op.mult), "wb", "negh"),
            (lambda: V.tensor_copy(T.nmh[:], T.nmi[:]), "nmi", "nm0"),
            (lambda: V.tensor_scalar(T.c2[:], T.c1[:], 0.25, ROUND64, Op.mult, Op.add), "c1", "c2")]:
        op("v", tag, fn, [read], [tag])

    def keys(c, h):
        r0, n = span(h)
        return T.kw[:].indirect(T.off[:, c * 64 + r0 * 16:c * 64 + (r0 + n) * 16])

    def fused(c, h):
        r0, n = span(h)
        op("v", "f%d%s" % (c, h), lambda: V.tensor_tensor(T.prod[:, tok(r0, n), c], keys(c, h), T.qall[:, tok(r0, n)], Op.mult),
           ["kw", "off"] + rs("q", r0, n), tags("prod%d" % c, h))

    def raw(q, c, h):
        op(q, "k%d%s" % (c, h), copy(q, T.rawk[:, c, tok(*span(h))], keys(c, h)), ["kw", "off"], tags("raw%d" % c, h))

    def times(c, h, runs, how="q"):
        r0, n = span(h)
        out = T.quick[:, col(h), c, :] if runs else T.prod[:, tok(r0, n), c]
        src, tag = (T.pQ, "pQ") if how == "q" else (T.qall, "q")
        op("v", "x%d%s" % (c, h), lambda: V.tensor_tensor(out, src[:, tok(r0, n)], T.rawk[:, c, tok(r0, n)], Op.mult),
           rs(tag, r0, n) + tags("raw%d" % c, h), tags("prod%d" % c, h), ["pQ"] if how == "q" else [])

    def stand(h):
        r0, n = span(h)
        pieces = [slice(c, c + 128) for c in range(256 * r0, 256 * (r0 + n), 128)]
        op("t", "q1" + h, [lambda s=s: PE.transpose(T.pQ[:, s], T.qall[:, s], ident) for s in pieces], ["wb"] + rs("q", r0, n), rs("pQ", r0, n), ["pQ"])
        op("v", "q2" + h, copy("v", T.qt[:, tok(r0, n)], T.pQ[:, tok(r0, n)]), rs("pQ", r0, n), rs("qt", r0, n), ["pQ"])
        op("t", "q3" + h, [lambda s=s: PE.transpose(T.pQ[:, s], T.qt[:, s], ident) for s in pieces], ["wb"] + rs("qt", r0, n), rs("pQ", r0, n), ["pQ"])

    def steps(l):
        nm = T.nmn if l else T.nmh
        op("t", "dn", [lambda c=c: PE.matmul(T.pX[:, 256 + c::4], identh, nm[:, c, :], c == 0, False) for c in range(4)]
           + [lambda c=c: PE.matmul(T.pX[:, 256 + c::4], T.negh[:], nm[:, c + 1, :], False, c == 2) for c in range(3)],
           ["wh", "negh", "nm%d" % l], blk("pX", 4, 4) + ["accpX"], ["pX"])

    def winners(l, h, b):
        cs = col(h)
        a, P = 4 * cs.start, T[b]
        how = dict(word.split(",") for word in KEYS[l].split())[h]
        for c in (0, 1):
            rhs = [T.quick[:, cs, c::2, i] if how[c::2] == "qq" else T.prod[:, 16 * cs.start + i:16 * cs.stop:16, c::2] for i in range(16)]
            op("t", "s%d%s" % (c, h), [lambda c=c: PE.matmul(P[:, c:128:2], ident, T.ramp[:], True, False)]
               + [lambda i=i, c=c, rhs=rhs: PE.matmul(P[:, c:128:2], T.zh[:, 15 - i:143 - i], rhs[i], False, i == 15) for i in range(16)],
               ["zh", "wb", "ramp"] + tags("prod%d" % c, h) + tags("prod%d" % (c + 2), h), [b + "0" if c else b + "1", "acc" + b], [b])
        both = blk(b, 0, 2)
        op("v", "w1" + h, lambda: V.tensor_tensor_scan(T.top[:, a:a + 128], T.none[:], P[:, 0:128], -RISE, Op.add, Op.max), both + ["none"], ["top" + b], [b])
        op("v", "w2" + h, lambda: V.tensor_tensor(T.keep[:, a + 1:a + 128], P[:, 1:128], T.top[:, a:a + 127], Op.is_le), both + ["top" + b, "keep"], ["keep" + b], [b])
        op("v", "w3" + h, lambda: V.tensor_tensor_scan(T.run[:, a:a + 128], T.keep[:, a:a + 128], T.pX[:, 256 + a:384 + a], 0.0, Op.mult, Op.add),
           ["keep" + b] + blk("pX", 4, 4), tags("run", h), ["pX"])
        op("v", "w5" + h, copy("v", T.wu[:, l, cs], won(h)), tags("run", h), tags("wu%d" % l, h))

    def won(h):
        return T.run[:, 4 * col(h).start + 3:4 * col(h).stop:4]

    def names(l):
        src, dst, sem = T.w16[:, l, :], T.wr[:, l, rank, :], "aw%d" % l
        op("v", "w4", copy("v", src, won("*")), tags("run", "*"), tags("w%d" % l, "*"))
        send("tell", [(r, m, sem, src, dst) for r, m in parcels(["a", "b", "m"])], tags("w%d" % l, "*"), [(sem, ["wr%d" % l])])
        NP, nb = at("pA", 4, 4), blk("pA", 4, 4)
        pairs = [(r, c) for r in range(N) if r != rank for c in range(4)]
        op("t", "nA", [lambda: PE.matmul(NP, identh, T.nmh[:], True, False), lambda: PE.matmul(NP, ident, T.cbig[:], False, False)]
           + [lambda c=c: PE.matmul(at("pA", 4 + c, 1), shifth, T.w16[:, l, :], False, False) for c in range(4)],
           ["wh", "wb", "nm0", "cbig"] + tags("w%d" % l, "*"), nb + ["accpA"], ["pA"])
        op("t", "nB", [lambda r=r, c=c: PE.matmul(at("pA", 4 + c, 1), shifth, T.wr[:, l, r, :], False, (r, c) == pairs[-1]) for r, c in pairs],
           ["wh", "wr%d" % l], nb + ["accpA"], ["pA"])
        op("s", "hb", lambda: S.activation(T.hb[:], NP, Act.Identity, bias=1023.5, scale=-1.0), nb, ["hb"], ["pA"])
        op("v", "nn", lambda: V.tensor_tensor(T.nmn[:], NP, T.hb[:], Op.add), nb + ["hb"], ["nmn", "nm%d" % (l + 1)], ["pA"])
        op("v", "off", copy("v", T.off[:], T.nmn[:]), ["nmn"], ["off"])

    F = T.pF[:, 0:2, 0:33]

    def turn(P, w, sel, alone=False):
        return [lambda j=j: PE.matmul(P[32 * j:32 * j + 32], w, sel[:, :, :, 4 * j:4 * j + 4], alone, alone) for j in range(4)]

    def count(k, h, b):
        H, hb = at(b, 2, 2), blk(b, 2, 2)
        op("v", "up%d" % k, lambda: V.tensor_scalar(T.hw[:, k], won(h), ROUND64 - 31.5, None, Op.add), tags("run", h), ["hw%d" % k])
        op("t", "hi%d" % k, turn(H, T.hw[:, k], T.selb, True), ["selb", "hw%d" % k], hb + ["acc" + b], [b])
        op("v", "dv%d" % k, lambda: V.tensor_tensor(T.dv[:, k], H, T.c1[:], Op.add), hb + ["c1"], ["dv%d" % k], [b])
        b = ("pF", "pA")[k]
        L, lb = at(b, 4, 2), blk(b, 4, 2)
        edge = T.pF[:, 4, 0:2] if k == 0 else T.pA[:, 256:258]
        op("t", "lo%d" % k, [lambda: PE.matmul(L, identh, T.c2[:], True, False)] + turn(L, won(h), T.sel),
           ["wh", "c2", "sel"] + tags("run", h), lb + ["acc" + b], [b])
        op("t", "ng%d" % k, turn(L, T.hw[:, k], T.seln) + [lambda: PE.matmul(edge, identh, T.zh[:, 0:2], False, True)],
           ["seln", "wh", "zh", "hw%d" % k], lb + ["acc" + b], [b])
        for u0 in range(0, 8, 2):
            op("v", "oh%d" % k, [lambda u=u: V.tensor_scalar(T.oh[:, 8 * k:8 * k + 8, u, :], T.dv[:, k], ROUND64 + 256.0 * u, 4096.0, Op.is_equal, Op.mult)
                                 for u in (u0, u0 + 1)], ["dv%d" % k], ["oh%d%d" % (k, u0)])
            op("s", "th%d" % k, [lambda u=u: S.activation(T.th[:, 8 * k:8 * k + 8, u::8, :], L, Act.Sigmoid, bias=-256.0 * u - EDGE, scale=128.0)
                                 for u in (u0, u0 + 1)], lb, ["th%d%d" % (k, u0)], [b])
        ends = [lambda: PE.matmul(F, ident, T.minus[:], k == 0, k == 1)]
        sums = [lambda gr=gr, i=i: PE.matmul(T.pF[32 * (gr % 4):32 * (gr % 4) + 32, gr // 4, 0:32], T.oh[:, 8 * k + gr, :, i::4], T.th[:, 8 * k + gr, :, i],
                                              False, False) for gr in range(8) for i in range(4)]
        op("t", "sum%d" % k, ends + sums if k == 0 else sums + ends,
           ["wb", "minus"] + ["%s%d%d" % (x, k, u) for x in ("oh", "th") for u in range(0, 8, 2)], blk("pF", 0, 2) + ["accpF"], ["pF"])

    def biases(l):
        last = l == NL - 1
        j = NL if last else l
        if last:
            op("s", "blo", lambda: S.activation(T.bs[:, NL], T.bs[:, l], Act.Identity, bias=-float(NL)), ["b%d" % l], ["b%d" % NL])
        new = T.bout[:] if last else T.bs[:, l + 1]
        FT, even, odd = at("pB", 4, 2), T.pB[:, 256:384:2], T.pB[:, 257:384:2]
        fb, tb = blk("pF", 0, 2), blk("pB", 4, 2) + ["accpB"]
        op("t", "Tb", [lambda: PE.matmul(FT, ident, T.bs[:, j], True, False), lambda: PE.matmul(odd, ident, T.four[:], False, False)],
           ["wb", "four", "b%d" % j], tb, ["pB"])
        op("v", "post", lambda: V.tensor_scalar(T.i2[:], F, ROUND4096, -ROUND4096, Op.add, Op.add), fb, ["i2"], ["pF"])
        op("v", "post", lambda: V.tensor_scalar(T.up[:], F, 2.0 ** -12, 1024.0, Op.mult, Op.add), fb, ["up"], ["pF"])
        op("v", "post", lambda: V.tensor_tensor(T.ee[:], F, T.i2[:], Op.subtract), fb + ["i2"], ["ee"], ["pF"])
        op("t", "Tu", [lambda: PE.matmul(odd, T.negh[:], T.up[:, :, 0:32], False, False), lambda: PE.matmul(odd, identh, T.up[:, :, 1:33], False, False)],
           ["wh", "negh", "up"], tb, ["pB"])
        op("t", "Te", [lambda: PE.matmul(odd, identh, T.ee[:, :, 1:33], False, False), lambda: PE.matmul(even, T.negh[:], T.ee[:, :, 0:32], False, True)],
           ["wh", "negh", "ee"], tb, ["pB"])
        op("v", "post", lambda: V.tensor_tensor(new, FT, T.bs[:, j], Op.max), tb + ["b%d" % j], ["bout" if last else "b%d" % (l + 1)], ["pB"])
        if last:
            dma("y", "bias", "oyb", [(T.yb[4 * half:4 * half + 4, :], T.bout[:, half, :]) for half in range(2)], ["bout"], ["yb"])
        else:
            dma("y", "bias", "bias%d" % l, [(bias_rows(T.kw, half), T.bs[:, l + 1, half, :]) for half in range(2)], ["b%d" % (l + 1)], ["kw", "kw%d" % (l + 1)])

    out_j, in_j = (2, 0) if rank < mate else (0, 2)

    def chosen(l, k, h):
        return (T.uw, T.vw)[k][:].indirect(T.wu[:, l, col(h)])

    def pick(l, what, q):
        kind, h = what
        k = "uv".index(kind)
        r0, n = span(h)
        out = T.away[:, 2 * l + k, tok(r0 - rem0, n)] if h in "rab" else T.near[:, 2 * l + k, {"l": tok(min(1, out_j), 2), "m": tok(out_j)}[h]]
        op(q, kind.upper() + h, copy(q, out, chosen(l, k, h)), [kind + "w"] + tags("wu%d" % l, h), tags("%s%dp" % (kind, l), h))

    def give(l, word):
        what = word.rstrip("+").split(".")
        items, reads, lands = [], ["kw%d" % (l + 1)] if word[-1] == "+" else [], []
        for (kind, h), (r, mask) in zip(what, parcels(what)):
            k, sem = 2 * l + "uv".index(kind), "a%d%s%s" % (l, kind, h)
            sides = (T.near[:, k, tok(out_j)],) * 2 if h == "m" else (T.away[:, k, tok(r - rem0)], T.came[:, k, rank - loc0])
            items.append((r, mask, sem) + sides)
            reads += tags("%s%dp" % (kind, l), h)
            lands.append((sem, tags("%s%dc" % (kind, l), h)))
        send(word, items, reads, lands)

    X, xb, M = at("pX", 0, 4), blk("pX", 0, 4), at("pM", 0, 4)
    mixes, mixed = [0] * NL, [0] * NL

    def mix(l, name, rhs, reads):
        def fn():
            mixed[l] += 1
            return PE.matmul(M, T.m32[:], rhs, mixed[l] == 1, mixed[l] == mixes[l])
        op("t", name, fn, ["m32", "mix%d" % l, "mixp%d" % l] + reads, ["pM_%d" % mixes[l]], ["pM"])
        mixes[l] += 1

    def columns(l, h):
        if h == "r":
            return [rem0, rem0 + 1], (lambda k, i, a=0, n=256: T.came[:, 2 * l + k, i, a:a + n] if n <= 256 else T.came[:, 2 * l + k]), [far_a - rem0, far_b - rem0]
        j0 = min(1, in_j)
        ranks = [rank if j == 1 else mate for j in (j0, j0 + 1)]
        return ranks, (lambda k, i, a=0, n=256: T.near[:, 2 * l + k, 256 * (j0 + i) + a:256 * (j0 + i) + a + n]), [ranks.index(rank), ranks.index(mate)]

    def have(l, kind, r):
        return "%s%d%s_%d" % (kind, l, "p" if r == rank else "c", r)

    def narrow(l, h, b):
        n = int(h == "l")
        ranks, src, order = columns(l, h)
        D, C, W = T[b][:, 0:32], T[b][:, 64:96], T[b][0:64, 128:256]
        for i in order:
            y = 2 * n + i
            op("v", "pu" + h, lambda i=i, y=y: V.tensor_tensor(T.pu[:, y], X, src(0, i), Op.mult), xb + [have(l, "u", ranks[i])], ["pu%d" % y], ["pX"])
            op("t", "D" + h, [fn for j in range(2) for fn in (
                lambda i=i, j=j: PE.matmul(D[:, 16 * i + 8 * j:16 * i + 8 * j + 8], src(0, i, 128 * j, 128), T.half[:], True, False),
                lambda i=i, y=y, j=j: PE.matmul(D[:, 16 * i + 8 * j:16 * i + 8 * j + 8], T.pu[:, y, 128 * j:128 * j + 128], T.fold[:], False, True))],
               ["fold", "half", "pu%d" % y], [b + "0"], [b])
        op("s", "sg" + h, lambda: S.activation(T.sn[:, n], D, Act.Sigmoid, scale=2.0), [b + "0"], ["sn" + h], [b])
        op("v", "sm" + h, lambda: V.tensor_tensor(T.sp[:, n, 0:32], D, T.sn[:, n], Op.mult), [b + "0", "sn" + h], ["sp" + h], [b])
        op("v", "sm" + h, lambda: V.tensor_tensor(C, D, T.sn[:, n], Op.mult), [b + "0", "sn" + h], [b + "1"], [b])
        op("v", "sd" + h, lambda: V.tensor_tensor(T.sp[:, n, 32:64], C, T.sp[:, n, 0:32], Op.subtract), [b + "1", "sp" + h], ["sl" + h], [b])
        op("t", "W" + h, lambda: PE.matmul(W, T.sp[:, n], ident, True, True), ["wb", "sp" + h, "sl" + h], blk(b, 2, 2), [b])
        op("s", "sq" + h, copy("s", T.sq[0:64, n], W), blk(b, 2, 2), ["sq" + h], [b])
        op("t", "E" + h, [lambda k=k: PE.matmul(at(b, 2 * k, 2), T.wide[0:64, 8 * k:8 * k + 8, :], T.sq[0:64, n], True, True) for k in range(4)],
           ["wide0", "wide1", "sq" + h], blk(b, 0, 8), [b])
        vs = [have(l, "v", r) for r in ranks]
        if l in PAIRED:
            first, second = order
            P, y = at(b, 4 * first, 4), 2 * n + 1
            op("v", "yy" + h, lambda: V.tensor_tensor(P, P, src(1, first), Op.mult), [vs[first]], blk(b, 4 * first, 4), [b])
            op("v", "yy" + h, lambda: V.tensor_tensor(T.yy[:, y], at(b, 4 * second, 4), src(1, second), Op.mult), [vs[second]] + blk(b, 4 * second, 4), ["y%d" % y], [b])
            op("v", "ad" + h, lambda: V.tensor_tensor(T.yy[:, y], P, T.yy[:, y], Op.add), blk(b, 4 * first, 4), ["y%d" % y], [b])
            mix(l, "mix" + h, T.yy[:, y], ["y%d" % y])
            return
        op("v", "yy" + h, lambda: V.tensor_tensor(T.yy[:, 2 * n:2 * n + 2], at(b, 0, 8), src(1, 0, 0, 512), Op.mult), blk(b, 0, 8) + vs, rs("y", 2 * n, 2), [b])
        for i in order:
            mix(l, "mix" + h, T.yy[:, 2 * n + i], ["y%d" % (2 * n + i)])

    def full(l, h, bank):
        ranks, src, order = columns(l, h)
        for i, p in zip(order, "ab" if h == "r" else "om"):
            y = 2 * int(h == "l") + i
            b, j = ("pB", 0) if p == "o" else (bank, 4 * i)
            E, eb = at(b, j, 4), blk(b, j, 4)
            if p == "o":
                op("v", "puo", lambda y=y: V.tensor_tensor(T.pu[:, y], chosen(l, 0, "o"), T.xo[:], Op.mult), ["xo", "uw"] + tags("wu%d" % l, "o"), ["pu%d" % y])
            else:
                op("v", "pu" + p, lambda i=i, y=y: V.tensor_tensor(T.pu[:, y], X, src(0, i), Op.mult), xb + [have(l, "u", ranks[i])], ["pu%d" % y], ["pX"])
            op("t", "D" + p, lambda y=y, E=E: PE.matmul(E, T.bd[:], T.pu[:, y], True, True), ["bd", "pu%d" % y], eb + ["acc" + b], [b])
            op("s", "sg" + p, lambda y=y, E=E: S.activation(T.sg[:, y], E, Act.Sigmoid, scale=4.0), eb, ["sg%d" % y], [b])
            if p == "o":
                op("v", "smo", lambda y=y, E=E: V.tensor_tensor(T.sg[:, y], E, T.sg[:, y], Op.mult), eb, ["sg%d" % y], [b])
                op("v", "yyo", lambda y=y: V.tensor_tensor(T.yy[:, y], chosen(l, 1, "o"), T.sg[:, y], Op.mult), ["sg%d" % y, "vw"] + tags("wu%d" % l, "o"), ["y%d" % y])
            else:
                op("v", "sm" + p, lambda y=y, E=E: V.tensor_tensor(E, E, T.sg[:, y], Op.mult), ["sg%d" % y], eb, [b])
                op("v", "yy" + p, lambda i=i, y=y, E=E: V.tensor_tensor(T.yy[:, y], E, src(1, i), Op.mult), eb + [have(l, "v", ranks[i])], ["y%d" % y], [b])
            mix(l, "mix" + p, T.yy[:, y], ["y%d" % y])

    def tokens(l):
        mix(l, "mixx", T.sx[:], ["sx"])
        done = rs("pM_", 0, 5) + ["less"]

        def squash(out, s=slice(0, 256)):
            return lambda: S.activation(out, T.pM[:, s], Act.Sigmoid, bias=T.less[:, 0:1], scale=2.0)

        def stretch(out, s=slice(0, 256)):
            return lambda: S.activation(out, T.sx[:, s], Act.Identity, bias=-1.0, scale=2.0)
        if l == NL - 1:
            for k, s in enumerate((slice(0, 128), slice(128, 256))):
                op("s", "new%d" % k, squash(T.sx[:, s], s), done + ["sx"], ["sx%d" % k], ["pM"])
                op("vs"[k], "out%d" % k, stretch(T.xo[:, s], s) if k else (lambda s=s: V.tensor_scalar(T.xo[:, s], T.sx[:, s], 2.0, -1.0, Op.mult, Op.add)),
                   ["sx%d" % k] + rs("pu", 0, 4), ["xo%d" % k])
                dma("ys"[k], "out%d" % k, "oyx%d" % k, [(T.yx[:, s], T.xo[:, s])], ["xo%d" % k], ["yx%d" % k])
            return
        op("s", "new", squash(T.sx[:]), done, ["sx", "mix%d" % (l + 1)], ["pM"])
        if l == NL - 2:
            op("s", "newp", stretch(X), ["sx"], xb, ["pX"])
            op("s", "news", stretch(T.xo[:]), ["sx"], ["xo"])
        else:
            op("s", "newp", squash(X), done, xb + ["mixp%d" % (l + 1)], ["pM", "pX"])

    for l in range(NL):
        layer[0] = l
        steps(l)
        if l == 0:
            for h in "omab":
                stand(h)
            for h, how in (word.split(",") for word in EARLY.split()):
                for c, q in enumerate(how):
                    raw(q, c, h)
            for c in range(4):
                fused(c, "o")
            for h, how in (word.split(",") for word in MEET.split()):
                for c, x in enumerate(how):
                    times(c, h, h != "m", x)
            op("t", "less", lambda: PE.matmul(T.pM[:, 510:512], T.mb[:], T.minus[:, 0:2], True, True), ["mb", "minus"], blk("pM", 0, 8), ["pM"])
            op("s", "less", copy("s", T.less[:], T.pM[:, 510:512]), blk("pM", 0, 8), ["less", "mix0"], ["pM"])
            op("s", "x", lambda: S.activation(X, T.xb[:], Act.Identity, bias=0.5, scale=0.5), ["xb"], xb, ["pX"])
            op("s", "prep", copy("s", T.m32[:], T.mb[:]), ["mb"], ["m32"])
            op("s", "prep", lambda: S.activation(T.sx[:], T.xb[:], Act.Identity, bias=0.5, scale=0.5), ["xb"], ["sx"])
        else:
            for h, how in (word.split(",") for word in KEYS[l].split()):
                for c, x in enumerate(how):
                    if x == "f":
                        fused(c, h)
                    else:
                        raw("s", c, h)
                        times(c, h, how[c & 1::2] == "qq")
        halves = list(zip("rl" if l else "lr", ("pA", "pB")))
        for h, b in halves:
            winners(l, h, b)
        for k, (h, b) in enumerate(halves):
            count(k, h, b)
        if l < NL - 1:
            names(l)
            biases(l)
        for word in PICKS[l].split():
            pick(l, *word.split(","))
        for word in GIVES[l].split():
            give(l, word)
        for h, b in (("r", "pE"), ("l", "pG")):
            (narrow if l < NL - 1 else full)(l, h, b)
        if l == NL - 1:
            biases(l)
        tokens(l)

    issue(g, T, topo, core, calls)


def arrange(calls):
    lastw, readers, before = {}, {}, []
    for i, c in enumerate(calls):
        need = {lastw[r] for r in list(c["reads"]) + list(c["writes"]) if r in lastw}
        for r in c["writes"]:
            need.update(readers.get(r, []))
        if "after" in c:
            need.add(c["after"])
        before.append(need - {i})
        for r in c["reads"]:
            readers.setdefault(r, []).append(i)
        for r in c["writes"]:
            lastw[r], readers[r] = i, []
    steps, order, done = {}, [], set()
    for i, c in enumerate(calls):
        if c["kind"] != "land":
            steps.setdefault("%s%d%s" % (c["q"], *c["name"]), []).append(i)

    def put(i):
        if i not in done:
            done.add(i)
            for j in sorted(before[i]):
                put(j)
            order.append(calls[i])
            for j, c in enumerate(calls):
                if c.get("after") == i:
                    put(j)
    for word in ORDER.split():
        name, _, n = word.partition("*")
        rest = steps.get(name, [])
        for _ in range(min(int(n or 99), len(rest))):
            put(rest.pop(0))
    for i in range(len(calls)):
        put(i)
    return order


def issue(g, T, topo, core, calls):
    Q = {"v": g.vector, "s": g.scalar, "t": g.tensor, "g": g, "y": g.sync}
    known = {q: {} for q in Q}
    count, lastw, readers, bank = {}, {}, {}, {}

    def wait(q, ev):
        sem, n, snap, _src = ev
        if known[q].get(sem, 0) >= n:
            return
        Q[q].wait_ge(T.sem[sem], n)
        known[q][sem] = n
        for k, m in snap.items():
            if known[q].get(k, 0) < m:
                known[q][k] = m

    for c in arrange(calls):
        q, kind, reads, writes = c["q"], c["kind"], c["reads"], c["writes"]
        if kind == "land":
            count[c["sem"]] = c["n"]
            ev, reads = (c["sem"], c["n"], {}, c["sem"]), []
        else:
            src = q if kind == "op" else kind
            need = [lastw[r] for r in reads if r in lastw]
            for r in writes:
                need += [ev for ev in [lastw.get(r)] + readers.get(r, []) if ev and (ev[3], src) != ("t", "t")]
            for b in c["banks"]:
                need += [ev for o, ev in bank.get(b, {}).items() if o != q]
            if c["name"][1] == "late" and "cg" in count:
                need.append(("cg", count["cg"], {}, "g"))
            for ev in sorted(need, key=lambda ev: -ev[1]):
                wait(q, ev)
            if kind == "op":
                sem = "c" + q
                for f in c["fns"][:-1]:
                    f()
                c["fns"][-1]().then_inc(T.sem[sem], 1)
                count[sem] = count.get(sem, 0) + 1
            elif kind == "dma":
                sem = c["sem"]
                for out, in_ in c["pairs"]:
                    Q[q].dma_start(out, in_).then_inc(T.sem[sem], 16)
                count[sem] = 16 * len(c["pairs"])
            else:
                sem, tr = "sent", []
                for r, m, s, a, b in c["items"]:
                    rid, pid = topo.addr(T.cores[r], core)
                    tr.append(RemoteDMATransfer(dst_ids=[DstId(rid=rid, pnc=pid)], dma_engine_mask=m, remote_sem=T.sem[s], src=a, dst=b))
                    count[sem] = count.get(sem, 0) + bin(m).count("1")
                g.remote_dma_fused(tr, local_sem=T.sem[sem])
                reads, writes = [], [sem]
            ev = (sem, count[sem], dict(known[q]), src)
        for r in reads:
            readers.setdefault(r, []).append(ev)
        for r in writes:
            lastw[r], readers[r] = ev, []
        for b in c["banks"]:
            bank.setdefault(b, {})[q] = ev
    for sem in sorted(count, key=lambda s: s[0] == "o"):
        wait("g", (sem, count[sem], {}, None))
